import numpy as np, ml_dtypes
CORES = [35,38,43,46]
N = 4
BF = ml_dtypes.bfloat16
W, K, P, RO, LIM = 8192, 16, 256, 6, 72
def hashed(u, v):
    u = u & 4095; v = v & 4095
    return ((u * v >> 5) + 37 * u) & (W - 1)
def probe(w, v):
    s = np.matmul(w, v.astype(np.float32)).astype(np.int64)
    return hashed(s[:, :, 0], s[:, :, 1])
def masks(rng, size):
    o = np.argsort(np.argsort(rng.random((N, 8, 16, K)), axis=2), axis=2)
    return (o < size[:, :, None, :]).astype(np.int32)
def parts(rng):
    x = rng.integers(0, 256, (N, 8, 16, W), dtype=np.uint8).astype(np.int32)
    return x, masks(rng, rng.integers(4, 12, (N, 8, K))), rng.integers(0, 256, (N, 8, 16, P)), rng.integers(0, 256, (N, 8, 16, 2))
def pack(x, m, z, w):
    return {a: np.ascontiguousarray(v.reshape(N, 128, n)).astype(np.float32).astype(BF) for a, v, n in (("xr", x, W), ("m0", m, K), ("z0", z, P), ("wt", w, 2))}
def setup_inputs(rng):
    return pack(*parts(rng))
def setup_inputs_spread(rng):
    def uneven(n):
        v = (np.exp2(8 * rng.random((N, 8, 1, n))) * rng.random((N, 8, 16, n))).astype(np.int32)
        return np.where(rng.random((N, 8, 1, n)) < 0.5, v, 255 - v)
    lo = rng.choice(np.array([0, 2, 5]), (N, 8, 1))
    return pack(uneven(W), masks(rng, lo + ((17 - lo) * rng.random((N, 8, K))).astype(np.int64)), uneven(P), np.exp2(8 * rng.random((N, 8, 16, 2))).astype(np.int64))
def setup_inputs_ends(rng):
    def two(n): return 255 * rng.integers(0, 2, (N, 8, 16, n), dtype=np.int32)
    x, z, w = two(W), two(P), two(2); m = rng.integers(0, 2, (N, 8, 16, K))
    s = 255 * rng.integers(0, 2, (8, 8, 1)); s[7] = 255
    z[N - 1, :, :8] = s; x[N - 1, :, :8] = 255 - s
    z[1, 7, :8] = 255; x[1, 7, :8] = 0
    for q, g in [(N - 1, g) for g in range(8)] + [(1, 7)]:
        a = rng.integers(0, 8, K); b = (a + rng.integers(1, 8, K)) % 8
        m[q, g, a, np.arange(K)] = 1; m[q, g, b, np.arange(K)] = 1
    m[1, 7, :, K - 1] = 0; m[1, 7, 15, K - 1] = 1
    w[N - 1, 7] = 255; m[N - 1, 7, :, 0] = 1; m[N - 1, 7, :, K - 1] = 1
    for i in (0, 1, 6, P - 1): z[N - 1, 7, :, i] = 255
    x[N - 1, 7, :, int(hashed(16 * 255 * 255, 16 * 255 * 255))] = 0
    for i in (0, 3, P - 1): z[0, 7, :, i] = 0
    x[0, 7, :, 0] = 0; m[0, 6, :, K - 1] = 0
    for g, e in ((7, 0), (5, 1)):
        w[2, g, :, e] = 255; w[2, g, :, 1 - e] = 255 * (rng.permutation(16) < rng.integers(1, 16))
        m[2, g, :, 0] = 1; x[2, g, 0] = 0
        for i in (0, 3, P - 1): z[2, g, :, i] = 255
        x[2, g, :, int(hashed(255 * int(np.sum(w[2, g, :, 0])), 255 * int(np.sum(w[2, g, :, 1]))))] = 255
    x[2, 6, 14:16] = 0; z[2, 6, 14:16, :8] = 255
    m[2, 6, :, 0] = 0; m[2, 6, 14] = 0; m[2, 6, 14:16, 0] = 1
    return pack(x, m, z, w)
def setup_inputs_corners(rng):
    x, m, z, w = parts(rng); idx = np.concatenate([np.arange(0, P, 2), np.array([P - 1])])
    t = np.argwhere(hashed(np.arange(256)[:, None], np.arange(256)[None, :]) == W - 1)
    for q in range(N):
        order = rng.permutation(8)
        want = {0: 0, 1: 7, N - 2: 0, N - 1: 4}.get(q)
        if want is not None:
            i = int(np.argmax(order == want)); order[i] = order[7]; order[7] = want
        for g in range(8):
            a, b, c, e = x[q, g], m[q, g], z[q, g], w[q, g]; kind = int(order[g])
            if kind == 0: b[:, 0] = 0
            if kind == 1: b[:] = 1
            if kind == 2:
                b[:] = 1; b[:, K - 1] = 0; b[15, K - 1] = 1
            if kind == 3:
                a[:] = rng.integers(250, 256, a.shape); c[:] = rng.integers(0, 6, c.shape)
                b[:] = np.argsort(np.argsort(rng.random((16, K)), axis=0), axis=0) < rng.integers(2, 4, (1, K))
            if kind == 4:
                e[:] = 0; e[0, 0] = 1; e[1, 1] = 1; b[0:2] = 1
                p = t[rng.integers(0, len(t), len(idx))]; c[0, idx] = p[:, 0]; c[1, idx] = p[:, 1]; c[0, 1] = 0
            if kind == 5:
                e[:] = 0; e[0] = 15; e[1] = 27; b[0:2] = 1; c[0, idx] = 255; c[1, idx] = 10
            if kind == 6:
                a[:] = 128; c[:] = 128 + rng.choice(np.array([-LIM - 1, -LIM, LIM, LIM + 1]), c.shape)
    p = t[rng.integers(0, len(t))]; odd = np.arange(2 * int(rng.integers(0, P // 4)) + 1, P, 2)
    m[N - 1, 7, :, 0] = 0; m[N - 1, 7, 0:2, 0] = 1; x[N - 1, 7, 0:2, W - 1] = p
    z[N - 1, 7, 0] = 0; z[N - 1, 7, 0, odd] = p[0]; z[N - 1, 7, 1, odd] = p[1]
    z[N - 2, 7, 0] = p[0]; z[N - 2, 7, 1] = p[1]; x[N - 2, 7, :, 0] = 0
    o = rng.permutation(256)[:P]
    w[1, 7] = 0; w[1, 7, 0, 0] = 1; m[1, 7, :, 0] = 0; m[1, 7, 0, 0] = 1; z[1, 7, 0] = o
    z[0, 7, 0] = o[P - 1]; x[0, 7, :, 0] = 0
    return pack(x, m, z, w)
def setup_inputs_crowd(rng):
    x, m, z, w = parts(rng); role = rng.permutation(N)
    for q in range(N):
        r = int(role[q]); k = rng.permutation(8)
        if r == 1: k = np.roll(k, 4 - int(np.argmax(k == rng.integers(3, 5))))
        if r < 3: x[q] = rng.integers(200, 256, (8, 16, W))
        if r < 2: z[q] = rng.integers(0, 101, (8, 16, P))
        if r == 2: z[q] = rng.integers(200, 256, (8, 16, P))
        w[q, k[0]] = 0; w[q, k[1]] = 0
        for g in k[2:4]:
            w[q, g] = 0; w[q, g, 0] = 1; m[q, g, 0] = 1
            c = int(rng.integers(0, 100)) if r < 2 else int(rng.integers(200, 255))
            z[q, g, 0] = c; z[q, g, 0, int(rng.integers(0, P))] = c + 1
        if r == 1: z[q, k[4], :, int(rng.integers(0, P))] = 210
        if r == 2: z[q, k[4], :, int(rng.integers(0, P))] = 50
    return pack(x, m, z, w)
def check_inputs(d):
    bad = []
    for k, lo, hi in (("xr", 0, 255), ("m0", 0, 1), ("z0", 0, 255), ("wt", 0, 255)):
        a = np.asarray(d[k]).astype(np.float32)
        if not (np.min(a) >= lo and np.max(a) <= hi): bad.append("range of " + k)
        elif np.any(a != np.floor(a)): bad.append("whole numbers in " + k)
    return bad
def reference(xr, m0, z0, wt):
    X = xr.astype(np.float32).astype(np.int16).reshape(N, 8, 16, W)
    M = np.repeat(m0.astype(np.float32).astype(np.int16).reshape(N, 8, 16, K)[..., None], P, axis=4)
    z = z0.astype(np.float32).astype(np.int16).reshape(N, 8, 16, P)
    w = np.ascontiguousarray(wt.astype(np.float32).reshape(N, 8, 16, 2).transpose(0, 1, 3, 2))
    A = np.zeros(N, np.int64); kk = np.arange(K)[None, None, :, None]; steps = []
    for t in range(RO):
        zk = z[:, :, :, None, :]
        h = probe(w, (M * zk).reshape(N, 8, 16, K * P))
        Xh = np.take_along_axis(X, h[:, :, None, :], 3).reshape(N, 8, 16, K, P)
        F = M * (np.abs(Xh - zk) > LIM)
        ok = np.add.reduce(F, axis=2, dtype=np.int16) <= (1 + (A & 1))[:, None, None, None]
        j = np.where(np.any(ok, axis=2), np.argmax(ok, axis=2), K)
        first = F * (np.add.accumulate(F, axis=2, dtype=np.int16) == 1)
        U = np.max(first * (kk < j[:, :, None, :])[:, :, None], axis=3)
        hit = (j < K)[:, :, None, :]; s = np.where(j < K, j, 0)[:, :, None, None, :]
        U = np.maximum(U, hit * np.take_along_axis(M, s, 3)[:, :, :, 0])
        xs = np.take_along_axis(Xh, s, 3)[:, :, :, 0]
        new = np.where(hit, np.abs(z - xs), (z + xs) >> 1)
        down = (kk[:, :, 1:] <= j[:, :, None, :])[:, :, None]
        M = np.concatenate([U[:, :, :, None], np.where(down, M[:, :, :, :-1], M[:, :, :, 1:])], axis=3)
        if t < RO - 1:
            place = probe(w, U * z)
            for q in range(N):
                for g in range(8):
                    v, i = np.unique(place[q, g], return_index=True)
                    X[q, g][:, v] = z[q, g][:, i]
        A = np.add.reduce((j == K).astype(np.int64), axis=(1, 2))
        steps.append(new); z = np.roll(new, 1, axis=0)
    return {"ym": M.reshape(N, 128, K * P).astype(np.float32).astype(BF), "yz": np.stack(steps, axis=3).reshape(N, 128, RO * P).astype(np.float32).astype(BF)}

@@ -1,0 +1,675 @@
+from concourse.mybir import AluOpType as ALU, AxisListType, ActivationFunctionType as AF
+
+NC = 2
+PC = 256 // NC
+CC = PC // 16
+RS = 16 * PC
+RO = 6
+BIG = 2.0 ** 40
+WIN = [(0, 3), (4, 6), (7, 9), (10, 12), (13, 15)]
+KG = [(6, 10), (10, 13), (13, 16), (0, 3), (3, 6)]
+HWM = PC + 5 * CC
+
+BF, F32, I32, U16 = "bfloat16", "float32", "int32", "uint16"
+_S = dict(
+    X=(8208, BF), Xh=(8192, BF), Mw=(8192, BF), e=(NC * 21 * PC, BF), G=(NC * 21 * PC, BF),
+    zin=(6 * 256, BF), yzb=(6 * 256, BF), ymb=(4096, BF), m0s=(16, BF), wts=(16, BF),
+    MZ=(NC * 5 * PC, BF), TH=(NC * 5 * PC, BF), I1=(NC * 2 * HWM, I32), I2=(NC * HWM, I32), off=(NC * HWM, U16),
+    W=(512, BF), MW=(512, BF), H=(512, BF), Hv=(512, BF), Cq=(5 * 512, BF), sel=(512, BF), one=(PC, BF),
+    bot=(256, BF), miss=(256, BF), mcnt=(8, F32), sc=(256, F32), idx=(16, U16), xs=(256, BF), ms=(256, BF),
+    b2=(256, I32), t1=(256, F32), e1=(256, I32), UZ=(256, BF), J1=(32, I32), J2=(16, I32), J3=(32, I32), hl=(32, BF),
+    aD=(256, F32), sD=(256, F32), xo=(32, U16), ai=(8, I32), thr=(8, F32),
+    al=(512, BF), rk=(512, BF), Es=(15 * 256, BF), Ed=(5 * 256, BF), to=(80, U16),
+    pi=(8, I32), col=(16, F32), Dn=(128, F32), Gn=(128, F32), Rn=(256, F32), Nn=(144, F32), N16=(256, F32),
+    Id=(128, BF), O=(128, BF), E=(144, BF), A=(144, BF), B=(144, BF), SE=(144, BF), RE=(144, BF), KE=(144, BF),
+    OM=(128, BF), AM=(128, BF), BM=(128, BF), CM=(2048, BF), SM=(2048, BF), mf=(32, F32), wf=(8, F32),
+    pw=(64, F32), pc=(64, F32), dl=(256, F32), Wn=(16, F32), Lq=(640, BF), Ld=(640, BF),
+    BI=(128, BF), nBO=(128, BF), I2O=(128, BF), QO=(128, BF), QI=(128, BF), nI=(128, BF), n5I=(128, BF), n5O=(128, BF),
+    Os=(128, BF), OK=(128, BF), Tl=(128, BF), TB=(128, BF), RSm=(128, BF), RDm=(128, BF), Zc=(128, BF),
+    Dm=(15 * 128, BF), S1=(16, F32), S2=(16, F32), Ci=(PC, BF), Kx=(256, BF), Kn=(256, F32), Cd=(256, BF), Ct=(5 * CC, BF),
+    Af=(128, F32), Cm=(PC, BF), Oa=(128, BF), Ob=(128, BF), K4=(128, BF), K8=(128, BF), JF=(32, F32), MT=(128, BF), su=(512, F32), F1=(NC * 2 * HWM, F32),
+)
+SCRATCH = {k: ("sbuf", [128, n], d) for k, (n, d) in _S.items()}
+for _b in range(8):
+    SCRATCH["P%d" % _b] = ("psum", [128, 512], F32)
+NDMA = 20
+SEMAPHORES = (["cv", "ca", "cp", "cg", "sent"] + ["d%d" % k for k in range(NDMA)]
+              + ["r%d_%d" % (t, c) for t in range(1, RO) for c in range(NC)])
+
+CY, PCY, LAT, RLAT, DLAT = 1.0, 0.45, 80.0, 2500.0, 2200.0
+GF, SF = 1.56, 3.8
+BON1, BON2, ONLY, FM, SU, SUB, DF = 1000.0, 5000.0, 0, 1, 3, 2, 4
+MZA, UZA, FJ = 0, 0, 0
+BONA, BONH, BON3, BON4, BON5, BON6 = 0.0, 0.0, 2000.0, 2000.0, 2000.0, 0.0
+ITER, PB, STEP = 100, 20, 300.0
+NG, INIT, ALTP, SLACK, GAM = 4, 0, 2000.0, 100.0, 50.0
+
+
+def R(n, a, b, s=1):
+    return (n, a, b, s)
+
+
+def width(r):
+    return (r[2] - r[1] + r[3] - 1) // r[3]
+
+
+def two(*rs):
+    return all(r[0] in _S and _S[r[0]][1] in (BF, U16) for r in rs)
+
+
+def build():
+    ops = []
+    bonus = [0.0]
+
+    def add(eng, call, rd, wr, cost, **kw):
+        ops.append(dict(eng=eng, call=call, rd=[r for r in rd if isinstance(r, tuple)], wr=wr, cost=cost, bonus=bonus[0], **kw))
+
+    def vc(n):
+        return 45.0 + max(40.0, n) * CY
+
+    def ts(o, i, s1, op0, s2=None, op1=None):
+        add("v", ("ts", o, i, s1, s2, op0, op1), [i, s1, s2], [o], vc(width(o) * (0.5 if two(o, i) else 1)))
+
+    def tt(o, a, b, op):
+        ps = a[0] not in _S or b[0] not in _S
+        add("v", ("tt", o, a, b, op), [a, b], [o], vc(width(o) * (1 if ps else 2)))
+
+    def cp(o, i):
+        add("v", ("cp", o, i), [i], [o], vc(width(o) * (0.5 if two(o, i) else 1)))
+
+    def ms(o, v):
+        add("v", ("ms", o, v), [], [o], vc(width(o) * 0.5))
+
+    def scan(o, d0, d1, init, op0, op1):
+        add("v", ("scan", o, d0, d1, init, op0, op1), [d0, d1], [o], vc(width(o)))
+
+    def red(o, i):
+        add("v", ("red", o, i), [i], [o], vc(width(i)))
+
+    def act(o, i, f, bias=0.0, scale=1.0, acc=None):
+        add("a", ("act", o, i, f, bias, scale, acc), [i, bias, scale], [o] + ([acc] if acc else []), vc(width(o)) + 30)
+
+    def either(fa, fv):
+        fa()
+        fv()
+        v, a = ops.pop(), ops.pop()
+        ops.append(dict(a, rd=a["rd"] + v["rd"], alt={"a": (a["call"], a["cost"]), "v": (v["call"], v["cost"])}))
+
+    def gat(o, win, offs, only=False):
+        if only:
+            return add("a", ("gat", "a", o, win, offs), [win, offs], [o], 60 + GF * CY * width(o))
+        either(*[lambda e=e: add(e, ("gat", e, o, win, offs), [win, offs], [o], 60 + GF * CY * width(o)) for e in "av"])
+
+    def lin(o, i, scale, bias=0.0):
+        either(lambda: act(o, i, AF.Identity, bias=bias, scale=scale), lambda: ts(o, i, scale, ALU.mult, bias, ALU.add))
+
+    def iota(o, pat, base, cm):
+        add("g", ("iota", o, pat, base, cm), [], [o], 130 + 2 * CY * width(o))
+
+    def mm(groups, first=True, last=True, f=1):
+        rd, cost, calls = [], 30.0, []
+        for o, terms in groups:
+            for k, tm in enumerate(terms):
+                oo = tm[2] if len(tm) > 2 else o
+                calls.append((oo, tm[0], tm[1], first and k == 0, last and k == len(terms) - 1))
+                rd += [tm[0], tm[1]]
+                cost += max(64, width(tm[1])) * PCY * f
+        add("p", ("mm", calls), rd, [o for o, _ in groups], cost, first=first, last=last, bank=groups[0][0][0])
+
+    nd = [0]
+
+    def dma(o, i, rd, wr, nbytes):
+        add("s", ("dma", o, i, nd[0]), rd, wr, 60.0, lat=DLAT + nbytes / 180.0)
+        nd[0] += 1
+
+    def full(n):
+        return R(n, 0, 128)
+
+    def c1(n, k):
+        return R(n, k, k + 1)
+
+    def view(n, r):
+        return R(n, 15 - r, 143 - r)
+
+    dma(R("zin", 0, 256), ("z0", 0, 256), [], [R("zin", 0, 256)], 65536)
+    dma(R("wts", 0, 2), ("wt", 0, 2), [], [R("wts", 0, 2)], 512)
+    dma(R("m0s", 0, 16), ("m0", 0, 16), [], [R("m0s", 0, 16)], 4096)
+    for k in range(2):
+        r = R("X", 16 + 4096 * k, 16 + 4096 * (k + 1))
+        dma(r, ("xr", 4096 * k, 4096 * (k + 1)), [], [r], 1 << 20 + k)
+    for ch in range(NC * INIT):
+        for n in ("Xh", "Mw"):
+            r = R(n, 2 * RS * ch + RS, 2 * RS * (ch + 1))
+            dma(r, ("xr", 0, RS), [R("X", 16, 8208)], [r], 1 << 20)
+
+    iota(c1("pi", 0), [[0, 1]], 0, 1)
+    iota(full("Gn"), [[16, 8], [0, 16]], 0, 0)
+    iota(R("Nn", 0, 144), [[1, 144]], -15, 0)
+    iota(full("Dn"), [[1, 128]], 0, -1)
+    iota(R("Rn", 0, 256), [[0, 16], [1, 16]], 0, 0)
+    iota(R("N16", 0, PC), [[16, PC]], 32768, 0)
+    iota(R("Ct", 0, 5 * CC), [[0, 5], [256, CC]], 0, 0)
+    ts(c1("pi", 1), c1("pi", 0), 15, ALU.bitwise_and)
+    ts(c1("pi", 2), c1("pi", 0), 112, ALU.bitwise_and)
+    cp(R("col", 0, 3), R("pi", 0, 3))
+    rc, gc = c1("col", 1), c1("col", 2)
+    ts(full("O"), full("Gn"), gc, ALU.is_equal)
+    ts(R("E", 0, 144), R("Nn", 0, 144), gc, ALU.is_equal)
+    ts(full("Id"), full("Dn"), 0.0, ALU.is_equal)
+    cp(R("wf", 0, 2), R("wts", 0, 2))
+    for g in range(8):
+        ts(R("OM", 16 * g, 16 * g + 16), R("m0s", 0, 16), c1("O", 16 * g), ALU.mult)
+    lin(full("AM"), full("OM"), c1("wf", 0))
+    lin(full("BM"), full("OM"), c1("wf", 1))
+    lin(R("A", 0, 144), R("E", 0, 144), c1("wf", 0))
+    lin(R("B", 0, 144), R("E", 0, 144), c1("wf", 1))
+    cp(R("mf", 16, 32), R("m0s", 0, 16))
+    ts(R("dl", 0, 256), R("Rn", 0, 256), rc, ALU.is_equal)
+    ms(R("pc", 0, 64), 0.0)
+    for k, (q, init) in enumerate(((2.0 ** -10, 2.0 ** 86), (0.5, 2.0 ** 16), (2.0, 2.0 ** -16), (2.0, 2.0 ** 15))):
+        if k < 3:
+            ms(R("pc", 16 * k, 16 * k + 16), q)
+        scan(R("pw", 16 * k, 16 * k + 16), R("pc", 16 * min(k, 2), 16 * min(k, 2) + 16), R("pc", 48, 64), init, ALU.mult, ALU.add)
+    tt(R("pw", 0, 64), R("pw", 0, 64), R("dl", 0, 64), ALU.mult)
+    for k in range(3):
+        red(c1("col", 3 + k), R("pw", 16 * k, 16 * k + 16))
+    wc, w0c, iwc = c1("col", 3), c1("col", 4), c1("col", 5)
+    ts(R("mf", 0, 16), R("m0s", 0, 16), wc, ALU.mult)
+    lin(R("SE", 0, 144), R("E", 0, 144), wc)
+    for s in range(16):
+        lin(R("CM", 128 * s, 128 * s + 128), view("E", s), c1("mf", 16 + s))
+        lin(R("SM", 128 * s, 128 * s + 128), view("E", s), c1("mf", s))
+    for n, src, v in (("nI", "Id", -1.0), ("BI", "Id", BIG), ("nBO", "O", -BIG), ("QO", "O", 2.0 ** 30), ("QI", "Id", 2.0 ** 28),
+                      ("n5I", "Id", -512.0), ("n5O", "O", -512.0), ("OK", "O", -RS / 2.0), ("I2O", "Id", -2.0 ** 31)):
+        lin(full(n), full(src), v)
+    ts(full("Os"), full("O"), rc, ALU.mult, -0.5, ALU.mult)
+    tt(full("Zc"), full("O"), full("Id"), ALU.add)
+    tt(full("I2O"), full("I2O"), full("QO"), ALU.add)
+    ms(R("one", 0, PC), 1.0)
+    ts(full("Tl"), R("Rn", 0, 128), rc, ALU.is_lt)
+    tt(full("Tl"), full("Tl"), full("O"), ALU.mult)
+    ts(full("TB"), full("Tl"), -2.0, ALU.mult)
+    tt(full("TB"), full("TB"), full("Id"), ALU.add)
+    ts(full("TB"), full("TB"), iwc, ALU.mult)
+    ms(R("Lq", 0, 640), 0.0)
+    for q, (a, b) in enumerate(WIN):
+        for p in range(a, b + 1):
+            ts(R("Lq", 128 * q + p, 128 * q + 128, 16), R("O", p, 128, 16), 2.0 ** (5 * p - 37), ALU.mult)
+    ts(c1("col", 6), rc, 4.5, ALU.is_lt)
+    ts(R("Ld", 0, 640), R("Lq", 0, 640), c1("col", 6), ALU.mult)
+    tt(R("N16", 0, PC), R("N16", 0, PC), R("dl", 0, PC), ALU.mult)
+    ts(R("Ci", 0, PC), R("N16", 0, PC), -32768.0, ALU.add)
+    ts(R("Kx", 0, 256), R("Rn", 0, 256), 0.0, ALU.is_equal, -2.0 ** 22, ALU.mult)
+    lin(R("Cm", 0, PC), R("dl", 0, PC), 2.0 ** 21 + 4096, -2.0 ** 21)
+    lin(full("K8"), full("Id"), 256.0)
+    lin(full("Oa"), full("O"), c1("wf", 0))
+    lin(full("Ob"), full("O"), c1("wf", 1))
+    lin(full("K4"), full("Id"), 4096.0)
+    mm([(R("P0", 0, 128), [(full("OM"), full("Id"))])])
+    lin(full("MT"), R("P0", 0, 128), 1.0)
+    ts(R("Kn", 0, 256), R("Rn", 0, 256), 0.0, ALU.is_equal, 2.0 ** 29, ALU.mult)
+    ts(R("Cd", 0, 256), R("Rn", 0, 256), rc, ALU.is_ge, 2.0 ** 28, ALU.mult)
+    ts(R("Cd", 0, 256), R("Cd", 0, 256), rc, ALU.add)
+    ms(R("Cd", 15, 256, 16), 16.0)
+    ts(R("S1", 0, 16), R("dl", 0, 16), -1.0, ALU.mult, 2.0, ALU.add)
+    ts(R("S2", 0, 16), R("dl", 0, 16), 32768.0, ALU.mult, -16384.0, ALU.add)
+    for r in range(15):
+        ts(R("Dm", 128 * r, 128 * r + 128), full("Zc"), c1("S1", r), ALU.is_equal, c1("S2", r), ALU.mult)
+    ms(full("Af"), 1.0 / 16)
+    ms(c1("thr", 0), 1.5 * 2.0 ** 30)
+    ts(c1("col", 7), rc, 16.0, ALU.mult)
+    for ch in range(NC):
+        b = 2 * PC * ch
+        ms(R("W", b + PC, b + 2 * PC), 0.0)
+        lin(R("W", b, b + PC), R("one", 0, PC), w0c)
+        for s in range(16):
+            lin(R("Mw", 2 * RS * ch + s, 2 * RS * ch + RS, 16), R("one", 0, PC), c1("mf", 16 + s))
+    lin(R("RE", 0, 144), R("E", 0, 144), rc)
+    lin(R("KE", 0, 144), R("E", 0, 144), float(RS))
+    ts(full("RDm"), full("Id"), -64.0, ALU.mult)
+    tt(full("RSm"), full("RDm"), full("O"), ALU.add)
+    tt(full("RSm"), full("RSm"), full("Tl"), ALU.subtract)
+    tt(full("RSm"), full("RSm"), full("Id"), ALU.subtract)
+    tt(full("RDm"), full("RDm"), full("Tl"), ALU.add)
+
+    def bottom(ch):
+        b = 2 * PC * ch
+        pb = R("P2", 384, 384 + PC)
+        mm([(pb, [(full("TB"), R("W", b, b + PC))])])
+        act(R("bot", PC * ch, PC * ch + PC), pb, AF.Sign, bias=0.5, scale=-1.0)
+
+    def hashed(src, bank, o, n, i1, a1, i2, a2):
+        uv, u, v, x = R(i1, a1, a1 + 2 * n), R(i1, a1, a1 + n), R(i1, a1 + n, a1 + 2 * n), R(i2, a2, a2 + n)
+        if _S[i1][1] == F32:
+            act(uv, src, AF.Identity, bias=2.0 ** 23 - 0.5, scale=2.0 ** -12 + 2.0 ** -34)
+            act(uv, uv, AF.Identity, bias=2.0 ** 35, scale=-4096.0)
+            tt(uv, src, uv, ALU.add)
+            tt(x, u, v, ALU.mult)
+            lin(R(bank, o, o + n), u, 37.0)
+        else:
+            cp(uv, src)
+            ts(uv, uv, 4095, ALU.bitwise_and)
+            tt(x, u, v, ALU.mult)
+            ts(R(bank, o, o + n), u, 37.0, ALU.mult)
+        ts(x, x, 5, ALU.arith_shift_right)
+        tt(x, x, R(bank, o, o + n), ALU.add)
+        return x
+
+    for ch in range(NC):
+        bottom(ch)
+    rot = [0]
+
+    def dbank():
+        rot[0] = (rot[0] + 1) % 2
+        return "P%d" % rot[0]
+
+    Xg = R("X", 16, 8208)
+    for t in range(RO):
+        for ch in range(NC - 1, -1, -1):
+            z = R("zin", 256 * t + PC * ch, 256 * t + PC * ch + PC)
+            xb, eb, mb, ob, wb, pb = 2 * RS * ch, 21 * PC * ch, 5 * PC * ch, HWM * ch, 2 * PC * ch, PC * ch
+            hw, cw = PC + t * CC, (2 * PC if t else PC)
+
+            def dyn(n, k):
+                return R(n, xb + RS + k, xb + 2 * RS, 16)
+
+            def half(n, k, base=wb):
+                return R(n, base + k * PC, base + k * PC + PC)
+
+            def pt(n):
+                return R(n, pb, pb + PC)
+
+            bonus[0] = BON1 * ch
+            zp = R("P3", 2 * HWM, 2 * HWM + PC)
+            if MZA >> ch & 1:
+                for a in range(0, t, 2):
+                    ks, bk = list(range(a, min(a + 2, t))), "P4"
+                    mm([(R(bk, (2 + k - a) * PC, (3 + k - a) * PC), [(full("Id"), z), (full("K8"), dyn("Mw", k))]) for k in ks])
+                    act(R("MZ", mb + a * PC, mb + (ks[-1] + 1) * PC), R(bk, 2 * PC, (2 + len(ks)) * PC), AF.Relu, bias=-256.0)
+            elif t:
+                mm([(zp, [(full("Id"), z)])])
+                for k in range(t):
+                    tt(R("MZ", mb + k * PC, mb + k * PC + PC), dyn("Mw", k), zp, ALU.mult)
+            fm = FM and t > 0
+            k4 = lambda n: [(full("K4"), R("one", 0, n))] if fm else []
+            mm([(R("P3", 0, PC), k4(PC) + [(full("AM"), z)]), (R("P3", hw, hw + PC), k4(PC) + [(full("BM"), z)])])
+            if t:
+                mm([(R("P3", o + PC, o + hw), k4(t * CC) + [(view(n, r), R("MZ", mb + r, mb + t * PC, 16)) for r in range(16)])
+                    for n, o in (("A", 0), ("B", hw))])
+            x = hashed(R("P3", 0, 2 * hw), "P3", 0, hw, "F1" if fm else "I1", 2 * ob, "I2", ob)
+            ts(x, x, 8191, ALU.bitwise_and)
+            cp(R("off", ob, ob + hw), x)
+            for k in range(NG):
+                q = PC // NG
+                gat(R("Xh", xb + 16 * q * k, xb + 16 * q * (k + 1)), Xg, R("off", ob + q * k, ob + q * (k + 1)),
+                    ch == 0 and k < ONLY and t > 0)
+            for k in range(t):
+                gat(dyn("Xh", k), Xg, R("off", ob + PC + CC * k, ob + PC + CC * (k + 1)), ch == 0 and ONLY == NG)
+            bonus[0] = BON2 if ch else BON6
+            PS = PC // SUB
+            per = 512 // PS
+            blocks = [(sb * PS, PS, list(range(a, a + per))) for sb in range(SUB) for a in range(0, 16, per)]
+            dblk = [(0, PC, list(range(16 + a, 16 + min(a + 512 // PC, t)))) for a in range(0, t, 512 // PC)]
+            blocks = blocks[:DF] + dblk + blocks[DF:]
+            for p0, pn, bl in blocks:
+                bk = dbank()
+                st = bl[0] < 16
+                zz = R(z[0], z[1] + p0, z[1] + p0 + pn)
+                mm([(R(bk, j * pn, j * pn + pn),
+                     [(full("Id"), R("Xh", xb + 16 * p0 + s, xb + 16 * (p0 + pn), 16) if st else dyn("Xh", s - 16)), (full("nI"), zz)])
+                    for j, s in enumerate(bl)])
+                n, g0 = len(bl) * pn, eb + 16 * p0 + bl[0] * pn
+                ee, gg = R("e", g0, g0 + n), R("G", g0, g0 + n)
+                if st:
+                    act(ee, R(bk, 0, n), AF.Abs)
+                    ts(gg, ee, 72.5, ALU.is_gt)
+                else:
+                    act(R(bk, 0, n), R(bk, 0, n), AF.Abs)
+                    tt(gg, R(bk, 0, n), R("TH", mb + (bl[0] - 16) * PC, mb + (bl[0] - 16) * PC + n), ALU.is_gt)
+                for bank, sm, dm in (("P4", "CM", "E"), ("P5", "SM", "SE")):
+                    mm([(R(bank, p0, p0 + pn) if st else R(bank, PC, 2 * PC),
+                         [(R(sm, 128 * s, 128 * s + 128) if st else view(dm, s - 16), R("G", g0 + j * pn, g0 + j * pn + pn))
+                          for j, s in enumerate(bl)])], first=bl[0] in (0, 16), last=bl[-1] in (15, 15 + t))
+            hot = BONA if ch == 0 else BON3
+            bonus[0] = hot
+            cwr = lambda n: R(n, wb, wb + cw)
+            cwr2 = lambda n: R(n, wb, wb + 2 * PC)
+            act(R("P4", 0, cw), R("P4", 0, cw), AF.Relu, bias=c1("thr", t % 2), scale=-2.0 ** 30)
+            tt(cwr("MW"), cwr("W"), R("P4", 0, cw), ALU.min)
+            hs = [0, 1] if t else [0]
+            mm([(R("P6", k * PC, k * PC + PC), [(full("QI"), R("one", 0, PC) if k else pt("bot"))]
+                 + [(full("I2O" if j == k else "QO"), half("MW", j)) for j in hs]) for k in hs])
+            act(cwr("sel"), R("P6", 0, cw), AF.Sign)
+            mm([(R("P6", 2 * PC, 3 * PC), [(full("O"), half("MW", j)) for j in hs])])
+            act(pt("miss"), R("P6", 2 * PC, 3 * PC), AF.Relu, bias=1.0, scale=-1.0, acc=c1("mcnt", ch))
+            ib = R("P6", 3 * PC, 4 * PC)
+            mm([(ib, [(full("Id"), R("Ci", 0, PC))] + [(full("Os"), half("sel", j)) for j in hs]
+                 + ([(full("OK"), half("sel", 1))] if t else []))])
+            scan(pt("sc"), R("Kx", 0, PC), ib, 0.0, ALU.add, ALU.max)
+            ix = R("idx", CC * ch, CC * ch + CC)
+            ts(ix, R("sc", pb + 15, pb + PC, 16), 120.0 + 8 * RS if t else 60.0, ALU.add)
+            gat(pt("ms"), R("Mw", xb, xb + 2 * RS), ix)
+            bonus[0] = BONH if ch == 0 else BON4
+            gat(pt("xs"), R("Xh", xb, xb + 2 * RS), ix)
+            x0 = dyn("Xh", t - 1) if t else R("Xh", xb, xb + RS, 16)
+            y1, y2, bs, th = [R("P7", k * PC, k * PC + PC) for k in range(4)]
+            mm([(bs, [(full("Id"), z), (full("Id"), x0)] + [(full("n5O"), half("MW", j)) for j in hs])])
+            ts(pt("b2"), bs, 0.5, ALU.mult, -0.25, ALU.add)
+            mm([(y1, [(full("Id"), z), (full("n5I"), pt("miss")), (full("nI"), pt("xs"))]),
+                (y2, [(full("nI"), z), (full("n5I"), pt("miss")), (full("Id"), pt("xs"))])])
+            tt(pt("t1"), y1, pt("b2"), ALU.max)
+            new = R("yzb", 256 * t + pb, 256 * t + pb + PC)
+            tt(new, y2, pt("t1"), ALU.max)
+            if t < RO - 1:
+                zn = R("zin", 256 * (t + 1) + pb, 256 * (t + 1) + pb + PC)
+                add("g", ("send", zn, new, "r%d_%d" % (t + 1, ch)), [new], [zn], 300.0, lat=RLAT)
+            bonus[0] = hot
+            act(cwr("H"), R("P5", 0, cw), AF.Sqrt)
+            mm([(R("P2", k * PC, PC + k * PC), [(full("BI"), half("W", k))]
+                 + [(full("nBO"), half("MW", j)) for j in hs]) for k in hs])
+            tt(cwr("Hv"), cwr("H"), R("P2", 0, cw), ALU.min)
+            terms = []
+            for q, (a, b) in enumerate(WIN):
+                cb = 512 * q + wb
+                lo = 2.0 ** (38 - 5 * (b + 1)) if b < 15 else 0.0
+                ts(R("Cq", cb, cb + cw), cwr("Hv"), 2.0 ** (38 - 5 * (a - 1)) if a else BIG, ALU.min, lo, ALU.max)
+                terms += [(R("Ld" if j else "Lq", 128 * q, 128 * q + 128), half("Cq", j, cb)) for j in hs]
+            xx = R("P2", 2 * PC, 3 * PC)
+            mm([(xx, terms)])
+            cp(pt("e1"), xx)
+            ts(pt("e1"), pt("e1"), 62, ALU.bitwise_and)
+            mm([(th, [(full("Id"), pt("miss")), (full("nI"), pt("ms"))])])
+            tt(dyn("Mw", t), pt("e1"), th, ALU.is_gt)
+            bonus[0] = 0.0
+            tt(cwr("W"), cwr("W"), R("P6", 0, cw), ALU.min)
+            either(lambda: act(half("W", 1), half("W", 1), AF.Relu, bias=c1("pw", 48 + t)),
+                   lambda: ts(half("W", 1), half("W", 1), c1("pw", 48 + t), ALU.max))
+            either(lambda: act(half("W", 0), half("W", 0), AF.Relu), lambda: ts(half("W", 0), half("W", 0), 0.0, ALU.max))
+            if t < RO - 1:
+                lin(R("TH", mb + t * PC, mb + t * PC + PC), dyn("Mw", t), -227.5, 300.0)
+                bottom(ch)
+                bonus[0] = hot
+                if UZA >> ch & 1:
+                    mm([(bs, [(full("Id"), z), (full("K8"), dyn("Mw", t))])])
+                    act(pt("UZ"), bs, AF.Relu, bias=-256.0)
+                else:
+                    mm([(bs, [(full("Id"), z)])])
+                    tt(pt("UZ"), dyn("Mw", t), bs, ALU.mult)
+                o, jb = 2 * HWM + PC + 2 * CC * ch, 2 * CC * ch
+                if SU >> ch & 1:
+                    mm([(yy, [(full("Id"), R("Cm", 0, PC)), (full(n), pt("UZ"))]) for yy, n in ((y1, "Oa"), (y2, "Ob"))])
+                    scan(cwr2("su"), R("Kx", 0, 2 * PC), R("P7", 0, 2 * PC), 0.0, ALU.add, ALU.max)
+                    src = R("su", wb + 15, wb + 2 * PC, 16)
+                else:
+                    mm([(R("P3", o + k * CC, o + k * CC + CC), [(full("K4"), R("one", 0, CC))]
+                         + [(view(n, r), R("UZ", pb + r, pb + PC, 16)) for r in range(16)]) for k, n in enumerate("AB")])
+                    src = R("P3", o, o + 2 * CC)
+                x = hashed(src, "P3", o, CC, "JF" if FJ >> ch & 1 else "J1", jb, "J2", CC * ch)
+                ts(R("J3", jb, jb + CC), x, 8128, ALU.bitwise_and)
+                ts(R("J3", jb + CC, jb + 2 * CC), x, 63, ALU.bitwise_and)
+                cp(R("hl", jb, jb + 2 * CC), R("J3", jb, jb + 2 * CC))
+                dd = R("P5", 2 * PC, 3 * PC)
+                mm([(dd, [(full("Id"), R("Cd", 0, PC))]
+                     + [(R("Dm", 128 * r, 128 * r + 128) if r < 15 else full("Id"), R("hl", jb + CC * k, jb + CC * k + CC),
+                         R("P5", 2 * PC + r, 3 * PC, 16)) for r in range(16) for k in range(2)])])
+                act(pt("aD"), dd, AF.Abs)
+                scan(pt("sD"), R("Kn", 0, PC), pt("aD"), 0.0, ALU.add, ALU.min)
+                cp(R("xo", jb, jb + 2 * CC, 2), R("sD", pb + 15, pb + PC, 16))
+        bonus[0] = 0.0
+        if t in (RO - 2, RO - 1):
+            a = 0 if t == RO - 2 else 256 * t
+            r = R("yzb", a, 256 * t + 256)
+            dma(("yz", a, 256 * t + 256), r, [r], [], 65536 * (5 if t == RO - 2 else 1))
+        if t == RO - 1:
+            break
+        pa = R("P7", 2 * PC, 2 * PC + 1)
+        mm([(pa, [(full("Af"), c1("mcnt", ch)) for ch in range(NC)])], f=4)
+        cp(c1("ai", 0), pa)
+        ts(c1("ai", 0), c1("ai", 0), 1, ALU.bitwise_and)
+        ts(c1("thr", (t + 1) % 2), c1("ai", 0), 1.5, ALU.add, 2.0 ** 30, ALU.mult)
+        for c in range(15, -1, -1):
+            bonus[0] = BONA if c < CC else BON5
+            zz = R("zin", 256 * t + 16 * c, 256 * t + 16 * c + 16)
+            add("v", ("sca", R("X", 0, 8208), R("xo", 2 * c, 2 * c + 1), zz), [zz, c1("xo", 2 * c)], [R("X", 0, 8208)],
+                50 + 16 * SF * CY)
+
+    bonus[0] = 0.0
+    for ch in range(NC - 1, -1, -1):
+        wb, pb, xb = 2 * PC * ch, PC * ch, 2 * RS * ch
+        es = lambda k: R("Es", (15 * ch + k - 1) * PC, (15 * ch + k) * PC)
+        ed = lambda k: R("Ed", (5 * ch + k - 1) * PC, (5 * ch + k) * PC)
+        ym = lambda k: R("ymb", 256 * k + pb, 256 * k + pb + PC)
+        act(R("al", wb, wb + 2 * PC), R("W", wb, wb + 2 * PC), AF.Sign)
+        s, d = R("al", wb, wb + PC), R("al", wb + PC, wb + 2 * PC)
+        mm([(R("P3", 0, PC), [(full("RSm"), s), (full("O"), d)]), (R("P3", PC, 2 * PC), [(full("RDm"), d)])])
+        lin(R("rk", wb, wb + 2 * PC), R("P3", 0, 2 * PC), 1.0, 64.0)
+        lin(ym(0), R("Mw", xb + RS + 5, xb + 2 * RS, 16), 1.0)
+        for k in range(1, 16):
+            ts(es(k), R("rk", wb, wb + PC), float(k), ALU.is_equal)
+            if k < 6:
+                ts(ed(k), R("rk", wb + PC, wb + 2 * PC), float(k), ALU.is_equal)
+        pi = R("P3", 2 * PC, 2 * PC + 5 * CC)
+        mm([(pi, [(full("Id"), R("Ct", 0, 5 * CC))]
+             + [(view("RE", r), R("Es", es(1)[1] + r, es(5)[2], 16)) for r in range(16)]
+             + [(view(m, r), R("Ed", ed(1)[1] + r, ed(5)[2], 16)) for m in ("RE", "KE") for r in range(16)])])
+        ts(R("to", 5 * CC * ch, 5 * CC * (ch + 1)), pi, c1("col", 7), ALU.add)
+        for k in range(1, 6):
+            gat(ym(k), R("Mw", xb, xb + 2 * RS), R("to", CC * (5 * ch + k - 1), CC * (5 * ch + k)))
+        for k in range(6, 16):
+            pp = R(("P3", "P2", "P7")[k % 3] if ch else dbank(), 384, 384 + PC)
+            mm([(pp, [(full("MT"), es(k))])])
+            lin(ym(k), pp, 1.0)
+    for a, b in KG:
+        r = R("ymb", 256 * a, 256 * b)
+        dma(("ym", 256 * a, 256 * b), r, [r], [], 65536 * (b - a))
+    return ops
+
+
+def schedule(ops):
+    n = len(ops)
+    hist = {}
+    for k, o in enumerate(ops):
+        deps = set()
+        for r, w in [(r, False) for r in o["rd"]] + [(r, True) for r in o["wr"]]:
+            for j, a, b, ww, sp in hist.get(r[0], []):
+                if (w or ww) and a < r[2] and r[1] < b and j != k and not (sp == r[3] > 1 and (a - r[1]) % sp):
+                    deps.add(j)
+        for r, w in [(r, False) for r in o["rd"]] + [(r, True) for r in o["wr"]]:
+            h = hist.setdefault(r[0], [])
+            if w and r[3] == 1:
+                h[:] = [x for x in h if not (r[1] <= x[1] and x[2] <= r[2])]
+            h.append((k, r[1], r[2], w, r[3]))
+        o["deps"] = deps
+        o["banks"] = set(r[0] for r in o["rd"] + o["wr"] if r[0] not in _S)
+    succ = [[] for _ in ops]
+    for k, o in enumerate(ops):
+        for j in o["deps"]:
+            succ[j].append(k)
+    pr = [0.0] * n
+    for k in range(n - 1, -1, -1):
+        pr[k] = ops[k]["cost"] + ops[k].get("lat", LAT) + max([pr[j] for j in succ[k]] + [0.0])
+    pr = [p + o["bonus"] for p, o in zip(pr, ops)]
+    left = [len(o["deps"]) for o in ops]
+    at = [0.0] * n
+    ready = {e: [] for e in "vapgs"}
+
+    def put(k):
+        for e in ops[k].get("alt", ops[k]["eng"]):
+            ready[e].append(k)
+
+    for k in range(n):
+        if not left[k]:
+            put(k)
+    free = {e: 0.0 for e in "vapgs"}
+    bank_t, bank_o, opened, order = {}, {}, {}, []
+    while len(order) < n:
+        best = None
+        for e in "vapgs":
+            cand = []
+            for k in ready[e]:
+                o = ops[k]
+                if e == "p" and o["first"] and opened.get(o["bank"]):
+                    continue
+                st = max([free[e], at[k]] + [bank_t[b] for b in o["banks"] if b in bank_t and ops[bank_o[b]]["eng"] != e])
+                cand.append((st, k))
+            if cand:
+                t0 = min(c[0] for c in cand)
+                pen = ALTP if e == "v" else 0.0
+                k = max((c for c in cand if c[0] <= t0 + SLACK),
+                        key=lambda c: pr[c[1]] - GAM * (c[0] - t0) - (pen if "alt" in ops[c[1]] else 0.0))
+                if best is None or k[0] < best[0]:
+                    best = k + (e,)
+        st, k, e = best
+        o = ops[k]
+        for x in o.get("alt", e):
+            ready[x].remove(k)
+        if "alt" in o:
+            o["eng"] = e
+            o["call"], o["cost"] = o["alt"][e]
+        order.append(k)
+        o["t0"] = st
+        free[e] = st + o["cost"]
+        done = free[e] + o.get("lat", LAT)
+        o["t1"] = done
+        if e == "p":
+            opened[o["bank"]] = not o["last"]
+        for b in o["banks"]:
+            if b in bank_o and ops[bank_o[b]]["eng"] != e:
+                o["deps"].add(bank_o[b])
+            bank_t[b], bank_o[b] = done, k
+        for j in succ[k]:
+            at[j] = max(at[j], free[e] if e == "p" and ops[j]["eng"] == "p" else done)
+            left[j] -= 1
+            if not left[j]:
+                put(j)
+    return order
+
+
+def plan():
+    extra, best, seed = {}, None, 1
+    for it in range(ITER):
+        ops = build()
+        for k, x in extra.items():
+            ops[k]["bonus"] += x
+        order = schedule(ops)
+        end = max(o["t1"] for o in ops)
+        if best is None or end < best[0]:
+            best = (end, ops, order, dict(extra))
+        elif end > best[0] + 1500.0:
+            extra = dict(best[3])
+            ops, order = best[1], best[2]
+        prev, last = {}, {}
+        for k in order:
+            prev[k] = last.get(ops[k]["eng"])
+            last[ops[k]["eng"]] = k
+        k = max(range(len(ops)), key=lambda j: ops[j]["t1"])
+        while k is not None:
+            o = ops[k]
+            d = max(o["deps"], key=lambda j: ops[j]["t1"]) if o["deps"] else None
+            p = prev[k]
+            seed = (seed * 1103515245 + 12345) % 2147483648
+            if p is not None and (d is None or ops[p]["t0"] + ops[p]["cost"] >= ops[d]["t1"]) and p not in o["deps"]:
+                if seed % 100 < PB:
+                    extra[k] = extra.get(k, 0.0) + STEP
+                    extra[p] = extra.get(p, 0.0) - STEP
+                k = p
+            else:
+                k = d
+    return best[1], best[2]
+
+
+_PLAN = []
+
+
+def rank_program(g, core, T, topo):
+    rank = T.rank_of(core)
+    if rank is None:
+        return
+    if not _PLAN:
+        _PLAN.extend(plan())
+    ops, order = _PLAN
+    nxt = T.cores[(rank + 1) % len(T.cores)]
+    prv = T.cores[(rank - 1) % len(T.cores)]
+    rid, pid, _ = topo.addr(nxt)
+    NE = 8
+    mask = sum(1 << e for e in topo.engines(core, nxt)[:NE])
+    assert len(topo.engines(prv, core)) >= NE and topo.may_write(core, nxt)
+    Q = dict(v=g.vector, a=g.scalar, p=g.tensor, g=g, s=g.sync)
+
+    def ap(r):
+        if not isinstance(r, tuple):
+            return r
+        return T[r[0]][:, r[1]:r[2]] if len(r) == 3 or r[3] == 1 else T[r[0]][:, r[1]:r[2]:r[3]]
+
+    def skip(j, o):
+        p = ops[j]
+        return p["eng"] == o["eng"] == "p"
+
+    pos = {k: i for i, k in enumerate(order)}
+    need = set()
+    for o in ops:
+        last = {}
+        o["w"] = []
+        for j in o["deps"]:
+            if skip(j, o):
+                continue
+            if ops[j]["call"][0] in ("dma", "send"):
+                o["w"].append(j)
+            elif pos[j] > pos[last.get(ops[j]["eng"], j)] or ops[j]["eng"] not in last:
+                last[ops[j]["eng"]] = j
+        o["w"] += list(last.values())
+        need.update(last.values())
+    cnt = {e: 0 for e in "vapg"}
+    token, seen, sends = {}, {}, 0
+    for k in order:
+        o = ops[k]
+        q, c = Q[o["eng"]], o["call"]
+        for j in sorted(o["w"]):
+            s, v = token[j]
+            if seen.get((o["eng"], s), 0) < v:
+                q.wait_ge(T.sem[s], v)
+                seen[(o["eng"], s)] = v
+        f = c[0]
+        if f == "dma":
+            q.dma_start(ap(c[1]), ap(c[2])).then_inc(T.sem["d%d" % c[3]], 16)
+            token[k] = ("d%d" % c[3], 16)
+            continue
+        if f == "send":
+            g.remote_dma(ap(c[1]), ap(c[2]), T.sem[c[3]], T.sem.sent, pid, rid, mask)
+            token[k] = (c[3], NE)
+            sends += NE
+            continue
+        if f == "ts":
+            ins = (q.tensor_scalar(ap(c[1]), ap(c[2]), ap(c[3]), None, c[5]) if c[6] is None
+                   else q.tensor_scalar(ap(c[1]), ap(c[2]), ap(c[3]), ap(c[4]), c[5], c[6]))
+        elif f == "tt":
+            ins = q.tensor_tensor(ap(c[1]), ap(c[2]), ap(c[3]), c[4])
+        elif f == "cp":
+            ins = q.tensor_copy(ap(c[1]), ap(c[2]))
+        elif f == "ms":
+            ins = q.memset(ap(c[1]), c[2])
+        elif f == "scan":
+            ins = q.tensor_tensor_scan(ap(c[1]), ap(c[2]), ap(c[3]), c[4], c[5], c[6])
+        elif f == "red":
+            ins = q.tensor_reduce(ap(c[1]), ap(c[2]), AxisListType.X, ALU.add)
+        elif f == "act":
+            ins = q.activation(ap(c[1]), ap(c[2]), c[3], bias=ap(c[4]), scale=ap(c[5]), accum_out=ap(c[6]))
+        elif f == "gat":
+            src = ap(c[3]).indirect(ap(c[4]))
+            ins = q.tensor_copy(ap(c[2]), src) if c[1] == "v" else q.activation(ap(c[2]), src, AF.Copy)
+        elif f == "sca":
+            ins = q.tensor_copy(ap(c[1]).indirect(ap(c[2])), ap(c[3]))
+        elif f == "iota":
+            ins = (q.iota(ap(c[1]), c[2], c[3], c[4]) if _S[c[1][0]][1] == I32
+                   else q.iota(ap(c[1]), c[2], c[3], c[4], allow_small_or_imprecise_dtypes=True))
+        else:
+            for m in c[1]:
+                ins = q.matmul(ap(m[0]), ap(m[1]), ap(m[2]), m[3], m[4])
+        if k in need:
+            cnt[o["eng"]] += 1
+            ins.then_inc(T.sem["c" + o["eng"]], 1)
+            token[k] = ("c" + o["eng"], cnt[o["eng"]])
+    for k, (s, v) in token.items():
+        if ops[k]["call"][0] == "dma":
+            g.sync.wait_ge(T.sem[s], v)
+    g.wait_ge(T.sem.sent, sends)

@@ -26,8 +26,8 @@ _S = dict(
     pw=(64, F32), pc=(64, F32), dl=(256, F32), Wn=(16, F32), Lq=(640, BF), Ld=(640, BF),
     BI=(128, BF), nBO=(128, BF), I2O=(128, BF), QO=(128, BF), QI=(128, BF), nI=(128, BF), n5I=(128, BF), n5O=(128, BF),
     Os=(128, BF), OK=(128, BF), Tl=(128, BF), TB=(128, BF), RSm=(128, BF), RDm=(128, BF), Zc=(128, BF),
-    Dm=(15 * 128, BF), S1=(16, F32), S2=(16, F32), Ci=(PC, BF), Kx=(256, BF), Kn=(256, F32), Cd=(256, BF), Ct=(5 * CC, BF),
-    Af=(128, F32), Cm=(PC, BF), Oa=(128, BF), Ob=(128, BF), K4=(128, BF), K8=(128, BF), JF=(32, F32), MT=(128, BF), su=(512, F32), F1=(NC * 2 * HWM, F32),
+    Dm=(15 * 128, BF), S1=(16, F32), S2=(16, F32), Ci=(PC, BF), Kx=(512, BF), Kn=(256, F32), Cd=(256, BF), Ct=(5 * CC, BF),
+    Af=(128, F32), Cm=(256, BF), Oa=(128, BF), Ob=(128, BF), n5P=(128, BF), b1=(256, F32), ry=(768, BF), K8=(128, BF), OW=(128, BF), JF=(32, F32), MT=(128, BF), su=(512, F32), F1=(NC * 2 * HWM, F32),
 )
 SCRATCH = {k: ("sbuf", [128, n], d) for k, (n, d) in _S.items()}
 for _b in range(8):
@@ -36,17 +36,30 @@ NDMA = 20
 SEMAPHORES = (["cv", "ca", "cp", "cg", "sent"] + ["d%d" % k for k in range(NDMA)]
               + ["r%d_%d" % (t, c) for t in range(1, RO) for c in range(NC)])
 
-CY, PCY, LAT, RLAT, DLAT = 1.0, 0.45, 80.0, 2500.0, 2200.0
-GF, SF = 1.56, 3.8
+DLAT = 2200.0
+_M = dict(CY=0.95, PCY=0.48, LAT=170.0, RLAT=3200.0, OV=55.0, MINC=0.0, GF=1.56, SF=3.8, XB=1 << 20, END=190000.0)
+MODELS = [_M, dict(_M, CY=0.83, PCY=0.42, OV=50.0, END=174000.0), dict(_M, CY=1.0, PCY=0.5, OV=60.0, END=197000.0),
+          dict(_M, CY=1.2, PCY=0.6, OV=72.0, GF=1.7, END=227000.0)]
+TUNED = [-2,0,-1,4,2,-11,-10,8,4,1,5,2,7,-4,0,6,0,-1,18,0,-6,-1,19,-9,0,-1,2,-3,1,-18,3,2,4,0,0,-1,-1,6,-3,-1,6,0,0,0,0,-3,-14,-19,1,4,-24,-10,11,1,-2,-1,17,0,-16,2,0,0,0,0,0,1,0,0,1,12,0,1,2,3,4,2,-8,1,-3,0,0,-4,7,0,4,-11,4,0,-8,1,5,4,-2,0,4,-1,-4,0,0,-4,-2,6,2,4,-1,12,-5,-4,-1,4,6,-1,-1,-2,8,-2,0,-4,26,-1,3,0,5,1,10,16,-8,8,4,-7,-4,11,1,12,0,-7,1,5,-2,0,4,-2,-5,-4,6,1,1,2,-9,-5,0,13,0,0,0,-3,0,0,-1,0,2,0,1,2,0,10,-6,-9,-6,2,3,9,4,3,-5,3,-6,-7,-1,-1,0,0,0,0,0,-2,2,0,0,0,0,0,-2,1,5,3,-6,6,2,2,4,1,0,1,-4,0,4,0,-1,-3,1,-4,-7,-1,0,-1,2,4,1,5,0,0,0,-9,1,-6,-1,0,0,-12,0,2,4,-4,1,0,-1,6,-12,-11,-4,-2,-3,0,0,2,0,2,0,4,-2,-2,10,0,0,19,6,0,-2,-8,0,2,2,-1,0,0,7,-1,1,0,-2,2,0,1,0,-8,-5,12,-9,-13,0,-14,0,11,-4,-11,-8,-1,2,-11,-1,4,-8,2,0,4,3,-1,8,7,16,-2,7,0,0,-1,0,0,-2,4,-3,-2,-4,1,-3,5,4,6,-2,20,1,-2,21,0,0,1,1,-9,8]
 BON1, BON2, ONLY, FM, SU, SUB, DF = 1000.0, 5000.0, 0, 1, 3, 2, 4
-MZA, UZA, FJ = 0, 0, 0
+MZA, UZA, FJ, PSM, PP, MG, HA, XS, XM = 0, 0, 0, 16, 0, 0, 0, 3, 1
 BONA, BONH, BON3, BON4, BON5, BON6 = 0.0, 0.0, 2000.0, 2000.0, 2000.0, 0.0
-ITER, PB, STEP = 100, 20, 300.0
+ITER = 1500
 NG, INIT, ALTP, SLACK, GAM = 4, 0, 2000.0, 100.0, 50.0
 
 
 def R(n, a, b, s=1):
     return (n, a, b, s)
+
+
+RG = (dict(bot=(0, 256), zp=(2, 0), v=(6, 0), T=(7, 0), ib=(7, 256), y1=(1, 0), y2=(1, 256), bs=(3, 0), th=(3, 256), x=(0, 0),
+           j=(7, 0), D=(5, 0), pa=(7, 256), pi=(7, 0)) if NC == 1 else
+      dict(bot=(2, 384), zp=(3, 2 * HWM), v=(3, None), T=(6, 256), ib=(6, 384), y1=(7, 0), y2=(7, 128), bs=(7, 256), th=(7, 384),
+           x=(2, 256), j=(3, 2 * HWM + PC), D=(5, 256), pa=(7, 256), pi=(3, 256)))
+
+
+def rg(n, w=PC, o=0, s=1):
+    return R("P%d" % RG[n][0], RG[n][1] + o, RG[n][1] + (w if s > 1 else o + w), s)
 
 
 def width(r):
@@ -57,15 +70,19 @@ def two(*rs):
     return all(r[0] in _S and _S[r[0]][1] in (BF, U16) for r in rs)
 
 
-def build():
+def build(M):
+    CY, PCY, LAT, RLAT, OV, MINC, GF, SF, XB = [M[k] for k in ("CY", "PCY", "LAT", "RLAT", "OV", "MINC", "GF", "SF", "XB")]
     ops = []
-    bonus = [0.0]
+    bonus = [0.0, 0]
 
-    def add(eng, call, rd, wr, cost, **kw):
-        ops.append(dict(eng=eng, call=call, rd=[r for r in rd if isinstance(r, tuple)], wr=wr, cost=cost, bonus=bonus[0], **kw))
+    def add(eng, call, rd, wr, cost, lat=LAT, **kw):
+        w = wr[0] if wr else ("", 0)
+        key = (bonus[1], call[0], w[0], w[1] % 256 if w[0] in ("zin", "yzb") else w[1] // 16 if w[0] in ("Mw", "TH") else w[1])
+        ops.append(dict(eng=eng, call=call, rd=[r for r in rd if isinstance(r, tuple)], wr=wr, cost=cost, lat=lat,
+                        bonus=bonus[0], key=key, **kw))
 
     def vc(n):
-        return 45.0 + max(40.0, n) * CY
+        return OV + max(MINC, n) * CY
 
     def ts(o, i, s1, op0, s2=None, op1=None):
         add("v", ("ts", o, i, s1, s2, op0, op1), [i, s1, s2], [o], vc(width(o) * (0.5 if two(o, i) else 1)))
@@ -136,7 +153,7 @@ def build():
     dma(R("m0s", 0, 16), ("m0", 0, 16), [], [R("m0s", 0, 16)], 4096)
     for k in range(2):
         r = R("X", 16 + 4096 * k, 16 + 4096 * (k + 1))
-        dma(r, ("xr", 4096 * k, 4096 * (k + 1)), [], [r], 1 << 20 + k)
+        dma(r, ("xr", 4096 * k, 4096 * (k + 1)), [], [r], XB * (k + 1))
     for ch in range(NC * INIT):
         for n in ("Xh", "Mw"):
             r = R(n, 2 * RS * ch + RS, 2 * RS * (ch + 1))
@@ -163,7 +180,6 @@ def build():
     lin(full("BM"), full("OM"), c1("wf", 1))
     lin(R("A", 0, 144), R("E", 0, 144), c1("wf", 0))
     lin(R("B", 0, 144), R("E", 0, 144), c1("wf", 1))
-    cp(R("mf", 16, 32), R("m0s", 0, 16))
     ts(R("dl", 0, 256), R("Rn", 0, 256), rc, ALU.is_equal)
     ms(R("pc", 0, 64), 0.0)
     for k, (q, init) in enumerate(((2.0 ** -10, 2.0 ** 86), (0.5, 2.0 ** 16), (2.0, 2.0 ** -16), (2.0, 2.0 ** 15))):
@@ -176,11 +192,15 @@ def build():
     wc, w0c, iwc = c1("col", 3), c1("col", 4), c1("col", 5)
     ts(R("mf", 0, 16), R("m0s", 0, 16), wc, ALU.mult)
     lin(R("SE", 0, 144), R("E", 0, 144), wc)
+    lin(full("OW"), full("OM"), wc)
     for s in range(16):
-        lin(R("CM", 128 * s, 128 * s + 128), view("E", s), c1("mf", 16 + s))
-        lin(R("SM", 128 * s, 128 * s + 128), view("E", s), c1("mf", s))
+        add("g", ("sel", R("CM", 128 * s, 128 * s + 128), full("OM"), s), [full("OM")], [R("CM", 128 * s, 128 * s + 128)], 170 + 256 * CY)
+        if s < PSM:
+            add("g", ("sel", R("SM", 128 * s, 128 * s + 128), full("OW"), s), [full("OW")], [R("SM", 128 * s, 128 * s + 128)], 170 + 256 * CY)
+        else:
+            lin(R("SM", 128 * s, 128 * s + 128), view("E", s), c1("mf", s))
     for n, src, v in (("nI", "Id", -1.0), ("BI", "Id", BIG), ("nBO", "O", -BIG), ("QO", "O", 2.0 ** 30), ("QI", "Id", 2.0 ** 28),
-                      ("n5I", "Id", -512.0), ("n5O", "O", -512.0), ("OK", "O", -RS / 2.0), ("I2O", "Id", -2.0 ** 31)):
+                      ("n5I", "Id", 1.0 / 512), ("OK", "O", -RS / 2.0), ("I2O", "Id", -2.0 ** 31)):
         lin(full(n), full(src), v)
     ts(full("Os"), full("O"), rc, ALU.mult, -0.5, ALU.mult)
     tt(full("Zc"), full("O"), full("Id"), ALU.add)
@@ -199,12 +219,12 @@ def build():
     ts(R("Ld", 0, 640), R("Lq", 0, 640), c1("col", 6), ALU.mult)
     tt(R("N16", 0, PC), R("N16", 0, PC), R("dl", 0, PC), ALU.mult)
     ts(R("Ci", 0, PC), R("N16", 0, PC), -32768.0, ALU.add)
-    ts(R("Kx", 0, 256), R("Rn", 0, 256), 0.0, ALU.is_equal, -2.0 ** 22, ALU.mult)
-    lin(R("Cm", 0, PC), R("dl", 0, PC), 2.0 ** 21 + 4096, -2.0 ** 21)
+    for k in range(0, 512 if MG else 2 * PC, 256):
+        ts(R("Kx", k, k + 256), R("Rn", 0, 256), 0.0, ALU.is_equal, -2.0 ** 22, ALU.mult)
+    lin(R("Cm", 0, 256), R("dl", 0, 256), 2.0 ** 21, -2.0 ** 21)
     lin(full("K8"), full("Id"), 256.0)
     lin(full("Oa"), full("O"), c1("wf", 0))
     lin(full("Ob"), full("O"), c1("wf", 1))
-    lin(full("K4"), full("Id"), 4096.0)
     mm([(R("P0", 0, 128), [(full("OM"), full("Id"))])])
     lin(full("MT"), R("P0", 0, 128), 1.0)
     ts(R("Kn", 0, 256), R("Rn", 0, 256), 0.0, ALU.is_equal, 2.0 ** 29, ALU.mult)
@@ -215,15 +235,21 @@ def build():
     ts(R("S2", 0, 16), R("dl", 0, 16), 32768.0, ALU.mult, -16384.0, ALU.add)
     for r in range(15):
         ts(R("Dm", 128 * r, 128 * r + 128), full("Zc"), c1("S1", r), ALU.is_equal, c1("S2", r), ALU.mult)
-    ms(full("Af"), 1.0 / 16)
+    ms(full("Af"), 1.0 / 8192)
     ms(c1("thr", 0), 1.5 * 2.0 ** 30)
     ts(c1("col", 7), rc, 16.0, ALU.mult)
     for ch in range(NC):
         b = 2 * PC * ch
         ms(R("W", b + PC, b + 2 * PC), 0.0)
         lin(R("W", b, b + PC), R("one", 0, PC), w0c)
-        for s in range(16):
-            lin(R("Mw", 2 * RS * ch + s, 2 * RS * ch + RS, 16), R("one", 0, PC), c1("mf", 16 + s))
+        if ch == NC - 1:
+            n, a = 16, 2 * RS * ch
+            cp(R("Mw", a, a + 16), R("m0s", 0, 16))
+            while n < RS:
+                cp(R("Mw", a + n, a + 2 * n), R("Mw", a, a + n))
+                n *= 2
+            for c in range(ch):
+                dma(R("Mw", 2 * RS * c, 2 * RS * c + RS), R("Mw", a, a + RS), [R("Mw", a, a + RS)], [R("Mw", 2 * RS * c, 2 * RS * c + RS)], 1 << 19)
     lin(R("RE", 0, 144), R("E", 0, 144), rc)
     lin(R("KE", 0, 144), R("E", 0, 144), float(RS))
     ts(full("RDm"), full("Id"), -64.0, ALU.mult)
@@ -234,20 +260,31 @@ def build():
 
     def bottom(ch):
         b = 2 * PC * ch
-        pb = R("P2", 384, 384 + PC)
+        pb = rg("bot")
         mm([(pb, [(full("TB"), R("W", b, b + PC))])])
         act(R("bot", PC * ch, PC * ch + PC), pb, AF.Sign, bias=0.5, scale=-1.0)
 
     def hashed(src, bank, o, n, i1, a1, i2, a2):
         uv, u, v, x = R(i1, a1, a1 + 2 * n), R(i1, a1, a1 + n), R(i1, a1 + n, a1 + 2 * n), R(i2, a2, a2 + n)
+        parts = [(uv, src[0])] if len(src) == 1 else [(u, src[0]), (v, src[1])]
         if _S[i1][1] == F32:
-            act(uv, src, AF.Identity, bias=2.0 ** 23 - 0.5, scale=2.0 ** -12 + 2.0 ** -34)
-            act(uv, uv, AF.Identity, bias=2.0 ** 35, scale=-4096.0)
-            tt(uv, src, uv, ALU.add)
-            tt(x, u, v, ALU.mult)
-            lin(R(bank, o, o + n), u, 37.0)
+            for d, s in parts:
+                act(d, s, AF.Identity, bias=2.0 ** 23 - 0.5, scale=2.0 ** -12 + 2.0 ** -34)
+                act(d, d, AF.Relu, bias=-2.0 ** 35, scale=4096.0)
+                if not (PP and src[0][0] == bank):
+                    tt(d, s, d, ALU.subtract)
+            up = R(bank, o, o + n)
+            if PP and src[0][0] == bank:
+                tt(v, src[1] if len(src) > 1 else R(bank, o + n, o + 2 * n), v, ALU.subtract)
+                tt(up, up, u, ALU.subtract)
+                tt(x, up, v, ALU.mult)
+                lin(up, up, 37.0)
+            else:
+                tt(x, u, v, ALU.mult)
+                lin(up, u, 37.0)
         else:
-            cp(uv, src)
+            for d, s in parts:
+                cp(d, s)
             ts(uv, uv, 4095, ALU.bitwise_and)
             tt(x, u, v, ALU.mult)
             ts(R(bank, o, o + n), u, 37.0, ALU.mult)
@@ -279,8 +316,8 @@ def build():
             def pt(n):
                 return R(n, pb, pb + PC)
 
-            bonus[0] = BON1 * ch
-            zp = R("P3", 2 * HWM, 2 * HWM + PC)
+            bonus[0], bonus[1] = BON1 * ch, ch + 1
+            zp = rg("zp")
             if MZA >> ch & 1:
                 for a in range(0, t, 2):
                     ks, bk = list(range(a, min(a + 2, t))), "P4"
@@ -291,12 +328,14 @@ def build():
                 for k in range(t):
                     tt(R("MZ", mb + k * PC, mb + k * PC + PC), dyn("Mw", k), zp, ALU.mult)
             fm = FM and t > 0
-            k4 = lambda n: [(full("K4"), R("one", 0, n))] if fm else []
-            mm([(R("P3", 0, PC), k4(PC) + [(full("AM"), z)]), (R("P3", hw, hw + PC), k4(PC) + [(full("BM"), z)])])
-            if t:
-                mm([(R("P3", o + PC, o + hw), k4(t * CC) + [(view(n, r), R("MZ", mb + r, mb + t * PC, 16)) for r in range(16)])
-                    for n, o in (("A", 0), ("B", hw))])
-            x = hashed(R("P3", 0, 2 * hw), "P3", 0, hw, "F1" if fm else "I1", 2 * ob, "I2", ob)
+            k4 = lambda n: []
+            vb, vo = ("P3", hw) if NC > 1 else ("P6", 0)
+            for n, bk, o in (("A", "P3", 0), ("B", vb, vo)):
+                mm([(R(bk, o, o + PC), k4(PC) + [(full(n + "M"), z)])])
+                if t:
+                    mm([(R(bk, o + PC, o + hw), k4(t * CC) + [(view(n, r), R("MZ", mb + r, mb + t * PC, 16)) for r in range(16)])])
+            x = hashed([R("P3", 0, 2 * hw)] if NC > 1 else [R("P3", 0, hw), R("P6", 0, hw)], "P3", 0, hw,
+                       "F1" if fm else "I1", 2 * ob, "I2", ob)
             ts(x, x, 8191, ALU.bitwise_and)
             cp(R("off", ob, ob + hw), x)
             for k in range(NG):
@@ -340,9 +379,9 @@ def build():
             mm([(R("P6", k * PC, k * PC + PC), [(full("QI"), R("one", 0, PC) if k else pt("bot"))]
                  + [(full("I2O" if j == k else "QO"), half("MW", j)) for j in hs]) for k in hs])
             act(cwr("sel"), R("P6", 0, cw), AF.Sign)
-            mm([(R("P6", 2 * PC, 3 * PC), [(full("O"), half("MW", j)) for j in hs])])
-            act(pt("miss"), R("P6", 2 * PC, 3 * PC), AF.Relu, bias=1.0, scale=-1.0, acc=c1("mcnt", ch))
-            ib = R("P6", 3 * PC, 4 * PC)
+            mm([(rg("T"), [(full("O"), half("MW", j)) for j in hs])])
+            act(pt("miss"), rg("T"), AF.Relu, bias=512.0, scale=-512.0, acc=c1("mcnt", ch))
+            ib = rg("ib")
             mm([(ib, [(full("Id"), R("Ci", 0, PC))] + [(full("Os"), half("sel", j)) for j in hs]
                  + ([(full("OK"), half("sel", 1))] if t else []))])
             scan(pt("sc"), R("Kx", 0, PC), ib, 0.0, ALU.add, ALU.max)
@@ -352,14 +391,14 @@ def build():
             bonus[0] = BONH if ch == 0 else BON4
             gat(pt("xs"), R("Xh", xb, xb + 2 * RS), ix)
             x0 = dyn("Xh", t - 1) if t else R("Xh", xb, xb + RS, 16)
-            y1, y2, bs, th = [R("P7", k * PC, k * PC + PC) for k in range(4)]
-            mm([(bs, [(full("Id"), z), (full("Id"), x0)] + [(full("n5O"), half("MW", j)) for j in hs])])
-            ts(pt("b2"), bs, 0.5, ALU.mult, -0.25, ALU.add)
-            mm([(y1, [(full("Id"), z), (full("n5I"), pt("miss")), (full("nI"), pt("xs"))]),
-                (y2, [(full("nI"), z), (full("n5I"), pt("miss")), (full("Id"), pt("xs"))])])
-            tt(pt("t1"), y1, pt("b2"), ALU.max)
+            y1, y2, bs, th = rg("y1"), rg("y2"), rg("bs"), rg("th")
+            mm([(bs, [(full("Id"), z), (full("Id"), x0), (full("Id"), pt("miss"))])])
             new = R("yzb", 256 * t + pb, 256 * t + pb + PC)
-            tt(new, y2, pt("t1"), ALU.max)
+            ts(pt("b2"), bs, 0.5, ALU.mult, -256.25, ALU.add)
+            mm([(y1, [(full("Id"), z), (full("nI"), pt("xs"))])])
+            act(y1, y1, AF.Abs)
+            tt(y1, y1, pt("miss"), ALU.subtract)
+            tt(new, y1, pt("b2"), ALU.max)
             if t < RO - 1:
                 zn = R("zin", 256 * (t + 1) + pb, 256 * (t + 1) + pb + PC)
                 add("g", ("send", zn, new, "r%d_%d" % (t + 1, ch)), [new], [zn], 300.0, lat=RLAT)
@@ -374,11 +413,16 @@ def build():
                 lo = 2.0 ** (38 - 5 * (b + 1)) if b < 15 else 0.0
                 ts(R("Cq", cb, cb + cw), cwr("Hv"), 2.0 ** (38 - 5 * (a - 1)) if a else BIG, ALU.min, lo, ALU.max)
                 terms += [(R("Ld" if j else "Lq", 128 * q, 128 * q + 128), half("Cq", j, cb)) for j in hs]
-            xx = R("P2", 2 * PC, 3 * PC)
-            mm([(xx, terms)])
+            xx = rg("x")
+            cut = len(terms) * XS // 5
+            if cut and XM >> ch & 1:
+                mm([(xx, terms[:cut])], last=False)
+                mm([(xx, terms[cut:])], first=False)
+            else:
+                mm([(xx, terms)])
             cp(pt("e1"), xx)
             ts(pt("e1"), pt("e1"), 62, ALU.bitwise_and)
-            mm([(th, [(full("Id"), pt("miss")), (full("nI"), pt("ms"))])])
+            mm([(th, [(full("n5I"), pt("miss")), (full("nI"), pt("ms"))])])
             tt(dyn("Mw", t), pt("e1"), th, ALU.is_gt)
             bonus[0] = 0.0
             tt(cwr("W"), cwr("W"), R("P6", 0, cw), ALU.min)
@@ -395,26 +439,32 @@ def build():
                 else:
                     mm([(bs, [(full("Id"), z)])])
                     tt(pt("UZ"), dyn("Mw", t), bs, ALU.mult)
-                o, jb = 2 * HWM + PC + 2 * CC * ch, 2 * CC * ch
+                if MG and ch:
+                    continue
+                n, cc = (256, 16) if MG else (PC, CC)
+                jb = 2 * CC * ch
+                sb, so = ("P0", 0) if MG else y1[:2]
+                db, do = ("P1", 0) if MG else rg("D")[:2]
+                pn = lambda b: R(b, pb, pb + n)
                 if SU >> ch & 1:
-                    mm([(yy, [(full("Id"), R("Cm", 0, PC)), (full(n), pt("UZ"))]) for yy, n in ((y1, "Oa"), (y2, "Ob"))])
-                    scan(cwr2("su"), R("Kx", 0, 2 * PC), R("P7", 0, 2 * PC), 0.0, ALU.add, ALU.max)
-                    src = R("su", wb + 15, wb + 2 * PC, 16)
+                    mm([(R(sb, so + k * n, so + k * n + n), [(full("Id"), R("Cm", 0, n)), (full(m), pn("UZ"))])
+                        for k, m in enumerate(("Oa", "Ob"))])
+                    scan(R("su", wb, wb + 2 * n), R("Kx", 0, 2 * n), R(sb, so, so + 2 * n), 0.0, ALU.add, ALU.max)
+                    src = R("su", wb + 15, wb + 2 * n, 16)
                 else:
-                    mm([(R("P3", o + k * CC, o + k * CC + CC), [(full("K4"), R("one", 0, CC))]
-                         + [(view(n, r), R("UZ", pb + r, pb + PC, 16)) for r in range(16)]) for k, n in enumerate("AB")])
-                    src = R("P3", o, o + 2 * CC)
-                x = hashed(src, "P3", o, CC, "JF" if FJ >> ch & 1 else "J1", jb, "J2", CC * ch)
-                ts(R("J3", jb, jb + CC), x, 8128, ALU.bitwise_and)
-                ts(R("J3", jb + CC, jb + 2 * CC), x, 63, ALU.bitwise_and)
-                cp(R("hl", jb, jb + 2 * CC), R("J3", jb, jb + 2 * CC))
-                dd = R("P5", 2 * PC, 3 * PC)
-                mm([(dd, [(full("Id"), R("Cd", 0, PC))]
-                     + [(R("Dm", 128 * r, 128 * r + 128) if r < 15 else full("Id"), R("hl", jb + CC * k, jb + CC * k + CC),
-                         R("P5", 2 * PC + r, 3 * PC, 16)) for r in range(16) for k in range(2)])])
-                act(pt("aD"), dd, AF.Abs)
-                scan(pt("sD"), R("Kn", 0, PC), pt("aD"), 0.0, ALU.add, ALU.min)
-                cp(R("xo", jb, jb + 2 * CC, 2), R("sD", pb + 15, pb + PC, 16))
+                    mm([(rg("j", cc, jb + k * cc), [(view(m, r), R("UZ", pb + r, pb + n, 16)) for r in range(16)])
+                        for k, m in enumerate("AB")])
+                    src = rg("j", 2 * cc, jb)
+                x = hashed([src], rg("j")[0], rg("j")[1] + jb, cc, "JF" if FJ >> ch & 1 else "J1", jb, "J2", CC * ch)
+                ts(R("J3", jb, jb + cc), x, 8128, ALU.bitwise_and)
+                ts(R("J3", jb + cc, jb + 2 * cc), x, 63, ALU.bitwise_and)
+                cp(R("hl", jb, jb + 2 * cc), R("J3", jb, jb + 2 * cc))
+                mm([(R(db, do, do + n), [(full("Id"), R("Cd", 0, n))]
+                     + [(R("Dm", 128 * r, 128 * r + 128) if r < 15 else full("Id"), R("hl", jb + cc * k, jb + cc * k + cc),
+                         R(db, do + r, do + n, 16)) for r in range(16) for k in range(2)])])
+                act(pn("aD"), R(db, do, do + n), AF.Abs)
+                scan(pn("sD"), R("Kn", 0, n), pn("aD"), 0.0, ALU.add, ALU.min)
+                cp(R("xo", jb, jb + 2 * cc, 2), R("sD", pb + 15, pb + n, 16))
         bonus[0] = 0.0
         if t in (RO - 2, RO - 1):
             a = 0 if t == RO - 2 else 256 * t
@@ -422,13 +472,13 @@ def build():
             dma(("yz", a, 256 * t + 256), r, [r], [], 65536 * (5 if t == RO - 2 else 1))
         if t == RO - 1:
             break
-        pa = R("P7", 2 * PC, 2 * PC + 1)
+        pa = rg("pa", 1)
         mm([(pa, [(full("Af"), c1("mcnt", ch)) for ch in range(NC)])], f=4)
         cp(c1("ai", 0), pa)
         ts(c1("ai", 0), c1("ai", 0), 1, ALU.bitwise_and)
         ts(c1("thr", (t + 1) % 2), c1("ai", 0), 1.5, ALU.add, 2.0 ** 30, ALU.mult)
         for c in range(15, -1, -1):
-            bonus[0] = BONA if c < CC else BON5
+            bonus[0], bonus[1] = BONA if c < CC else BON5, 1 + c // CC
             zz = R("zin", 256 * t + 16 * c, 256 * t + 16 * c + 16)
             add("v", ("sca", R("X", 0, 8208), R("xo", 2 * c, 2 * c + 1), zz), [zz, c1("xo", 2 * c)], [R("X", 0, 8208)],
                 50 + 16 * SF * CY)
@@ -436,6 +486,7 @@ def build():
     bonus[0] = 0.0
     for ch in range(NC - 1, -1, -1):
         wb, pb, xb = 2 * PC * ch, PC * ch, 2 * RS * ch
+        bonus[1] = 10 + ch
         es = lambda k: R("Es", (15 * ch + k - 1) * PC, (15 * ch + k) * PC)
         ed = lambda k: R("Ed", (5 * ch + k - 1) * PC, (5 * ch + k) * PC)
         ym = lambda k: R("ymb", 256 * k + pb, 256 * k + pb + PC)
@@ -448,7 +499,7 @@ def build():
             ts(es(k), R("rk", wb, wb + PC), float(k), ALU.is_equal)
             if k < 6:
                 ts(ed(k), R("rk", wb + PC, wb + 2 * PC), float(k), ALU.is_equal)
-        pi = R("P3", 2 * PC, 2 * PC + 5 * CC)
+        pi = rg("pi", 5 * CC)
         mm([(pi, [(full("Id"), R("Ct", 0, 5 * CC))]
              + [(view("RE", r), R("Es", es(1)[1] + r, es(5)[2], 16)) for r in range(16)]
              + [(view(m, r), R("Ed", ed(1)[1] + r, ed(5)[2], 16)) for m in ("RE", "KE") for r in range(16)])])
@@ -456,7 +507,7 @@ def build():
         for k in range(1, 6):
             gat(ym(k), R("Mw", xb, xb + 2 * RS), R("to", CC * (5 * ch + k - 1), CC * (5 * ch + k)))
         for k in range(6, 16):
-            pp = R(("P3", "P2", "P7")[k % 3] if ch else dbank(), 384, 384 + PC)
+            pp = R(("P3", "P2", "P7")[k % 3] if ch else ("P0", "P1", "P4", "P5")[k % 4], 512 - PC, 512)
             mm([(pp, [(full("MT"), es(k))])])
             lin(ym(k), pp, 1.0)
     for a, b in KG:
@@ -465,7 +516,7 @@ def build():
     return ops
 
 
-def schedule(ops):
+def depend(ops):
     n = len(ops)
     hist = {}
     for k, o in enumerate(ops):
@@ -487,8 +538,14 @@ def schedule(ops):
             succ[j].append(k)
     pr = [0.0] * n
     for k in range(n - 1, -1, -1):
-        pr[k] = ops[k]["cost"] + ops[k].get("lat", LAT) + max([pr[j] for j in succ[k]] + [0.0])
-    pr = [p + o["bonus"] for p, o in zip(pr, ops)]
+        pr[k] = ops[k]["cost"] + ops[k]["lat"] + max([pr[j] for j in succ[k]] + [0.0])
+        ops[k]["pr"], ops[k]["succ"] = pr[k], succ[k]
+
+
+def schedule(ops):
+    n = len(ops)
+    succ = [o["succ"] for o in ops]
+    pr = [o["pr"] + o["bonus"] for o in ops]
     left = [len(o["deps"]) for o in ops]
     at = [0.0] * n
     ready = {e: [] for e in "vapgs"}
@@ -529,7 +586,7 @@ def schedule(ops):
         order.append(k)
         o["t0"] = st
         free[e] = st + o["cost"]
-        done = free[e] + o.get("lat", LAT)
+        done = free[e] + o["lat"]
         o["t1"] = done
         if e == "p":
             opened[o["bank"]] = not o["last"]
@@ -545,37 +602,48 @@ def schedule(ops):
     return order
 
 
-def plan():
-    extra, best, seed = {}, None, 1
-    for it in range(ITER):
-        ops = build()
-        for k, x in extra.items():
-            ops[k]["bonus"] += x
+def replay(ops, order, costs):
+    free, end, done = {}, [0.0] * len(ops), [0.0] * len(ops)
+    for k in order:
+        o = ops[k]
+        e = o["eng"]
+        st = free.get(e, 0.0)
+        for j in o["deps"]:
+            x = end[j] if e == "p" and ops[j]["eng"] == "p" else done[j]
+            if x > st:
+                st = x
+        end[k] = free[e] = st + costs[k][0][e]
+        done[k] = end[k] + costs[k][1]
+    return max(done)
+
+
+def plan(start=None, iters=None, seed=1):
+    base = build(MODELS[0])
+    depend(base)
+    costs = [[({e: c for e, (_, c) in o["alt"].items()} if "alt" in o else {o["eng"]: o["cost"]}, o["lat"]) for o in build(m)]
+             for m in MODELS[1:]]
+    keys = sorted(set(o["key"] for o in base if o["key"][0]))
+    extra = dict(zip(keys, start or []))
+    best = None
+    state = [seed]
+
+    def draw(n):
+        state[0] = (state[0] * 6364136223846793005 + 1442695040888963407) % 2 ** 64
+        return (state[0] >> 33) % n
+
+    for it in range((ITER if iters is None else iters) + 1):
+        trial = dict(extra)
+        if it:
+            for _ in range(1 + draw(5)):
+                k = keys[draw(len(keys))]
+                trial[k] = trial.get(k, 0) + (-8, -4, -2, -1, 1, 2, 4, 8)[draw(8)]
+        ops = [dict(o, deps=set(o["deps"]), bonus=o["bonus"] + 500.0 * trial.get(o["key"], 0)) for o in base]
         order = schedule(ops)
-        end = max(o["t1"] for o in ops)
-        if best is None or end < best[0]:
-            best = (end, ops, order, dict(extra))
-        elif end > best[0] + 1500.0:
-            extra = dict(best[3])
-            ops, order = best[1], best[2]
-        prev, last = {}, {}
-        for k in order:
-            prev[k] = last.get(ops[k]["eng"])
-            last[ops[k]["eng"]] = k
-        k = max(range(len(ops)), key=lambda j: ops[j]["t1"])
-        while k is not None:
-            o = ops[k]
-            d = max(o["deps"], key=lambda j: ops[j]["t1"]) if o["deps"] else None
-            p = prev[k]
-            seed = (seed * 1103515245 + 12345) % 2147483648
-            if p is not None and (d is None or ops[p]["t0"] + ops[p]["cost"] >= ops[d]["t1"]) and p not in o["deps"]:
-                if seed % 100 < PB:
-                    extra[k] = extra.get(k, 0.0) + STEP
-                    extra[p] = extra.get(p, 0.0) - STEP
-                k = p
-            else:
-                k = d
-    return best[1], best[2]
+        ends = [replay(ops, order, c) for c in costs]
+        val = sum(x / m["END"] for x, m in zip(ends, MODELS[1:]))
+        if best is None or val <= best[0]:
+            best, extra = (val, ops, order, ends), trial
+    return best[1], best[2], best[3], [extra.get(k, 0) for k in keys]
 
 
 _PLAN = []
@@ -586,7 +654,7 @@ def rank_program(g, core, T, topo):
     if rank is None:
         return
     if not _PLAN:
-        _PLAN.extend(plan())
+        _PLAN.extend(plan()[:2])
     ops, order = _PLAN
     nxt = T.cores[(rank + 1) % len(T.cores)]
     prv = T.cores[(rank - 1) % len(T.cores)]
@@ -659,6 +727,8 @@ def rank_program(g, core, T, topo):
             ins = q.tensor_copy(ap(c[2]), src) if c[1] == "v" else q.activation(ap(c[2]), src, AF.Copy)
         elif f == "sca":
             ins = q.tensor_copy(ap(c[1]).indirect(ap(c[2])), ap(c[3]))
+        elif f == "sel":
+            ins = q.affine_select(ap(c[1]), ap(c[2]), [[0, 8], [1, 16]], ALU.is_equal, 0.0, -c[3], 0)
         elif f == "iota":
             ins = (q.iota(ap(c[1]), c[2], c[3], c[4]) if _S[c[1][0]][1] == I32
                    else q.iota(ap(c[1]), c[2], c[3], c[4], allow_small_or_imprecise_dtypes=True))

@@ -1,68 +1,64 @@
 from concourse.mybir import AluOpType as ALU, AxisListType, ActivationFunctionType as AF
 
-NC = 2
-PC = 256 // NC
-CC = PC // 16
-RS = 16 * PC
-RO = 6
-BIG = 2.0 ** 40
-WIN = [(0, 3), (4, 6), (7, 9), (10, 12), (13, 15)]
+NC, PC, CC, RO = 2, 128, 8, 6
+B1, B2, MISS, XS = 1031, 2064, 6, 3088
+WIN = [(0, 2), (3, 5), (6, 8), (9, 11), (12, 15)]
 KG = [(6, 10), (10, 13), (13, 16), (0, 3), (3, 6)]
 HWM = PC + 5 * CC
+SC, CR = 113.0 / 128, 1.5 * 2.0 ** 30
+KO = [sum(8 * (16 + i) for i in range(t)) for t in range(RO + 1)]
+H54 = 2.0 ** 54
+FOLD = 41.0 * 2 ** 18
 
 BF, F32, I32, U16 = "bfloat16", "float32", "int32", "uint16"
 _S = dict(
-    X=(8208, BF), Xh=(8192, BF), Mw=(8192, BF), e=(NC * 21 * PC, BF), G=(NC * 21 * PC, BF),
+    X=(8208, BF), Xh=(NC * XS, BF), Mw=(NC * XS, BF), e=(NC * 16 * PC, BF), G=(NC * 21 * PC, BF),
     zin=(6 * 256, BF), yzb=(6 * 256, BF), ymb=(4096, BF), m0s=(16, BF), wts=(16, BF),
     MZ=(NC * 5 * PC, BF), TH=(NC * 5 * PC, BF), I1=(NC * 2 * HWM, I32), I2=(NC * HWM, I32), off=(NC * HWM, U16),
-    W=(512, BF), MW=(512, BF), H=(512, BF), Hv=(512, BF), Cq=(5 * 512, BF), sel=(512, BF), one=(PC, BF),
-    bot=(256, BF), miss=(256, BF), mcnt=(8, F32), sc=(256, F32), idx=(16, U16), xs=(256, BF), ms=(256, BF),
-    b2=(256, I32), t1=(256, F32), e1=(256, I32), UZ=(256, BF), J1=(32, I32), J2=(16, I32), J3=(32, I32), hl=(32, BF),
-    aD=(256, F32), sD=(256, F32), xo=(32, U16), ai=(8, I32), thr=(8, F32),
-    al=(512, BF), rk=(512, BF), Es=(15 * 256, BF), Ed=(5 * 256, BF), to=(80, U16),
-    pi=(8, I32), col=(16, F32), Dn=(128, F32), Gn=(128, F32), Rn=(256, F32), Nn=(144, F32), N16=(256, F32),
-    Id=(128, BF), O=(128, BF), E=(144, BF), A=(144, BF), B=(144, BF), SE=(144, BF), RE=(144, BF), KE=(144, BF),
-    OM=(128, BF), AM=(128, BF), BM=(128, BF), CM=(2048, BF), SM=(2048, BF), mf=(32, F32), wf=(8, F32),
-    pw=(64, F32), pc=(64, F32), dl=(256, F32), Wn=(16, F32), Lq=(640, BF), Ld=(640, BF),
-    BI=(128, BF), nBO=(128, BF), I2O=(128, BF), QO=(128, BF), QI=(128, BF), nI=(128, BF), n5I=(128, BF), n5O=(128, BF),
-    Os=(128, BF), OK=(128, BF), Tl=(128, BF), TB=(128, BF), RSm=(128, BF), RDm=(128, BF), Zc=(128, BF),
-    Dm=(15 * 128, BF), S1=(16, F32), S2=(16, F32), Ci=(PC, BF), Kx=(512, BF), Kn=(256, F32), Cd=(256, BF), Ct=(5 * CC, BF),
-    Af=(128, F32), Cm=(256, BF), Oa=(128, BF), Ob=(128, BF), n5P=(128, BF), b1=(256, F32), ry=(768, BF), K8=(128, BF), OW=(128, BF), JF=(32, F32), MT=(128, BF), su=(512, F32), F1=(NC * 2 * HWM, F32),
+    F1=(NC * 2 * HWM, F32), H=(512, BF), b=(512, BF), Cq=(5 * 512, BF), rank=(512, BF), pen=(512, BF),
+    mcnt=(8, F32), sc=(256, F32), idx=(16, U16), ds=(256, BF), ms=(256, BF), e1=(256, I32), UZ=(256, BF),
+    J1=(32, I32), J2=(16, I32), J3=(32, I32), hl=(32, BF), aD=(256, F32), sD=(256, F32), xo=(32, U16), ai=(8, I32),
+    su=(512, F32), rk=(256, BF), Es=(20 * PC, BF), Ew=(20 * PC, BF), se=(10 * PC, F32), to=(80, U16),
+    pi=(8, I32), col=(40, F32), penb=(8, F32), Dn=(128, F32), Gn=(128, F32), Gw=(256, F32), G32=(128, F32), Rn=(256, F32),
+    Nn=(144, F32), N8=(128, F32), Id=(128, BF), O=(128, BF), E=(144, BF), A=(144, BF), B=(144, BF),
+    OM=(128, BF), AM=(144, BF), BM=(144, BF), AH=(512, BF), BH=(512, BF), mf=(16, F32), wf=(8, F32),
+    pw=(16, F32), pc=(32, F32), dl=(256, F32), RB=(16, BF), RS=(256, BF), Of=(256, BF), Om=(256, BF), OA=(256, BF), OB=(256, BF),
+    Lq=(6 * 256, BF), IB=(256, BF), RE=(256, BF), KE=(256, BF), PN=(256, BF), pn=(256, BF), L=(128, BF), L2=(128, BF),
+    sI=(128, BF), nI=(128, BF), hI=(128, BF), gI=(128, BF), qI=(128, BF), I2x=(128, BF), zI=(128, BF), one=(PC, BF),
+    KD=(KO[RO], BF), rm=(2 * 168, BF), t1=(128, BF), t2=(128, BF), Zc=(128, BF), Dm=(15 * 128, BF), S1=(16, F32), S2=(16, F32), Ci=(PC, BF), Kx=(512, BF),
+    Kn=(256, F32), Cd=(256, BF), Af=(128, F32), Cm=(256, BF), Oa=(128, BF), Ob=(128, BF), K8=(128, BF), MT=(128, BF),
 )
 SCRATCH = {k: ("sbuf", [128, n], d) for k, (n, d) in _S.items()}
-for _b in range(8):
-    SCRATCH["P%d" % _b] = ("psum", [128, 512], F32)
-NDMA = 20
+W3 = dict(Hs0=32, Hs1=32, PR=32)
+for _k, _n in (("Hs0", 8), ("Hs1", 8), ("PR", 16)):
+    SCRATCH[_k] = ("sbuf", [128, _n, 32], BF)
+    _S[_k] = (32 * _n, BF)
+for _b in ("P0", "P1", "P2", "P3", "P4", "P5", "Q0", "Q1"):
+    SCRATCH[_b] = ("psum", [128, 512], F32)
+NDMA = 16
 SEMAPHORES = (["cv", "ca", "cp", "cg", "sent"] + ["d%d" % k for k in range(NDMA)]
               + ["r%d_%d" % (t, c) for t in range(1, RO) for c in range(NC)])
 
 DLAT = 2200.0
-_M = dict(CY=0.95, PCY=0.48, LAT=170.0, RLAT=3200.0, OV=55.0, MINC=0.0, GF=1.56, SF=3.8, XB=1 << 20, END=190000.0)
-MODELS = [_M, dict(_M, CY=0.83, PCY=0.42, OV=50.0, END=174000.0), dict(_M, CY=1.0, PCY=0.5, OV=60.0, END=197000.0),
-          dict(_M, CY=1.2, PCY=0.6, OV=72.0, GF=1.7, END=227000.0)]
-TUNED = [-2,0,-1,4,2,-11,-10,8,4,1,5,2,7,-4,0,6,0,-1,18,0,-6,-1,19,-9,0,-1,2,-3,1,-18,3,2,4,0,0,-1,-1,6,-3,-1,6,0,0,0,0,-3,-14,-19,1,4,-24,-10,11,1,-2,-1,17,0,-16,2,0,0,0,0,0,1,0,0,1,12,0,1,2,3,4,2,-8,1,-3,0,0,-4,7,0,4,-11,4,0,-8,1,5,4,-2,0,4,-1,-4,0,0,-4,-2,6,2,4,-1,12,-5,-4,-1,4,6,-1,-1,-2,8,-2,0,-4,26,-1,3,0,5,1,10,16,-8,8,4,-7,-4,11,1,12,0,-7,1,5,-2,0,4,-2,-5,-4,6,1,1,2,-9,-5,0,13,0,0,0,-3,0,0,-1,0,2,0,1,2,0,10,-6,-9,-6,2,3,9,4,3,-5,3,-6,-7,-1,-1,0,0,0,0,0,-2,2,0,0,0,0,0,-2,1,5,3,-6,6,2,2,4,1,0,1,-4,0,4,0,-1,-3,1,-4,-7,-1,0,-1,2,4,1,5,0,0,0,-9,1,-6,-1,0,0,-12,0,2,4,-4,1,0,-1,6,-12,-11,-4,-2,-3,0,0,2,0,2,0,4,-2,-2,10,0,0,19,6,0,-2,-8,0,2,2,-1,0,0,7,-1,1,0,-2,2,0,1,0,-8,-5,12,-9,-13,0,-14,0,11,-4,-11,-8,-1,2,-11,-1,4,-8,2,0,4,3,-1,8,7,16,-2,7,0,0,-1,0,0,-2,4,-3,-2,-4,1,-3,5,4,6,-2,20,1,-2,21,0,0,1,1,-9,8]
-BON1, BON2, ONLY, FM, SU, SUB, DF = 1000.0, 5000.0, 0, 1, 3, 2, 4
-MZA, UZA, FJ, PSM, PP, MG, HA, XS, XM = 0, 0, 0, 16, 0, 0, 0, 3, 1
-BONA, BONH, BON3, BON4, BON5, BON6 = 0.0, 0.0, 2000.0, 2000.0, 2000.0, 0.0
-ITER = 1500
-NG, INIT, ALTP, SLACK, GAM = 4, 0, 2000.0, 100.0, 50.0
+_M = dict(CY=0.95, PCY=0.48, LAT=170.0, RLAT=3200.0, OV=55.0, GF=1.56, SF=3.8, XB=1 << 20, END=150000.0)
+MODELS = [_M, dict(_M, CY=0.83, PCY=0.42, OV=50.0, END=135000.0), dict(_M, CY=1.0, PCY=0.5, OV=60.0, END=155000.0),
+          dict(_M, CY=1.2, PCY=0.6, OV=72.0, GF=1.7, END=180000.0)]
+OPT = dict(FM=3, MZA=0, UZA=0, SCV=3, AB=(0, 0), NG=2, DF=1, ND=3, WAW=0, BON1=1000.0, BON2=5000.0, BON3=2000.0, BON4=2000.0,
+           BON5=2000.0, ALTP=6000.0, SLACK=100.0, GAM=50.0, ITER=600)
 
 
 def R(n, a, b, s=1):
     return (n, a, b, s)
 
 
-RG = (dict(bot=(0, 256), zp=(2, 0), v=(6, 0), T=(7, 0), ib=(7, 256), y1=(1, 0), y2=(1, 256), bs=(3, 0), th=(3, 256), x=(0, 0),
-           j=(7, 0), D=(5, 0), pa=(7, 256), pi=(7, 0)) if NC == 1 else
-      dict(bot=(2, 384), zp=(3, 2 * HWM), v=(3, None), T=(6, 256), ib=(6, 384), y1=(7, 0), y2=(7, 128), bs=(7, 256), th=(7, 384),
-           x=(2, 256), j=(3, 2 * HWM + PC), D=(5, 256), pa=(7, 256), pi=(3, 256)))
-
-
-def rg(n, w=PC, o=0, s=1):
-    return R("P%d" % RG[n][0], RG[n][1] + o, RG[n][1] + (w if s > 1 else o + w), s)
+def R3(n, g0, g1, a, b, s=1):
+    return (n, W3[n] * g0 + a, W3[n] * (g1 - 1) + b, 1, (g0, g1, a, b, s))
 
 
 def width(r):
+    if len(r) == 5:
+        g0, g1, a, b, s = r[4]
+        return (g1 - g0) * ((b - a + s - 1) // s)
     return (r[2] - r[1] + r[3] - 1) // r[3]
 
 
@@ -71,18 +67,21 @@ def two(*rs):
 
 
 def build(M):
-    CY, PCY, LAT, RLAT, OV, MINC, GF, SF, XB = [M[k] for k in ("CY", "PCY", "LAT", "RLAT", "OV", "MINC", "GF", "SF", "XB")]
+    CY, PCY, LAT, RLAT, OV, GF, SF, XB = [M[k] for k in ("CY", "PCY", "LAT", "RLAT", "OV", "GF", "SF", "XB")]
     ops = []
     bonus = [0.0, 0]
 
     def add(eng, call, rd, wr, cost, lat=LAT, **kw):
         w = wr[0] if wr else ("", 0)
-        key = (bonus[1], call[0], w[0], w[1] % 256 if w[0] in ("zin", "yzb") else w[1] // 16 if w[0] in ("Mw", "TH") else w[1])
+        a = w[1] % 256 if w[0] in ("zin", "yzb") else 0 if w[0] in ("TH", "penb", "P0", "P1", "P2") else w[1]
+        if w[0] in ("Mw", "Xh") and w[1] % XS >= B2:
+            a = -1 - (w[1] % XS == B2 + MISS)
+        key = (bonus[1], call[0], "P0" if w[0] in ("P1", "P2") else w[0], a)
         ops.append(dict(eng=eng, call=call, rd=[r for r in rd if isinstance(r, tuple)], wr=wr, cost=cost, lat=lat,
                         bonus=bonus[0], key=key, **kw))
 
     def vc(n):
-        return OV + max(MINC, n) * CY
+        return OV + n * CY
 
     def ts(o, i, s1, op0, s2=None, op1=None):
         add("v", ("ts", o, i, s1, s2, op0, op1), [i, s1, s2], [o], vc(width(o) * (0.5 if two(o, i) else 1)))
@@ -112,9 +111,7 @@ def build(M):
         v, a = ops.pop(), ops.pop()
         ops.append(dict(a, rd=a["rd"] + v["rd"], alt={"a": (a["call"], a["cost"]), "v": (v["call"], v["cost"])}))
 
-    def gat(o, win, offs, only=False):
-        if only:
-            return add("a", ("gat", "a", o, win, offs), [win, offs], [o], 60 + GF * CY * width(o))
+    def gat(o, win, offs):
         either(*[lambda e=e: add(e, ("gat", e, o, win, offs), [win, offs], [o], 60 + GF * CY * width(o)) for e in "av"])
 
     def lin(o, i, scale, bias=0.0):
@@ -123,12 +120,13 @@ def build(M):
     def iota(o, pat, base, cm):
         add("g", ("iota", o, pat, base, cm), [], [o], 130 + 2 * CY * width(o))
 
-    def mm(groups, first=True, last=True, f=1):
+    def mm(groups, first=True, last=True, f=1, one=False):
         rd, cost, calls = [], 30.0, []
-        for o, terms in groups:
+        for n, (o, terms) in enumerate(groups):
             for k, tm in enumerate(terms):
                 oo = tm[2] if len(tm) > 2 else o
-                calls.append((oo, tm[0], tm[1], first and k == 0, last and k == len(terms) - 1))
+                calls.append((oo, tm[0], tm[1], first and k == 0 and not (one and n),
+                              last and k == len(terms) - 1 and not (one and n < len(groups) - 1)))
                 rd += [tm[0], tm[1]]
                 cost += max(64, width(tm[1])) * PCY * f
         add("p", ("mm", calls), rd, [o for o, _ in groups], cost, first=first, last=last, bank=groups[0][0][0])
@@ -142,11 +140,21 @@ def build(M):
     def full(n):
         return R(n, 0, 128)
 
+    def wide(n):
+        return R(n, 0, 256)
+
     def c1(n, k):
         return R(n, k, k + 1)
 
     def view(n, r):
         return R(n, 15 - r, 143 - r)
+
+    ncol = [4]
+
+    def column(src, s1, op0, s2=None, op1=None):
+        ncol[0] += 1
+        ts(c1("col", ncol[0]), src, s1, op0, s2, op1)
+        return c1("col", ncol[0])
 
     dma(R("zin", 0, 256), ("z0", 0, 256), [], [R("zin", 0, 256)], 65536)
     dma(R("wts", 0, 2), ("wt", 0, 2), [], [R("wts", 0, 2)], 512)
@@ -154,317 +162,307 @@ def build(M):
     for k in range(2):
         r = R("X", 16 + 4096 * k, 16 + 4096 * (k + 1))
         dma(r, ("xr", 4096 * k, 4096 * (k + 1)), [], [r], XB * (k + 1))
-    for ch in range(NC * INIT):
-        for n in ("Xh", "Mw"):
-            r = R(n, 2 * RS * ch + RS, 2 * RS * (ch + 1))
-            dma(r, ("xr", 0, RS), [R("X", 16, 8208)], [r], 1 << 20)
 
     iota(c1("pi", 0), [[0, 1]], 0, 1)
     iota(full("Gn"), [[16, 8], [0, 16]], 0, 0)
-    iota(R("Nn", 0, 144), [[1, 144]], -15, 0)
     iota(full("Dn"), [[1, 128]], 0, -1)
-    iota(R("Rn", 0, 256), [[0, 16], [1, 16]], 0, 0)
-    iota(R("N16", 0, PC), [[16, PC]], 32768, 0)
-    iota(R("Ct", 0, 5 * CC), [[0, 5], [256, CC]], 0, 0)
-    ts(c1("pi", 1), c1("pi", 0), 15, ALU.bitwise_and)
-    ts(c1("pi", 2), c1("pi", 0), 112, ALU.bitwise_and)
-    cp(R("col", 0, 3), R("pi", 0, 3))
-    rc, gc = c1("col", 1), c1("col", 2)
+    iota(R("Nn", 0, 144), [[1, 144]], -15, 0)
+    iota(wide("Rn"), [[0, 16], [1, 16]], 0, 0)
+    iota(wide("Gw"), [[-128, 2], [32, 8], [0, 16]], 0, 0)
+    iota(full("G32"), [[32, 4], [0, 32]], 0, 0)
+    iota(full("N8"), [[8, PC]], 32768, 0)
+    for k, v in enumerate((15, 112, 31, 96)):
+        ts(c1("pi", 1 + k), c1("pi", 0), v, ALU.bitwise_and)
+    cp(R("col", 0, 5), R("pi", 0, 5))
+    rc, gc, row, g32 = [c1("col", k) for k in range(1, 5)]
     ts(full("O"), full("Gn"), gc, ALU.is_equal)
     ts(R("E", 0, 144), R("Nn", 0, 144), gc, ALU.is_equal)
     ts(full("Id"), full("Dn"), 0.0, ALU.is_equal)
     cp(R("wf", 0, 2), R("wts", 0, 2))
+    cp(R("mf", 0, 16), R("m0s", 0, 16))
     for g in range(8):
         ts(R("OM", 16 * g, 16 * g + 16), R("m0s", 0, 16), c1("O", 16 * g), ALU.mult)
-    lin(full("AM"), full("OM"), c1("wf", 0))
-    lin(full("BM"), full("OM"), c1("wf", 1))
-    lin(R("A", 0, 144), R("E", 0, 144), c1("wf", 0))
-    lin(R("B", 0, 144), R("E", 0, 144), c1("wf", 1))
-    ts(R("dl", 0, 256), R("Rn", 0, 256), rc, ALU.is_equal)
-    ms(R("pc", 0, 64), 0.0)
-    for k, (q, init) in enumerate(((2.0 ** -10, 2.0 ** 86), (0.5, 2.0 ** 16), (2.0, 2.0 ** -16), (2.0, 2.0 ** 15))):
-        if k < 3:
-            ms(R("pc", 16 * k, 16 * k + 16), q)
-        scan(R("pw", 16 * k, 16 * k + 16), R("pc", 16 * min(k, 2), 16 * min(k, 2) + 16), R("pc", 48, 64), init, ALU.mult, ALU.add)
-    tt(R("pw", 0, 64), R("pw", 0, 64), R("dl", 0, 64), ALU.mult)
-    for k in range(3):
-        red(c1("col", 3 + k), R("pw", 16 * k, 16 * k + 16))
-    wc, w0c, iwc = c1("col", 3), c1("col", 4), c1("col", 5)
-    ts(R("mf", 0, 16), R("m0s", 0, 16), wc, ALU.mult)
-    lin(R("SE", 0, 144), R("E", 0, 144), wc)
-    lin(full("OW"), full("OM"), wc)
+    for k, n in enumerate("AB"):
+        ms(R(n + "M", 0, 8), 0.0)
+        ms(R(n + "M", 136, 144), 0.0)
+        lin(R(n + "M", 8, 136), full("OM"), c1("wf", k))
+        lin(R(n, 0, 144), R("E", 0, 144), c1("wf", k))
+        for h in range(2):
+            for b in range(2):
+                o, i = R(n + "H", 128 * (2 * h + b), 128 * (2 * h + b + 1)), R(n + "M", 8 + 8 * (h - b), 136 + 8 * (h - b))
+                add("g", ("sel", o, i, b), [i], [o], 170 + 256 * CY)
+    ts(wide("dl"), wide("Rn"), rc, ALU.is_equal)
+    ms(R("pc", 0, 16), 2.0 ** -10)
+    ms(R("pc", 16, 32), 0.0)
+    scan(R("pw", 0, 16), R("pc", 0, 16), R("pc", 16, 32), 2.0 ** 78, ALU.mult, ALU.add)
+    tt(R("pw", 0, 16), R("pw", 0, 16), R("dl", 0, 16), ALU.mult)
+    ncol[0] += 1
+    wc = c1("col", ncol[0])
+    red(wc, R("pw", 0, 16))
+    ts(R("RB", 0, 8), R("O", 0, 128, 16), -H54, ALU.mult, H54, ALU.mult)
+    ts(R("RB", 8, 16), R("O", 0, 128, 16), wc, ALU.mult)
     for s in range(16):
-        add("g", ("sel", R("CM", 128 * s, 128 * s + 128), full("OM"), s), [full("OM")], [R("CM", 128 * s, 128 * s + 128)], 170 + 256 * CY)
-        if s < PSM:
-            add("g", ("sel", R("SM", 128 * s, 128 * s + 128), full("OW"), s), [full("OW")], [R("SM", 128 * s, 128 * s + 128)], 170 + 256 * CY)
-        else:
-            lin(R("SM", 128 * s, 128 * s + 128), view("E", s), c1("mf", s))
-    for n, src, v in (("nI", "Id", -1.0), ("BI", "Id", BIG), ("nBO", "O", -BIG), ("QO", "O", 2.0 ** 30), ("QI", "Id", 2.0 ** 28),
-                      ("n5I", "Id", 1.0 / 512), ("OK", "O", -RS / 2.0), ("I2O", "Id", -2.0 ** 31)):
-        lin(full(n), full(src), v)
-    ts(full("Os"), full("O"), rc, ALU.mult, -0.5, ALU.mult)
-    tt(full("Zc"), full("O"), full("Id"), ALU.add)
-    tt(full("I2O"), full("I2O"), full("QO"), ALU.add)
+        lin(R("RS", 16 * s, 16 * s + 16), R("RB", 0, 16), c1("mf", s))
+    for n, v in (("sI", SC), ("nI", -SC), ("hI", 0.5), ("gI", -0.5), ("qI", 0.25), ("I2x", 2.0), ("zI", 1.0 / 128), ("K8", 256.0)):
+        lin(full(n), full("Id"), v)
     ms(R("one", 0, PC), 1.0)
-    ts(full("Tl"), R("Rn", 0, 128), rc, ALU.is_lt)
-    tt(full("Tl"), full("Tl"), full("O"), ALU.mult)
-    ts(full("TB"), full("Tl"), -2.0, ALU.mult)
-    tt(full("TB"), full("TB"), full("Id"), ALU.add)
-    ts(full("TB"), full("TB"), iwc, ALU.mult)
-    ms(R("Lq", 0, 640), 0.0)
+    live = column(row, 11.0, ALU.is_ge)
+    r0 = column(row, 0.0, ALU.is_equal)
+    up = column(row, 22.0, ALU.is_ge)
+    lowr = column(r0, -8.0, ALU.mult, live, ALU.add)
+    lowr = column(lowr, up, ALU.subtract)
+    ts(wide("Of"), wide("Gw"), g32, ALU.is_equal)
+    lin(wide("Om"), wide("Of"), live)
+    lin(wide("OA"), wide("Of"), lowr)
+    lin(wide("OB"), wide("Of"), up)
+    ms(R("Lq", 0, 6 * 256), 0.0)
     for q, (a, b) in enumerate(WIN):
         for p in range(a, b + 1):
-            ts(R("Lq", 128 * q + p, 128 * q + 128, 16), R("O", p, 128, 16), 2.0 ** (5 * p - 37), ALU.mult)
-    ts(c1("col", 6), rc, 4.5, ALU.is_lt)
-    ts(R("Ld", 0, 640), R("Lq", 0, 640), c1("col", 6), ALU.mult)
-    tt(R("N16", 0, PC), R("N16", 0, PC), R("dl", 0, PC), ALU.mult)
-    ts(R("Ci", 0, PC), R("N16", 0, PC), -32768.0, ALU.add)
-    for k in range(0, 512 if MG else 2 * PC, 256):
-        ts(R("Kx", k, k + 256), R("Rn", 0, 256), 0.0, ALU.is_equal, -2.0 ** 22, ALU.mult)
-    lin(R("Cm", 0, 256), R("dl", 0, 256), 2.0 ** 21, -2.0 ** 21)
-    lin(full("K8"), full("Id"), 256.0)
-    lin(full("Oa"), full("O"), c1("wf", 0))
-    lin(full("Ob"), full("O"), c1("wf", 1))
+            for k, src in ([(q, "Om")] if q < 4 else [(4, "OA"), (5, "OB")]):
+                lin(R("Lq", 256 * k + p, 256 * k + 256, 16), R(src, p, 256, 16), 2.0 ** (5 * p - 33))
+    st = column(row, 16.0, ALU.is_ge)
+    step = column(st, 2.0, ALU.mult, live, ALU.subtract)
+    for r, v in ((15, 1 - B2), (23, B1 - 8), (31, B2 + MISS - B1 - 8)):
+        x = column(row, float(r), ALU.is_equal, float(v), ALU.mult)
+        step = column(x, step, ALU.add)
+    lin(wide("IB"), wide("Of"), step)
+    base = column(r0, 16.5, ALU.mult, -15.0, ALU.add)
+    cp(c1("penb", 0), base)
+    first = column(row, -16.0, ALU.add, live, ALU.mult)
+    ca = column(live, -63.0, ALU.mult)
+    cb = column(row, 10.0, ALU.is_ge, 64.0, ALU.mult)
+    x = column(row, 31.0, ALU.not_equal)
+    cb = column(cb, x, ALU.mult)
+    ts(full("L"), full("Dn"), 0.0, ALU.is_equal, ca, ALU.mult)
+    ts(full("L2"), full("Dn"), 1.0, ALU.is_equal, cb, ALU.mult)
+    tt(full("L"), full("L"), full("L2"), ALU.add)
+    ms(R("PR", 128, 256), 0.0)
+    ms(R("PR", 384, 512), 0.0)
+    x = column(r0, H54, ALU.mult, H54, ALU.mult)
+    ts(full("t1"), full("G32"), g32, ALU.is_equal, x, ALU.mult)
+    ts(full("t2"), full("Id"), -64.0 * H54, ALU.mult, H54, ALU.mult)
+    tt(full("PR"), full("t1"), full("t2"), ALU.add)
+    lin(R("PR", 256, 384), full("Id"), 2.0 ** 78)
+    ms(R("KD", 0, KO[RO]), 1.0)
+    for t in range(RO):
+        ms(R("KD", KO[t], KO[t + 1], 16 + t), 0.0)
+    x = column(row, 31.0, ALU.is_equal)
+    lin(full("Af"), R("one", 0, PC), x)
+    for ch in range(NC):
+        ms(R("Hs%d" % ch, 0, 256), 0.0)
+        ms(R3("Hs%d" % ch, 0, 8, 0, 1), 2.0 ** 78)
+        for h in range(2):
+            lin(R("rank", 256 * ch + PC * h, 256 * ch + PC * h + PC), R("one", 0, PC), first)
+    tt(full("Zc"), full("O"), full("Id"), ALU.add)
+    tt(full("N8"), full("N8"), full("dl"), ALU.mult)
+    ts(full("Ci"), full("N8"), -32768.0, ALU.add)
+    for k in range(0, 512, 256):
+        ts(R("Kx", k, k + 256), wide("Rn"), 0.0, ALU.is_equal, -2.0 ** 22, ALU.mult)
+    lin(wide("Cm"), wide("dl"), 2.0 ** 21, -2.0 ** 21)
+    ts(full("Oa"), full("O"), c1("wf", 0), ALU.mult, 128.0, ALU.mult)
+    ts(full("Ob"), full("O"), c1("wf", 1), ALU.mult, 128.0, ALU.mult)
     mm([(R("P0", 0, 128), [(full("OM"), full("Id"))])])
     lin(full("MT"), R("P0", 0, 128), 1.0)
-    ts(R("Kn", 0, 256), R("Rn", 0, 256), 0.0, ALU.is_equal, 2.0 ** 29, ALU.mult)
-    ts(R("Cd", 0, 256), R("Rn", 0, 256), rc, ALU.is_ge, 2.0 ** 28, ALU.mult)
-    ts(R("Cd", 0, 256), R("Cd", 0, 256), rc, ALU.add)
+    ts(wide("Kn"), wide("Rn"), 0.0, ALU.is_equal, 2.0 ** 29, ALU.mult)
+    ts(wide("Cd"), wide("Rn"), rc, ALU.is_ge, 2.0 ** 28, ALU.mult)
+    ts(wide("Cd"), wide("Cd"), rc, ALU.add)
     ms(R("Cd", 15, 256, 16), 16.0)
     ts(R("S1", 0, 16), R("dl", 0, 16), -1.0, ALU.mult, 2.0, ALU.add)
     ts(R("S2", 0, 16), R("dl", 0, 16), 32768.0, ALU.mult, -16384.0, ALU.add)
     for r in range(15):
         ts(R("Dm", 128 * r, 128 * r + 128), full("Zc"), c1("S1", r), ALU.is_equal, c1("S2", r), ALU.mult)
-    ms(full("Af"), 1.0 / 8192)
-    ms(c1("thr", 0), 1.5 * 2.0 ** 30)
-    ts(c1("col", 7), rc, 16.0, ALU.mult)
+    a = XS * (NC - 1)
+    for h in range(2):
+        n, o = 8, a + B1 * h
+        cp(R("Mw", o, o + 8), R("m0s", 8 * h, 8 * h + 8))
+        while n < 8 * PC:
+            lin(R("Mw", o + n, o + 2 * n), R("Mw", o, o + n), 1.0)
+            n *= 2
+        ms(R("Mw", o + n, a + (B2 if h else B1)), 0.0)
+    dma(R("Mw", 0, B2), R("Mw", a, a + B2), [R("Mw", a, a + B2)], [R("Mw", 0, B2)], 1 << 19)
     for ch in range(NC):
-        b = 2 * PC * ch
-        ms(R("W", b + PC, b + 2 * PC), 0.0)
-        lin(R("W", b, b + PC), R("one", 0, PC), w0c)
-        if ch == NC - 1:
-            n, a = 16, 2 * RS * ch
-            cp(R("Mw", a, a + 16), R("m0s", 0, 16))
-            while n < RS:
-                cp(R("Mw", a + n, a + 2 * n), R("Mw", a, a + n))
-                n *= 2
-            for c in range(ch):
-                dma(R("Mw", 2 * RS * c, 2 * RS * c + RS), R("Mw", a, a + RS), [R("Mw", a, a + RS)], [R("Mw", 2 * RS * c, 2 * RS * c + RS)], 1 << 19)
-    lin(R("RE", 0, 144), R("E", 0, 144), rc)
-    lin(R("KE", 0, 144), R("E", 0, 144), float(RS))
-    ts(full("RDm"), full("Id"), -64.0, ALU.mult)
-    tt(full("RSm"), full("RDm"), full("O"), ALU.add)
-    tt(full("RSm"), full("RSm"), full("Tl"), ALU.subtract)
-    tt(full("RSm"), full("RSm"), full("Id"), ALU.subtract)
-    tt(full("RDm"), full("RDm"), full("Tl"), ALU.add)
+        ms(R("Mw", XS * ch + B2 + MISS, XS * (ch + 1), 8), 0.0)
+    hi = column(row, 24.0, ALU.is_ge)
+    x = column(row, -16.0, ALU.add, hi, ALU.subtract)
+    y = column(row, -1.0, ALU.mult, 15.0, ALU.add)
+    lin(wide("RE"), wide("Of"), column(x, y, ALU.max))
+    x = column(row, 16.0, ALU.is_lt, float(B2), ALU.mult)
+    lin(wide("KE"), wide("Of"), column(hi, 1024.0, ALU.mult, x, ALU.add))
+    ts(wide("pn"), wide("Rn"), first, ALU.is_equal, st, ALU.mult)
+    tt(wide("PN"), wide("pn"), wide("Of"), ALU.mult)
 
-    def bottom(ch):
-        b = 2 * PC * ch
-        pb = rg("bot")
-        mm([(pb, [(full("TB"), R("W", b, b + PC))])])
-        act(R("bot", PC * ch, PC * ch + PC), pb, AF.Sign, bias=0.5, scale=-1.0)
+    def penalty(ch, t):
+        o, i, c = R("pen", 256 * ch, 256 * ch + 256), R("rank", 256 * ch, 256 * ch + 256), c1("penb", t % 2)
+        either(lambda: act(o, i, AF.Relu, bias=c), lambda: ts(o, i, c, ALU.add, 0.0, ALU.max))
 
-    def hashed(src, bank, o, n, i1, a1, i2, a2):
+    def hashed(src, up, i1, a1, i2, a2):
+        n = width(up)
         uv, u, v, x = R(i1, a1, a1 + 2 * n), R(i1, a1, a1 + n), R(i1, a1 + n, a1 + 2 * n), R(i2, a2, a2 + n)
-        parts = [(uv, src[0])] if len(src) == 1 else [(u, src[0]), (v, src[1])]
         if _S[i1][1] == F32:
-            for d, s in parts:
-                act(d, s, AF.Identity, bias=2.0 ** 23 - 0.5, scale=2.0 ** -12 + 2.0 ** -34)
-                act(d, d, AF.Relu, bias=-2.0 ** 35, scale=4096.0)
-                if not (PP and src[0][0] == bank):
-                    tt(d, s, d, ALU.subtract)
-            up = R(bank, o, o + n)
-            if PP and src[0][0] == bank:
-                tt(v, src[1] if len(src) > 1 else R(bank, o + n, o + 2 * n), v, ALU.subtract)
-                tt(up, up, u, ALU.subtract)
-                tt(x, up, v, ALU.mult)
-                lin(up, up, 37.0)
-            else:
-                tt(x, u, v, ALU.mult)
-                lin(up, u, 37.0)
+            act(uv, src, AF.Identity, bias=2.0 ** 23 - 0.5, scale=2.0 ** -12 + 2.0 ** -34)
+            act(uv, uv, AF.Relu, bias=-2.0 ** 35, scale=4096.0)
+            tt(uv, src, uv, ALU.subtract)
+            lin(up, u, 1184.0, -FOLD)
         else:
-            for d, s in parts:
-                cp(d, s)
+            cp(uv, src)
             ts(uv, uv, 4095, ALU.bitwise_and)
-            tt(x, u, v, ALU.mult)
-            ts(R(bank, o, o + n), u, 37.0, ALU.mult)
-        ts(x, x, 5, ALU.arith_shift_right)
-        tt(x, x, R(bank, o, o + n), ALU.add)
+            ts(up, u, 1184.0, ALU.mult, -FOLD, ALU.add)
+        tt(x, u, v, ALU.mult)
+        tt(x, x, up, ALU.add)
         return x
 
     for ch in range(NC):
-        bottom(ch)
+        penalty(ch, 0)
     rot = [0]
 
     def dbank():
-        rot[0] = (rot[0] + 1) % 2
+        rot[0] = (rot[0] + 1) % OPT["ND"]
         return "P%d" % rot[0]
 
     Xg = R("X", 16, 8208)
     for t in range(RO):
         for ch in range(NC - 1, -1, -1):
             z = R("zin", 256 * t + PC * ch, 256 * t + PC * ch + PC)
-            xb, eb, mb, ob, wb, pb = 2 * RS * ch, 21 * PC * ch, 5 * PC * ch, HWM * ch, 2 * PC * ch, PC * ch
-            hw, cw = PC + t * CC, (2 * PC if t else PC)
+            xb, gb, mb, ob, wb, pb = XS * ch, 21 * PC * ch, 5 * PC * ch, HWM * ch, 256 * ch, PC * ch
+            hw, Q, Hs, Mb = PC + t * CC, "Q%d" % ch, "Hs%d" % ch, "P%d" % (4 + ch)
 
-            def dyn(n, k):
-                return R(n, xb + RS + k, xb + 2 * RS, 16)
+            def slot(n, s):
+                a = xb + (B1 * (s // 8) + s % 8 if s < 16 else B2 + s - 16)
+                return R(n, a, a + 8 * PC - 7, 8)
 
             def half(n, k, base=wb):
                 return R(n, base + k * PC, base + k * PC + PC)
 
+            def both(n, base=wb):
+                return R(n, base, base + 2 * PC)
+
             def pt(n):
                 return R(n, pb, pb + PC)
 
-            bonus[0], bonus[1] = BON1 * ch, ch + 1
-            zp = rg("zp")
-            if MZA >> ch & 1:
-                for a in range(0, t, 2):
-                    ks, bk = list(range(a, min(a + 2, t))), "P4"
-                    mm([(R(bk, (2 + k - a) * PC, (3 + k - a) * PC), [(full("Id"), z), (full("K8"), dyn("Mw", k))]) for k in ks])
-                    act(R("MZ", mb + a * PC, mb + (ks[-1] + 1) * PC), R(bk, 2 * PC, (2 + len(ks)) * PC), AF.Relu, bias=-256.0)
+            def mr(a, n=PC):
+                return R(Mb, a, a + n)
+
+            bonus[0], bonus[1] = OPT["BON1"] * ch, ch + 1
+            zp = R("P3", 2 * HWM, 2 * HWM + PC)
+            if OPT["MZA"] >> ch & 1:
+                for a in range(0, t, 4):
+                    ks, bk = list(range(a, min(a + 4, t))), dbank()
+                    mm([(R(bk, (k - a) * PC, (1 + k - a) * PC), [(full("Id"), z), (full("K8"), slot("Mw", 16 + k))]) for k in ks])
+                    act(R("MZ", mb + a * PC, mb + (ks[-1] + 1) * PC), R(bk, 0, len(ks) * PC), AF.Relu, bias=-256.0)
             elif t:
                 mm([(zp, [(full("Id"), z)])])
                 for k in range(t):
-                    tt(R("MZ", mb + k * PC, mb + k * PC + PC), dyn("Mw", k), zp, ALU.mult)
-            fm = FM and t > 0
-            k4 = lambda n: []
-            vb, vo = ("P3", hw) if NC > 1 else ("P6", 0)
-            for n, bk, o in (("A", "P3", 0), ("B", vb, vo)):
-                mm([(R(bk, o, o + PC), k4(PC) + [(full(n + "M"), z)])])
+                    tt(R("MZ", mb + k * PC, mb + k * PC + PC), slot("Mw", 16 + k), zp, ALU.mult)
+            for n, o in (("A", 0), ("B", hw)):
+                mm([(R("P3", o + 64 * h, o + 64 * h + 64),
+                     [(R(n + "H", 128 * (2 * h + b), 128 * (2 * h + b + 1)), R(z[0], z[1] + b, z[2], 2)) for b in range(2)])
+                    for h in range(2)])
                 if t:
-                    mm([(R(bk, o + PC, o + hw), k4(t * CC) + [(view(n, r), R("MZ", mb + r, mb + t * PC, 16)) for r in range(16)])])
-            x = hashed([R("P3", 0, 2 * hw)] if NC > 1 else [R("P3", 0, hw), R("P6", 0, hw)], "P3", 0, hw,
-                       "F1" if fm else "I1", 2 * ob, "I2", ob)
-            ts(x, x, 8191, ALU.bitwise_and)
+                    mm([(R("P3", o + PC, o + hw), [(view(n, r), R("MZ", mb + r, mb + t * PC, 16)) for r in range(16)])])
+            x = hashed(R("P3", 0, 2 * hw), R("P3", 0, hw), "F1" if OPT["FM"] >> ch & 1 else "I1", 2 * ob, "I2", ob)
+            ts(x, x, 5, ALU.arith_shift_right, 8191, ALU.bitwise_and)
             cp(R("off", ob, ob + hw), x)
-            for k in range(NG):
-                q = PC // NG
-                gat(R("Xh", xb + 16 * q * k, xb + 16 * q * (k + 1)), Xg, R("off", ob + q * k, ob + q * (k + 1)),
-                    ch == 0 and k < ONLY and t > 0)
+            c0, W = 16 - t, 16 + t
+            mm([(R(Q, 0, 16 * W), [(half("pen", 0), R3("PR", 0, 16, c0, 32))]),
+                (R(Q, 4 * W, 8 * W), [(half("pen", 1), R3("PR", 0, 4, c0, 32))]),
+                (R(Q, 12 * W, 16 * W), [(half("pen", 1), R3("PR", 8, 12, c0, 32))])], last=False, one=True)
+            q = 64 // OPT["NG"]
+            for h in range(2):
+                for k in range(OPT["NG"]):
+                    a = xb + B1 * h + 16 * q * k
+                    gat(R("Xh", a, a + 16 * q), Xg, R("off", ob + 64 * h + q * k, ob + 64 * h + q * (k + 1)))
             for k in range(t):
-                gat(dyn("Xh", k), Xg, R("off", ob + PC + CC * k, ob + PC + CC * (k + 1)), ch == 0 and ONLY == NG)
-            bonus[0] = BON2 if ch else BON6
-            PS = PC // SUB
-            per = 512 // PS
-            blocks = [(sb * PS, PS, list(range(a, a + per))) for sb in range(SUB) for a in range(0, 16, per)]
-            dblk = [(0, PC, list(range(16 + a, 16 + min(a + 512 // PC, t)))) for a in range(0, t, 512 // PC)]
-            blocks = blocks[:DF] + dblk + blocks[DF:]
-            for p0, pn, bl in blocks:
-                bk = dbank()
-                st = bl[0] < 16
-                zz = R(z[0], z[1] + p0, z[1] + p0 + pn)
-                mm([(R(bk, j * pn, j * pn + pn),
-                     [(full("Id"), R("Xh", xb + 16 * p0 + s, xb + 16 * (p0 + pn), 16) if st else dyn("Xh", s - 16)), (full("nI"), zz)])
-                    for j, s in enumerate(bl)])
-                n, g0 = len(bl) * pn, eb + 16 * p0 + bl[0] * pn
-                ee, gg = R("e", g0, g0 + n), R("G", g0, g0 + n)
-                if st:
-                    act(ee, R(bk, 0, n), AF.Abs)
-                    ts(gg, ee, 72.5, ALU.is_gt)
+                gat(slot("Xh", 16 + k), Xg, R("off", ob + PC + CC * k, ob + PC + CC * (k + 1)))
+            bonus[0] = OPT["BON2"] * ch
+            blocks = [list(range(a, a + 4)) for a in range(0, 16, 4)]
+            dblk = [list(range(16 + a, 16 + min(a + 4, t))) for a in range(0, t, 4)]
+            blocks = blocks[:OPT["DF"]] + dblk + blocks[OPT["DF"]:]
+            for bl in blocks:
+                bk, n, g0 = dbank(), len(bl) * PC, gb + bl[0] * PC
+                mm([(R(bk, j * PC, j * PC + PC), [(full("sI"), slot("Xh", s)), (full("nI"), z)]) for j, s in enumerate(bl)])
+                dd, gg = R(bk, 0, n), R("G", g0, g0 + n)
+                if bl[0] >= 16:
+                    act(dd, dd, AF.Abs)
+                    tt(gg, dd, R("TH", mb + (bl[0] - 16) * PC, mb + (bl[0] - 16) * PC + n), ALU.is_gt)
+                elif OPT["AB"][ch] >> bl[0] // 4 & 1:
+                    ee = R("e", (16 * ch + bl[0]) * PC, (16 * ch + bl[0]) * PC + n)
+                    act(ee, dd, AF.Abs)
+                    ts(gg, ee, 64.0, ALU.is_gt)
                 else:
-                    act(R(bk, 0, n), R(bk, 0, n), AF.Abs)
-                    tt(gg, R(bk, 0, n), R("TH", mb + (bl[0] - 16) * PC, mb + (bl[0] - 16) * PC + n), ALU.is_gt)
-                for bank, sm, dm in (("P4", "CM", "E"), ("P5", "SM", "SE")):
-                    mm([(R(bank, p0, p0 + pn) if st else R(bank, PC, 2 * PC),
-                         [(R(sm, 128 * s, 128 * s + 128) if st else view(dm, s - 16), R("G", g0 + j * pn, g0 + j * pn + pn))
-                          for j, s in enumerate(bl)])], first=bl[0] in (0, 16), last=bl[-1] in (15, 15 + t))
-            hot = BONA if ch == 0 else BON3
+                    ts(gg, dd, CR, ALU.add, CR, ALU.not_equal)
+                mm([(R(Q, t + s if s < 16 else t + 15 - s, 16 * W, W),
+                     [(R("G", g0 + j * PC, g0 + j * PC + PC), R("RS", 16 * s, 16 * s + 16) if s < 16 else R("RB", 0, 16))])
+                    for j, s in enumerate(bl)], first=False, last=bl is blocks[-1], one=True)
+            mm([(mr(0), [(full("qI"), R("one", 0, PC)), (full("hI"), z), (full("gI"), slot("Xh", 15 + t if t else 0))])])
+            ts(slot("Xh", 16 + MISS), mr(0), 1.5 * 2.0 ** 23, ALU.add, 1.5 * 2.0 ** 23, ALU.subtract)
+            hot = OPT["BON3"] * ch
             bonus[0] = hot
-            cwr = lambda n: R(n, wb, wb + cw)
-            cwr2 = lambda n: R(n, wb, wb + 2 * PC)
-            act(R("P4", 0, cw), R("P4", 0, cw), AF.Relu, bias=c1("thr", t % 2), scale=-2.0 ** 30)
-            tt(cwr("MW"), cwr("W"), R("P4", 0, cw), ALU.min)
-            hs = [0, 1] if t else [0]
-            mm([(R("P6", k * PC, k * PC + PC), [(full("QI"), R("one", 0, PC) if k else pt("bot"))]
-                 + [(full("I2O" if j == k else "QO"), half("MW", j)) for j in hs]) for k in hs])
-            act(cwr("sel"), R("P6", 0, cw), AF.Sign)
-            mm([(rg("T"), [(full("O"), half("MW", j)) for j in hs])])
-            act(pt("miss"), rg("T"), AF.Relu, bias=512.0, scale=-512.0, acc=c1("mcnt", ch))
-            ib = rg("ib")
-            mm([(ib, [(full("Id"), R("Ci", 0, PC))] + [(full("Os"), half("sel", j)) for j in hs]
-                 + ([(full("OK"), half("sel", 1))] if t else []))])
-            scan(pt("sc"), R("Kx", 0, PC), ib, 0.0, ALU.add, ALU.max)
+            rm = R("rm", 168 * ch, 168 * ch + 8 * W)
+            scan(rm, R("KD", KO[t], KO[t + 1]), R(Q, 0, 8 * W), 0.0, ALU.mult, ALU.max)
+            tt(R3(Hs, 0, 8, c0, 32), R(Q, 8 * W, 16 * W), rm, ALU.max)
+            mm([(R(Q, PC * h, PC * h + PC), [(R(Hs, PC * h, PC * h + PC), full("Id"))]) for h in range(2)])
+            act(both("b"), R(Q, 0, 256), AF.Relu, bias=1.0, scale=-2.0 ** -106, acc=c1("mcnt", ch))
+            act(both("H"), R(Q, 0, 256), AF.Sqrt)
+            mm([(mr(PC), [(full("Id"), full("Ci"))] + [(half("IB", h, 0), half("b", h)) for h in range(2)])])
+            scan(pt("sc"), R("Kx", 0, PC), mr(PC), 0.0, ALU.add, ALU.max)
             ix = R("idx", CC * ch, CC * ch + CC)
-            ts(ix, R("sc", pb + 15, pb + PC, 16), 120.0 + 8 * RS if t else 60.0, ALU.add)
-            gat(pt("ms"), R("Mw", xb, xb + 2 * RS), ix)
-            bonus[0] = BONH if ch == 0 else BON4
-            gat(pt("xs"), R("Xh", xb, xb + 2 * RS), ix)
-            x0 = dyn("Xh", t - 1) if t else R("Xh", xb, xb + RS, 16)
-            y1, y2, bs, th = rg("y1"), rg("y2"), rg("bs"), rg("th")
-            mm([(bs, [(full("Id"), z), (full("Id"), x0), (full("Id"), pt("miss"))])])
+            ts(ix, R("sc", pb + 15, pb + PC, 16), float(B2 + 4), ALU.add)
+            gat(pt("ms"), R("Mw", xb, xb + XS), ix)
+            bonus[0] = OPT["BON4"] * ch
+            win = R("Xh", xb, xb + XS)
+            add("v", ("gtt", pt("ds"), win, ix, z, ALU.subtract), [win, ix, z], [pt("ds")], 60 + GF * CY * PC)
             new = R("yzb", 256 * t + pb, 256 * t + pb + PC)
-            ts(pt("b2"), bs, 0.5, ALU.mult, -256.25, ALU.add)
-            mm([(y1, [(full("Id"), z), (full("nI"), pt("xs"))])])
-            act(y1, y1, AF.Abs)
-            tt(y1, y1, pt("miss"), ALU.subtract)
-            tt(new, y1, pt("b2"), ALU.max)
+            act(new, pt("ds"), AF.Abs)
             if t < RO - 1:
                 zn = R("zin", 256 * (t + 1) + pb, 256 * (t + 1) + pb + PC)
                 add("g", ("send", zn, new, "r%d_%d" % (t + 1, ch)), [new], [zn], 300.0, lat=RLAT)
             bonus[0] = hot
-            act(cwr("H"), R("P5", 0, cw), AF.Sqrt)
-            mm([(R("P2", k * PC, PC + k * PC), [(full("BI"), half("W", k))]
-                 + [(full("nBO"), half("MW", j)) for j in hs]) for k in hs])
-            tt(cwr("Hv"), cwr("H"), R("P2", 0, cw), ALU.min)
             terms = []
             for q, (a, b) in enumerate(WIN):
                 cb = 512 * q + wb
-                lo = 2.0 ** (38 - 5 * (b + 1)) if b < 15 else 0.0
-                ts(R("Cq", cb, cb + cw), cwr("Hv"), 2.0 ** (38 - 5 * (a - 1)) if a else BIG, ALU.min, lo, ALU.max)
-                terms += [(R("Ld" if j else "Lq", 128 * q, 128 * q + 128), half("Cq", j, cb)) for j in hs]
-            xx = rg("x")
-            cut = len(terms) * XS // 5
-            if cut and XM >> ch & 1:
-                mm([(xx, terms[:cut])], last=False)
-                mm([(xx, terms[cut:])], first=False)
-            else:
-                mm([(xx, terms)])
+                lo = 2.0 ** (34 - 5 * (b + 1)) if b < 15 else 0.0
+                ts(both("Cq", cb), both("H"), 2.0 ** (34 - 5 * (a - 1)), ALU.min, lo, ALU.max)
+                terms += [(half("Lq", h, 256 * k), half("Cq", h, cb)) for k in ([q] if q < 4 else [4, 5]) for h in range(2)]
+            xx = R(Q, 2 * PC, 3 * PC)
+            mm([(xx, terms[:6])], last=False)
+            ops[-1]["rd"].append(both("b"))
+            mm([(xx, terms[6:])], first=False, last=False)
+            mm([(xx, [(full("I2x"), pt("ms"))])], first=False)
             cp(pt("e1"), xx)
             ts(pt("e1"), pt("e1"), 62, ALU.bitwise_and)
-            mm([(th, [(full("n5I"), pt("miss")), (full("nI"), pt("ms"))])])
-            tt(dyn("Mw", t), pt("e1"), th, ALU.is_gt)
+            U = slot("Mw", 16 + t) if t < RO - 1 else R("ymb", pb, pb + PC)
+            ts(U, pt("e1"), 1.0, ALU.min)
             bonus[0] = 0.0
-            tt(cwr("W"), cwr("W"), R("P6", 0, cw), ALU.min)
-            either(lambda: act(half("W", 1), half("W", 1), AF.Relu, bias=c1("pw", 48 + t)),
-                   lambda: ts(half("W", 1), half("W", 1), c1("pw", 48 + t), ALU.max))
-            either(lambda: act(half("W", 0), half("W", 0), AF.Relu), lambda: ts(half("W", 0), half("W", 0), 0.0, ALU.max))
+            sp = mr(2 * PC, 2 * PC)
+            if OPT["SCV"] >> ch & 1:
+                mm([(sp, [(full("L"), both("b"))])])
+                tt(both("rank"), sp, both("rank"), ALU.add)
+            else:
+                mm([(sp, [(full("L"), both("b")), (full("Id"), both("rank"))])])
+                lin(both("rank"), sp, 1.0)
             if t < RO - 1:
-                lin(R("TH", mb + t * PC, mb + t * PC + PC), dyn("Mw", t), -227.5, 300.0)
-                bottom(ch)
+                lin(R("TH", mb + t * PC, mb + t * PC + PC), U, -236.0, 300.0)
                 bonus[0] = hot
-                if UZA >> ch & 1:
-                    mm([(bs, [(full("Id"), z), (full("K8"), dyn("Mw", t))])])
-                    act(pt("UZ"), bs, AF.Relu, bias=-256.0)
+                zs = mr(0)
+                if OPT["UZA"] >> ch & 1:
+                    mm([(zs, [(full("zI"), z), (full("I2x"), U)])])
+                    act(pt("UZ"), zs, AF.Relu, bias=-2.0)
                 else:
-                    mm([(bs, [(full("Id"), z)])])
-                    tt(pt("UZ"), dyn("Mw", t), bs, ALU.mult)
-                if MG and ch:
-                    continue
-                n, cc = (256, 16) if MG else (PC, CC)
+                    mm([(zs, [(full("zI"), z)])])
+                    tt(pt("UZ"), pt("e1"), zs, ALU.min)
                 jb = 2 * CC * ch
-                sb, so = ("P0", 0) if MG else y1[:2]
-                db, do = ("P1", 0) if MG else rg("D")[:2]
-                pn = lambda b: R(b, pb, pb + n)
-                if SU >> ch & 1:
-                    mm([(R(sb, so + k * n, so + k * n + n), [(full("Id"), R("Cm", 0, n)), (full(m), pn("UZ"))])
-                        for k, m in enumerate(("Oa", "Ob"))])
-                    scan(R("su", wb, wb + 2 * n), R("Kx", 0, 2 * n), R(sb, so, so + 2 * n), 0.0, ALU.add, ALU.max)
-                    src = R("su", wb + 15, wb + 2 * n, 16)
-                else:
-                    mm([(rg("j", cc, jb + k * cc), [(view(m, r), R("UZ", pb + r, pb + n, 16)) for r in range(16)])
-                        for k, m in enumerate("AB")])
-                    src = rg("j", 2 * cc, jb)
-                x = hashed([src], rg("j")[0], rg("j")[1] + jb, cc, "JF" if FJ >> ch & 1 else "J1", jb, "J2", CC * ch)
-                ts(R("J3", jb, jb + cc), x, 8128, ALU.bitwise_and)
-                ts(R("J3", jb + cc, jb + 2 * cc), x, 63, ALU.bitwise_and)
-                cp(R("hl", jb, jb + 2 * cc), R("J3", jb, jb + 2 * cc))
-                mm([(R(db, do, do + n), [(full("Id"), R("Cd", 0, n))]
-                     + [(R("Dm", 128 * r, 128 * r + 128) if r < 15 else full("Id"), R("hl", jb + cc * k, jb + cc * k + cc),
-                         R(db, do + r, do + n, 16)) for r in range(16) for k in range(2)])])
-                act(pn("aD"), R(db, do, do + n), AF.Abs)
-                scan(pn("sD"), R("Kn", 0, n), pn("aD"), 0.0, ALU.add, ALU.min)
-                cp(R("xo", jb, jb + 2 * cc, 2), R("sD", pb + 15, pb + n, 16))
+                mm([(mr(k * PC), [(full("Id"), full("Cm")), (full(m), pt("UZ"))]) for k, m in enumerate(("Oa", "Ob"))])
+                scan(both("su"), wide("Kx"), mr(0, 2 * PC), 0.0, ALU.add, ALU.max)
+                x = hashed(R("su", wb + 15, wb + 2 * PC, 16), R(Q, 3 * PC, 3 * PC + CC), "J1", jb, "J2", CC * ch)
+                ts(R("J3", jb, jb + CC), x, 5, ALU.arith_shift_right, 8128, ALU.bitwise_and)
+                ts(R("J3", jb + CC, jb + 2 * CC), x, 5, ALU.arith_shift_right, 63, ALU.bitwise_and)
+                cp(R("hl", jb, jb + 2 * CC), R("J3", jb, jb + 2 * CC))
+                mm([(xx, [(full("Id"), full("Cd"))]
+                     + [(R("Dm", 128 * r, 128 * r + 128) if r < 15 else full("Id"), R("hl", jb + CC * k, jb + CC * k + CC),
+                         R(Q, 2 * PC + r, 3 * PC, 16)) for r in range(16) for k in range(2)])])
+                act(pt("aD"), xx, AF.Abs)
+                scan(pt("sD"), full("Kn"), pt("aD"), 0.0, ALU.add, ALU.min)
+                cp(R("xo", jb, jb + 2 * CC, 2), R("sD", pb + 15, pb + PC, 16))
         bonus[0] = 0.0
         if t in (RO - 2, RO - 1):
             a = 0 if t == RO - 2 else 256 * t
@@ -472,43 +470,45 @@ def build(M):
             dma(("yz", a, 256 * t + 256), r, [r], [], 65536 * (5 if t == RO - 2 else 1))
         if t == RO - 1:
             break
-        pa = rg("pa", 1)
+        bonus[1] = 3
+        pa = R("P3", 2 * HWM + PC, 2 * HWM + PC + 1)
         mm([(pa, [(full("Af"), c1("mcnt", ch)) for ch in range(NC)])], f=4)
         cp(c1("ai", 0), pa)
         ts(c1("ai", 0), c1("ai", 0), 1, ALU.bitwise_and)
-        ts(c1("thr", (t + 1) % 2), c1("ai", 0), 1.5, ALU.add, 2.0 ** 30, ALU.mult)
+        ts(c1("penb", (t + 1) % 2), c1("ai", 0), r0, ALU.mult, base, ALU.add)
+        for ch in range(NC - 1, -1, -1):
+            penalty(ch, t + 1)
         for c in range(15, -1, -1):
-            bonus[0], bonus[1] = BONA if c < CC else BON5, 1 + c // CC
+            bonus[0], bonus[1] = OPT["BON5"] * (c // CC), 1 + c // CC
             zz = R("zin", 256 * t + 16 * c, 256 * t + 16 * c + 16)
             add("v", ("sca", R("X", 0, 8208), R("xo", 2 * c, 2 * c + 1), zz), [zz, c1("xo", 2 * c)], [R("X", 0, 8208)],
                 50 + 16 * SF * CY)
 
     bonus[0] = 0.0
     for ch in range(NC - 1, -1, -1):
-        wb, pb, xb = 2 * PC * ch, PC * ch, 2 * RS * ch
+        wb, pb, xb = 256 * ch, PC * ch, XS * ch
         bonus[1] = 10 + ch
-        es = lambda k: R("Es", (15 * ch + k - 1) * PC, (15 * ch + k) * PC)
-        ed = lambda k: R("Ed", (5 * ch + k - 1) * PC, (5 * ch + k) * PC)
         ym = lambda k: R("ymb", 256 * k + pb, 256 * k + pb + PC)
-        act(R("al", wb, wb + 2 * PC), R("W", wb, wb + 2 * PC), AF.Sign)
-        s, d = R("al", wb, wb + PC), R("al", wb + PC, wb + 2 * PC)
-        mm([(R("P3", 0, PC), [(full("RSm"), s), (full("O"), d)]), (R("P3", PC, 2 * PC), [(full("RDm"), d)])])
-        lin(R("rk", wb, wb + 2 * PC), R("P3", 0, 2 * PC), 1.0, 64.0)
-        lin(ym(0), R("Mw", xb + RS + 5, xb + 2 * RS, 16), 1.0)
-        for k in range(1, 16):
-            ts(es(k), R("rk", wb, wb + PC), float(k), ALU.is_equal)
-            if k < 6:
-                ts(ed(k), R("rk", wb + PC, wb + 2 * PC), float(k), ALU.is_equal)
-        pi = rg("pi", 5 * CC)
-        mm([(pi, [(full("Id"), R("Ct", 0, 5 * CC))]
-             + [(view("RE", r), R("Es", es(1)[1] + r, es(5)[2], 16)) for r in range(16)]
-             + [(view(m, r), R("Ed", ed(1)[1] + r, ed(5)[2], 16)) for m in ("RE", "KE") for r in range(16)])])
-        ts(R("to", 5 * CC * ch, 5 * CC * (ch + 1)), pi, c1("col", 7), ALU.add)
-        for k in range(1, 6):
-            gat(ym(k), R("Mw", xb, xb + 2 * RS), R("to", CC * (5 * ch + k - 1), CC * (5 * ch + k)))
+        ew = lambda k, h: R("Ew", (10 * ch + 2 * k - 2 + h) * PC, (10 * ch + 2 * k - 1 + h) * PC)
+        rk = R("rk", pb, pb + PC)
+        pp = R("P%d" % (4 + ch), 0, PC)
+        mm([(pp, [(R("PN", PC * h, PC * h + PC), R("rank", wb + PC * h, wb + PC * h + PC)) for h in range(2)])])
+        lin(rk, pp, 1.0)
+        for ks in ((1, 2, 3), (4, 5)):
+            bk, n, a = dbank(), len(ks) * PC, (5 * ch + ks[0] - 1)
+            for k in ks:
+                ts(R("Ew", ew(k, 0)[1], ew(k, 1)[2]), R("rank", wb, wb + 256), float(k), ALU.is_equal)
+            mm([(R(bk, j * PC, j * PC + PC), [(full("Id"), full("Ci"))]
+                 + [(R(m, PC * h, PC * h + PC), ew(k, h)) for m in ("RE", "KE") for h in range(2)]) for j, k in enumerate(ks)])
+            scan(R("se", a * PC, a * PC + n), R("Kx", 0, n), R(bk, 0, n), 0.0, ALU.add, ALU.max)
+            cp(R("to", a * CC, (a + len(ks)) * CC), R("se", a * PC + 15, a * PC + n, 16))
+            for k in ks:
+                gat(ym(k), R("Mw", xb, xb + XS), R("to", CC * (5 * ch + k - 1), CC * (5 * ch + k)))
         for k in range(6, 16):
-            pp = R(("P3", "P2", "P7")[k % 3] if ch else ("P0", "P1", "P4", "P5")[k % 4], 512 - PC, 512)
-            mm([(pp, [(full("MT"), es(k))])])
+            es = R("Es", (10 * ch + k - 6) * PC, (10 * ch + k - 5) * PC)
+            ts(es, rk, float(k), ALU.is_equal)
+            pp = R(dbank(), 512 - PC, 512)
+            mm([(pp, [(full("MT"), es)])])
             lin(ym(k), pp, 1.0)
     for a, b in KG:
         r = R("ymb", 256 * a, 256 * b)
@@ -527,7 +527,7 @@ def depend(ops):
                     deps.add(j)
         for r, w in [(r, False) for r in o["rd"]] + [(r, True) for r in o["wr"]]:
             h = hist.setdefault(r[0], [])
-            if w and r[3] == 1:
+            if w and r[3] == 1 and len(r) == 4:
                 h[:] = [x for x in h if not (r[1] <= x[1] and x[2] <= r[2])]
             h.append((k, r[1], r[2], w, r[3]))
         o["deps"] = deps
@@ -542,6 +542,10 @@ def depend(ops):
         ops[k]["pr"], ops[k]["succ"] = pr[k], succ[k]
 
 
+def inline(p, o):
+    return p["eng"] == o["eng"] == "p" or (OPT["WAW"] and p["call"][0] == o["call"][0] == "sca")
+
+
 def schedule(ops):
     n = len(ops)
     succ = [o["succ"] for o in ops]
@@ -549,6 +553,7 @@ def schedule(ops):
     left = [len(o["deps"]) for o in ops]
     at = [0.0] * n
     ready = {e: [] for e in "vapgs"}
+    ALTP, SLACK, GAM = OPT["ALTP"], OPT["SLACK"], OPT["GAM"]
 
     def put(k):
         for e in ops[k].get("alt", ops[k]["eng"]):
@@ -565,7 +570,7 @@ def schedule(ops):
             cand = []
             for k in ready[e]:
                 o = ops[k]
-                if e == "p" and o["first"] and opened.get(o["bank"]):
+                if o["banks"] and (e != "p" or o["first"]) and any(opened.get(b) for b in o["banks"]):
                     continue
                 st = max([free[e], at[k]] + [bank_t[b] for b in o["banks"] if b in bank_t and ops[bank_o[b]]["eng"] != e])
                 cand.append((st, k))
@@ -576,6 +581,8 @@ def schedule(ops):
                         key=lambda c: pr[c[1]] - GAM * (c[0] - t0) - (pen if "alt" in ops[c[1]] else 0.0))
                 if best is None or k[0] < best[0]:
                     best = k + (e,)
+        if best is None:
+            return None
         st, k, e = best
         o = ops[k]
         for x in o.get("alt", e):
@@ -595,7 +602,7 @@ def schedule(ops):
                 o["deps"].add(bank_o[b])
             bank_t[b], bank_o[b] = done, k
         for j in succ[k]:
-            at[j] = max(at[j], free[e] if e == "p" and ops[j]["eng"] == "p" else done)
+            at[j] = max(at[j], free[e] if inline(o, ops[j]) else done)
             left[j] -= 1
             if not left[j]:
                 put(j)
@@ -609,7 +616,7 @@ def replay(ops, order, costs):
         e = o["eng"]
         st = free.get(e, 0.0)
         for j in o["deps"]:
-            x = end[j] if e == "p" and ops[j]["eng"] == "p" else done[j]
+            x = end[j] if inline(ops[j], o) else done[j]
             if x > st:
                 st = x
         end[k] = free[e] = st + costs[k][0][e]
@@ -617,13 +624,13 @@ def replay(ops, order, costs):
     return max(done)
 
 
-def plan(start=None, iters=None, seed=1):
+def plan(iters=None, seed=1):
     base = build(MODELS[0])
     depend(base)
     costs = [[({e: c for e, (_, c) in o["alt"].items()} if "alt" in o else {o["eng"]: o["cost"]}, o["lat"]) for o in build(m)]
              for m in MODELS[1:]]
     keys = sorted(set(o["key"] for o in base if o["key"][0]))
-    extra = dict(zip(keys, start or []))
+    extra = {}
     best = None
     state = [seed]
 
@@ -631,7 +638,7 @@ def plan(start=None, iters=None, seed=1):
         state[0] = (state[0] * 6364136223846793005 + 1442695040888963407) % 2 ** 64
         return (state[0] >> 33) % n
 
-    for it in range((ITER if iters is None else iters) + 1):
+    for it in range((OPT["ITER"] if iters is None else iters) + 1):
         trial = dict(extra)
         if it:
             for _ in range(1 + draw(5)):
@@ -639,11 +646,13 @@ def plan(start=None, iters=None, seed=1):
                 trial[k] = trial.get(k, 0) + (-8, -4, -2, -1, 1, 2, 4, 8)[draw(8)]
         ops = [dict(o, deps=set(o["deps"]), bonus=o["bonus"] + 500.0 * trial.get(o["key"], 0)) for o in base]
         order = schedule(ops)
+        if order is None:
+            continue
         ends = [replay(ops, order, c) for c in costs]
         val = sum(x / m["END"] for x, m in zip(ends, MODELS[1:]))
         if best is None or val <= best[0]:
             best, extra = (val, ops, order, ends), trial
-    return best[1], best[2], best[3], [extra.get(k, 0) for k in keys]
+    return best[1], best[2], best[3]
 
 
 _PLAN = []
@@ -667,11 +676,12 @@ def rank_program(g, core, T, topo):
     def ap(r):
         if not isinstance(r, tuple):
             return r
+        if len(r) == 5:
+            g0, g1, a, b, s = r[4]
+            return T[r[0]][:, g0:g1, a:b:s] if s > 1 else T[r[0]][:, g0:g1, a:b]
+        if r[0] in W3:
+            return T[r[0]][:, r[1] // W3[r[0]]:r[2] // W3[r[0]], :]
         return T[r[0]][:, r[1]:r[2]] if len(r) == 3 or r[3] == 1 else T[r[0]][:, r[1]:r[2]:r[3]]
-
-    def skip(j, o):
-        p = ops[j]
-        return p["eng"] == o["eng"] == "p"
 
     pos = {k: i for i, k in enumerate(order)}
     need = set()
@@ -679,7 +689,7 @@ def rank_program(g, core, T, topo):
         last = {}
         o["w"] = []
         for j in o["deps"]:
-            if skip(j, o):
+            if inline(ops[j], o):
                 continue
             if ops[j]["call"][0] in ("dma", "send"):
                 o["w"].append(j)
@@ -712,6 +722,8 @@ def rank_program(g, core, T, topo):
                    else q.tensor_scalar(ap(c[1]), ap(c[2]), ap(c[3]), ap(c[4]), c[5], c[6]))
         elif f == "tt":
             ins = q.tensor_tensor(ap(c[1]), ap(c[2]), ap(c[3]), c[4])
+        elif f == "gtt":
+            ins = q.tensor_tensor(ap(c[1]), ap(c[2]).indirect(ap(c[3])), ap(c[4]), c[5])
         elif f == "cp":
             ins = q.tensor_copy(ap(c[1]), ap(c[2]))
         elif f == "ms":
@@ -728,7 +740,7 @@ def rank_program(g, core, T, topo):
         elif f == "sca":
             ins = q.tensor_copy(ap(c[1]).indirect(ap(c[2])), ap(c[3]))
         elif f == "sel":
-            ins = q.affine_select(ap(c[1]), ap(c[2]), [[0, 8], [1, 16]], ALU.is_equal, 0.0, -c[3], 0)
+            ins = q.affine_select(ap(c[1]), ap(c[2]), [[0, 8], [1, 2], [0, 8]], ALU.is_equal, 0.0, -c[3], 0)
         elif f == "iota":
             ins = (q.iota(ap(c[1]), c[2], c[3], c[4]) if _S[c[1][0]][1] == I32
                    else q.iota(ap(c[1]), c[2], c[3], c[4], allow_small_or_imprecise_dtypes=True))

@@ -1,10 +1,9 @@
+import math
 from concourse.mybir import AluOpType as ALU, AxisListType, ActivationFunctionType as AF
 
 NC, PC, CC, RO = 2, 128, 8, 6
 B1, B2, MISS, XS = 1031, 2064, 6, 3088
 WIN = [(0, 2), (3, 5), (6, 8), (9, 11), (12, 15)]
-KG = [(6, 10), (10, 13), (13, 16), (0, 3), (3, 6)]
-HWM = PC + 5 * CC
 SC, CR = 113.0 / 128, 1.5 * 2.0 ** 30
 KO = [sum(8 * (16 + i) for i in range(t)) for t in range(RO + 1)]
 H54 = 2.0 ** 54
@@ -12,27 +11,26 @@ FOLD = 41.0 * 2 ** 18
 
 BF, F32, I32, U16 = "bfloat16", "float32", "int32", "uint16"
 _S = dict(
-    X=(8208, BF), Xh=(NC * XS, BF), Mw=(NC * XS, BF), e=(NC * 16 * PC, BF), G=(NC * 21 * PC, BF),
+    X=(8208, BF), Xh=(NC * XS, BF), Mw=(NC * XS, BF), G=(NC * 21 * PC, BF),
     zin=(6 * 256, BF), yzb=(6 * 256, BF), ymb=(4096, BF), m0s=(16, BF), wts=(16, BF),
-    MZ=(NC * 5 * PC, BF), TH=(NC * 5 * PC, BF), I1=(NC * 2 * HWM, I32), I2=(NC * HWM, I32), off=(NC * HWM, U16),
-    F1=(NC * 2 * HWM, F32), H=(512, BF), b=(512, BF), Cq=(5 * 512, BF), rank=(512, BF), pen=(512, BF),
-    mcnt=(8, F32), sc=(256, F32), idx=(16, U16), ds=(256, BF), ms=(256, BF), e1=(256, I32), UZ=(256, BF),
-    J1=(32, I32), J2=(16, I32), J3=(32, I32), hl=(32, BF), aD=(256, F32), sD=(256, F32), xo=(32, U16), ai=(8, I32),
+    MZ=(NC * 5 * PC, BF), TH=(NC * 5 * PC, BF), I1=(512, I32), I2=(256, I32), off=(256, U16), F1=(512, F32),
+    I3=(160, I32), I4=(80, I32), ofd=(80, U16), H=(512, BF), b=(512, BF), Cq=(5 * 512, BF), rank=(512, BF), pen=(512, BF),
+    rm=(2 * 168, BF), mcnt=(8, F32), sc=(256, F32), idx=(16, U16), ds=(256, BF), ms=(256, BF), e1=(256, F32), y1=(256, F32),
+    UZ=(256, BF), J1=(32, I32), J2=(16, I32), J3=(32, I32), hl=(32, BF), aD=(256, F32), sD=(256, F32), xo=(32, U16), ai=(8, I32),
     su=(512, F32), rk=(256, BF), Es=(20 * PC, BF), Ew=(20 * PC, BF), se=(10 * PC, F32), to=(80, U16),
-    pi=(8, I32), col=(40, F32), penb=(8, F32), Dn=(128, F32), Gn=(128, F32), Gw=(256, F32), G32=(128, F32), Rn=(256, F32),
-    Nn=(144, F32), N8=(128, F32), Id=(128, BF), O=(128, BF), E=(144, BF), A=(144, BF), B=(144, BF),
-    OM=(128, BF), AM=(144, BF), BM=(144, BF), AH=(512, BF), BH=(512, BF), mf=(16, F32), wf=(8, F32),
-    pw=(16, F32), pc=(32, F32), dl=(256, F32), RB=(16, BF), RS=(256, BF), Of=(256, BF), Om=(256, BF), OA=(256, BF), OB=(256, BF),
-    Lq=(6 * 256, BF), IB=(256, BF), RE=(256, BF), KE=(256, BF), PN=(256, BF), pn=(256, BF), L=(128, BF), L2=(128, BF),
-    sI=(128, BF), nI=(128, BF), hI=(128, BF), gI=(128, BF), qI=(128, BF), I2x=(128, BF), zI=(128, BF), one=(PC, BF),
-    KD=(KO[RO], BF), rm=(2 * 168, BF), t1=(128, BF), t2=(128, BF), Zc=(128, BF), Dm=(15 * 128, BF), S1=(16, F32), S2=(16, F32), Ci=(PC, BF), Kx=(512, BF),
-    Kn=(256, F32), Cd=(256, BF), Af=(128, F32), Cm=(256, BF), Oa=(128, BF), Ob=(128, BF), K8=(128, BF), MT=(128, BF),
+    pi=(8, I32), col=(40, F32), penb=(8, F32), Gn=(128, F32), Gw=(256, F32), G32=(128, F32), Rn=(128, F32), R32=(32, F32),
+    ge=(32, F32), eq=(32, F32), Nn=(144, F32), N8=(128, F32), Id=(136, BF), O=(128, BF), E=(144, BF), A=(144, BF), B=(144, BF),
+    mf=(16, F32), wf=(8, F32), pw=(16, F32), pc=(32, F32), dl=(128, F32), RB=(16, BF), RS=(256, BF),
+    IB=(256, BF), RE=(256, BF), KE=(256, BF), PN=(256, BF), L=(128, BF), L2=(128, BF),
+    sI=(128, BF), nI=(128, BF), hI=(128, BF), gI=(128, BF), qI=(128, BF), uI=(128, BF), dI=(128, BF), K8=(128, BF), one=(256, BF),
+    KD=(KO[RO], BF), t1=(128, BF), t2=(128, BF), Dm=(15 * 128, BF), Ci=(PC, BF), Kx=(384, BF),
+    Kn=(128, BF), Cd=(128, BF), Af=(128, F32), Cm=(128, BF), Oa=(128, BF), Ob=(128, BF), MT=(128, BF),
 )
 SCRATCH = {k: ("sbuf", [128, n], d) for k, (n, d) in _S.items()}
-W3 = dict(Hs0=32, Hs1=32, PR=32)
-for _k, _n in (("Hs0", 8), ("Hs1", 8), ("PR", 16)):
-    SCRATCH[_k] = ("sbuf", [128, _n, 32], BF)
-    _S[_k] = (32 * _n, BF)
+W3 = dict(Hs0=32, Hs1=32, PR=32, OM=16, AH=16, BH=16, Of=16, Lq=16)
+for _k, _n in (("Hs0", 8), ("Hs1", 8), ("PR", 16), ("OM", 8), ("AH", 32), ("BH", 32), ("Of", 16), ("Lq", 96)):
+    SCRATCH[_k] = ("sbuf", [128, _n, W3[_k]], BF)
+    _S[_k] = (W3[_k] * _n, BF)
 for _b in ("P0", "P1", "P2", "P3", "P4", "P5", "Q0", "Q1"):
     SCRATCH[_b] = ("psum", [128, 512], F32)
 NDMA = 16
@@ -40,25 +38,24 @@ SEMAPHORES = (["cv", "ca", "cp", "cg", "sent"] + ["d%d" % k for k in range(NDMA)
               + ["r%d_%d" % (t, c) for t in range(1, RO) for c in range(NC)])
 
 DLAT = 2200.0
-_M = dict(CY=0.95, PCY=0.48, LAT=170.0, RLAT=3200.0, OV=55.0, GF=1.56, SF=3.8, XB=1 << 20, END=150000.0)
-MODELS = [_M, dict(_M, CY=0.83, PCY=0.42, OV=50.0, END=135000.0), dict(_M, CY=1.0, PCY=0.5, OV=60.0, END=155000.0),
-          dict(_M, CY=1.2, PCY=0.6, OV=72.0, GF=1.7, END=180000.0)]
-OPT = dict(FM=3, MZA=0, UZA=0, SCV=3, AB=(0, 0), NG=2, DF=1, ND=3, WAW=0, BON1=1000.0, BON2=5000.0, BON3=2000.0, BON4=2000.0,
-           BON5=2000.0, ALTP=6000.0, SLACK=100.0, GAM=50.0, ITER=600)
+_M = dict(CY=0.87, PCY=0.44, LAT=170.0, RLAT=3200.0, OV=52.0, AO=30.0, GF=1.56, SF=3.8, BW=240.0)
+MODELS = [_M]
+OPT = dict(JUDGE=[], HB=("P4", "P3"), BK=("40122", "35555", "1"), KG=((6, 10), (10, 14), (14, 16), (1, 4), (4, 6), (0, 1)),
+           MZA=3, UZA=0, SCV=0, YA=0, FM=3, NG=2, DF=4, MSP=12, CUT=(6, 12), GM=1,
+           BIAS=300.0, TEMP=100.0, PK=0.4, ITER=18000)
 
 
 def R(n, a, b, s=1):
     return (n, a, b, s)
 
 
-def R3(n, g0, g1, a, b, s=1):
-    return (n, W3[n] * g0 + a, W3[n] * (g1 - 1) + b, 1, (g0, g1, a, b, s))
+def R3(n, g0, g1, a, b):
+    return (n, W3[n] * g0 + a, W3[n] * (g1 - 1) + b, 1, (g0, g1, a, b, 1))
 
 
 def width(r):
     if len(r) == 5:
-        g0, g1, a, b, s = r[4]
-        return (g1 - g0) * ((b - a + s - 1) // s)
+        return (r[4][1] - r[4][0]) * (r[4][3] - r[4][2])
     return (r[2] - r[1] + r[3] - 1) // r[3]
 
 
@@ -67,18 +64,18 @@ def two(*rs):
 
 
 def build(M):
-    CY, PCY, LAT, RLAT, OV, GF, SF, XB = [M[k] for k in ("CY", "PCY", "LAT", "RLAT", "OV", "GF", "SF", "XB")]
+    CY, PCY, LAT, RLAT, OV, AO, GF, SF, BW = [M[k] for k in ("CY", "PCY", "LAT", "RLAT", "OV", "AO", "GF", "SF", "BW")]
     ops = []
-    bonus = [0.0, 0]
+    tag = ["set", 0]
 
     def add(eng, call, rd, wr, cost, lat=LAT, **kw):
         w = wr[0] if wr else ("", 0)
-        a = w[1] % 256 if w[0] in ("zin", "yzb") else 0 if w[0] in ("TH", "penb", "P0", "P1", "P2") else w[1]
+        a = w[1] % 256 if w[0] in ("zin", "yzb") else 0 if w[0] in ("TH", "penb", "MZ", "P0", "P1", "P2") else w[1]
         if w[0] in ("Mw", "Xh") and w[1] % XS >= B2:
             a = -1 - (w[1] % XS == B2 + MISS)
-        key = (bonus[1], call[0], "P0" if w[0] in ("P1", "P2") else w[0], a)
+        key = (tag[1], tag[0], call[0], "P0" if w[0] in ("P1", "P2") else w[0], a)
         ops.append(dict(eng=eng, call=call, rd=[r for r in rd if isinstance(r, tuple)], wr=wr, cost=cost, lat=lat,
-                        bonus=bonus[0], key=key, **kw))
+                        grp=(tag[1], tag[0]), key=key, **kw))
 
     def vc(n):
         return OV + n * CY
@@ -103,7 +100,7 @@ def build(M):
         add("v", ("red", o, i), [i], [o], vc(width(i)))
 
     def act(o, i, f, bias=0.0, scale=1.0, acc=None):
-        add("a", ("act", o, i, f, bias, scale, acc), [i, bias, scale], [o] + ([acc] if acc else []), vc(width(o)) + 30)
+        add("a", ("act", o, i, f, bias, scale, acc), [i, bias, scale], [o] + ([acc] if acc else []), vc(width(o)) + AO)
 
     def either(fa, fv):
         fa()
@@ -111,14 +108,17 @@ def build(M):
         v, a = ops.pop(), ops.pop()
         ops.append(dict(a, rd=a["rd"] + v["rd"], alt={"a": (a["call"], a["cost"]), "v": (v["call"], v["cost"])}))
 
-    def gat(o, win, offs):
-        either(*[lambda e=e: add(e, ("gat", e, o, win, offs), [win, offs], [o], 60 + GF * CY * width(o)) for e in "av"])
+    def gat(o, win, offs, plus=None):
+        either(*[lambda e=e: add(e, ("gat", e, o, win, offs, plus), [win, offs, plus], [o], 60 + GF * CY * width(o)) for e in "av"])
 
     def lin(o, i, scale, bias=0.0):
         either(lambda: act(o, i, AF.Identity, bias=bias, scale=scale), lambda: ts(o, i, scale, ALU.mult, bias, ALU.add))
 
     def iota(o, pat, base, cm):
         add("g", ("iota", o, pat, base, cm), [], [o], 130 + 2 * CY * width(o))
+
+    def select(o, i, pat, base, cm, op=ALU.is_equal, fill=0.0):
+        add("g", ("sel", o, i, pat, base, cm, op, fill), [i], [o], 170 + 2 * CY * width(o))
 
     def mm(groups, first=True, last=True, f=1, one=False):
         rd, cost, calls = [], 30.0, []
@@ -129,12 +129,12 @@ def build(M):
                               last and k == len(terms) - 1 and not (one and n < len(groups) - 1)))
                 rd += [tm[0], tm[1]]
                 cost += max(64, width(tm[1])) * PCY * f
-        add("p", ("mm", calls), rd, [o for o, _ in groups], cost, first=first, last=last, bank=groups[0][0][0])
+        add("p", ("mm", calls), rd, [o for o, _ in groups], cost)
 
     nd = [0]
 
-    def dma(o, i, rd, wr, nbytes):
-        add("s", ("dma", o, i, nd[0]), rd, wr, 60.0, lat=DLAT + nbytes / 180.0)
+    def dma(o, i, rd, wr, nbytes, **kw):
+        add("s", ("dma", o, i, nd[0]), rd, wr, max(60.0, nbytes / BW), lat=DLAT, **kw)
         nd[0] += 1
 
     def full(n):
@@ -156,18 +156,21 @@ def build(M):
         ts(c1("col", ncol[0]), src, s1, op0, s2, op1)
         return c1("col", ncol[0])
 
-    dma(R("zin", 0, 256), ("z0", 0, 256), [], [R("zin", 0, 256)], 65536)
-    dma(R("wts", 0, 2), ("wt", 0, 2), [], [R("wts", 0, 2)], 512)
-    dma(R("m0s", 0, 16), ("m0", 0, 16), [], [R("m0s", 0, 16)], 4096)
+    dma(R("wts", 0, 2), ("wt", 0, 2), [], [R("wts", 0, 2)], 512, boost=30000.0)
+    dma(R("m0s", 0, 16), ("m0", 0, 16), [], [R("m0s", 0, 16)], 4096, boost=30000.0)
+    dma(R("zin", 0, 256), ("z0", 0, 256), [], [R("zin", 0, 256)], 65536, boost=20000.0)
     for k in range(2):
         r = R("X", 16 + 4096 * k, 16 + 4096 * (k + 1))
-        dma(r, ("xr", 4096 * k, 4096 * (k + 1)), [], [r], XB * (k + 1))
+        dma(r, ("xr", 4096 * k, 4096 * (k + 1)), [], [r], 1 << 20)
 
+    ID = R("Id", 1, 129)
+    ms(wide("one"), 1.0)
     iota(c1("pi", 0), [[0, 1]], 0, 1)
     iota(full("Gn"), [[16, 8], [0, 16]], 0, 0)
-    iota(full("Dn"), [[1, 128]], 0, -1)
+    select(R("Id", 0, 129), R("one", 0, 129), [[1, 129]], -1, -1)
+    iota(R("R32", 0, 32), [[1, 32]], 0, 0)
     iota(R("Nn", 0, 144), [[1, 144]], -15, 0)
-    iota(wide("Rn"), [[0, 16], [1, 16]], 0, 0)
+    iota(full("Rn"), [[0, 8], [1, 16]], 0, 0)
     iota(wide("Gw"), [[-128, 2], [32, 8], [0, 16]], 0, 0)
     iota(full("G32"), [[32, 4], [0, 32]], 0, 0)
     iota(full("N8"), [[8, PC]], 32768, 0)
@@ -177,100 +180,80 @@ def build(M):
     rc, gc, row, g32 = [c1("col", k) for k in range(1, 5)]
     ts(full("O"), full("Gn"), gc, ALU.is_equal)
     ts(R("E", 0, 144), R("Nn", 0, 144), gc, ALU.is_equal)
-    ts(full("Id"), full("Dn"), 0.0, ALU.is_equal)
     cp(R("wf", 0, 2), R("wts", 0, 2))
     cp(R("mf", 0, 16), R("m0s", 0, 16))
     for g in range(8):
         ts(R("OM", 16 * g, 16 * g + 16), R("m0s", 0, 16), c1("O", 16 * g), ALU.mult)
     for k, n in enumerate("AB"):
-        ms(R(n + "M", 0, 8), 0.0)
-        ms(R(n + "M", 136, 144), 0.0)
-        lin(R(n + "M", 8, 136), full("OM"), c1("wf", k))
+        ms(R(n + "H", 0, 512), 0.0)
         lin(R(n, 0, 144), R("E", 0, 144), c1("wf", k))
+        lin(full("O" + n.lower()), full("O"), c1("wf", k))
         for h in range(2):
             for b in range(2):
-                o, i = R(n + "H", 128 * (2 * h + b), 128 * (2 * h + b + 1)), R(n + "M", 8 + 8 * (h - b), 136 + 8 * (h - b))
-                add("g", ("sel", o, i, b), [i], [o], 170 + 256 * CY)
-    ts(wide("dl"), wide("Rn"), rc, ALU.is_equal)
-    ms(R("pc", 0, 16), 2.0 ** -10)
+                a = 8 * (2 * h + b)
+                lin(R3(n + "H", a, a + 8, 8 * b, 8 * b + 8), R3("OM", 0, 8, 8 * h, 8 * h + 8), c1("wf", k))
+    ts(full("dl"), full("Rn"), rc, ALU.is_equal)
+    ms(R("pc", 0, 16), 2.0 ** -5)
     ms(R("pc", 16, 32), 0.0)
-    scan(R("pw", 0, 16), R("pc", 0, 16), R("pc", 16, 32), 2.0 ** 78, ALU.mult, ALU.add)
+    scan(R("pw", 0, 16), R("pc", 0, 16), R("pc", 16, 32), 2.0 ** 39, ALU.mult, ALU.add)
     tt(R("pw", 0, 16), R("pw", 0, 16), R("dl", 0, 16), ALU.mult)
     ncol[0] += 1
-    wc = c1("col", ncol[0])
-    red(wc, R("pw", 0, 16))
+    unit = c1("col", ncol[0])
+    red(unit, R("pw", 0, 16))
     ts(R("RB", 0, 8), R("O", 0, 128, 16), -H54, ALU.mult, H54, ALU.mult)
-    ts(R("RB", 8, 16), R("O", 0, 128, 16), wc, ALU.mult)
+    ts(R("RB", 8, 16), R("O", 0, 128, 16), unit, ALU.mult, unit, ALU.mult)
     for s in range(16):
         lin(R("RS", 16 * s, 16 * s + 16), R("RB", 0, 16), c1("mf", s))
-    for n, v in (("sI", SC), ("nI", -SC), ("hI", 0.5), ("gI", -0.5), ("qI", 0.25), ("I2x", 2.0), ("zI", 1.0 / 128), ("K8", 256.0)):
-        lin(full(n), full("Id"), v)
-    ms(R("one", 0, PC), 1.0)
-    live = column(row, 11.0, ALU.is_ge)
-    r0 = column(row, 0.0, ALU.is_equal)
-    up = column(row, 22.0, ALU.is_ge)
-    lowr = column(r0, -8.0, ALU.mult, live, ALU.add)
-    lowr = column(lowr, up, ALU.subtract)
+    for n, v in (("sI", SC), ("nI", -SC), ("hI", 0.5), ("gI", -0.5), ("qI", 0.25), ("uI", unit), ("K8", 256.0), ("dI", -16384.0)):
+        lin(full(n), ID, v)
+    ops[-1]["boost"] = 20000.0
+    magic = column(unit, 1.5 * 2.0 ** 28, ALU.mult)
+    less = column(rc, 14.5, ALU.is_lt, -0.75, ALU.mult)
+    ts(R("ge", 0, 32), R("R32", 0, 32), row, ALU.is_le)
+    ts(R("eq", 0, 32), R("R32", 0, 32), row, ALU.is_equal)
+    live, r0 = c1("ge", 11), c1("eq", 0)
     ts(wide("Of"), wide("Gw"), g32, ALU.is_equal)
-    lin(wide("Om"), wide("Of"), live)
-    lin(wide("OA"), wide("Of"), lowr)
-    lin(wide("OB"), wide("Of"), up)
     ms(R("Lq", 0, 6 * 256), 0.0)
-    for q, (a, b) in enumerate(WIN):
-        for p in range(a, b + 1):
-            for k, src in ([(q, "Om")] if q < 4 else [(4, "OA"), (5, "OB")]):
-                lin(R("Lq", 256 * k + p, 256 * k + 256, 16), R(src, p, 256, 16), 2.0 ** (5 * p - 33))
-    st = column(row, 16.0, ALU.is_ge)
-    step = column(st, 2.0, ALU.mult, live, ALU.subtract)
+    lowr = column(column(r0, -8.0, ALU.mult, live, ALU.add), c1("ge", 22), ALU.subtract)
+    for k, c in enumerate([live] * 4 + [lowr, c1("ge", 22)]):
+        a, b = WIN[min(k, 4)]
+        lin(R3("Lq", 16 * k, 16 * k + 16, a, b + 1), R3("Of", 0, 16, a, b + 1), c)
+    step = column(c1("ge", 16), 2.0, ALU.mult, live, ALU.subtract)
     for r, v in ((15, 1 - B2), (23, B1 - 8), (31, B2 + MISS - B1 - 8)):
-        x = column(row, float(r), ALU.is_equal, float(v), ALU.mult)
-        step = column(x, step, ALU.add)
+        step = column(c1("eq", r), float(v), ALU.mult, step, ALU.add)
     lin(wide("IB"), wide("Of"), step)
-    base = column(r0, 16.5, ALU.mult, -15.0, ALU.add)
-    cp(c1("penb", 0), base)
+    ts(c1("penb", 0), r0, 16.5, ALU.mult, -15.0, ALU.add)
+    base = column(c1("penb", 0), 0.0, ALU.add)
     first = column(row, -16.0, ALU.add, live, ALU.mult)
-    ca = column(live, -63.0, ALU.mult)
-    cb = column(row, 10.0, ALU.is_ge, 64.0, ALU.mult)
-    x = column(row, 31.0, ALU.not_equal)
-    cb = column(cb, x, ALU.mult)
-    ts(full("L"), full("Dn"), 0.0, ALU.is_equal, ca, ALU.mult)
-    ts(full("L2"), full("Dn"), 1.0, ALU.is_equal, cb, ALU.mult)
+    lin(full("L"), ID, column(live, -63.0, ALU.mult))
+    lin(full("L2"), full("Id"), column(c1("ge", 10), c1("eq", 31), ALU.subtract, 64.0, ALU.mult))
     tt(full("L"), full("L"), full("L2"), ALU.add)
     ms(R("PR", 128, 256), 0.0)
     ms(R("PR", 384, 512), 0.0)
-    x = column(r0, H54, ALU.mult, H54, ALU.mult)
-    ts(full("t1"), full("G32"), g32, ALU.is_equal, x, ALU.mult)
-    ts(full("t2"), full("Id"), -64.0 * H54, ALU.mult, H54, ALU.mult)
+    ts(full("t1"), full("G32"), g32, ALU.is_equal, column(r0, H54, ALU.mult, H54, ALU.mult), ALU.mult)
+    ts(full("t2"), ID, -64.0 * H54, ALU.mult, H54, ALU.mult)
     tt(full("PR"), full("t1"), full("t2"), ALU.add)
-    lin(R("PR", 256, 384), full("Id"), 2.0 ** 78)
-    ms(R("KD", 0, KO[RO]), 1.0)
-    for t in range(RO):
-        ms(R("KD", KO[t], KO[t + 1], 16 + t), 0.0)
-    x = column(row, 31.0, ALU.is_equal)
-    lin(full("Af"), R("one", 0, PC), x)
+    lin(R("PR", 256, 384), ID, 2.0 ** 78)
+    lin(full("Af"), full("one"), c1("eq", 31))
     for ch in range(NC):
         ms(R("Hs%d" % ch, 0, 256), 0.0)
         ms(R3("Hs%d" % ch, 0, 8, 0, 1), 2.0 ** 78)
-        for h in range(2):
-            lin(R("rank", 256 * ch + PC * h, 256 * ch + PC * h + PC), R("one", 0, PC), first)
-    tt(full("Zc"), full("O"), full("Id"), ALU.add)
+        lin(R("rank", 256 * ch, 256 * ch + 256), wide("one"), first)
     tt(full("N8"), full("N8"), full("dl"), ALU.mult)
-    ts(full("Ci"), full("N8"), -32768.0, ALU.add)
-    for k in range(0, 512, 256):
-        ts(R("Kx", k, k + 256), wide("Rn"), 0.0, ALU.is_equal, -2.0 ** 22, ALU.mult)
-    lin(wide("Cm"), wide("dl"), 2.0 ** 21, -2.0 ** 21)
-    ts(full("Oa"), full("O"), c1("wf", 0), ALU.mult, 128.0, ALU.mult)
-    ts(full("Ob"), full("O"), c1("wf", 1), ALU.mult, 128.0, ALU.mult)
-    mm([(R("P0", 0, 128), [(full("OM"), full("Id"))])])
+    lin(full("Ci"), full("N8"), 1.0, -32768.0)
+    for n, w, v in (("Kx", 384, -2.0 ** 22), ("Kn", 128, 2.0 ** 29)):
+        ms(R(n, 0, w), 0.0)
+        ms(R(n, 0, w, 16), v)
+    for t in range(RO):
+        select(R("KD", KO[t], KO[t + 1]), R("one", 0, 8 * (16 + t)), [[0, 8], [1, 16 + t]], 0, 0, ALU.not_equal)
+    lin(full("Cm"), full("dl"), 2.0 ** 21, -2.0 ** 21)
+    mm([(R("P0", 0, 128), [(full("OM"), ID)])])
     lin(full("MT"), R("P0", 0, 128), 1.0)
-    ts(wide("Kn"), wide("Rn"), 0.0, ALU.is_equal, 2.0 ** 29, ALU.mult)
-    ts(wide("Cd"), wide("Rn"), rc, ALU.is_ge, 2.0 ** 28, ALU.mult)
-    ts(wide("Cd"), wide("Cd"), rc, ALU.add)
-    ms(R("Cd", 15, 256, 16), 16.0)
-    ts(R("S1", 0, 16), R("dl", 0, 16), -1.0, ALU.mult, 2.0, ALU.add)
-    ts(R("S2", 0, 16), R("dl", 0, 16), 32768.0, ALU.mult, -16384.0, ALU.add)
+    ts(full("Cd"), full("Rn"), rc, ALU.is_ge, 2.0 ** 28, ALU.mult)
+    lin(full("Cd"), full("Cd"), 1.0, rc)
+    ms(R("Cd", 15, 128, 16), 16.0)
     for r in range(15):
-        ts(R("Dm", 128 * r, 128 * r + 128), full("Zc"), c1("S1", r), ALU.is_equal, c1("S2", r), ALU.mult)
+        select(R("Dm", 128 * r, 128 * r + 128), full("dI"), [[1, 128]], -1 - r, -1, ALU.not_equal, 16384.0)
     a = XS * (NC - 1)
     for h in range(2):
         n, o = 8, a + B1 * h
@@ -278,18 +261,17 @@ def build(M):
         while n < 8 * PC:
             lin(R("Mw", o + n, o + 2 * n), R("Mw", o, o + n), 1.0)
             n *= 2
-        ms(R("Mw", o + n, a + (B2 if h else B1)), 0.0)
-    dma(R("Mw", 0, B2), R("Mw", a, a + B2), [R("Mw", a, a + B2)], [R("Mw", 0, B2)], 1 << 19)
+        if OPT["GM"]:
+            select(R("Mw", B1 * h, B1 * h + n), R("Mw", o, o + n), [[0, n]], 0, 0)
+        else:
+            lin(R("Mw", B1 * h, B1 * h + n), R("Mw", o, o + n), 1.0)
     for ch in range(NC):
         ms(R("Mw", XS * ch + B2 + MISS, XS * (ch + 1), 8), 0.0)
-    hi = column(row, 24.0, ALU.is_ge)
-    x = column(row, -16.0, ALU.add, hi, ALU.subtract)
-    y = column(row, -1.0, ALU.mult, 15.0, ALU.add)
-    lin(wide("RE"), wide("Of"), column(x, y, ALU.max))
-    x = column(row, 16.0, ALU.is_lt, float(B2), ALU.mult)
-    lin(wide("KE"), wide("Of"), column(hi, 1024.0, ALU.mult, x, ALU.add))
-    ts(wide("pn"), wide("Rn"), first, ALU.is_equal, st, ALU.mult)
-    tt(wide("PN"), wide("pn"), wide("Of"), ALU.mult)
+    x = column(row, -16.0, ALU.add, c1("ge", 24), ALU.subtract)
+    lin(wide("RE"), wide("Of"), column(column(row, -1.0, ALU.mult, 15.0, ALU.add), x, ALU.max))
+    x = column(c1("ge", 16), -float(B2), ALU.mult, float(B2), ALU.add)
+    lin(wide("KE"), wide("Of"), column(c1("ge", 24), 1024.0, ALU.mult, x, ALU.add))
+    select(wide("PN"), wide("one"), [[-128, 2], [32, 8], [1, 16]], 16, -1)
 
     def penalty(ch, t):
         o, i, c = R("pen", 256 * ch, 256 * ch + 256), R("rank", 256 * ch, 256 * ch + 256), c1("penb", t % 2)
@@ -301,30 +283,38 @@ def build(M):
         if _S[i1][1] == F32:
             act(uv, src, AF.Identity, bias=2.0 ** 23 - 0.5, scale=2.0 ** -12 + 2.0 ** -34)
             act(uv, uv, AF.Relu, bias=-2.0 ** 35, scale=4096.0)
-            tt(uv, src, uv, ALU.subtract)
-            lin(up, u, 1184.0, -FOLD)
+            vp = R(src[0], src[1] + n, src[2])
+            tt(u, up, u, ALU.subtract)
+            tt(vp, vp, v, ALU.subtract)
+            lin(v, u, 1184.0, -FOLD)
+            tt(vp, vp, u, ALU.mult)
+            tt(x, vp, v, ALU.add)
         else:
             cp(uv, src)
             ts(uv, uv, 4095, ALU.bitwise_and)
             ts(up, u, 1184.0, ALU.mult, -FOLD, ALU.add)
-        tt(x, u, v, ALU.mult)
-        tt(x, x, up, ALU.add)
+            tt(x, u, v, ALU.mult)
+            tt(x, x, up, ALU.add)
         return x
+
+    def place_list(o, x):
+        ts(x, x, 5, ALU.arith_shift_right, 8191, ALU.bitwise_and)
+        cp(o, x)
 
     for ch in range(NC):
         penalty(ch, 0)
     rot = [0]
 
     def dbank():
-        rot[0] = (rot[0] + 1) % OPT["ND"]
+        rot[0] = (rot[0] + 1) % 3
         return "P%d" % rot[0]
 
     Xg = R("X", 16, 8208)
     for t in range(RO):
-        for ch in range(NC - 1, -1, -1):
+        for part, ch in ((0, 1), (0, 0), (1, 1), (1, 0)):
             z = R("zin", 256 * t + PC * ch, 256 * t + PC * ch + PC)
-            xb, gb, mb, ob, wb, pb = XS * ch, 21 * PC * ch, 5 * PC * ch, HWM * ch, 256 * ch, PC * ch
-            hw, Q, Hs, Mb = PC + t * CC, "Q%d" % ch, "Hs%d" % ch, "P%d" % (4 + ch)
+            xb, gb, mb, wb, pb = XS * ch, 21 * PC * ch, 5 * PC * ch, 256 * ch, PC * ch
+            Q, Hs, hb = "Q%d" % ch, "Hs%d" % ch, OPT["HB"][ch]
 
             def slot(n, s):
                 a = xb + (B1 * (s // 8) + s % 8 if s < 16 else B2 + s - 16)
@@ -339,30 +329,35 @@ def build(M):
             def pt(n):
                 return R(n, pb, pb + PC)
 
-            def mr(a, n=PC):
-                return R(Mb, a, a + n)
+            def mr(kind, a, n=PC):
+                return R("P" + OPT["BK"][ch][kind], a, a + n)
 
-            bonus[0], bonus[1] = OPT["BON1"] * ch, ch + 1
-            zp = R("P3", 2 * HWM, 2 * HWM + PC)
-            if OPT["MZA"] >> ch & 1:
-                for a in range(0, t, 4):
-                    ks, bk = list(range(a, min(a + 4, t))), dbank()
-                    mm([(R(bk, (k - a) * PC, (1 + k - a) * PC), [(full("Id"), z), (full("K8"), slot("Mw", 16 + k))]) for k in ks])
-                    act(R("MZ", mb + a * PC, mb + (ks[-1] + 1) * PC), R(bk, 0, len(ks) * PC), AF.Relu, bias=-256.0)
-            elif t:
-                mm([(zp, [(full("Id"), z)])])
-                for k in range(t):
-                    tt(R("MZ", mb + k * PC, mb + k * PC + PC), slot("Mw", 16 + k), zp, ALU.mult)
-            for n, o in (("A", 0), ("B", hw)):
-                mm([(R("P3", o + 64 * h, o + 64 * h + 64),
-                     [(R(n + "H", 128 * (2 * h + b), 128 * (2 * h + b + 1)), R(z[0], z[1] + b, z[2], 2)) for b in range(2)])
-                    for h in range(2)])
-                if t:
-                    mm([(R("P3", o + PC, o + hw), [(view(n, r), R("MZ", mb + r, mb + t * PC, 16)) for r in range(16)])])
-            x = hashed(R("P3", 0, 2 * hw), R("P3", 0, hw), "F1" if OPT["FM"] >> ch & 1 else "I1", 2 * ob, "I2", ob)
-            ts(x, x, 5, ALU.arith_shift_right, 8191, ALU.bitwise_and)
-            cp(R("off", ob, ob + hw), x)
+            if not part:
+                tag[:] = "mz", ch + 1
+                zb = t * PC * ch
+                if OPT["MZA"] >> ch & 1:
+                    for a in range(0, t, 2):
+                        ks = list(range(a, min(a + 2, t)))
+                        mm([(R(hb, (2 + k - a) * PC, (3 + k - a) * PC), [(ID, z), (full("K8"), slot("Mw", 16 + k))]) for k in ks])
+                        act(R("MZ", zb + a * PC, zb + (ks[-1] + 1) * PC), R(hb, 2 * PC, (2 + len(ks)) * PC), AF.Relu, bias=-256.0)
+                elif t:
+                    mm([(R(hb, 3 * PC, 4 * PC), [(ID, z)])])
+                    for k in range(t):
+                        tt(R("MZ", zb + k * PC, zb + k * PC + PC), slot("Mw", 16 + k), R(hb, 3 * PC, 4 * PC), ALU.mult)
+                tag[0] = "hash"
+                for k, n in enumerate(("AH", "BH")):
+                    mm([(R(hb, k * PC + 64 * h, k * PC + 64 * h + 64),
+                         [(R(n, 128 * (2 * h + b), 128 * (2 * h + b + 1)), R(z[0], z[1] + b, z[2], 2)) for b in range(2)])
+                        for h in range(2)])
+                place_list(pt("off"), hashed(R(hb, 0, 2 * PC), R(hb, 0, PC), "F1" if OPT["FM"] >> ch & 1 else "I1", wb, "I2", pb))
+                if t and not ch:
+                    tag[0], n = "dyn", 2 * t * CC
+                    for k, m in enumerate("AB"):
+                        mm([(R(hb, 2 * PC + k * n, 2 * PC + k * n + n), [(view(m, r), R("MZ", r, 2 * t * PC, 16)) for r in range(16)])])
+                    place_list(R("ofd", 0, n), hashed(R(hb, 2 * PC, 2 * PC + 2 * n), R(hb, 2 * PC, 2 * PC + n), "I3", 0, "I4", 0))
+                continue
             c0, W = 16 - t, 16 + t
+            tag[:] = "gather", ch + 1
             mm([(R(Q, 0, 16 * W), [(half("pen", 0), R3("PR", 0, 16, c0, 32))]),
                 (R(Q, 4 * W, 8 * W), [(half("pen", 1), R3("PR", 0, 4, c0, 32))]),
                 (R(Q, 12 * W, 16 * W), [(half("pen", 1), R3("PR", 8, 12, c0, 32))])], last=False, one=True)
@@ -370,10 +365,10 @@ def build(M):
             for h in range(2):
                 for k in range(OPT["NG"]):
                     a = xb + B1 * h + 16 * q * k
-                    gat(R("Xh", a, a + 16 * q), Xg, R("off", ob + 64 * h + q * k, ob + 64 * h + q * (k + 1)))
+                    gat(R("Xh", a, a + 16 * q), Xg, R("off", pb + 64 * h + q * k, pb + 64 * h + q * (k + 1)))
             for k in range(t):
-                gat(slot("Xh", 16 + k), Xg, R("off", ob + PC + CC * k, ob + PC + CC * (k + 1)))
-            bonus[0] = OPT["BON2"] * ch
+                gat(slot("Xh", 16 + k), Xg, R("ofd", CC * (t * ch + k), CC * (t * ch + k + 1)))
+            tag[0] = "compare"
             blocks = [list(range(a, a + 4)) for a in range(0, 16, 4)]
             dblk = [list(range(16 + a, 16 + min(a + 4, t))) for a in range(0, t, 4)]
             blocks = blocks[:OPT["DF"]] + dblk + blocks[OPT["DF"]:]
@@ -384,39 +379,40 @@ def build(M):
                 if bl[0] >= 16:
                     act(dd, dd, AF.Abs)
                     tt(gg, dd, R("TH", mb + (bl[0] - 16) * PC, mb + (bl[0] - 16) * PC + n), ALU.is_gt)
-                elif OPT["AB"][ch] >> bl[0] // 4 & 1:
-                    ee = R("e", (16 * ch + bl[0]) * PC, (16 * ch + bl[0]) * PC + n)
-                    act(ee, dd, AF.Abs)
-                    ts(gg, ee, 64.0, ALU.is_gt)
                 else:
                     ts(gg, dd, CR, ALU.add, CR, ALU.not_equal)
                 mm([(R(Q, t + s if s < 16 else t + 15 - s, 16 * W, W),
                      [(R("G", g0 + j * PC, g0 + j * PC + PC), R("RS", 16 * s, 16 * s + 16) if s < 16 else R("RB", 0, 16))])
                     for j, s in enumerate(bl)], first=False, last=bl is blocks[-1], one=True)
-            mm([(mr(0), [(full("qI"), R("one", 0, PC)), (full("hI"), z), (full("gI"), slot("Xh", 15 + t if t else 0))])])
-            ts(slot("Xh", 16 + MISS), mr(0), 1.5 * 2.0 ** 23, ALU.add, 1.5 * 2.0 ** 23, ALU.subtract)
-            hot = OPT["BON3"] * ch
-            bonus[0] = hot
+                ops[-1]["gid"] = (t, ch)
+            tag[0] = "miss"
+            mm([(mr(0, 0), [(full("qI"), full("one")), (full("hI"), z), (full("gI"), slot("Xh", 15 + t if t else 0))])])
+            if OPT["YA"] >> ch & 1:
+                act(pt("y1"), mr(0, 0), AF.Identity, bias=1.5 * 2.0 ** 23)
+                act(slot("Xh", 16 + MISS), pt("y1"), AF.Identity, bias=-1.5 * 2.0 ** 23)
+            else:
+                ts(slot("Xh", 16 + MISS), mr(0, 0), 1.5 * 2.0 ** 23, ALU.add, 1.5 * 2.0 ** 23, ALU.subtract)
+            tag[0] = "match"
             rm = R("rm", 168 * ch, 168 * ch + 8 * W)
             scan(rm, R("KD", KO[t], KO[t + 1]), R(Q, 0, 8 * W), 0.0, ALU.mult, ALU.max)
             tt(R3(Hs, 0, 8, c0, 32), R(Q, 8 * W, 16 * W), rm, ALU.max)
-            mm([(R(Q, PC * h, PC * h + PC), [(R(Hs, PC * h, PC * h + PC), full("Id"))]) for h in range(2)])
+            mm([(R(Q, PC * h, PC * h + PC), [(R(Hs, PC * h, PC * h + PC), ID)]) for h in range(2)])
             act(both("b"), R(Q, 0, 256), AF.Relu, bias=1.0, scale=-2.0 ** -106, acc=c1("mcnt", ch))
             act(both("H"), R(Q, 0, 256), AF.Sqrt)
-            mm([(mr(PC), [(full("Id"), full("Ci"))] + [(half("IB", h, 0), half("b", h)) for h in range(2)])])
-            scan(pt("sc"), R("Kx", 0, PC), mr(PC), 0.0, ALU.add, ALU.max)
+            mm([(mr(1, PC), [(ID, full("Ci"))] + [(half("IB", h, 0), half("b", h)) for h in range(2)])])
+            scan(pt("sc"), R("Kx", 0, PC), mr(1, PC), 0.0, ALU.add, ALU.max)
             ix = R("idx", CC * ch, CC * ch + CC)
             ts(ix, R("sc", pb + 15, pb + PC, 16), float(B2 + 4), ALU.add)
-            gat(pt("ms"), R("Mw", xb, xb + XS), ix)
-            bonus[0] = OPT["BON4"] * ch
+            gat(pt("ms"), R("Mw", xb, xb + XS), ix, less)
+            tag[0] = "header"
             win = R("Xh", xb, xb + XS)
-            add("v", ("gtt", pt("ds"), win, ix, z, ALU.subtract), [win, ix, z], [pt("ds")], 60 + GF * CY * PC)
             new = R("yzb", 256 * t + pb, 256 * t + pb + PC)
+            add("v", ("gtt", pt("ds"), win, ix, z, ALU.subtract), [win, ix, z], [pt("ds")], 60 + GF * CY * PC)
             act(new, pt("ds"), AF.Abs)
             if t < RO - 1:
                 zn = R("zin", 256 * (t + 1) + pb, 256 * (t + 1) + pb + PC)
                 add("g", ("send", zn, new, "r%d_%d" % (t + 1, ch)), [new], [zn], 300.0, lat=RLAT)
-            bonus[0] = hot
+            tag[0] = "mask"
             terms = []
             for q, (a, b) in enumerate(WIN):
                 cb = 512 * q + wb
@@ -424,54 +420,54 @@ def build(M):
                 ts(both("Cq", cb), both("H"), 2.0 ** (34 - 5 * (a - 1)), ALU.min, lo, ALU.max)
                 terms += [(half("Lq", h, 256 * k), half("Cq", h, cb)) for k in ([q] if q < 4 else [4, 5]) for h in range(2)]
             xx = R(Q, 2 * PC, 3 * PC)
-            mm([(xx, terms[:6])], last=False)
-            ops[-1]["rd"].append(both("b"))
-            mm([(xx, terms[6:])], first=False, last=False)
-            mm([(xx, [(full("I2x"), pt("ms"))])], first=False)
-            cp(pt("e1"), xx)
-            ts(pt("e1"), pt("e1"), 62, ALU.bitwise_and)
+            terms.insert(OPT["MSP"], (full("uI"), pt("ms")))
+            cuts = [0] + list(OPT["CUT"]) + [len(terms)]
+            for a, b in zip(cuts, cuts[1:]):
+                mm([(xx, terms[a:b])], first=not a, last=b == len(terms))
+                if not a:
+                    ops[-1]["rd"].append(both("b"))
+            ts(pt("e1"), xx, magic, ALU.add, magic, ALU.subtract)
             U = slot("Mw", 16 + t) if t < RO - 1 else R("ymb", pb, pb + PC)
-            ts(U, pt("e1"), 1.0, ALU.min)
-            bonus[0] = 0.0
-            sp = mr(2 * PC, 2 * PC)
+            tt(U, xx, pt("e1"), ALU.is_gt)
+            tag[0] = "rank"
+            sp = mr(2, 2 * PC, 2 * PC)
             if OPT["SCV"] >> ch & 1:
                 mm([(sp, [(full("L"), both("b"))])])
                 tt(both("rank"), sp, both("rank"), ALU.add)
             else:
-                mm([(sp, [(full("L"), both("b")), (full("Id"), both("rank"))])])
+                mm([(sp, [(full("L"), both("b")), (ID, both("rank"))])])
                 lin(both("rank"), sp, 1.0)
             if t < RO - 1:
                 lin(R("TH", mb + t * PC, mb + t * PC + PC), U, -236.0, 300.0)
-                bonus[0] = hot
-                zs = mr(0)
+                tag[0] = "name"
+                zs = mr(3, 0)
                 if OPT["UZA"] >> ch & 1:
-                    mm([(zs, [(full("zI"), z), (full("I2x"), U)])])
-                    act(pt("UZ"), zs, AF.Relu, bias=-2.0)
+                    mm([(zs, [(ID, z), (full("K8"), U)])])
+                    act(pt("UZ"), zs, AF.Relu, bias=-256.0)
                 else:
-                    mm([(zs, [(full("zI"), z)])])
-                    tt(pt("UZ"), pt("e1"), zs, ALU.min)
+                    mm([(zs, [(ID, z)])])
+                    tt(pt("UZ"), U, zs, ALU.mult)
                 jb = 2 * CC * ch
-                mm([(mr(k * PC), [(full("Id"), full("Cm")), (full(m), pt("UZ"))]) for k, m in enumerate(("Oa", "Ob"))])
-                scan(both("su"), wide("Kx"), mr(0, 2 * PC), 0.0, ALU.add, ALU.max)
-                x = hashed(R("su", wb + 15, wb + 2 * PC, 16), R(Q, 3 * PC, 3 * PC + CC), "J1", jb, "J2", CC * ch)
+                mm([(mr(4, k * PC), [(ID, full("Cm")), (full(m), pt("UZ"))]) for k, m in enumerate(("Oa", "Ob"))])
+                scan(both("su"), wide("Kx"), mr(4, 0, 2 * PC), 0.0, ALU.add, ALU.max)
+                x = hashed(R("su", wb + 15, wb + 2 * PC, 16), R(Q, 0, CC), "J1", jb, "J2", CC * ch)
                 ts(R("J3", jb, jb + CC), x, 5, ALU.arith_shift_right, 8128, ALU.bitwise_and)
                 ts(R("J3", jb + CC, jb + 2 * CC), x, 5, ALU.arith_shift_right, 63, ALU.bitwise_and)
                 cp(R("hl", jb, jb + 2 * CC), R("J3", jb, jb + 2 * CC))
-                mm([(xx, [(full("Id"), full("Cd"))]
-                     + [(R("Dm", 128 * r, 128 * r + 128) if r < 15 else full("Id"), R("hl", jb + CC * k, jb + CC * k + CC),
-                         R(Q, 2 * PC + r, 3 * PC, 16)) for r in range(16) for k in range(2)])])
+                mm([(xx, [(ID, full("Cd"))] + [
+                    (R("Dm", 128 * r, 128 * r + 128) if r < 15 else ID, R("hl", jb + CC * k, jb + CC * k + CC),
+                     R(Q, 2 * PC + r, 3 * PC, 16)) for k in range(2) for r in range(16)])])
                 act(pt("aD"), xx, AF.Abs)
                 scan(pt("sD"), full("Kn"), pt("aD"), 0.0, ALU.add, ALU.min)
                 cp(R("xo", jb, jb + 2 * CC, 2), R("sD", pb + 15, pb + PC, 16))
-        bonus[0] = 0.0
+        tag[:] = "rank", 3
         if t in (RO - 2, RO - 1):
             a = 0 if t == RO - 2 else 256 * t
             r = R("yzb", a, 256 * t + 256)
             dma(("yz", a, 256 * t + 256), r, [r], [], 65536 * (5 if t == RO - 2 else 1))
         if t == RO - 1:
             break
-        bonus[1] = 3
-        pa = R("P3", 2 * HWM + PC, 2 * HWM + PC + 1)
+        pa = R("P" + OPT["BK"][2], PC, PC + 1)
         mm([(pa, [(full("Af"), c1("mcnt", ch)) for ch in range(NC)])], f=4)
         cp(c1("ai", 0), pa)
         ts(c1("ai", 0), c1("ai", 0), 1, ALU.bitwise_and)
@@ -479,38 +475,35 @@ def build(M):
         for ch in range(NC - 1, -1, -1):
             penalty(ch, t + 1)
         for c in range(15, -1, -1):
-            bonus[0], bonus[1] = OPT["BON5"] * (c // CC), 1 + c // CC
+            tag[:] = "write", 1 + c // CC
             zz = R("zin", 256 * t + 16 * c, 256 * t + 16 * c + 16)
-            add("v", ("sca", R("X", 0, 8208), R("xo", 2 * c, 2 * c + 1), zz), [zz, c1("xo", 2 * c)], [R("X", 0, 8208)],
-                50 + 16 * SF * CY)
+            add("v", ("sca", R("X", 0, 8208), c1("xo", 2 * c), zz), [zz, c1("xo", 2 * c)], [R("X", 0, 8208)], 50 + 16 * SF * CY)
 
-    bonus[0] = 0.0
     for ch in range(NC - 1, -1, -1):
         wb, pb, xb = 256 * ch, PC * ch, XS * ch
-        bonus[1] = 10 + ch
-        ym = lambda k: R("ymb", 256 * k + pb, 256 * k + pb + PC)
+        tag[:] = "end", 10 + ch
         ew = lambda k, h: R("Ew", (10 * ch + 2 * k - 2 + h) * PC, (10 * ch + 2 * k - 1 + h) * PC)
-        rk = R("rk", pb, pb + PC)
         pp = R("P%d" % (4 + ch), 0, PC)
         mm([(pp, [(R("PN", PC * h, PC * h + PC), R("rank", wb + PC * h, wb + PC * h + PC)) for h in range(2)])])
-        lin(rk, pp, 1.0)
+        lin(R("rk", pb, pb + PC), pp, 1.0)
         for ks in ((1, 2, 3), (4, 5)):
             bk, n, a = dbank(), len(ks) * PC, (5 * ch + ks[0] - 1)
             for k in ks:
                 ts(R("Ew", ew(k, 0)[1], ew(k, 1)[2]), R("rank", wb, wb + 256), float(k), ALU.is_equal)
-            mm([(R(bk, j * PC, j * PC + PC), [(full("Id"), full("Ci"))]
+            mm([(R(bk, j * PC, j * PC + PC), [(ID, full("Ci"))]
                  + [(R(m, PC * h, PC * h + PC), ew(k, h)) for m in ("RE", "KE") for h in range(2)]) for j, k in enumerate(ks)])
             scan(R("se", a * PC, a * PC + n), R("Kx", 0, n), R(bk, 0, n), 0.0, ALU.add, ALU.max)
             cp(R("to", a * CC, (a + len(ks)) * CC), R("se", a * PC + 15, a * PC + n, 16))
             for k in ks:
-                gat(ym(k), R("Mw", xb, xb + XS), R("to", CC * (5 * ch + k - 1), CC * (5 * ch + k)))
-        for k in range(6, 16):
-            es = R("Es", (10 * ch + k - 6) * PC, (10 * ch + k - 5) * PC)
-            ts(es, rk, float(k), ALU.is_equal)
-            pp = R(dbank(), 512 - PC, 512)
-            mm([(pp, [(full("MT"), es)])])
-            lin(ym(k), pp, 1.0)
-    for a, b in KG:
+                gat(R("ymb", 256 * k + pb, 256 * k + pb + PC), R("Mw", xb, xb + XS), R("to", CC * (5 * ch + k - 1), CC * (5 * ch + k)))
+    tag[1] = 12
+    for k in range(6, 16, 2):
+        for j in range(k, k + 2):
+            ts(R("Es", 256 * (j - 6), 256 * (j - 5)), wide("rk"), float(j), ALU.is_equal)
+        pp = R(("P3", "P4", "P5")[k // 2 % 3], 0, 512)
+        mm([(pp, [(full("MT"), R("Es", 256 * (k - 6), 256 * (k - 4)))])])
+        lin(R("ymb", 256 * k, 256 * k + 512), pp, 1.0)
+    for a, b in OPT["KG"]:
         r = R("ymb", 256 * a, 256 * b)
         dma(("ym", 256 * a, 256 * b), r, [r], [], 65536 * (b - a))
     return ops
@@ -543,116 +536,180 @@ def depend(ops):
 
 
 def inline(p, o):
-    return p["eng"] == o["eng"] == "p" or (OPT["WAW"] and p["call"][0] == o["call"][0] == "sca")
+    return p["eng"] == o["eng"] == "p"
 
 
-def schedule(ops):
-    n = len(ops)
-    succ = [o["succ"] for o in ops]
-    pr = [o["pr"] + o["bonus"] for o in ops]
-    left = [len(o["deps"]) for o in ops]
-    at = [0.0] * n
-    ready = {e: [] for e in "vapgs"}
-    ALTP, SLACK, GAM = OPT["ALTP"], OPT["SLACK"], OPT["GAM"]
-
-    def put(k):
-        for e in ops[k].get("alt", ops[k]["eng"]):
-            ready[e].append(k)
-
+def place(P, prio, bias):
+    succ, eng, cost, lat, banks = P
+    n = len(eng)
+    p = list(prio)
     for k in range(n):
-        if not left[k]:
-            put(k)
-    free = {e: 0.0 for e in "vapgs"}
-    bank_t, bank_o, opened, order = {}, {}, {}, []
-    while len(order) < n:
-        best = None
-        for e in "vapgs":
-            cand = []
-            for k in ready[e]:
-                o = ops[k]
-                if o["banks"] and (e != "p" or o["first"]) and any(opened.get(b) for b in o["banks"]):
-                    continue
-                st = max([free[e], at[k]] + [bank_t[b] for b in o["banks"] if b in bank_t and ops[bank_o[b]]["eng"] != e])
-                cand.append((st, k))
-            if cand:
-                t0 = min(c[0] for c in cand)
-                pen = ALTP if e == "v" else 0.0
-                k = max((c for c in cand if c[0] <= t0 + SLACK),
-                        key=lambda c: pr[c[1]] - GAM * (c[0] - t0) - (pen if "alt" in ops[c[1]] else 0.0))
-                if best is None or k[0] < best[0]:
-                    best = k + (e,)
-        if best is None:
-            return None
-        st, k, e = best
-        o = ops[k]
-        for x in o.get("alt", e):
-            ready[x].remove(k)
-        if "alt" in o:
-            o["eng"] = e
-            o["call"], o["cost"] = o["alt"][e]
-        order.append(k)
-        o["t0"] = st
-        free[e] = st + o["cost"]
-        done = free[e] + o["lat"]
-        o["t1"] = done
-        if e == "p":
-            opened[o["bank"]] = not o["last"]
-        for b in o["banks"]:
-            if b in bank_o and ops[bank_o[b]]["eng"] != e:
-                o["deps"].add(bank_o[b])
-            bank_t[b], bank_o[b] = done, k
-        for j in succ[k]:
-            at[j] = max(at[j], free[e] if inline(o, ops[j]) else done)
-            left[j] -= 1
-            if not left[j]:
-                put(j)
-    return order
+        x = p[k]
+        for j, _ in succ[k]:
+            if p[j] > x:
+                p[j] = x
+    at, by, held, st, eo = [0.0] * n, [-1] * n, [-1] * n, [0.0] * n, list(eng)
+    qs = {e: ([], [], []) for e in "vapgs"}
+    bk = {b: ([], []) for bs in banks for b in bs}
+    end, last = 0.0, 0
+    for k in sorted(range(n), key=lambda k: -p[k]):
+        best, la = None, lat[k]
+        for e in (eo[k] or "av"):
+            c, t, h = cost[k][e], at[k], -1
+            ss, ee, who = qs[e]
+            m = i = len(ss)
+            while i and ee[i - 1] > t:
+                i -= 1
+            moved = True
+            while moved:
+                while i < m and ss[i] < t + c:
+                    if ee[i] > t:
+                        t, h = ee[i], who[i]
+                    i += 1
+                moved = False
+                for b in banks[k]:
+                    s0, iv = bk[b]
+                    j = len(s0)
+                    while j and s0[j - 1] > t - 1800.0:
+                        j -= 1
+                    while j < len(s0) and s0[j] < t + c + la:
+                        if iv[j][1] != e and t < iv[j][0]:
+                            t, moved, h = iv[j][0], True, iv[j][2]
+                        j += 1
+                while moved and i < m and ee[i] <= t:
+                    i += 1
+            v = t + c + (bias[k] if e == "v" else 0.0)
+            if best is None or v < best[0]:
+                best = (v, t, c, e, i, h)
+        _, t, c, e, i, held[k] = best
+        for x, y in zip(qs[e], (t, t + c, k)):
+            x.insert(i, y)
+        for b in banks[k]:
+            s0, iv = bk[b]
+            j = len(s0)
+            while j and s0[j - 1] > t:
+                j -= 1
+            s0.insert(j, t)
+            iv.insert(j, (t + c + la, e, k))
+        st[k], eo[k] = t, e
+        x = t + c
+        if x + la > end:
+            end, last = x + la, k
+        for j, pp in succ[k]:
+            y = x if pp else x + la
+            if y > at[j]:
+                at[j], by[j] = y, k
+    pairs = []
+    while last >= 0:
+        if held[last] >= 0:
+            pairs.append((last, held[last]))
+        last = held[last] if held[last] >= 0 else by[last]
+    return st, eo, end, pairs
 
 
-def replay(ops, order, costs):
-    free, end, done = {}, [0.0] * len(ops), [0.0] * len(ops)
-    for k in order:
-        o = ops[k]
-        e = o["eng"]
-        st = free.get(e, 0.0)
-        for j in o["deps"]:
-            x = end[j] if inline(ops[j], o) else done[j]
-            if x > st:
-                st = x
-        end[k] = free[e] = st + costs[k][0][e]
-        done[k] = end[k] + costs[k][1]
-    return max(done)
+def prices(ops):
+    return [({e: c for e, (_, c) in o["alt"].items()} if "alt" in o else {o["eng"]: o["cost"]}, o["lat"]) for o in ops]
 
 
 def plan(iters=None, seed=1):
     base = build(MODELS[0])
     depend(base)
-    costs = [[({e: c for e, (_, c) in o["alt"].items()} if "alt" in o else {o["eng"]: o["cost"]}, o["lat"]) for o in build(m)]
-             for m in MODELS[1:]]
-    keys = sorted(set(o["key"] for o in base if o["key"][0]))
-    extra = {}
-    best = None
+    n, iters = len(base), OPT["ITER"] if iters is None else iters
+    above, pre, succ = [0] * n, [], [[] for _ in base]
+    for k, o in enumerate(base):
+        for j in o["deps"]:
+            above[k] |= above[j]
+        pre.append([(j, inline(base[j], o)) for j in sorted(o["deps"]) if not above[k] >> j & 1])
+        for j, pp in pre[k]:
+            succ[j].append((k, pp))
+        for j in o["deps"]:
+            above[k] |= 1 << j
+    P = (succ, [None if "alt" in o else o["eng"] for o in base], [c for c, _ in prices(base)],
+         [o["lat"] for o in base], [sorted(o["banks"]) for o in base])
+    others = [prices(build(m)) for m in OPT["JUDGE"]]
+
+    def judged(st, eo, val):
+        order, last, wait = sorted(range(n), key=lambda k: st[k]), {}, [None] * n
+        for k in order if others else ():
+            w = pre[k]
+            for b in P[4][k]:
+                if b in last and eo[last[b]] != eo[k]:
+                    w = w + [(last[b], False)]
+                last[b] = k
+            wait[k] = w
+        for cs, m in zip(others, OPT["JUDGE"]):
+            free, end, done = dict.fromkeys("vapgs", 0.0), [0.0] * n, [0.0] * n
+            for k in order:
+                e = eo[k]
+                t = free[e]
+                for j, pp in wait[k]:
+                    x = end[j] if pp else done[j]
+                    if x > t:
+                        t = x
+                c, la = cs[k]
+                end[k] = free[e] = t = t + c[e]
+                done[k] = t + la
+            val += max(done) * m["W"]
+        return val / (1 + len(others))
+
     state = [seed]
 
-    def draw(n):
+    def rnd():
         state[0] = (state[0] * 6364136223846793005 + 1442695040888963407) % 2 ** 64
-        return (state[0] >> 33) % n
+        return ((state[0] >> 33) + 1) / 2.0 ** 31
 
-    for it in range((OPT["ITER"] if iters is None else iters) + 1):
-        trial = dict(extra)
-        if it:
-            for _ in range(1 + draw(5)):
-                k = keys[draw(len(keys))]
-                trial[k] = trial.get(k, 0) + (-8, -4, -2, -1, 1, 2, 4, 8)[draw(8)]
-        ops = [dict(o, deps=set(o["deps"]), bonus=o["bonus"] + 500.0 * trial.get(o["key"], 0)) for o in base]
-        order = schedule(ops)
-        if order is None:
+    def one(xs):
+        return xs[min(int(rnd() * len(xs)), len(xs) - 1)]
+
+    kin, gin = {}, {}
+    for k, o in enumerate(base):
+        kin.setdefault(o["key"], []).append(k)
+        gin.setdefault(o["grp"], []).append(k)
+    grps, keys = sorted(gin), sorted(k for k in kin if k[0])
+    cp, cb = [o["pr"] + o.get("boost", 0.0) for o in base], [OPT["BIAS"]] * n
+    best, cur, own, pairs, ceo = None, None, 0.0, [], None
+    for it in range(iters + 1):
+        p, b = list(cp), cb
+        if it and (rnd() < 0.3 or not pairs):
+            d = (rnd() * 2 - 1) * 1500
+            for k in gin[one(grps)] if rnd() < 0.3 else kin[one(keys)]:
+                p[k] += d
+        elif it:
+            k, h = one(pairs)
+            wide, y = rnd() < OPT["PK"], rnd()
+            alts = [j for j in (k, h) if "alt" in base[j]]
+            if alts and y < 0.4:
+                j, b = one(alts), list(cb)
+                for i in kin[base[j]["key"]] if wide else [j]:
+                    b[i] = 5000.0 if ceo[j] == "v" else -5000.0
+            else:
+                d = max(p[h] - p[k], 0.0) + 1.0 + 200 * rnd()
+                j, d = (k, d) if y < 0.7 else (h, -d)
+                for i in kin[base[j]["key"]] if wide else [j]:
+                    p[i] += d
+        st, eo, val, pp = place(P, p, b)
+        if cur is not None and val > own + 1500.0:
             continue
-        ends = [replay(ops, order, c) for c in costs]
-        val = sum(x / m["END"] for x, m in zip(ends, MODELS[1:]))
-        if best is None or val <= best[0]:
-            best, extra = (val, ops, order, ends), trial
-    return best[1], best[2], best[3]
+        mine, val = val, judged(st, eo, val)
+        if cur is None or val <= cur - OPT["TEMP"] * max(0.02, 1 - it / (iters + 1)) * math.log(rnd()):
+            cp, cb, cur, own, pairs, ceo = p, b, val, mine, pp, eo
+        if best is None or val < best[0]:
+            best = (val, st, eo)
+    order = sorted(range(n), key=lambda k: (best[1][k], k))
+    last = {base[k]["gid"]: k for k in order if "gid" in base[k]}
+    for k in order:
+        o = base[k]
+        if "gid" in o:
+            c = o["call"][1]
+            o["call"] = ("mm", c[:-1] + [c[-1][:4] + (last[o["gid"]] == k,)])
+        o["eng"] = best[2][k]
+        if "alt" in o:
+            o["call"], o["cost"] = o["alt"][o["eng"]]
+        for b in o["banks"]:
+            if b in last and base[last[b]]["eng"] != o["eng"]:
+                o["deps"].add(last[b])
+            last[b] = k
+    return base, order, best[0]
 
 
 _PLAN = []
@@ -677,8 +734,7 @@ def rank_program(g, core, T, topo):
         if not isinstance(r, tuple):
             return r
         if len(r) == 5:
-            g0, g1, a, b, s = r[4]
-            return T[r[0]][:, g0:g1, a:b:s] if s > 1 else T[r[0]][:, g0:g1, a:b]
+            return T[r[0]][:, r[4][0]:r[4][1], r[4][2]:r[4][3]]
         if r[0] in W3:
             return T[r[0]][:, r[1] // W3[r[0]]:r[2] // W3[r[0]], :]
         return T[r[0]][:, r[1]:r[2]] if len(r) == 3 or r[3] == 1 else T[r[0]][:, r[1]:r[2]:r[3]]
@@ -736,11 +792,15 @@ def rank_program(g, core, T, topo):
             ins = q.activation(ap(c[1]), ap(c[2]), c[3], bias=ap(c[4]), scale=ap(c[5]), accum_out=ap(c[6]))
         elif f == "gat":
             src = ap(c[3]).indirect(ap(c[4]))
-            ins = q.tensor_copy(ap(c[2]), src) if c[1] == "v" else q.activation(ap(c[2]), src, AF.Copy)
+            if c[5]:
+                ins = (q.tensor_scalar(ap(c[2]), src, ap(c[5]), None, ALU.add) if c[1] == "v"
+                       else q.activation(ap(c[2]), src, AF.Identity, bias=ap(c[5])))
+            else:
+                ins = q.tensor_copy(ap(c[2]), src) if c[1] == "v" else q.activation(ap(c[2]), src, AF.Copy)
         elif f == "sca":
             ins = q.tensor_copy(ap(c[1]).indirect(ap(c[2])), ap(c[3]))
         elif f == "sel":
-            ins = q.affine_select(ap(c[1]), ap(c[2]), [[0, 8], [1, 2], [0, 8]], ALU.is_equal, 0.0, -c[3], 0)
+            ins = q.affine_select(ap(c[1]), ap(c[2]), c[3], c[6], c[7], c[4], c[5])
         elif f == "iota":
             ins = (q.iota(ap(c[1]), c[2], c[3], c[4]) if _S[c[1][0]][1] == I32
                    else q.iota(ap(c[1]), c[2], c[3], c[4], allow_small_or_imprecise_dtypes=True))

@@ -20,11 +20,11 @@ _S = dict(
     su=(512, F32), rk=(256, BF), Es=(20 * PC, BF), Ew=(20 * PC, BF), se=(10 * PC, F32), to=(80, U16),
     pi=(8, I32), col=(40, F32), penb=(8, F32), Gn=(128, F32), Gw=(256, F32), G32=(128, F32), Rn=(128, F32), R32=(32, F32),
     ge=(32, F32), eq=(32, F32), Nn=(144, F32), N8=(128, F32), Id=(136, BF), O=(128, BF), E=(144, BF), A=(144, BF), B=(144, BF),
-    mf=(16, F32), wf=(8, F32), pw=(16, F32), pc=(32, F32), dl=(128, F32), RB=(16, BF), RS=(256, BF),
+    ub=(8, BF), q1=(512, BF), mI=(128, BF), PL=(256, BF), LT=(128, BF), mf=(16, F32), wf=(8, F32), pw=(16, F32), pc=(32, F32), dl=(128, F32), RB=(16, BF), RS=(256, BF),
     IB=(256, BF), RE=(256, BF), KE=(256, BF), PN=(256, BF), L=(128, BF), L2=(128, BF),
     sI=(128, BF), nI=(128, BF), hI=(128, BF), gI=(128, BF), qI=(128, BF), uI=(128, BF), dI=(128, BF), K8=(128, BF), one=(256, BF),
     KD=(KO[RO], BF), t1=(128, BF), t2=(128, BF), Dm=(15 * 128, BF), Ci=(PC, BF), Kx=(384, BF),
-    Kn=(128, BF), Cd=(128, BF), Af=(128, F32), Cm=(128, BF), Oa=(128, BF), Ob=(128, BF), MT=(128, BF),
+    Kn=(128, BF), Cd=(128, BF), Af=(128, F32), Cm=(256, BF), Oa=(128, BF), Ob=(128, BF), MT=(128, BF),
 )
 SCRATCH = {k: ("sbuf", [128, n], d) for k, (n, d) in _S.items()}
 W3 = dict(Hs0=32, Hs1=32, PR=32, OM=16, AH=16, BH=16, Of=16, Lq=16)
@@ -38,11 +38,15 @@ SEMAPHORES = (["cv", "ca", "cp", "cg", "sent"] + ["d%d" % k for k in range(NDMA)
               + ["r%d_%d" % (t, c) for t in range(1, RO) for c in range(NC)])
 
 DLAT = 2200.0
-_M = dict(CY=0.87, PCY=0.44, LAT=170.0, RLAT=3200.0, OV=52.0, AO=30.0, GF=1.56, SF=3.8, BW=240.0)
+_M = dict(CY=0.87, PCY=0.44, LAT=170.0, RLAT=3200.0, OV=52.0, AO=30.0, GF=1.56, SF=3.8, BW=240.0, R0=2000.0, MINC=0.0, PS=0.0)
 MODELS = [_M]
-OPT = dict(JUDGE=[], HB=("P4", "P3"), BK=("40122", "35555", "1"), KG=((6, 10), (10, 14), (14, 16), (1, 4), (4, 6), (0, 1)),
-           MZA=3, UZA=0, SCV=0, YA=0, FM=3, NG=2, DF=4, MSP=12, CUT=(6, 12), GM=1,
-           BIAS=300.0, TEMP=100.0, PK=0.4, ITER=18000)
+OPT = dict(JUDGE=[dict(_M, MINC=64.0, OV=30.0, RLAT=4300.0, LAT=200.0, W=0.95),
+                  dict(_M, PS=60.0, AO=80.0, CY=0.95, PCY=0.52, GF=1.8, LAT=130.0, W=0.87),
+                  dict(_M, MINC=64.0, OV=45.0, CY=0.83, PCY=0.5, LAT=110.0, RLAT=2600.0, BW=330.0, W=1.0)],
+           HB=("P4", "P3"), BK=("40122", "35333", "1"), KG=((6, 10), (10, 14), (14, 16), (1, 4), (4, 6), (0, 1)),
+           MZB=((("P0", 0, 3), ("P1", 0, 2)), (("P5", 0, 4), ("P5", 0, 1))), PM=0, PRE=0, ND=3, DB="P5", MZA=3, UZA=0, SCV=0, YA=0, FM=3, NG=2, DF=(4, 4),
+           START=({(1, "header"): 3000.0, (1, "dyn"): 1000.0},), MSP=12, CUT=(4, 8, 12), GM=1,
+           BIAS=300.0, TEMP=60.0, PK=0.6, ITER=15000)
 
 
 def R(n, a, b, s=1):
@@ -74,11 +78,13 @@ def build(M):
         if w[0] in ("Mw", "Xh") and w[1] % XS >= B2:
             a = -1 - (w[1] % XS == B2 + MISS)
         key = (tag[1], tag[0], call[0], "P0" if w[0] in ("P1", "P2") else w[0], a)
+        if eng in "va" and any(r[0] not in _S for r in list(rd) + wr if isinstance(r, tuple)):
+            cost += M["PS"]
         ops.append(dict(eng=eng, call=call, rd=[r for r in rd if isinstance(r, tuple)], wr=wr, cost=cost, lat=lat,
                         grp=(tag[1], tag[0]), key=key, **kw))
 
     def vc(n):
-        return OV + n * CY
+        return OV + max(n, M["MINC"]) * CY
 
     def ts(o, i, s1, op0, s2=None, op1=None):
         add("v", ("ts", o, i, s1, s2, op0, op1), [i, s1, s2], [o], vc(width(o) * (0.5 if two(o, i) else 1)))
@@ -156,8 +162,8 @@ def build(M):
         ts(c1("col", ncol[0]), src, s1, op0, s2, op1)
         return c1("col", ncol[0])
 
-    dma(R("wts", 0, 2), ("wt", 0, 2), [], [R("wts", 0, 2)], 512, boost=30000.0)
     dma(R("m0s", 0, 16), ("m0", 0, 16), [], [R("m0s", 0, 16)], 4096, boost=30000.0)
+    dma(R("wts", 0, 2), ("wt", 0, 2), [], [R("wts", 0, 2)], 512, boost=30000.0)
     dma(R("zin", 0, 256), ("z0", 0, 256), [], [R("zin", 0, 256)], 65536, boost=20000.0)
     for k in range(2):
         r = R("X", 16 + 4096 * k, 16 + 4096 * (k + 1))
@@ -193,18 +199,22 @@ def build(M):
                 a = 8 * (2 * h + b)
                 lin(R3(n + "H", a, a + 8, 8 * b, 8 * b + 8), R3("OM", 0, 8, 8 * h, 8 * h + 8), c1("wf", k))
     ts(full("dl"), full("Rn"), rc, ALU.is_equal)
-    ms(R("pc", 0, 16), 2.0 ** -5)
+    ms(R("pc", 0, 16), 2.0 ** -10)
     ms(R("pc", 16, 32), 0.0)
-    scan(R("pw", 0, 16), R("pc", 0, 16), R("pc", 16, 32), 2.0 ** 39, ALU.mult, ALU.add)
+    scan(R("pw", 0, 16), R("pc", 0, 16), R("pc", 16, 32), 2.0 ** 78, ALU.mult, ALU.add)
     tt(R("pw", 0, 16), R("pw", 0, 16), R("dl", 0, 16), ALU.mult)
     ncol[0] += 1
-    unit = c1("col", ncol[0])
-    red(unit, R("pw", 0, 16))
+    wc = c1("col", ncol[0])
+    red(wc, R("pw", 0, 16))
+    act(c1("ub", 0), wc, AF.Sqrt)
+    ops[-1]["cost"] += 1300.0
+    ops[-1]["boost"] = 20000.0
+    unit = column(c1("ub", 0), 1.0, ALU.mult)
     ts(R("RB", 0, 8), R("O", 0, 128, 16), -H54, ALU.mult, H54, ALU.mult)
-    ts(R("RB", 8, 16), R("O", 0, 128, 16), unit, ALU.mult, unit, ALU.mult)
+    ts(R("RB", 8, 16), R("O", 0, 128, 16), wc, ALU.mult)
     for s in range(16):
         lin(R("RS", 16 * s, 16 * s + 16), R("RB", 0, 16), c1("mf", s))
-    for n, v in (("sI", SC), ("nI", -SC), ("hI", 0.5), ("gI", -0.5), ("qI", 0.25), ("uI", unit), ("K8", 256.0), ("dI", -16384.0)):
+    for n, v in (("sI", SC), ("nI", -SC), ("hI", 0.5), ("gI", -0.5), ("qI", 0.25), ("uI", unit), ("K8", 256.0), ("mI", -1.0), ("dI", -16384.0)):
         lin(full(n), ID, v)
     ops[-1]["boost"] = 20000.0
     magic = column(unit, 1.5 * 2.0 ** 28, ALU.mult)
@@ -246,7 +256,8 @@ def build(M):
         ms(R(n, 0, w, 16), v)
     for t in range(RO):
         select(R("KD", KO[t], KO[t + 1]), R("one", 0, 8 * (16 + t)), [[0, 8], [1, 16 + t]], 0, 0, ALU.not_equal)
-    lin(full("Cm"), full("dl"), 2.0 ** 21, -2.0 ** 21)
+    for k in range(2):
+        lin(R("Cm", PC * k, PC * k + PC), full("dl"), 2.0 ** 21, -2.0 ** 21)
     mm([(R("P0", 0, 128), [(full("OM"), ID)])])
     lin(full("MT"), R("P0", 0, 128), 1.0)
     ts(full("Cd"), full("Rn"), rc, ALU.is_ge, 2.0 ** 28, ALU.mult)
@@ -272,6 +283,10 @@ def build(M):
     x = column(c1("ge", 16), -float(B2), ALU.mult, float(B2), ALU.add)
     lin(wide("KE"), wide("Of"), column(c1("ge", 24), 1024.0, ALU.mult, x, ALU.add))
     select(wide("PN"), wide("one"), [[-128, 2], [32, 8], [1, 16]], 16, -1)
+    mm([(R("P1", 0, 128), [(full("L"), ID)])])
+    lin(full("LT"), R("P1", 0, 128), 1.0)
+    mm([(R("P2", 0, 256), [(full("LT"), wide("PN"))])])
+    lin(wide("PL"), R("P2", 0, 256), 1.0)
 
     def penalty(ch, t):
         o, i, c = R("pen", 256 * ch, 256 * ch + 256), R("rank", 256 * ch, 256 * ch + 256), c1("penb", t % 2)
@@ -306,7 +321,7 @@ def build(M):
     rot = [0]
 
     def dbank():
-        rot[0] = (rot[0] + 1) % 3
+        rot[0] = (rot[0] + 1) % OPT["ND"]
         return "P%d" % rot[0]
 
     Xg = R("X", 16, 8208)
@@ -336,22 +351,43 @@ def build(M):
                 tag[:] = "mz", ch + 1
                 zb = t * PC * ch
                 if OPT["MZA"] >> ch & 1:
-                    for a in range(0, t, 2):
-                        ks = list(range(a, min(a + 2, t)))
-                        mm([(R(hb, (2 + k - a) * PC, (3 + k - a) * PC), [(ID, z), (full("K8"), slot("Mw", 16 + k))]) for k in ks])
-                        act(R("MZ", zb + a * PC, zb + (ks[-1] + 1) * PC), R(hb, 2 * PC, (2 + len(ks)) * PC), AF.Relu, bias=-256.0)
+                    a = 0
+                    for bk, o, n in OPT["MZB"][ch]:
+                        ks = list(range(a, min(a + n, t)))
+                        if ks:
+                            mm([(R(bk, (o + k - a) * PC, (o + 1 + k - a) * PC), [(ID, z), (full("K8"), slot("Mw", 16 + k))]) for k in ks])
+                            act(R("MZ", zb + a * PC, zb + (ks[-1] + 1) * PC), R(bk, o * PC, (o + len(ks)) * PC), AF.Relu, bias=-256.0)
+                        a += n
                 elif t:
                     mm([(R(hb, 3 * PC, 4 * PC), [(ID, z)])])
                     for k in range(t):
                         tt(R("MZ", zb + k * PC, zb + k * PC + PC), slot("Mw", 16 + k), R(hb, 3 * PC, 4 * PC), ALU.mult)
                 tag[0] = "hash"
-                for k, n in enumerate(("AH", "BH")):
+                def sums(k, less=None):
                     mm([(R(hb, k * PC + 64 * h, k * PC + 64 * h + 64),
-                         [(R(n, 128 * (2 * h + b), 128 * (2 * h + b + 1)), R(z[0], z[1] + b, z[2], 2)) for b in range(2)])
-                        for h in range(2)])
-                place_list(pt("off"), hashed(R(hb, 0, 2 * PC), R(hb, 0, PC), "F1" if OPT["FM"] >> ch & 1 else "I1", wb, "I2", pb))
+                         [(R("AB"[k] + "H", 128 * (2 * h + b), 128 * (2 * h + b + 1)), R(z[0], z[1] + b, z[2], 2)) for b in range(2)]
+                         + ([(ID, R(less, wb + k * PC + 64 * h, wb + k * PC + 64 * h + 64))] if less else [])) for h in range(2)])
+
+                for k in range(2):
+                    sums(k)
+                if OPT["PM"] >> ch & 1:
+                    act(both("F1"), R(hb, 0, 2 * PC), AF.Identity, bias=2.0 ** 23 - 0.5, scale=2.0 ** -12 + 2.0 ** -34)
+                    act(both("q1"), both("F1"), AF.Relu, bias=-2.0 ** 35, scale=4096.0)
+                    for k in range(2):
+                        sums(k, "q1")
+                        for m in ops[-1]["call"][1][2::3]:
+                            ops[-1]["call"][1][ops[-1]["call"][1].index(m)] = (m[0], full("mI")) + m[2:]
+                        ops[-1]["rd"].append(full("mI"))
+                    u, w, vp = half("F1", 0), half("F1", 1), R(hb, PC, 2 * PC)
+                    lin(u, R(hb, 0, PC), 1.0)
+                    lin(w, u, 1184.0, -FOLD)
+                    tt(vp, vp, u, ALU.mult)
+                    tt(pt("I2"), vp, w, ALU.add)
+                    place_list(pt("off"), pt("I2"))
+                else:
+                    place_list(pt("off"), hashed(R(hb, 0, 2 * PC), R(hb, 0, PC), "F1" if OPT["FM"] >> ch & 1 else "I1", wb, "I2", pb))
                 if t and not ch:
-                    tag[0], n = "dyn", 2 * t * CC
+                    tag[0], n, hb = "dyn", 2 * t * CC, OPT["DB"]
                     for k, m in enumerate("AB"):
                         mm([(R(hb, 2 * PC + k * n, 2 * PC + k * n + n), [(view(m, r), R("MZ", r, 2 * t * PC, 16)) for r in range(16)])])
                     place_list(R("ofd", 0, n), hashed(R(hb, 2 * PC, 2 * PC + 2 * n), R(hb, 2 * PC, 2 * PC + n), "I3", 0, "I4", 0))
@@ -371,7 +407,7 @@ def build(M):
             tag[0] = "compare"
             blocks = [list(range(a, a + 4)) for a in range(0, 16, 4)]
             dblk = [list(range(16 + a, 16 + min(a + 4, t))) for a in range(0, t, 4)]
-            blocks = blocks[:OPT["DF"]] + dblk + blocks[OPT["DF"]:]
+            blocks = blocks[:OPT["DF"][ch]] + dblk + blocks[OPT["DF"][ch]:]
             for bl in blocks:
                 bk, n, g0 = dbank(), len(bl) * PC, gb + bl[0] * PC
                 mm([(R(bk, j * PC, j * PC + PC), [(full("sI"), slot("Xh", s)), (full("nI"), z)]) for j, s in enumerate(bl)])
@@ -399,7 +435,13 @@ def build(M):
             mm([(R(Q, PC * h, PC * h + PC), [(R(Hs, PC * h, PC * h + PC), ID)]) for h in range(2)])
             act(both("b"), R(Q, 0, 256), AF.Relu, bias=1.0, scale=-2.0 ** -106, acc=c1("mcnt", ch))
             act(both("H"), R(Q, 0, 256), AF.Sqrt)
-            mm([(mr(1, PC), [(ID, full("Ci"))] + [(half("IB", h, 0), half("b", h)) for h in range(2)])])
+            if OPT["PRE"] & 2:
+                mm([(mr(1, PC), [(ID, full("Ci"))])], last=False)
+                ops[-1]["wr"] = [mr(1, 0, 512)]
+                mm([(mr(1, PC), [(half("IB", h, 0), half("b", h)) for h in range(2)])], first=False)
+                ops[-1]["wr"] = [mr(1, 0, 512)]
+            else:
+                mm([(mr(1, PC), [(ID, full("Ci"))] + [(half("IB", h, 0), half("b", h)) for h in range(2)])])
             scan(pt("sc"), R("Kx", 0, PC), mr(1, PC), 0.0, ALU.add, ALU.max)
             ix = R("idx", CC * ch, CC * ch + CC)
             ts(ix, R("sc", pb + 15, pb + PC, 16), float(B2 + 4), ALU.add)
@@ -411,7 +453,7 @@ def build(M):
             act(new, pt("ds"), AF.Abs)
             if t < RO - 1:
                 zn = R("zin", 256 * (t + 1) + pb, 256 * (t + 1) + pb + PC)
-                add("g", ("send", zn, new, "r%d_%d" % (t + 1, ch)), [new], [zn], 300.0, lat=RLAT)
+                add("g", ("send", zn, new, "r%d_%d" % (t + 1, ch)), [new], [zn], 300.0, lat=RLAT + (0 if t else M["R0"]))
             tag[0] = "mask"
             terms = []
             for q, (a, b) in enumerate(WIN):
@@ -430,6 +472,9 @@ def build(M):
             U = slot("Mw", 16 + t) if t < RO - 1 else R("ymb", pb, pb + PC)
             tt(U, xx, pt("e1"), ALU.is_gt)
             tag[0] = "rank"
+            if t == RO - 1:
+                mm([(mr(2, 0), [(half("PN", h, 0), half("rank", h)) for h in range(2)] + [(half("PL", h, 0), half("b", h)) for h in range(2)])])
+                lin(pt("rk"), mr(2, 0), 1.0)
             sp = mr(2, 2 * PC, 2 * PC)
             if OPT["SCV"] >> ch & 1:
                 mm([(sp, [(full("L"), both("b"))])])
@@ -448,7 +493,13 @@ def build(M):
                     mm([(zs, [(ID, z)])])
                     tt(pt("UZ"), U, zs, ALU.mult)
                 jb = 2 * CC * ch
-                mm([(mr(4, k * PC), [(ID, full("Cm")), (full(m), pt("UZ"))]) for k, m in enumerate(("Oa", "Ob"))])
+                if OPT["PRE"] & 1:
+                    mm([(mr(4, 0, 2 * PC), [(ID, wide("Cm"))])], last=False)
+                    ops[-1]["wr"] = [mr(4, 0, 512)]
+                    mm([(mr(4, k * PC), [(full(m), pt("UZ"))]) for k, m in enumerate(("Oa", "Ob"))], first=False, one=True)
+                    ops[-1]["wr"] = [mr(4, 0, 512)]
+                else:
+                    mm([(mr(4, k * PC), [(ID, full("Cm")), (full(m), pt("UZ"))]) for k, m in enumerate(("Oa", "Ob"))])
                 scan(both("su"), wide("Kx"), mr(4, 0, 2 * PC), 0.0, ALU.add, ALU.max)
                 x = hashed(R("su", wb + 15, wb + 2 * PC, 16), R(Q, 0, CC), "J1", jb, "J2", CC * ch)
                 ts(R("J3", jb, jb + CC), x, 5, ALU.arith_shift_right, 8128, ALU.bitwise_and)
@@ -461,11 +512,9 @@ def build(M):
                 scan(pt("sD"), full("Kn"), pt("aD"), 0.0, ALU.add, ALU.min)
                 cp(R("xo", jb, jb + 2 * CC, 2), R("sD", pb + 15, pb + PC, 16))
         tag[:] = "rank", 3
-        if t in (RO - 2, RO - 1):
-            a = 0 if t == RO - 2 else 256 * t
-            r = R("yzb", a, 256 * t + 256)
-            dma(("yz", a, 256 * t + 256), r, [r], [], 65536 * (5 if t == RO - 2 else 1))
         if t == RO - 1:
+            r = R("yzb", 256 * t, 256 * t + 256)
+            dma(("yz", 256 * t, 256 * t + 256), r, [r], [], 65536)
             break
         pa = R("P" + OPT["BK"][2], PC, PC + 1)
         mm([(pa, [(full("Af"), c1("mcnt", ch)) for ch in range(NC)])], f=4)
@@ -478,14 +527,14 @@ def build(M):
             tag[:] = "write", 1 + c // CC
             zz = R("zin", 256 * t + 16 * c, 256 * t + 16 * c + 16)
             add("v", ("sca", R("X", 0, 8208), c1("xo", 2 * c), zz), [zz, c1("xo", 2 * c)], [R("X", 0, 8208)], 50 + 16 * SF * CY)
+        if t == RO - 2:
+            r = R("yzb", 0, 256 * t + 256)
+            dma(("yz", 0, 256 * t + 256), r, [r, Xg], [], 65536 * (t + 1))
 
     for ch in range(NC - 1, -1, -1):
         wb, pb, xb = 256 * ch, PC * ch, XS * ch
         tag[:] = "end", 10 + ch
         ew = lambda k, h: R("Ew", (10 * ch + 2 * k - 2 + h) * PC, (10 * ch + 2 * k - 1 + h) * PC)
-        pp = R("P%d" % (4 + ch), 0, PC)
-        mm([(pp, [(R("PN", PC * h, PC * h + PC), R("rank", wb + PC * h, wb + PC * h + PC)) for h in range(2)])])
-        lin(R("rk", pb, pb + PC), pp, 1.0)
         for ks in ((1, 2, 3), (4, 5)):
             bk, n, a = dbank(), len(ks) * PC, (5 * ch + ks[0] - 1)
             for k in ks:
@@ -542,12 +591,7 @@ def inline(p, o):
 def place(P, prio, bias):
     succ, eng, cost, lat, banks = P
     n = len(eng)
-    p = list(prio)
-    for k in range(n):
-        x = p[k]
-        for j, _ in succ[k]:
-            if p[j] > x:
-                p[j] = x
+    p = prio
     at, by, held, st, eo = [0.0] * n, [-1] * n, [-1] * n, [0.0] * n, list(eng)
     qs = {e: ([], [], []) for e in "vapgs"}
     bk = {b: ([], []) for bs in banks for b in bs}
@@ -629,8 +673,10 @@ def plan(iters=None, seed=1):
     others = [prices(build(m)) for m in OPT["JUDGE"]]
 
     def judged(st, eo, val):
+        if not others:
+            return val
         order, last, wait = sorted(range(n), key=lambda k: st[k]), {}, [None] * n
-        for k in order if others else ():
+        for k in order:
             w = pre[k]
             for b in P[4][k]:
                 if b in last and eo[last[b]] != eo[k]:
@@ -666,10 +712,17 @@ def plan(iters=None, seed=1):
         kin.setdefault(o["key"], []).append(k)
         gin.setdefault(o["grp"], []).append(k)
     grps, keys = sorted(gin), sorted(k for k in kin if k[0])
-    cp, cb = [o["pr"] + o.get("boost", 0.0) for o in base], [OPT["BIAS"]] * n
-    best, cur, own, pairs, ceo = None, None, 0.0, [], None
-    for it in range(iters + 1):
-        p, b = list(cp), cb
+    starts = [[o["pr"] + o.get("boost", 0.0) + s.get(o["grp"], 0.0) for o in base] for s in OPT["START"]]
+    best, short = None, iters // (2 * len(starts)) if len(starts) > 1 else iters + 1
+    for step in range(iters + 1):
+        run, it = divmod(step, short)
+        if run >= len(starts):
+            it, span = step - short * len(starts) + 1, iters - short * len(starts) + 1
+            if it == 1:
+                cur, _, ceo, cp, cb, own, pairs = best
+        elif not it:
+            cp, cb, cur, own, pairs, ceo, span = starts[run], [OPT["BIAS"]] * n, None, 0.0, [], None, short
+        p, b, d = list(cp), cb, 0.0 if it else 1.0
         if it and (rnd() < 0.3 or not pairs):
             d = (rnd() * 2 - 1) * 1500
             for k in gin[one(grps)] if rnd() < 0.3 else kin[one(keys)]:
@@ -687,14 +740,25 @@ def plan(iters=None, seed=1):
                 j, d = (k, d) if y < 0.7 else (h, -d)
                 for i in kin[base[j]["key"]] if wide else [j]:
                     p[i] += d
+        if d > 0:
+            for k in range(n - 1, -1, -1):
+                for j, _ in succ[k]:
+                    if p[j] > p[k]:
+                        p[k] = p[j]
+        elif d < 0:
+            for k in range(n):
+                x = p[k]
+                for j, _ in succ[k]:
+                    if p[j] > x:
+                        p[j] = x
         st, eo, val, pp = place(P, p, b)
         if cur is not None and val > own + 1500.0:
             continue
         mine, val = val, judged(st, eo, val)
-        if cur is None or val <= cur - OPT["TEMP"] * max(0.02, 1 - it / (iters + 1)) * math.log(rnd()):
+        if cur is None or val <= cur - OPT["TEMP"] * max(0.02, 1 - it / span) * math.log(rnd()):
             cp, cb, cur, own, pairs, ceo = p, b, val, mine, pp, eo
         if best is None or val < best[0]:
-            best = (val, st, eo)
+            best = (val, st, eo, p, b, mine, pp)
     order = sorted(range(n), key=lambda k: (best[1][k], k))
     last = {base[k]["gid"]: k for k in order if "gid" in base[k]}
     for k in order:
@@ -725,9 +789,9 @@ def rank_program(g, core, T, topo):
     nxt = T.cores[(rank + 1) % len(T.cores)]
     prv = T.cores[(rank - 1) % len(T.cores)]
     rid, pid, _ = topo.addr(nxt)
-    NE = 8
-    mask = sum(1 << e for e in topo.engines(core, nxt)[:NE])
-    assert len(topo.engines(prv, core)) >= NE and topo.may_write(core, nxt)
+    nout = nin = 8
+    mask = sum(1 << e for e in topo.engines(core, nxt)[:nout])
+    assert len(topo.engines(prv, core)) >= nin and topo.may_write(core, nxt)
     Q = dict(v=g.vector, a=g.scalar, p=g.tensor, g=g, s=g.sync)
 
     def ap(r):
@@ -770,8 +834,8 @@ def rank_program(g, core, T, topo):
             continue
         if f == "send":
             g.remote_dma(ap(c[1]), ap(c[2]), T.sem[c[3]], T.sem.sent, pid, rid, mask)
-            token[k] = (c[3], NE)
-            sends += NE
+            token[k] = (c[3], nin)
+            sends += nout
             continue
         if f == "ts":
             ins = (q.tensor_scalar(ap(c[1]), ap(c[2]), ap(c[3]), None, c[5]) if c[6] is None

@@ -2,33 +2,37 @@ import math
 from concourse.mybir import AluOpType as ALU, AxisListType, ActivationFunctionType as AF
 
 NC, PC, CC, RO = 2, 128, 8, 6
-B1, B2, MISS, XS = 1031, 2064, 6, 3088
+B1, B2, B3, XS, MISS = 1028, 2059, 3090, 4112, 21
 WIN = [(0, 2), (3, 5), (6, 8), (9, 11), (12, 15)]
 SC, CR = 113.0 / 128, 1.5 * 2.0 ** 30
+NB, M12 = 19, 1.5 * 2.0 ** 35
 KO = [sum(8 * (16 + i) for i in range(t)) for t in range(RO + 1)]
 H54 = 2.0 ** 54
 FOLD = 41.0 * 2 ** 18
 
 BF, F32, I32, U16 = "bfloat16", "float32", "int32", "uint16"
+MAT = "sI nI hI gI qI uI dI K8 C1 C2 C3 MI MN RI RN".split()
 _S = dict(
-    X=(8208, BF), Xh=(NC * XS, BF), Mw=(NC * XS, BF), G=(NC * 21 * PC, BF),
+    X=(8208, BF), Xh=(NC * XS, BF), Mw=(NC * XS, BF),
     zin=(6 * 256, BF), yzb=(6 * 256, BF), ymb=(4096, BF), m0s=(16, BF), wts=(16, BF),
     MZ=(NC * 5 * PC, BF), TH=(NC * 5 * PC, BF), I1=(512, I32), I2=(256, I32), off=(256, U16), F1=(512, F32),
     I3=(160, I32), I4=(80, I32), ofd=(80, U16), H=(512, BF), b=(512, BF), Cq=(5 * 512, BF), rank=(512, BF), pen=(512, BF),
-    rm=(2 * 168, BF), mcnt=(8, F32), sc=(256, F32), idx=(16, U16), ds=(256, BF), ms=(256, BF), e1=(256, F32), y1=(256, F32),
-    UZ=(256, BF), J1=(32, I32), J2=(16, I32), J3=(32, I32), hl=(32, BF), aD=(256, F32), sD=(256, F32), xo=(32, U16), ai=(8, I32),
-    su=(512, F32), rk=(256, BF), Es=(20 * PC, BF), Ew=(20 * PC, BF), se=(10 * PC, F32), to=(80, U16),
+    mcnt=(8, F32), sc=(256, F32), idx=(16, U16), ds=(256, BF), ms=(256, BF), e1=(256, F32), y1=(256, F32),
+    J1=(48, F32), J2=(16, I32), J3=(32, I32), hl=(32, BF), aD=(256, F32), sD=(256, F32), xo=(32, U16), ai=(8, I32),
+    su=(32 * NB, F32), Ku=(16 * NB, F32), rk=(256, BF), Es=(20 * PC, BF), to=(80, U16),
+    PA=(7 * 96, F32), AJ=(80, F32), lr=(8, U16), BI=(128, F32), NI=(128, F32),
     pi=(8, I32), col=(40, F32), penb=(8, F32), Gn=(128, F32), Gw=(256, F32), G32=(128, F32), Rn=(128, F32), R32=(32, F32),
     ge=(32, F32), eq=(32, F32), Nn=(144, F32), N8=(128, F32), Id=(136, BF), O=(128, BF), E=(144, BF), A=(144, BF), B=(144, BF),
-    ub=(8, BF), q1=(512, BF), mI=(128, BF), PL=(256, BF), LT=(128, BF), mf=(16, F32), wf=(8, F32), pw=(16, F32), pc=(32, F32), dl=(128, F32), RB=(16, BF), RS=(256, BF),
-    IB=(256, BF), RE=(256, BF), KE=(256, BF), PN=(256, BF), L=(128, BF), L2=(128, BF),
-    sI=(128, BF), nI=(128, BF), hI=(128, BF), gI=(128, BF), qI=(128, BF), uI=(128, BF), dI=(128, BF), K8=(128, BF), one=(256, BF),
-    KD=(KO[RO], BF), t1=(128, BF), t2=(128, BF), Dm=(15 * 128, BF), Ci=(PC, BF), Kx=(384, BF),
-    Kn=(128, BF), Cd=(128, BF), Af=(128, F32), Cm=(256, BF), Oa=(128, BF), Ob=(128, BF), MT=(128, BF),
+    ub=(8, BF), PL=(256, BF), LT=(128, BF), mf=(16, F32), wf=(8, F32), pw=(16, F32), pc=(32, F32), dl=(128, F32), RB=(16, BF),
+    IB=(256, BF), PN=(256, BF), L=(128, BF), L2=(128, BF),
+    one=(512, BF), AN=(512, BF), BN=(512, BF), mat=(128 * len(MAT), BF),
+    KD=(KO[RO], BF), rm=(2 * 168, BF), t1=(128, BF), t2=(128, BF), Dm=(15 * 128, BF), Ci=(PC, BF), Kx=(PC, BF),
+    Kn=(128, BF), Cd=(128, BF), Af=(128, F32), Oa=(128, BF), Ob=(128, BF), MT=(128, BF),
 )
 SCRATCH = {k: ("sbuf", [128, n], d) for k, (n, d) in _S.items()}
-W3 = dict(Hs0=32, Hs1=32, PR=32, OM=16, AH=16, BH=16, Of=16, Lq=16)
-for _k, _n in (("Hs0", 8), ("Hs1", 8), ("PR", 16), ("OM", 8), ("AH", 32), ("BH", 32), ("Of", 16), ("Lq", 96)):
+W3 = dict(Hs0=32, Hs1=32, PR=32, OM=16, AH=16, BH=16, Of=16, Lq=16, G=PC, UZ=NB, Cm=NB, RS=128)
+for _k, _n in (("Hs0", 8), ("Hs1", 8), ("PR", 8), ("OM", 8), ("AH", 32), ("BH", 32), ("Of", 16), ("Lq", 96),
+               ("G", NC * 21), ("UZ", 16), ("Cm", 8), ("RS", 2)):
     SCRATCH[_k] = ("sbuf", [128, _n, W3[_k]], BF)
     _S[_k] = (W3[_k] * _n, BF)
 for _b in ("P0", "P1", "P2", "P3", "P4", "P5", "Q0", "Q1"):
@@ -37,30 +41,35 @@ NDMA = 16
 SEMAPHORES = (["cv", "ca", "cp", "cg", "sent"] + ["d%d" % k for k in range(NDMA)]
               + ["r%d_%d" % (t, c) for t in range(1, RO) for c in range(NC)])
 
-DLAT = 2200.0
-_M = dict(CY=0.87, PCY=0.44, LAT=170.0, RLAT=3200.0, OV=52.0, AO=30.0, GF=1.56, SF=3.8, BW=240.0, R0=2000.0, MINC=0.0, PS=0.0)
+_M = dict(CY=0.87, PCY=0.46, LAT=180.0, RLAT=3000.0, OV=50.0, AO=30.0, GF=1.56, SF=3.8, BW=340.0, R0=2000.0, MINC=0.0, PS=0.0,
+          DLAT=1400.0)
 MODELS = [_M]
-OPT = dict(JUDGE=[dict(_M, MINC=64.0, OV=30.0, RLAT=4300.0, LAT=200.0, W=0.95),
+OPT = dict(JUDGE=[dict(_M, MINC=64.0, OV=25.0, RLAT=4000.0, LAT=230.0, BW=240.0, DLAT=2200.0, W=0.95),
                   dict(_M, PS=60.0, AO=80.0, CY=0.95, PCY=0.52, GF=1.8, LAT=130.0, W=0.87),
-                  dict(_M, MINC=64.0, OV=45.0, CY=0.83, PCY=0.5, LAT=110.0, RLAT=2600.0, BW=330.0, W=1.0)],
-           HB=("P4", "P3"), BK=("40122", "35333", "1"), KG=((6, 10), (10, 14), (14, 16), (1, 4), (4, 6), (0, 1)),
-           MZB=((("P0", 0, 3), ("P1", 0, 2)), (("P5", 0, 4), ("P5", 0, 1))), PM=0, PRE=0, ND=3, DB="P5", MZA=3, UZA=0, SCV=0, YA=0, FM=3, NG=2, DF=(4, 4),
-           START=({(1, "header"): 3000.0, (1, "dyn"): 1000.0},), MSP=12, CUT=(4, 8, 12), GM=1,
-           BIAS=300.0, TEMP=60.0, PK=0.6, ITER=15000)
+                  dict(_M, MINC=64.0, OV=45.0, CY=0.83, PCY=0.5, LAT=110.0, RLAT=2400.0, BW=400.0, DLAT=1000.0, W=1.0)],
+           HB=("P4", "P3"), HA=0, BK=("401224", "353335", "1", "1"), KG=((6, 8), (8, 12), (12, 16), (1, 4), (4, 6), (0, 1)),
+           MZB=((("P0", 0, 3), ("P1", 0, 2)), (("P5", 0, 4), ("P5", 0, 1))), PM=3, PRE=0, ND=3, DB=("P5", "P5"), DY=0, MZA=3, UZA=0, YA=0, FM=3, DF=(4, 4),
+           CA=(0, 0), NK=8, WO=(4, 0, 1, 2, 3),
+           START={(1, "header"): 3000.0, (1, "dyn"): 1000.0}, MSP=12, CUT=(4, 8, 10, 12), GM=1, GD=256,
+           BIAS=300.0, TEMP=40.0, PK=0.4, PR=0.4, FB=10, FAR=600.0, ITER=50000)
 
 
 def R(n, a, b, s=1):
     return (n, a, b, s)
 
 
-def R3(n, g0, g1, a, b):
-    return (n, W3[n] * g0 + a, W3[n] * (g1 - 1) + b, 1, (g0, g1, a, b, 1))
+def R3(n, g0, g1, a, b, s=1):
+    return (n, W3[n] * g0 + a, W3[n] * (g1 - 1) + b, 1, (g0, g1, a, b, s))
+
+
+def columns(r):
+    if len(r) == 5:
+        return [W3[r[0]] * g + c for g in range(r[4][0], r[4][1]) for c in range(*r[4][2:])]
+    return range(*r[1:])
 
 
 def width(r):
-    if len(r) == 5:
-        return (r[4][1] - r[4][0]) * (r[4][3] - r[4][2])
-    return (r[2] - r[1] + r[3] - 1) // r[3]
+    return len(columns(r))
 
 
 def two(*rs):
@@ -70,18 +79,22 @@ def two(*rs):
 def build(M):
     CY, PCY, LAT, RLAT, OV, AO, GF, SF, BW = [M[k] for k in ("CY", "PCY", "LAT", "RLAT", "OV", "AO", "GF", "SF", "BW")]
     ops = []
-    tag = ["set", 0]
+    tag, now = ["set", 0], [0]
 
     def add(eng, call, rd, wr, cost, lat=LAT, **kw):
         w = wr[0] if wr else ("", 0)
         a = w[1] % 256 if w[0] in ("zin", "yzb") else 0 if w[0] in ("TH", "penb", "MZ", "P0", "P1", "P2") else w[1]
-        if w[0] in ("Mw", "Xh") and w[1] % XS >= B2:
-            a = -1 - (w[1] % XS == B2 + MISS)
+        if w[0] in ("Mw", "Xh") and w[1] % XS < B1:
+            a = -1
+        if w[0] == "PA":
+            a = w[1] % 96
+        if w[0][:1] == "Q" and tag[0] == "compare":
+            a = min(call[1][0][1][1] % (21 * PC), 16 * PC)
         key = (tag[1], tag[0], call[0], "P0" if w[0] in ("P1", "P2") else w[0], a)
         if eng in "va" and any(r[0] not in _S for r in list(rd) + wr if isinstance(r, tuple)):
             cost += M["PS"]
         ops.append(dict(eng=eng, call=call, rd=[r for r in rd if isinstance(r, tuple)], wr=wr, cost=cost, lat=lat,
-                        grp=(tag[1], tag[0]), key=key, **kw))
+                        grp=(tag[1], tag[0]), key=key, step=now[0], **kw))
 
     def vc(n):
         return OV + max(n, M["MINC"]) * CY
@@ -140,11 +153,11 @@ def build(M):
     nd = [0]
 
     def dma(o, i, rd, wr, nbytes, **kw):
-        add("s", ("dma", o, i, nd[0]), rd, wr, max(60.0, nbytes / BW), lat=DLAT, **kw)
+        add("s", ("dma", o, i, nd[0]), rd, wr, max(60.0, nbytes / BW), lat=M["DLAT"], **kw)
         nd[0] += 1
 
     def full(n):
-        return R(n, 0, 128)
+        return R("mat", 128 * MAT.index(n), 128 * MAT.index(n) + 128) if n in MAT else R(n, 0, 128)
 
     def wide(n):
         return R(n, 0, 256)
@@ -170,7 +183,8 @@ def build(M):
         dma(r, ("xr", 4096 * k, 4096 * (k + 1)), [], [r], 1 << 20)
 
     ID = R("Id", 1, 129)
-    ms(wide("one"), 1.0)
+    unused = ([] if (OPT["CA"][0] | OPT["CA"][1]) & 31 else ["C1", "C2"]) + ([] if OPT["PM"] else ["C3"]) + ([] if OPT["YA"] else ["RI", "RN"])
+    ms(R("one", 0, 512), 1.0)
     iota(c1("pi", 0), [[0, 1]], 0, 1)
     iota(full("Gn"), [[16, 8], [0, 16]], 0, 0)
     select(R("Id", 0, 129), R("one", 0, 129), [[1, 129]], -1, -1)
@@ -178,8 +192,7 @@ def build(M):
     iota(R("Nn", 0, 144), [[1, 144]], -15, 0)
     iota(full("Rn"), [[0, 8], [1, 16]], 0, 0)
     iota(wide("Gw"), [[-128, 2], [32, 8], [0, 16]], 0, 0)
-    iota(full("G32"), [[32, 4], [0, 32]], 0, 0)
-    iota(full("N8"), [[8, PC]], 32768, 0)
+    iota(full("N8"), [[PC, 8], [0, 16]], 0, 8)
     for k, v in enumerate((15, 112, 31, 96)):
         ts(c1("pi", 1 + k), c1("pi", 0), v, ALU.bitwise_and)
     cp(R("col", 0, 5), R("pi", 0, 5))
@@ -187,7 +200,6 @@ def build(M):
     ts(full("O"), full("Gn"), gc, ALU.is_equal)
     ts(R("E", 0, 144), R("Nn", 0, 144), gc, ALU.is_equal)
     cp(R("wf", 0, 2), R("wts", 0, 2))
-    cp(R("mf", 0, 16), R("m0s", 0, 16))
     for g in range(8):
         ts(R("OM", 16 * g, 16 * g + 16), R("m0s", 0, 16), c1("O", 16 * g), ALU.mult)
     for k, n in enumerate("AB"):
@@ -212,54 +224,74 @@ def build(M):
     unit = column(c1("ub", 0), 1.0, ALU.mult)
     ts(R("RB", 0, 8), R("O", 0, 128, 16), -H54, ALU.mult, H54, ALU.mult)
     ts(R("RB", 8, 16), R("O", 0, 128, 16), wc, ALU.mult)
-    for s in range(16):
-        lin(R("RS", 16 * s, 16 * s + 16), R("RB", 0, 16), c1("mf", s))
-    for n, v in (("sI", SC), ("nI", -SC), ("hI", 0.5), ("gI", -0.5), ("qI", 0.25), ("uI", unit), ("K8", 256.0), ("mI", -1.0), ("dI", -16384.0)):
-        lin(full(n), ID, v)
+    mm([(R("P0", 0, 128), [(full("OM"), ID)])])
+    lin(full("MT"), R("P0", 0, 128), 1.0)
+    select(full("t1"), full("one"), [[-1, 16], [-16, 8]], 0, 1)
+    mm([(R("P3", 0, 128), [(full("MT"), full("t1"))])])
+    ts(full("RS"), R("P3", 0, 128), -H54, ALU.mult, H54, ALU.mult)
+    lin(R("RS", 128, 256), R("P3", 0, 128), wc)
+    for n, v in (("sI", SC), ("nI", -SC), ("hI", 0.5), ("gI", -0.5), ("qI", 0.25), ("uI", unit), ("K8", 256.0),
+                 ("C1", CR), ("MI", M12), ("MN", -M12), ("RI", 1.5 * 2 ** 23), ("RN", -1.5 * 2 ** 23),
+                 ("dI", -16384.0)):
+        if n not in unused:
+            lin(full(n), ID, v)
     ops[-1]["boost"] = 20000.0
     magic = column(unit, 1.5 * 2.0 ** 28, ALU.mult)
     less = column(rc, 14.5, ALU.is_lt, -0.75, ALU.mult)
     ts(R("ge", 0, 32), R("R32", 0, 32), row, ALU.is_le)
     ts(R("eq", 0, 32), R("R32", 0, 32), row, ALU.is_equal)
     live, r0 = c1("ge", 11), c1("eq", 0)
+    for n, a, b in (("C2", CR, 256.0), ("C3", 2048.0, -0.5)):
+        if n not in unused:
+            lin(full(n), full("one"), column(column(r0, a / b, ALU.mult, c1("eq", 1), ALU.add), b / 4, ALU.mult))
+    if OPT["PM"]:
+        for n in "AB":
+            lin(R(n + "N", 0, 512), R(n + "H", 0, 512), -1.0)
     ts(wide("Of"), wide("Gw"), g32, ALU.is_equal)
-    ms(R("Lq", 0, 6 * 256), 0.0)
+    for k in range(6):
+        ms(R("Lq", 256 * k, 256 * k + 256), 0.0)
     lowr = column(column(r0, -8.0, ALU.mult, live, ALU.add), c1("ge", 22), ALU.subtract)
     for k, c in enumerate([live] * 4 + [lowr, c1("ge", 22)]):
         a, b = WIN[min(k, 4)]
         lin(R3("Lq", 16 * k, 16 * k + 16, a, b + 1), R3("Of", 0, 16, a, b + 1), c)
-    step = column(c1("ge", 16), 2.0, ALU.mult, live, ALU.subtract)
-    for r, v in ((15, 1 - B2), (23, B1 - 8), (31, B2 + MISS - B1 - 8)):
-        step = column(c1("eq", r), float(v), ALU.mult, step, ALU.add)
+    step = live
+    for r in (15, 23, 31):
+        step = column(c1("eq", r), 1023.0, ALU.mult, step, ALU.add)
+    g128 = column(gc, -8.0, ALU.mult)
     lin(wide("IB"), wide("Of"), step)
     ts(c1("penb", 0), r0, 16.5, ALU.mult, -15.0, ALU.add)
     base = column(c1("penb", 0), 0.0, ALU.add)
     first = column(row, -16.0, ALU.add, live, ALU.mult)
-    lin(full("L"), ID, column(live, -63.0, ALU.mult))
-    lin(full("L2"), full("Id"), column(c1("ge", 10), c1("eq", 31), ALU.subtract, 64.0, ALU.mult))
-    tt(full("L"), full("L"), full("L2"), ALU.add)
-    ms(R("PR", 128, 256), 0.0)
-    ms(R("PR", 384, 512), 0.0)
-    ts(full("t1"), full("G32"), g32, ALU.is_equal, column(r0, H54, ALU.mult, H54, ALU.mult), ALU.mult)
-    ts(full("t2"), ID, -64.0 * H54, ALU.mult, H54, ALU.mult)
-    tt(full("PR"), full("t1"), full("t2"), ALU.add)
-    lin(R("PR", 256, 384), ID, 2.0 ** 78)
+    select(full("L"), ID, [[1, 128]], -1, -1, ALU.not_equal, 64.0)
+    select(full("L"), full("L"), [[1, 128]], 0, -1, ALU.not_equal, -63.0)
+    select(full("L"), full("L"), [[0, 4], [1, 32]], -11, 0, ALU.is_ge)
+    select(full("t2"), full("one"), [[-32, 4], [0, 32]], 0, 1)
+    select(full("t2"), full("t2"), [[1, 128]], 0, -1, ALU.not_equal, -64.0)
+    ts(full("PR"), full("t2"), H54, ALU.mult, H54, ALU.mult)
+    lin(R("PR", 128, 256), ID, 2.0 ** 78)
     lin(full("Af"), full("one"), c1("eq", 31))
+    lin(R("rank", 0, 512), R("one", 0, 512), first)
     for ch in range(NC):
-        ms(R("Hs%d" % ch, 0, 256), 0.0)
+        ms(R3("Hs%d" % ch, 0, 8, 0, 16), 0.0)
         ms(R3("Hs%d" % ch, 0, 8, 0, 1), 2.0 ** 78)
-        lin(R("rank", 256 * ch, 256 * ch + 256), wide("one"), first)
-    tt(full("N8"), full("N8"), full("dl"), ALU.mult)
-    lin(full("Ci"), full("N8"), 1.0, -32768.0)
-    for n, w, v in (("Kx", 384, -2.0 ** 22), ("Kn", 128, 2.0 ** 29)):
+    for n, w, v in (("Kx", 128, -2.0 ** 22), ("Kn", 128, 2.0 ** 29)):
         ms(R(n, 0, w), 0.0)
         ms(R(n, 0, w, 16), v)
+    ms(R("Ku", 0, 16 * NB), 0.0)
+    for k, v in ((0, -2.0 ** 22), (16, -2047.5), (17, M12), (18, -M12)):
+        ms(R("Ku", k, 16 * NB, NB), v)
     for t in range(RO):
         select(R("KD", KO[t], KO[t + 1]), R("one", 0, 8 * (16 + t)), [[0, 8], [1, 16 + t]], 0, 0, ALU.not_equal)
-    for k in range(2):
-        lin(R("Cm", PC * k, PC * k + PC), full("dl"), 2.0 ** 21, -2.0 ** 21)
-    mm([(R("P0", 0, 128), [(full("OM"), ID)])])
-    lin(full("MT"), R("P0", 0, 128), 1.0)
+    ms(R("UZ", 0, 16 * NB), 0.0)
+    ms(R3("Cm", 0, 8, 16, NB), -2.0 ** 21)
+    lin(R3("Cm", 0, 8, 0, 16), full("dl"), 2.0 ** 21, -2.0 ** 21)
+    tt(full("Ci"), full("N8"), R3("Cm", 0, 8, 0, 16), ALU.add)
+    iota(R("PA", 0, 96), [[1, 6], [0, 2], [PC, 8]], B1, 8)
+    for t in range(1, RO):
+        iota(R("PA", 96 * t, 96 * t + 16), [[0, 2], [PC, 8]], 5 - t, 8)
+    ts(R("lr", 0, 6), R("one", 0, 6), column(rc, 16.0, ALU.mult, 15.0, ALU.add), ALU.mult)
+    lin(full("BI"), ID, 8192.0)
+    lin(full("NI"), ID, -8192.0)
     ts(full("Cd"), full("Rn"), rc, ALU.is_ge, 2.0 ** 28, ALU.mult)
     lin(full("Cd"), full("Cd"), 1.0, rc)
     ms(R("Cd", 15, 128, 16), 16.0)
@@ -267,21 +299,20 @@ def build(M):
         select(R("Dm", 128 * r, 128 * r + 128), full("dI"), [[1, 128]], -1 - r, -1, ALU.not_equal, 16384.0)
     a = XS * (NC - 1)
     for h in range(2):
-        n, o = 8, a + B1 * h
+        n, o = 8, a + (B1, B2)[h]
         cp(R("Mw", o, o + 8), R("m0s", 8 * h, 8 * h + 8))
         while n < 8 * PC:
-            lin(R("Mw", o + n, o + 2 * n), R("Mw", o, o + n), 1.0)
+            if n < OPT["GD"]:
+                lin(R("Mw", o + n, o + 2 * n), R("Mw", o, o + n), 1.0)
+            else:
+                select(R("Mw", o + n, o + 2 * n), R("Mw", o, o + n), [[0, n]], 0, 0)
             n *= 2
         if OPT["GM"]:
-            select(R("Mw", B1 * h, B1 * h + n), R("Mw", o, o + n), [[0, n]], 0, 0)
+            select(R("Mw", o - a, o - a + n), R("Mw", o, o + n), [[0, n]], 0, 0)
         else:
-            lin(R("Mw", B1 * h, B1 * h + n), R("Mw", o, o + n), 1.0)
+            lin(R("Mw", o - a, o - a + n), R("Mw", o, o + n), 1.0)
     for ch in range(NC):
-        ms(R("Mw", XS * ch + B2 + MISS, XS * (ch + 1), 8), 0.0)
-    x = column(row, -16.0, ALU.add, c1("ge", 24), ALU.subtract)
-    lin(wide("RE"), wide("Of"), column(column(row, -1.0, ALU.mult, 15.0, ALU.add), x, ALU.max))
-    x = column(c1("ge", 16), -float(B2), ALU.mult, float(B2), ALU.add)
-    lin(wide("KE"), wide("Of"), column(c1("ge", 24), 1024.0, ALU.mult, x, ALU.add))
+        ms(R("Mw", XS * ch + B3, XS * ch + B3 + 8 * PC - 7, 8), 0.0)
     select(wide("PN"), wide("one"), [[-128, 2], [32, 8], [1, 16]], 16, -1)
     mm([(R("P1", 0, 128), [(full("L"), ID)])])
     lin(full("LT"), R("P1", 0, 128), 1.0)
@@ -316,8 +347,7 @@ def build(M):
         ts(x, x, 5, ALU.arith_shift_right, 8191, ALU.bitwise_and)
         cp(o, x)
 
-    for ch in range(NC):
-        penalty(ch, 0)
+    ts(R("pen", 0, 512), R("rank", 0, 512), c1("penb", 0), ALU.add, 0.0, ALU.max)
     rot = [0]
 
     def dbank():
@@ -326,13 +356,14 @@ def build(M):
 
     Xg = R("X", 16, 8208)
     for t in range(RO):
+        now[0] = t
         for part, ch in ((0, 1), (0, 0), (1, 1), (1, 0)):
             z = R("zin", 256 * t + PC * ch, 256 * t + PC * ch + PC)
             xb, gb, mb, wb, pb = XS * ch, 21 * PC * ch, 5 * PC * ch, 256 * ch, PC * ch
             Q, Hs, hb = "Q%d" % ch, "Hs%d" % ch, OPT["HB"][ch]
 
             def slot(n, s):
-                a = xb + (B1 * (s // 8) + s % 8 if s < 16 else B2 + s - 16)
+                a = xb + ((B1, B2)[s // 8] + s % 8 if s < 16 else B3 if s == MISS else 20 - s)
                 return R(n, a, a + 8 * PC - 7, 8)
 
             def half(n, k, base=wb):
@@ -363,21 +394,17 @@ def build(M):
                     for k in range(t):
                         tt(R("MZ", zb + k * PC, zb + k * PC + PC), slot("Mw", 16 + k), R(hb, 3 * PC, 4 * PC), ALU.mult)
                 tag[0] = "hash"
-                def sums(k, less=None):
-                    mm([(R(hb, k * PC + 64 * h, k * PC + 64 * h + 64),
-                         [(R("AB"[k] + "H", 128 * (2 * h + b), 128 * (2 * h + b + 1)), R(z[0], z[1] + b, z[2], 2)) for b in range(2)]
-                         + ([(ID, R(less, wb + k * PC + 64 * h, wb + k * PC + 64 * h + 64))] if less else [])) for h in range(2)])
+                def sums(sign):
+                    return [(R(hb, k * PC + 64 * h, k * PC + 64 * h + 64),
+                             [(R("AB"[k] + sign, 128 * (2 * h + b), 128 * (2 * h + b + 1)), R(z[0], z[1] + b, z[2], 2)) for b in range(2)])
+                            for k in range(2) for h in range(2)]
 
-                for k in range(2):
-                    sums(k)
                 if OPT["PM"] >> ch & 1:
-                    act(both("F1"), R(hb, 0, 2 * PC), AF.Identity, bias=2.0 ** 23 - 0.5, scale=2.0 ** -12 + 2.0 ** -34)
-                    act(both("q1"), both("F1"), AF.Relu, bias=-2.0 ** 35, scale=4096.0)
-                    for k in range(2):
-                        sums(k, "q1")
-                        for m in ops[-1]["call"][1][2::3]:
-                            ops[-1]["call"][1][ops[-1]["call"][1].index(m)] = (m[0], full("mI")) + m[2:]
-                        ops[-1]["rd"].append(full("mI"))
+                    uv = R(hb, 0, 2 * PC)
+                    mm([(uv, [(full("C3"), wide("one"))])], last=False)
+                    ops[-1]["wr"] = [R(hb, 0, 512)]
+                    mm(sums("N") + [(uv, [(full("MN"), wide("one")), (full("MI"), wide("one"))])] + sums("H"), first=False, one=True)
+                    ops[-1]["wr"] = [R(hb, 0, 512)]
                     u, w, vp = half("F1", 0), half("F1", 1), R(hb, PC, 2 * PC)
                     lin(u, R(hb, 0, PC), 1.0)
                     lin(w, u, 1184.0, -FOLD)
@@ -385,49 +412,81 @@ def build(M):
                     tt(pt("I2"), vp, w, ALU.add)
                     place_list(pt("off"), pt("I2"))
                 else:
+                    mm(sums("H"))
                     place_list(pt("off"), hashed(R(hb, 0, 2 * PC), R(hb, 0, PC), "F1" if OPT["FM"] >> ch & 1 else "I1", wb, "I2", pb))
-                if t and not ch:
-                    tag[0], n, hb = "dyn", 2 * t * CC, OPT["DB"]
+                if t and (OPT["DY"] or not ch):
+                    tag[0], n, hb = "dyn", (1 if OPT["DY"] else 2) * t * CC, OPT["DB"][ch]
+                    a = n * ch
                     for k, m in enumerate("AB"):
-                        mm([(R(hb, 2 * PC + k * n, 2 * PC + k * n + n), [(view(m, r), R("MZ", r, 2 * t * PC, 16)) for r in range(16)])])
-                    place_list(R("ofd", 0, n), hashed(R(hb, 2 * PC, 2 * PC + 2 * n), R(hb, 2 * PC, 2 * PC + n), "I3", 0, "I4", 0))
+                        mm([(R(hb, 2 * PC + k * n, 2 * PC + k * n + n), [(view(m, r), R("MZ", 16 * a + r, 16 * (a + n), 16)) for r in range(16)])])
+                    place_list(R("ofd", a, a + n), hashed(R(hb, 2 * PC, 2 * PC + 2 * n), R(hb, 2 * PC, 2 * PC + n), "I3", 2 * a, "I4", a))
                 continue
             c0, W = 16 - t, 16 + t
             tag[:] = "gather", ch + 1
-            mm([(R(Q, 0, 16 * W), [(half("pen", 0), R3("PR", 0, 16, c0, 32))]),
-                (R(Q, 4 * W, 8 * W), [(half("pen", 1), R3("PR", 0, 4, c0, 32))]),
-                (R(Q, 12 * W, 16 * W), [(half("pen", 1), R3("PR", 8, 12, c0, 32))])], last=False, one=True)
-            q = 64 // OPT["NG"]
+            mm([(R(Q, (8 * k + 4 * h) * W, (8 * k + 4 * h + 4) * W), [(half("pen", h), R3("PR", 4 * k, 4 * k + 4, c0, 32))])
+                for h in range(2) for k in range(2)], last=False, one=True)
+            ops[-1]["wr"] = [R(Q, 0, 512)]
             for h in range(2):
-                for k in range(OPT["NG"]):
-                    a = xb + B1 * h + 16 * q * k
-                    gat(R("Xh", a, a + 16 * q), Xg, R("off", pb + 64 * h + q * k, pb + 64 * h + q * (k + 1)))
+                for k in range(2):
+                    a = xb + (B1, B2)[h] + 512 * k
+                    gat(R("Xh", a, a + 512), Xg, R("off", pb + 64 * h + 32 * k, pb + 64 * h + 32 * (k + 1)))
             for k in range(t):
                 gat(slot("Xh", 16 + k), Xg, R("ofd", CC * (t * ch + k), CC * (t * ch + k + 1)))
             tag[0] = "compare"
-            blocks = [list(range(a, a + 4)) for a in range(0, 16, 4)]
-            dblk = [list(range(16 + a, 16 + min(a + 4, t))) for a in range(0, t, 4)]
-            blocks = blocks[:OPT["DF"][ch]] + dblk + blocks[OPT["DF"][ch]:]
-            for bl in blocks:
-                bk, n, g0 = dbank(), len(bl) * PC, gb + bl[0] * PC
-                mm([(R(bk, j * PC, j * PC + PC), [(full("sI"), slot("Xh", s)), (full("nI"), z)]) for j, s in enumerate(bl)])
-                dd, gg = R(bk, 0, n), R("G", g0, g0 + n)
-                if bl[0] >= 16:
+
+            def count(ss):
+                mm([(R(Q, t + s if s < 16 else t + 15 - s, 16 * W, W),
+                     [(R("G", gb + s * PC, gb + s * PC + PC), R3("RS", 0, 2, 8 * s, 8 * s + 8) if s < 16 else R("RB", 0, 16))])
+                    for s in ss], first=False, last=False, one=True)
+                ops[-1]["gid"] = (t, ch)
+
+            def differ(gg, parts, free, scalar):
+                dd = R(bk, 0, width(gg))
+                if scalar == 2:
+                    mm([(o, [(full("nI"), zz)]) for o, _, zz in parts], last=False, one=True)
+                    ops[-1]["wr"] = [R(bk, 0, 512)]
+                    mm([(o, [(full("sI"), x)]) for o, x, _ in parts], first=False, one=True)
+                    ops[-1]["wr"] = [R(bk, 0, 512)]
                     act(dd, dd, AF.Abs)
-                    tt(gg, dd, R("TH", mb + (bl[0] - 16) * PC, mb + (bl[0] - 16) * PC + n), ALU.is_gt)
+                    tt(gg, dd, free, ALU.is_gt)
+                    return
+                mm(([(dd, [(full("MI"), free)])] if free else []) + [(o, [(full("nI"), zz)]) for o, _, zz in parts], last=False, one=True)
+                ops[-1]["wr"] = [R(bk, 0, 512)]
+                more = [(full("MN"), free)] if free else []
+                if scalar:
+                    more += [(full(m), R("one", 0, dd[2])) for m in ("C1", "C2")]
+                mm([(o, [(full("sI"), x)]) for o, x, _ in parts] + [(dd, [m]) for m in more], first=False, one=True)
+                ops[-1]["wr"] = [R(bk, 0, 512)]
+                if scalar:
+                    act(gg, dd, AF.Abs, bias=-3.0 * 2 ** 22 - 1, scale=2.0 ** -8)
                 else:
                     ts(gg, dd, CR, ALU.add, CR, ALU.not_equal)
-                mm([(R(Q, t + s if s < 16 else t + 15 - s, 16 * W, W),
-                     [(R("G", g0 + j * PC, g0 + j * PC + PC), R("RS", 16 * s, 16 * s + 16) if s < 16 else R("RB", 0, 16))])
-                    for j, s in enumerate(bl)], first=False, last=bl is blocks[-1], one=True)
-                ops[-1]["gid"] = (t, ch)
+
+            blocks = [(h, k) for h in range(2) for k in range(2)]
+            dblk = [list(range(16 + a, 16 + min(a + 4, t))) for a in range(0, t, 4)]
+            for bl in blocks[:OPT["DF"][ch]] + dblk + blocks[OPT["DF"][ch]:]:
+                bk = dbank()
+                if bl[0] >= 16:
+                    n, g0, a = len(bl) * PC, gb + bl[0] * PC, mb + (bl[0] - 16) * PC
+                    differ(R("G", g0, g0 + n), [(R(bk, j * PC, j * PC + PC), slot("Xh", s), z) for j, s in enumerate(bl)],
+                           R("TH", a, a + n), OPT["CA"][ch] >> 4 & 3)
+                    count(bl)
+                else:
+                    h, k = bl
+                    a = xb + (B1, B2)[h] + 512 * k
+                    differ(R3("G", 21 * ch + 8 * h, 21 * ch + 8 * h + 8, 64 * k, 64 * k + 64),
+                           [(R(bk, 64 * s, 64 * s + 64), R("Xh", a + s, a + 512, 8), R("zin", z[1] + 64 * k, z[1] + 64 * k + 64))
+                            for s in range(8)], None, OPT["CA"][ch] >> (2 * h + k) & 1)
+                    if k:
+                        for a in range(0, 8, OPT["NK"]):
+                            count(range(8 * h + a, 8 * h + a + OPT["NK"]))
             tag[0] = "miss"
-            mm([(mr(0, 0), [(full("qI"), full("one")), (full("hI"), z), (full("gI"), slot("Xh", 15 + t if t else 0))])])
+            mm([(mr(0, 0), [(full("qI"), full("one")), (full("hI"), z), (full("gI"), slot("Xh", 15 + t if t else 0))]
+                 + ([(full("RI"), full("one")), (full("RN"), full("one"))] if OPT["YA"] >> ch & 1 else []))])
             if OPT["YA"] >> ch & 1:
-                act(pt("y1"), mr(0, 0), AF.Identity, bias=1.5 * 2.0 ** 23)
-                act(slot("Xh", 16 + MISS), pt("y1"), AF.Identity, bias=-1.5 * 2.0 ** 23)
+                lin(slot("Xh", MISS), mr(0, 0), 1.0)
             else:
-                ts(slot("Xh", 16 + MISS), mr(0, 0), 1.5 * 2.0 ** 23, ALU.add, 1.5 * 2.0 ** 23, ALU.subtract)
+                ts(slot("Xh", MISS), mr(0, 0), 1.5 * 2.0 ** 23, ALU.add, 1.5 * 2.0 ** 23, ALU.subtract)
             tag[0] = "match"
             rm = R("rm", 168 * ch, 168 * ch + 8 * W)
             scan(rm, R("KD", KO[t], KO[t + 1]), R(Q, 0, 8 * W), 0.0, ALU.mult, ALU.max)
@@ -444,19 +503,25 @@ def build(M):
                 mm([(mr(1, PC), [(ID, full("Ci"))] + [(half("IB", h, 0), half("b", h)) for h in range(2)])])
             scan(pt("sc"), R("Kx", 0, PC), mr(1, PC), 0.0, ALU.add, ALU.max)
             ix = R("idx", CC * ch, CC * ch + CC)
-            ts(ix, R("sc", pb + 15, pb + PC, 16), float(B2 + 4), ALU.add)
+            ts(ix, R("sc", pb + 15, pb + PC, 16), g128, ALU.add)
             gat(pt("ms"), R("Mw", xb, xb + XS), ix, less)
             tag[0] = "header"
             win = R("Xh", xb, xb + XS)
             new = R("yzb", 256 * t + pb, 256 * t + pb + PC)
-            add("v", ("gtt", pt("ds"), win, ix, z, ALU.subtract), [win, ix, z], [pt("ds")], 60 + GF * CY * PC)
-            act(new, pt("ds"), AF.Abs)
+            if OPT["HA"] >> ch & 1:
+                gat(pt("ds"), win, ix)
+                mm([(mr(5, 3 * PC), [(full("gI"), z), (full("hI"), pt("ds"))])])
+                act(new, mr(5, 3 * PC), AF.Abs, scale=2.0)
+            else:
+                add("v", ("gtt", pt("ds"), win, ix, z, ALU.subtract), [win, ix, z], [pt("ds")], 60 + GF * CY * PC)
+                act(new, pt("ds"), AF.Abs)
             if t < RO - 1:
                 zn = R("zin", 256 * (t + 1) + pb, 256 * (t + 1) + pb + PC)
                 add("g", ("send", zn, new, "r%d_%d" % (t + 1, ch)), [new], [zn], 300.0, lat=RLAT + (0 if t else M["R0"]))
             tag[0] = "mask"
             terms = []
-            for q, (a, b) in enumerate(WIN):
+            for q in OPT["WO"]:
+                a, b = WIN[q]
                 cb = 512 * q + wb
                 lo = 2.0 ** (34 - 5 * (b + 1)) if b < 15 else 0.0
                 ts(both("Cq", cb), both("H"), 2.0 ** (34 - 5 * (a - 1)), ALU.min, lo, ALU.max)
@@ -475,48 +540,61 @@ def build(M):
             if t == RO - 1:
                 mm([(mr(2, 0), [(half("PN", h, 0), half("rank", h)) for h in range(2)] + [(half("PL", h, 0), half("b", h)) for h in range(2)])])
                 lin(pt("rk"), mr(2, 0), 1.0)
-            sp = mr(2, 2 * PC, 2 * PC)
-            if OPT["SCV"] >> ch & 1:
-                mm([(sp, [(full("L"), both("b"))])])
-                tt(both("rank"), sp, both("rank"), ALU.add)
             else:
+                sp = mr(2, 2 * PC, 2 * PC)
                 mm([(sp, [(full("L"), both("b")), (ID, both("rank"))])])
                 lin(both("rank"), sp, 1.0)
-            if t < RO - 1:
-                lin(R("TH", mb + t * PC, mb + t * PC + PC), U, -236.0, 300.0)
+                lin(R("TH", mb + t * PC, mb + t * PC + PC), U, *((-236.0, 300.0) if OPT["CA"][ch] & 32 else (-1.0, 1.0)))
                 tag[0] = "name"
-                zs = mr(3, 0)
+                zs, uz, n = mr(3, 0), R3("UZ", 8 * ch, 8 * ch + 8, 0, 16), 8 * NB
                 if OPT["UZA"] >> ch & 1:
                     mm([(zs, [(ID, z), (full("K8"), U)])])
-                    act(pt("UZ"), zs, AF.Relu, bias=-256.0)
+                    act(uz, zs, AF.Relu, bias=-256.0)
                 else:
                     mm([(zs, [(ID, z)])])
-                    tt(pt("UZ"), U, zs, ALU.mult)
-                jb = 2 * CC * ch
+                    tt(uz, U, zs, ALU.mult)
+                jb, uz = 2 * CC * ch, R("UZ", n * ch, n * ch + n)
                 if OPT["PRE"] & 1:
-                    mm([(mr(4, 0, 2 * PC), [(ID, wide("Cm"))])], last=False)
+                    mm([(mr(4, k * n, n), [(ID, R("Cm", 0, n))]) for k in range(2)], last=False, one=True)
                     ops[-1]["wr"] = [mr(4, 0, 512)]
-                    mm([(mr(4, k * PC), [(full(m), pt("UZ"))]) for k, m in enumerate(("Oa", "Ob"))], first=False, one=True)
+                    mm([(mr(4, k * n, n), [(full(m), uz)]) for k, m in enumerate(("Oa", "Ob"))], first=False, one=True)
                     ops[-1]["wr"] = [mr(4, 0, 512)]
                 else:
-                    mm([(mr(4, k * PC), [(ID, full("Cm")), (full(m), pt("UZ"))]) for k, m in enumerate(("Oa", "Ob"))])
-                scan(both("su"), wide("Kx"), mr(4, 0, 2 * PC), 0.0, ALU.add, ALU.max)
-                x = hashed(R("su", wb + 15, wb + 2 * PC, 16), R(Q, 0, CC), "J1", jb, "J2", CC * ch)
+                    mm([(mr(4, k * n, n), [(ID, R("Cm", 0, n)), (full(m), uz)]) for k, m in enumerate(("Oa", "Ob"))])
+                sb, j1 = 2 * n * ch, 3 * CC * ch
+                scan(R("su", sb, sb + 2 * n), R("Ku", 0, 2 * n), mr(4, 0, 2 * n), 0.0, ALU.add, ALU.max)
+                tt(R("J1", j1, j1 + 2 * CC), R("su", sb + 15, sb + 2 * n, NB), R("su", sb + 18, sb + 2 * n, NB), ALU.subtract)
+                u, v, w = [R("J1", j1 + k * CC, j1 + k * CC + CC) for k in range(3)]
+                x = R("J2", CC * ch, CC * ch + CC)
+                ts(w, u, 1184.0, ALU.mult, -FOLD, ALU.add)
+                tt(v, u, v, ALU.mult)
+                tt(x, v, w, ALU.add)
                 ts(R("J3", jb, jb + CC), x, 5, ALU.arith_shift_right, 8128, ALU.bitwise_and)
                 ts(R("J3", jb + CC, jb + 2 * CC), x, 5, ALU.arith_shift_right, 63, ALU.bitwise_and)
                 cp(R("hl", jb, jb + 2 * CC), R("J3", jb, jb + 2 * CC))
-                mm([(xx, [(ID, full("Cd"))] + [
+                terms = [(ID, full("Cd"))] + [
                     (R("Dm", 128 * r, 128 * r + 128) if r < 15 else ID, R("hl", jb + CC * k, jb + CC * k + CC),
-                     R(Q, 2 * PC + r, 3 * PC, 16)) for k in range(2) for r in range(16)])])
+                     R(Q, 2 * PC + r, 3 * PC, 16)) for k in range(2) for r in range(16)]
+                if OPT["PRE"] & 4:
+                    mm([(xx, terms[:1])], last=False)
+                    mm([(xx, terms[1:])], first=False)
+                else:
+                    mm([(xx, terms)])
                 act(pt("aD"), xx, AF.Abs)
                 scan(pt("sD"), full("Kn"), pt("aD"), 0.0, ALU.add, ALU.min)
                 cp(R("xo", jb, jb + 2 * CC, 2), R("sD", pb + 15, pb + PC, 16))
+        tag[:] = "first", 3
+        old, low, pe = R("PA", 96 * t + 16, 96 * t + 96), R("PA", 96 * t, 96 * t + 80), R("P" + OPT["BK"][3], 384, 464)
+        gat(R("AJ", 0, 80), wide("sc"), R("lr", 0, 5))
+        mm([(pe, [(full("BI"), old), (full("NI"), R("AJ", 0, 80))])], f=4)
+        tt(pe, pe, low, ALU.max)
+        tt(R("PA", 96 * t + 112, 96 * t + 192), pe, old, ALU.min)
         tag[:] = "rank", 3
         if t == RO - 1:
             r = R("yzb", 256 * t, 256 * t + 256)
             dma(("yz", 256 * t, 256 * t + 256), r, [r], [], 65536)
             break
-        pa = R("P" + OPT["BK"][2], PC, PC + 1)
+        pa = R("P" + OPT["BK"][2], 511, 512)
         mm([(pa, [(full("Af"), c1("mcnt", ch)) for ch in range(NC)])], f=4)
         cp(c1("ai", 0), pa)
         ts(c1("ai", 0), c1("ai", 0), 1, ALU.bitwise_and)
@@ -531,20 +609,12 @@ def build(M):
             r = R("yzb", 0, 256 * t + 256)
             dma(("yz", 0, 256 * t + 256), r, [r, Xg], [], 65536 * (t + 1))
 
-    for ch in range(NC - 1, -1, -1):
-        wb, pb, xb = 256 * ch, PC * ch, XS * ch
-        tag[:] = "end", 10 + ch
-        ew = lambda k, h: R("Ew", (10 * ch + 2 * k - 2 + h) * PC, (10 * ch + 2 * k - 1 + h) * PC)
-        for ks in ((1, 2, 3), (4, 5)):
-            bk, n, a = dbank(), len(ks) * PC, (5 * ch + ks[0] - 1)
-            for k in ks:
-                ts(R("Ew", ew(k, 0)[1], ew(k, 1)[2]), R("rank", wb, wb + 256), float(k), ALU.is_equal)
-            mm([(R(bk, j * PC, j * PC + PC), [(ID, full("Ci"))]
-                 + [(R(m, PC * h, PC * h + PC), ew(k, h)) for m in ("RE", "KE") for h in range(2)]) for j, k in enumerate(ks)])
-            scan(R("se", a * PC, a * PC + n), R("Kx", 0, n), R(bk, 0, n), 0.0, ALU.add, ALU.max)
-            cp(R("to", a * CC, (a + len(ks)) * CC), R("se", a * PC + 15, a * PC + n, 16))
-            for k in ks:
-                gat(R("ymb", 256 * k + pb, 256 * k + pb + PC), R("Mw", xb, xb + XS), R("to", CC * (5 * ch + k - 1), CC * (5 * ch + k)))
+    tag[:] = "end", 10
+    ts(R("to", 0, 80), R("PA", 96 * RO + 16, 96 * RO + 96), g128, ALU.add)
+    for k in range(1, 6):
+        for ch in range(NC):
+            a = 16 * (k - 1) + CC * ch
+            gat(R("ymb", 256 * k + PC * ch, 256 * k + PC * ch + PC), R("Mw", XS * ch, XS * ch + XS), R("to", a, a + CC))
     tag[1] = 12
     for k in range(6, 16, 2):
         for j in range(k, k + 2):
@@ -563,15 +633,14 @@ def depend(ops):
     hist = {}
     for k, o in enumerate(ops):
         deps = set()
-        for r, w in [(r, False) for r in o["rd"]] + [(r, True) for r in o["wr"]]:
-            for j, a, b, ww, sp in hist.get(r[0], []):
-                if (w or ww) and a < r[2] and r[1] < b and j != k and not (sp == r[3] > 1 and (a - r[1]) % sp):
-                    deps.add(j)
-        for r, w in [(r, False) for r in o["rd"]] + [(r, True) for r in o["wr"]]:
-            h = hist.setdefault(r[0], [])
-            if w and r[3] == 1 and len(r) == 4:
-                h[:] = [x for x in h if not (r[1] <= x[1] and x[2] <= r[2])]
-            h.append((k, r[1], r[2], w, r[3]))
+        use = [(r[0], sum(1 << c for c in columns(r)), w) for rs, w in ((o["rd"], False), (o["wr"], True)) for r in rs]
+        for name, m, w in use:
+            deps.update(j for j, mm, ww in hist.get(name, []) if (w or ww) and m & mm)
+        for name, m, w in use:
+            h = hist.setdefault(name, [])
+            if w:
+                h[:] = [x for x in h if x[1] & ~m]
+            h.append((k, m, w))
         o["deps"] = deps
         o["banks"] = set(r[0] for r in o["rd"] + o["wr"] if r[0] not in _S)
     succ = [[] for _ in ops]
@@ -776,6 +845,254 @@ def plan(iters=None, seed=1):
     return base, order, best[0]
 
 
+def place(P, p, bias, back=False):
+    succ, cost, lat, banks, at0, tail, free0, bank0 = P
+    n = len(cost)
+    at, by, held, st, eo = list(at0), [-1] * n, [-1] * n, [0.0] * n, [""] * n
+    qs = {e: ([-1e9], [free0[e]], [-1]) for e in "vapgs"}
+    bk = {b: ([-1e9], [x], [e], [-1]) for b, (x, e) in bank0.items()}
+    end, last = 0.0, 0
+    for _, k in sorted(zip(p, range(n)), reverse=True):
+        best, bs = 1e18, banks[k]
+        l0, l1 = (lat[k], 0.0) if back else (0.0, lat[k])
+        for e, c in cost[k]:
+            t, h = at[k], -1
+            ss, ee, who = qs[e]
+            m = i = len(ss)
+            while i and ee[i - 1] > t:
+                i -= 1
+            moved = True
+            while moved:
+                while i < m and ss[i] < t + c:
+                    if ee[i] > t:
+                        t, h = ee[i], who[i]
+                    i += 1
+                moved = False
+                for b in bs:
+                    s0, e0, en, w0 = bk[b]
+                    j, x, y = len(s0) - 1, t + c + l1, t - 2500.0
+                    while s0[j] >= x:
+                        j -= 1
+                    while j >= 0:
+                        if e0[j] > t - l0 + 1e-6 and en[j] != e:
+                            t, moved, h = e0[j] + l0, True, w0[j]
+                            break
+                        if s0[j] < y:
+                            break
+                        j -= 1
+                while moved and i < m and ee[i] <= t:
+                    i += 1
+            v = t + c + bias[k] if e == "v" else t + c
+            if v < best:
+                best, bt, bc, be, bi, bh = v, t, c, e, i, h
+        held[k], st[k], eo[k] = bh, bt, be
+        x = bt + bc
+        ss, ee, who = qs[be]
+        ss.insert(bi, bt)
+        ee.insert(bi, x)
+        who.insert(bi, k)
+        y = x + l1
+        for b in bs:
+            s0, e0, en, w0 = bk[b]
+            j = len(s0)
+            while s0[j - 1] > bt - l0:
+                j -= 1
+            s0.insert(j, bt - l0)
+            e0.insert(j, y)
+            en.insert(j, be)
+            w0.insert(j, k)
+        if y + tail[k] > end:
+            end, last = y + tail[k], k
+        for j, d in succ[k]:
+            if x + d > at[j]:
+                at[j], by[j] = x + d, k
+    pairs = []
+    while last >= 0:
+        if held[last] >= 0:
+            pairs.append((last, held[last]))
+        last = held[last] if held[last] >= 0 else by[last]
+    return st, eo, end, pairs
+
+
+def plan(iters=None, seed=1):
+    base = build(MODELS[0])
+    depend(base)
+    N, iters = len(base), OPT["ITER"] if iters is None else iters
+    above, pre, succ = [0] * N, [], [[] for _ in base]
+    for k, o in enumerate(base):
+        for j in o["deps"]:
+            above[k] |= above[j]
+        pre.append([(j, inline(base[j], o)) for j in sorted(o["deps"]) if not above[k] >> j & 1])
+        for j, pp in pre[k]:
+            succ[j].append((k, pp))
+        for j in o["deps"]:
+            above[k] |= 1 << j
+    models = [prices(base)] + [prices(build(m)) for m in OPT["JUDGE"]]
+    weight = [1.0] + [m["W"] for m in OPT["JUDGE"]]
+    rest = []
+    for cs in models:
+        r = [0.0] * N
+        for k in range(N - 1, -1, -1):
+            c, la = min(cs[k][0].values()), cs[k][1]
+            r[k] = c + max([la] + [r[j] + (0.0 if pp else la) for j, pp in succ[k]])
+        rest.append(r)
+    state = [seed]
+
+    def rnd():
+        state[0] = (state[0] * 6364136223846793005 + 1442695040888963407) % 2 ** 64
+        return ((state[0] >> 33) + 1) / 2.0 ** 31
+
+    def one(xs):
+        return xs[min(int(rnd() * len(xs)), len(xs) - 1)]
+
+    banks = [sorted(o["banks"]) for o in base]
+    order, engine, fixed = [], [None] * N, [False] * N
+    free = [dict.fromkeys("vapgs", 0.0) for _ in models]
+    ends, dones = [[0.0] * N for _ in models], [[0.0] * N for _ in models]
+    user = {b: -1 for bs in banks for b in bs}
+    prio = [rest[0][k] + o.get("boost", 0.0) + OPT["START"].get(o["grp"], 0.0) for k, o in enumerate(base)]
+    lean = [OPT["BIAS"]] * N
+    for stage in range(RO - 1):
+        act = [k for k in range(N) if not fixed[k] and base[k]["step"] <= stage + 1]
+        loc = {k: i for i, k in enumerate(act)}
+        n = len(act)
+        lc = [[cs[k] for k in act] for cs in models]
+        lat = [la for _, la in lc[0]]
+        ls = [[(loc[j], 0.0 if pp else lat[i]) for j, pp in succ[k] if j in loc] for i, k in enumerate(act)]
+        lp = [[(loc[j], pp) for j, pp in pre[k] if j in loc] for k in act]
+        at0 = [[max([0.0] + [en[j] if pp else do[j] for j, pp in pre[k] if fixed[j]]) for k in act] for en, do in zip(ends, dones)]
+        tail = [[max([0.0] + [r[j] - (cs[k][1] if pp else 0.0) for j, pp in succ[k] if j not in loc]) for k in act]
+                for r, cs in zip(rest, models)]
+        lb = [banks[k] for k in act]
+        P = (ls, [list(c.items()) for c, _ in lc[0]], lat, lb, at0[0], tail[0], free[0],
+             {b: (dones[0][j], engine[j]) if j >= 0 else (0.0, "") for b, j in user.items()})
+        rp = [[(j, 0.0 if pp else lat[j]) for j, pp in lp[k]] for k in range(n)]
+        late = [lat[k] + tail[0][k] for k in range(n)], [0.0] * n, dict.fromkeys("vapgs", 0.0), dict.fromkeys(user, (-1e8, ""))
+
+        def judged(st, eo, val):
+            seq, last, wait, out = [k for _, k in sorted(zip(st, range(n)))], {}, [None] * n, [None] * n
+            for k in seq if len(models) > 1 else []:
+                w = lp[k]
+                for b in lb[k]:
+                    if b not in last:
+                        if user[b] >= 0 and engine[user[b]] != eo[k]:
+                            out[k] = (out[k] or []) + [user[b]]
+                    elif eo[last[b]] != eo[k]:
+                        w = w + [(last[b], False)]
+                    last[b] = k
+                wait[k] = w
+            for m in range(1, len(models)):
+                fr, end, done, cs, a0, tl, top = dict(free[m]), [0.0] * n, [0.0] * n, lc[m], at0[m], tail[m], 0.0
+                for k in seq:
+                    e = eo[k]
+                    t = fr[e]
+                    if a0[k] > t:
+                        t = a0[k]
+                    for j, pp in wait[k]:
+                        x = end[j] if pp else done[j]
+                        if x > t:
+                            t = x
+                    if out[k]:
+                        t = max([t] + [dones[m][j] for j in out[k]])
+                    c, la = cs[k]
+                    end[k] = fr[e] = t = t + c[e]
+                    done[k] = t = t + la
+                    if t + tl[k] > top:
+                        top = t + tl[k]
+                val += top * weight[m]
+            return val / len(models)
+
+        kin, gin = {}, {}
+        for i, k in enumerate(act):
+            kin.setdefault(base[k]["key"], []).append(i)
+            gin.setdefault(base[k]["grp"] + (base[k]["step"],), []).append(i)
+        grps, keys = sorted(gin), sorted(k for k in kin if k[0] or not stage)
+        kof = [kin[base[k]["key"]] for k in act]
+        span = iters // (RO - 1)
+        cp, cb, cur, own, pairs, ceo, best = [prio[k] for k in act], [lean[k] for k in act], None, 0.0, [], None, None
+        for it in range(span + 1):
+            p, b, d, moved = list(cp), cb, 0.0, []
+            if not it:
+                d, moved = 1e-3, list(range(n))
+            elif rnd() < OPT["PR"] or not pairs:
+                d, x = (rnd() * 2 - 1) * 1500, rnd()
+                moved = gin[one(grps)] if x < 0.3 else kin[one(keys)] if x < 0.7 else [one(kin[one(keys)])]
+            else:
+                k, h = one(pairs)
+                wide, y = rnd() < OPT["PK"], rnd()
+                alts = [j for j in (k, h) if len(P[1][j]) > 1]
+                if alts and y < 0.4:
+                    j, b = one(alts), list(cb)
+                    for i in kof[j] if wide else [j]:
+                        b[i] = 5000.0 if ceo[j] == "v" else -5000.0
+                else:
+                    d = max(p[h] - p[k], 0.0) + 1.0 + 200 * rnd()
+                    j, d = (k, d) if y < 0.7 else (h, -d)
+                    moved = kof[j] if wide else [j]
+            for i in moved:
+                p[i] += d
+            todo = list(moved)
+            while todo:
+                k = todo.pop()
+                x = p[k]
+                for j, _ in (lp if d > 0 else ls)[k]:
+                    if (p[j] <= x) if d > 0 else (p[j] >= x):
+                        p[j] = x + (1e-3 if d > 0 else -1e-3)
+                        todo.append(j)
+            st, eo, val, pp = place(P, p, b)
+            if it % OPT["FB"] == 0:
+                fix = [[x for x in P[1][k] if x[0] == eo[k]] for k in range(n)]
+                rs = place((rp, fix, lat, lb) + late, [st[k] + fix[k][0][1] + 1e-6 * k for k in range(n)], b, True)[0]
+                q = [rs[k] + fix[k][0][1] - 1e-6 * k for k in range(n)]
+                again = place(P, q, b)
+                if again[2] <= val + 100.0:
+                    (st, eo, val, pp), p = again, q
+            if cur is not None and val > own + OPT["FAR"]:
+                continue
+            mine, val = val, judged(st, eo, val)
+            if cur is None or val <= cur - OPT["TEMP"] * max(0.02, 1 - it / span) * math.log(rnd()):
+                cp, cb, cur, own, pairs, ceo = p, b, val, mine, pp, eo
+            if best is None or val < best[0]:
+                best = (val, st, eo, p, b)
+        value, st, eo, p, b = best
+        cut = max(st[loc[k]] for k in act if base[k]["call"][0] == "sca" and base[k]["step"] == stage) if stage < RO - 2 else 1e18
+        learnt = {}
+        for i, k in enumerate(act):
+            prio[k], lean[k] = p[i], b[i]
+            if base[k]["step"] == stage + 1:
+                learnt[base[k]["key"]] = (p[i] - rest[0][k], b[i])
+        for k, o in enumerate(base):
+            if o["step"] == stage + 2 and o["key"] in learnt:
+                prio[k], lean[k] = rest[0][k] + learnt[o["key"]][0], learnt[o["key"]][1]
+        for i in sorted(range(n), key=lambda i: (st[i], i)):
+            if st[i] > cut:
+                break
+            k, e = act[i], eo[i]
+            fixed[k], engine[k] = True, e
+            order.append(k)
+            for m, cs in enumerate(models):
+                t = max([free[m][e]] + [ends[m][j] if pp else dones[m][j] for j, pp in pre[k]]
+                        + [dones[m][user[x]] for x in banks[k] if user[x] >= 0 and engine[user[x]] != e])
+                ends[m][k] = free[m][e] = t + cs[k][0][e]
+                dones[m][k] = ends[m][k] + cs[k][1]
+            for x in banks[k]:
+                user[x] = k
+    last = {base[k]["gid"]: k for k in order if "gid" in base[k]}
+    for k in order:
+        o = base[k]
+        if "gid" in o:
+            c = o["call"][1]
+            o["call"] = ("mm", c[:-1] + [c[-1][:4] + (last[o["gid"]] == k,)])
+        o["eng"] = engine[k]
+        if "alt" in o:
+            o["call"], o["cost"] = o["alt"][o["eng"]]
+        for b in o["banks"]:
+            if b in last and base[last[b]]["eng"] != o["eng"]:
+                o["deps"].add(last[b])
+            last[b] = k
+    return base, order, [round(max(d)) for d in dones]
+
+
 _PLAN = []
 
 
@@ -798,7 +1115,8 @@ def rank_program(g, core, T, topo):
         if not isinstance(r, tuple):
             return r
         if len(r) == 5:
-            return T[r[0]][:, r[4][0]:r[4][1], r[4][2]:r[4][3]]
+            g0, g1, a, b, step = r[4]
+            return T[r[0]][:, g0:g1, a:b] if step == 1 else T[r[0]][:, g0:g1, a:b:step]
         if r[0] in W3:
             return T[r[0]][:, r[1] // W3[r[0]]:r[2] // W3[r[0]], :]
         return T[r[0]][:, r[1]:r[2]] if len(r) == 3 or r[3] == 1 else T[r[0]][:, r[1]:r[2]:r[3]]

@@ -15,19 +15,19 @@ MAT = "sI nI hI gI qI uI dI K8 C1 C2 C3 MI MN RI RN".split()
 _S = dict(
     X=(8208, BF), Xh=(NC * XS, BF), Mw=(NC * XS, BF),
     zin=(6 * 256, BF), yzb=(6 * 256, BF), ymb=(4096, BF), m0s=(16, BF), wts=(16, BF),
-    MZ=(NC * 5 * PC, BF), TH=(NC * 5 * PC, BF), I1=(512, I32), I2=(256, I32), off=(256, U16), F1=(512, F32),
+    MZ=(NC * 5 * PC, BF), TH=(NC * 5 * PC, BF), NM=(NC * 5 * PC, BF), I1=(512, I32), I2=(256, I32), off=(256, U16), F1=(512, F32),
     I3=(160, I32), I4=(80, I32), ofd=(80, U16), H=(512, BF), b=(512, BF), Cq=(5 * 512, BF), rank=(512, BF), pen=(512, BF),
-    mcnt=(8, F32), sc=(256, F32), idx=(16, U16), ds=(256, BF), ms=(256, BF), e1=(256, F32), y1=(256, F32),
-    J1=(48, F32), J2=(16, I32), J3=(32, I32), hl=(32, BF), aD=(256, F32), sD=(256, F32), xo=(32, U16), ai=(8, I32),
+    mcnt=(8, F32), sc=(256, F32), idx=(16, U16), ds=(256, BF), ms=(256, BF), e1=(256, F32), y1=(256, F32), Ct=(512, F32),
+    J1=(48, F32), J2=(16, I32), J3=(32, I32), hl=(32, BF), aD=(288, F32), sD=(288, BF), Wd=(192, BF), xo=(32, U16), ai=(8, I32),
     su=(32 * NB, F32), Ku=(16 * NB, F32), rk=(256, BF), Es=(20 * PC, BF), to=(80, U16),
     PA=(7 * 96, F32), AJ=(80, F32), lr=(8, U16), BI=(128, F32), NI=(128, F32),
     pi=(8, I32), col=(40, F32), penb=(8, F32), Gn=(128, F32), Gw=(256, F32), G32=(128, F32), Rn=(128, F32), R32=(32, F32),
-    ge=(32, F32), eq=(32, F32), Nn=(144, F32), N8=(128, F32), Id=(136, BF), O=(128, BF), E=(144, BF), A=(144, BF), B=(144, BF),
-    ub=(8, BF), PL=(256, BF), LT=(128, BF), mf=(16, F32), wf=(8, F32), pw=(16, F32), pc=(32, F32), dl=(128, F32), RB=(16, BF),
+    ge=(32, F32), eq=(32, F32), Nn=(288, F32), N8=(128, F32), Id=(136, BF), O=(128, BF), E=(144, BF), A=(144, BF), B=(144, BF),
+    ub=(16, BF), PL=(256, BF), LT=(128, BF), mf=(16, F32), wf=(8, F32), pw=(16, F32), pc=(32, F32), dl=(128, F32), RB=(16, BF),
     IB=(256, BF), PN=(256, BF), L=(128, BF), L2=(128, BF),
     one=(512, BF), AN=(512, BF), BN=(512, BF), mat=(128 * len(MAT), BF),
-    KD=(KO[RO], BF), rm=(2 * 168, BF), t1=(128, BF), t2=(128, BF), Dm=(15 * 128, BF), Ci=(PC, BF), Kx=(PC, BF),
-    Kn=(128, BF), Cd=(128, BF), Af=(128, F32), Oa=(128, BF), Ob=(128, BF), MT=(128, BF),
+    KD=(KO[RO], BF), rm=(2 * 168, BF), t1=(128, BF), t2=(128, BF), Dm=(8 * 128, BF), Ci=(PC, BF), Kx=(PC, BF),
+    Kn=(144, BF), Cd=(144, BF), Af=(128, F32), Oa=(128, BF), Ob=(128, BF), MT=(128, BF),
 )
 SCRATCH = {k: ("sbuf", [128, n], d) for k, (n, d) in _S.items()}
 W3 = dict(Hs0=32, Hs1=32, PR=32, OM=16, AH=16, BH=16, Of=16, Lq=16, G=PC, UZ=NB, Cm=NB, RS=128)
@@ -41,17 +41,17 @@ NDMA = 16
 SEMAPHORES = (["cv", "ca", "cp", "cg", "sent"] + ["d%d" % k for k in range(NDMA)]
               + ["r%d_%d" % (t, c) for t in range(1, RO) for c in range(NC)])
 
-_M = dict(CY=0.87, PCY=0.46, LAT=180.0, RLAT=3000.0, OV=50.0, AO=30.0, GF=1.56, SF=3.8, BW=340.0, R0=2000.0, MINC=0.0, PS=0.0,
-          DLAT=1400.0)
+_M = dict(CY=0.87, PCY=0.46, LAT=180.0, RLAT=3000.0, OV=50.0, AO=30.0, GF=1.56, SF=3.8, BW=400.0, R0=2000.0, MINC=0.0, PS=0.0,
+          DLAT=1100.0)
 MODELS = [_M]
 OPT = dict(JUDGE=[dict(_M, MINC=64.0, OV=25.0, RLAT=4000.0, LAT=230.0, BW=240.0, DLAT=2200.0, W=0.95),
                   dict(_M, PS=60.0, AO=80.0, CY=0.95, PCY=0.52, GF=1.8, LAT=130.0, W=0.87),
                   dict(_M, MINC=64.0, OV=45.0, CY=0.83, PCY=0.5, LAT=110.0, RLAT=2400.0, BW=400.0, DLAT=1000.0, W=1.0)],
-           HB=("P4", "P3"), HA=0, BK=("401224", "353335", "1", "1"), KG=((6, 8), (8, 12), (12, 16), (1, 4), (4, 6), (0, 1)),
-           MZB=((("P0", 0, 3), ("P1", 0, 2)), (("P5", 0, 4), ("P5", 0, 1))), PM=3, PRE=0, ND=3, DB=("P5", "P5"), DY=0, MZA=3, UZA=0, YA=0, FM=3, DF=(4, 4),
+           HB=("P4", "P3"), HA=(0, 0, 0, 0, 0, 0), BK=("401024", "355435", "1", "1"), KG=((6, 8), (8, 12), (12, 16), (1, 4), (4, 6), (0, 1)),
+           MZB=((("P0", 0, 3), ("P1", 0, 2)), (("P5", 0, 4), ("P5", 0, 1))), PM=3, PRE=7, ND=3, DB=("P5", "P5"), DY=0, MZA=3, UZA=0, YA=(0, 0, 0, 0, 0, 0), CT=(6, 6), FM=3, DF=(4, 4),
            CA=(0, 0), NK=8, WO=(4, 0, 1, 2, 3),
-           START={(1, "header"): 3000.0, (1, "dyn"): 1000.0}, MSP=12, CUT=(4, 8, 10, 12), GM=1, GD=256,
-           BIAS=300.0, TEMP=40.0, PK=0.4, PR=0.4, FB=10, FAR=600.0, ITER=50000)
+           START={(1, "header"): 3000.0, (1, "dyn"): 1000.0}, MSP=12, CUT=(4, 8, 10, 12), GM=2, GD=128, QA=(0, 0), EA=0, ZS=384, SP=(6, 4, 4, 2, 2, 2), CS=0, P0=1,
+           BIAS=300.0, TEMP=40.0, PK=0.4, PR=0.4, FB=10, LOOP=3, FAR=600.0, ITER=50000)
 
 
 def R(n, a, b, s=1):
@@ -62,10 +62,14 @@ def R3(n, g0, g1, a, b, s=1):
     return (n, W3[n] * g0 + a, W3[n] * (g1 - 1) + b, 1, (g0, g1, a, b, s))
 
 
+def RH(n, a, b, h):
+    return (n, a, b, 1, None, 64 * h)
+
+
 def columns(r):
     if len(r) == 5:
         return [W3[r[0]] * g + c for g in range(r[4][0], r[4][1]) for c in range(*r[4][2:])]
-    return range(*r[1:])
+    return range(*r[1:4])
 
 
 def width(r):
@@ -83,7 +87,7 @@ def build(M):
 
     def add(eng, call, rd, wr, cost, lat=LAT, **kw):
         w = wr[0] if wr else ("", 0)
-        a = w[1] % 256 if w[0] in ("zin", "yzb") else 0 if w[0] in ("TH", "penb", "MZ", "P0", "P1", "P2") else w[1]
+        a = w[1] % 256 if w[0] in ("zin", "yzb") else 0 if w[0] in ("TH", "NM", "penb", "MZ", "P0", "P1", "P2") else w[1]
         if w[0] in ("Mw", "Xh") and w[1] % XS < B1:
             a = -1
         if w[0] == "PA":
@@ -133,22 +137,28 @@ def build(M):
     def lin(o, i, scale, bias=0.0):
         either(lambda: act(o, i, AF.Identity, bias=bias, scale=scale), lambda: ts(o, i, scale, ALU.mult, bias, ALU.add))
 
+    def fill(o, v):
+        either(lambda: act(o, R("one", 0, width(o)), AF.Identity, bias=v, scale=0.0), lambda: ms(o, v))
+
     def iota(o, pat, base, cm):
         add("g", ("iota", o, pat, base, cm), [], [o], 130 + 2 * CY * width(o))
 
     def select(o, i, pat, base, cm, op=ALU.is_equal, fill=0.0):
         add("g", ("sel", o, i, pat, base, cm, op, fill), [i], [o], 170 + 2 * CY * width(o))
 
-    def mm(groups, first=True, last=True, f=1, one=False):
-        rd, cost, calls = [], 30.0, []
+    def mm(groups, first=True, last=True, f=1, one=False, parts=None):
+        calls = []
         for n, (o, terms) in enumerate(groups):
             for k, tm in enumerate(terms):
                 oo = tm[2] if len(tm) > 2 else o
                 calls.append((oo, tm[0], tm[1], first and k == 0 and not (one and n),
                               last and k == len(terms) - 1 and not (one and n < len(groups) - 1)))
-                rd += [tm[0], tm[1]]
-                cost += max(64, width(tm[1])) * PCY * f
-        add("p", ("mm", calls), rd, [o for o, _ in groups], cost)
+        n, wr = 1 if parts is None else parts, [o for o, _ in groups]
+        for k in range(n):
+            some = calls[k * len(calls) // n:(k + 1) * len(calls) // n]
+            add("p", ("mm", some), [x for c in some for x in c[1:3]], wr if n == 1 else [R(wr[0][0], 0, 512)],
+                (30.0 if n == 1 else 10.0) + sum(max(64, width(c[2])) * PCY * f for c in some))
+            ops[-1]["key"] += (k,)
 
     nd = [0]
 
@@ -183,7 +193,7 @@ def build(M):
         dma(r, ("xr", 4096 * k, 4096 * (k + 1)), [], [r], 1 << 20)
 
     ID = R("Id", 1, 129)
-    unused = ([] if (OPT["CA"][0] | OPT["CA"][1]) & 31 else ["C1", "C2"]) + ([] if OPT["PM"] else ["C3"]) + ([] if OPT["YA"] else ["RI", "RN"])
+    unused = ([] if (OPT["CA"][0] | OPT["CA"][1]) & 31 else ["C1", "C2"]) + ([] if OPT["PM"] else ["C3"]) + ([] if any(OPT["YA"]) else ["RI", "RN"])
     ms(R("one", 0, 512), 1.0)
     iota(c1("pi", 0), [[0, 1]], 0, 1)
     iota(full("Gn"), [[16, 8], [0, 16]], 0, 0)
@@ -191,17 +201,16 @@ def build(M):
     iota(R("R32", 0, 32), [[1, 32]], 0, 0)
     iota(R("Nn", 0, 144), [[1, 144]], -15, 0)
     iota(full("Rn"), [[0, 8], [1, 16]], 0, 0)
-    iota(wide("Gw"), [[-128, 2], [32, 8], [0, 16]], 0, 0)
     iota(full("N8"), [[PC, 8], [0, 16]], 0, 8)
-    for k, v in enumerate((15, 112, 31, 96)):
+    for k, v in enumerate((15, 112, 31)):
         ts(c1("pi", 1 + k), c1("pi", 0), v, ALU.bitwise_and)
-    cp(R("col", 0, 5), R("pi", 0, 5))
-    rc, gc, row, g32 = [c1("col", k) for k in range(1, 5)]
+    cp(R("col", 0, 4), R("pi", 0, 4))
+    rc, gc, row = [c1("col", k) for k in range(1, 4)]
     ts(full("O"), full("Gn"), gc, ALU.is_equal)
     ts(R("E", 0, 144), R("Nn", 0, 144), gc, ALU.is_equal)
     cp(R("wf", 0, 2), R("wts", 0, 2))
-    for g in range(8):
-        ts(R("OM", 16 * g, 16 * g + 16), R("m0s", 0, 16), c1("O", 16 * g), ALU.mult)
+    mm([(R("P4", 16 * g, 16 * g + 16), [(ID, R("m0s", 0, 16))]) for g in range(8)])
+    tt(full("OM"), R("P4", 0, 128), full("O"), ALU.mult)
     for k, n in enumerate("AB"):
         ms(R(n + "H", 0, 512), 0.0)
         lin(R(n, 0, 144), R("E", 0, 144), c1("wf", k))
@@ -214,14 +223,14 @@ def build(M):
     ms(R("pc", 0, 16), 2.0 ** -10)
     ms(R("pc", 16, 32), 0.0)
     scan(R("pw", 0, 16), R("pc", 0, 16), R("pc", 16, 32), 2.0 ** 78, ALU.mult, ALU.add)
-    tt(R("pw", 0, 16), R("pw", 0, 16), R("dl", 0, 16), ALU.mult)
-    ncol[0] += 1
-    wc = c1("col", ncol[0])
-    red(wc, R("pw", 0, 16))
-    act(c1("ub", 0), wc, AF.Sqrt)
+    act(R("ub", 0, 16), R("pw", 0, 16), AF.Sqrt)
     ops[-1]["cost"] += 1300.0
     ops[-1]["boost"] = 20000.0
-    unit = column(c1("ub", 0), 1.0, ALU.mult)
+    tt(R("pc", 0, 16), R("ub", 0, 16), R("dl", 0, 16), ALU.mult)
+    ncol[0] += 1
+    unit = c1("col", ncol[0])
+    red(unit, R("pc", 0, 16))
+    wc = column(unit, unit, ALU.mult)
     ts(R("RB", 0, 8), R("O", 0, 128, 16), -H54, ALU.mult, H54, ALU.mult)
     ts(R("RB", 8, 16), R("O", 0, 128, 16), wc, ALU.mult)
     mm([(R("P0", 0, 128), [(full("OM"), ID)])])
@@ -237,6 +246,7 @@ def build(M):
             lin(full(n), ID, v)
     ops[-1]["boost"] = 20000.0
     magic = column(unit, 1.5 * 2.0 ** 28, ALU.mult)
+    nomagic = column(unit, -1.5 * 2.0 ** 28, ALU.mult) if OPT["EA"] else None
     less = column(rc, 14.5, ALU.is_lt, -0.75, ALU.mult)
     ts(R("ge", 0, 32), R("R32", 0, 32), row, ALU.is_le)
     ts(R("eq", 0, 32), R("R32", 0, 32), row, ALU.is_equal)
@@ -247,20 +257,22 @@ def build(M):
     if OPT["PM"]:
         for n in "AB":
             lin(R(n + "N", 0, 512), R(n + "H", 0, 512), -1.0)
-    ts(wide("Of"), wide("Gw"), g32, ALU.is_equal)
+    select(wide("Of"), wide("one"), [[128, 2], [-32, 8], [0, 16]], 0, 1, ALU.is_ge)
+    select(wide("Of"), wide("Of"), [[-128, 2], [32, 8], [0, 16]], 31, -1, ALU.is_ge)
     for k in range(6):
-        ms(R("Lq", 256 * k, 256 * k + 256), 0.0)
+        fill(R("Lq", 256 * k, 256 * k + 256), 0.0)
     lowr = column(column(r0, -8.0, ALU.mult, live, ALU.add), c1("ge", 22), ALU.subtract)
     for k, c in enumerate([live] * 4 + [lowr, c1("ge", 22)]):
         a, b = WIN[min(k, 4)]
         lin(R3("Lq", 16 * k, 16 * k + 16, a, b + 1), R3("Of", 0, 16, a, b + 1), c)
-    step = live
-    for r in (15, 23, 31):
-        step = column(c1("eq", r), 1023.0, ALU.mult, step, ALU.add)
+    ncol[0] += 1
+    step = c1("col", ncol[0])
+    red(step, R("eq", 15, 32, 8))
+    step = column(step, 1023.0, ALU.mult, live, ALU.add)
     g128 = column(gc, -8.0, ALU.mult)
     lin(wide("IB"), wide("Of"), step)
-    ts(c1("penb", 0), r0, 16.5, ALU.mult, -15.0, ALU.add)
-    base = column(c1("penb", 0), 0.0, ALU.add)
+    base = column(r0, 16.5, ALU.mult, -15.0, ALU.add)
+    lin(full("pen"), full("one"), column(r0, 1.5, ALU.mult))
     first = column(row, -16.0, ALU.add, live, ALU.mult)
     select(full("L"), ID, [[1, 128]], -1, -1, ALU.not_equal, 64.0)
     select(full("L"), full("L"), [[1, 128]], 0, -1, ALU.not_equal, -63.0)
@@ -270,20 +282,19 @@ def build(M):
     ts(full("PR"), full("t2"), H54, ALU.mult, H54, ALU.mult)
     lin(R("PR", 128, 256), ID, 2.0 ** 78)
     lin(full("Af"), full("one"), c1("eq", 31))
-    lin(R("rank", 0, 512), R("one", 0, 512), first)
     for ch in range(NC):
-        ms(R3("Hs%d" % ch, 0, 8, 0, 16), 0.0)
-        ms(R3("Hs%d" % ch, 0, 8, 0, 1), 2.0 ** 78)
-    for n, w, v in (("Kx", 128, -2.0 ** 22), ("Kn", 128, 2.0 ** 29)):
-        ms(R(n, 0, w), 0.0)
-        ms(R(n, 0, w, 16), v)
-    ms(R("Ku", 0, 16 * NB), 0.0)
+        fill(R3("Hs%d" % ch, 0, 8, 0, 16), 0.0)
+        fill(R3("Hs%d" % ch, 0, 8, 0, 1), 2.0 ** 78)
+    for n, w, k, v in (("Kx", 128, 16, -2.0 ** 22), ("Kn", 144, 9, 2.0 ** 29)):
+        fill(R(n, 0, w), 0.0)
+        fill(R(n, 0, w, k), v)
+    fill(R("Ku", 0, 16 * NB), 0.0)
     for k, v in ((0, -2.0 ** 22), (16, -2047.5), (17, M12), (18, -M12)):
-        ms(R("Ku", k, 16 * NB, NB), v)
+        fill(R("Ku", k, 16 * NB, NB), v)
     for t in range(RO):
         select(R("KD", KO[t], KO[t + 1]), R("one", 0, 8 * (16 + t)), [[0, 8], [1, 16 + t]], 0, 0, ALU.not_equal)
-    ms(R("UZ", 0, 16 * NB), 0.0)
-    ms(R3("Cm", 0, 8, 16, NB), -2.0 ** 21)
+    fill(R3("UZ", 0, 16, 16, NB), 0.0)
+    fill(R3("Cm", 0, 8, 16, NB), -2.0 ** 21)
     lin(R3("Cm", 0, 8, 0, 16), full("dl"), 2.0 ** 21, -2.0 ** 21)
     tt(full("Ci"), full("N8"), R3("Cm", 0, 8, 0, 16), ALU.add)
     iota(R("PA", 0, 96), [[1, 6], [0, 2], [PC, 8]], B1, 8)
@@ -292,11 +303,19 @@ def build(M):
     ts(R("lr", 0, 6), R("one", 0, 6), column(rc, 16.0, ALU.mult, 15.0, ALU.add), ALU.mult)
     lin(full("BI"), ID, 8192.0)
     lin(full("NI"), ID, -8192.0)
-    ts(full("Cd"), full("Rn"), rc, ALU.is_ge, 2.0 ** 28, ALU.mult)
-    lin(full("Cd"), full("Cd"), 1.0, rc)
-    ms(R("Cd", 15, 128, 16), 16.0)
-    for r in range(15):
-        select(R("Dm", 128 * r, 128 * r + 128), full("dI"), [[1, 128]], -1 - r, -1, ALU.not_equal, 16384.0)
+    iota(R("Nn", 144, 288), [[0, 16], [2, 9]], 0, 0)
+    for h in range(2):
+        ts(RH("Cd", 0, 144, h), RH("Nn", 144, 288, h), float(h), ALU.add, RH("col", 1, 2, h), ALU.is_ge)
+        fill(R("Wd", 128 * h, 128 * h + 64), 0.0)
+        lin(RH("Wd", 64, 128, h), RH("Id", 1 + 64 * h, 65 + 64 * h, h), 1.0)
+    lin(R("Cd", 0, 144), R("Cd", 0, 144), 2.0 ** 28)
+    fill(R("Cd", 8, 144, 9), 16384.0)
+    for v in (64, -64):
+        select(full("dI"), full("dI"), [[1, 128]], v, -1, ALU.not_equal, -16384.0)
+    for r in range(8):
+        d = R("Dm", 128 * r, 128 * r + 128)
+        for h in range(2):
+            select(d, d if h else full("dI"), [[-1, 2], [1, 64]], 64 * h - 1 - 2 * r, -1, ALU.not_equal, 16384.0)
     a = XS * (NC - 1)
     for h in range(2):
         n, o = 8, a + (B1, B2)[h]
@@ -307,17 +326,14 @@ def build(M):
             else:
                 select(R("Mw", o + n, o + 2 * n), R("Mw", o, o + n), [[0, n]], 0, 0)
             n *= 2
-        if OPT["GM"]:
+        if OPT["GM"] == 2:
+            dma(R("Mw", o - a, o - a + n), R("Mw", o, o + n), [R("Mw", o, o + n)], [R("Mw", o - a - 8, o - a + n + 8)], 256 * n)
+        elif OPT["GM"]:
             select(R("Mw", o - a, o - a + n), R("Mw", o, o + n), [[0, n]], 0, 0)
         else:
             lin(R("Mw", o - a, o - a + n), R("Mw", o, o + n), 1.0)
     for ch in range(NC):
-        ms(R("Mw", XS * ch + B3, XS * ch + B3 + 8 * PC - 7, 8), 0.0)
-    select(wide("PN"), wide("one"), [[-128, 2], [32, 8], [1, 16]], 16, -1)
-    mm([(R("P1", 0, 128), [(full("L"), ID)])])
-    lin(full("LT"), R("P1", 0, 128), 1.0)
-    mm([(R("P2", 0, 256), [(full("LT"), wide("PN"))])])
-    lin(wide("PL"), R("P2", 0, 256), 1.0)
+        fill(R("Mw", XS * ch + B3, XS * ch + B3 + 8 * PC - 7, 8), 0.0)
 
     def penalty(ch, t):
         o, i, c = R("pen", 256 * ch, 256 * ch + 256), R("rank", 256 * ch, 256 * ch + 256), c1("penb", t % 2)
@@ -347,7 +363,6 @@ def build(M):
         ts(x, x, 5, ALU.arith_shift_right, 8191, ALU.bitwise_and)
         cp(o, x)
 
-    ts(R("pen", 0, 512), R("rank", 0, 512), c1("penb", 0), ALU.add, 0.0, ALU.max)
     rot = [0]
 
     def dbank():
@@ -386,7 +401,8 @@ def build(M):
                     for bk, o, n in OPT["MZB"][ch]:
                         ks = list(range(a, min(a + n, t)))
                         if ks:
-                            mm([(R(bk, (o + k - a) * PC, (o + 1 + k - a) * PC), [(ID, z), (full("K8"), slot("Mw", 16 + k))]) for k in ks])
+                            mm([(R(bk, (o + k - a) * PC, (o + 1 + k - a) * PC), [(ID, z), (full("K8"), slot("Mw", 16 + k))]) for k in ks],
+                               parts=min(OPT["SP"][3], len(ks)))
                             act(R("MZ", zb + a * PC, zb + (ks[-1] + 1) * PC), R(bk, o * PC, (o + len(ks)) * PC), AF.Relu, bias=-256.0)
                         a += n
                 elif t:
@@ -399,11 +415,12 @@ def build(M):
                              [(R("AB"[k] + sign, 128 * (2 * h + b), 128 * (2 * h + b + 1)), R(z[0], z[1] + b, z[2], 2)) for b in range(2)])
                             for k in range(2) for h in range(2)]
 
-                if OPT["PM"] >> ch & 1:
+                if OPT["PM"] >> ch & 1 and t >= OPT["P0"]:
                     uv = R(hb, 0, 2 * PC)
                     mm([(uv, [(full("C3"), wide("one"))])], last=False)
                     ops[-1]["wr"] = [R(hb, 0, 512)]
-                    mm(sums("N") + [(uv, [(full("MN"), wide("one")), (full("MI"), wide("one"))])] + sums("H"), first=False, one=True)
+                    mm(sums("N") + [(uv, [(full("MN"), wide("one")), (full("MI"), wide("one"))])] + sums("H"), first=False, one=True,
+                       parts=OPT["SP"][1])
                     ops[-1]["wr"] = [R(hb, 0, 512)]
                     u, w, vp = half("F1", 0), half("F1", 1), R(hb, PC, 2 * PC)
                     lin(u, R(hb, 0, PC), 1.0)
@@ -418,12 +435,13 @@ def build(M):
                     tag[0], n, hb = "dyn", (1 if OPT["DY"] else 2) * t * CC, OPT["DB"][ch]
                     a = n * ch
                     for k, m in enumerate("AB"):
-                        mm([(R(hb, 2 * PC + k * n, 2 * PC + k * n + n), [(view(m, r), R("MZ", 16 * a + r, 16 * (a + n), 16)) for r in range(16)])])
+                        mm([(R(hb, 2 * PC + k * n, 2 * PC + k * n + n), [(view(m, r), R("MZ", 16 * a + r, 16 * (a + n), 16)) for r in range(16)])],
+                           parts=OPT["SP"][2])
                     place_list(R("ofd", a, a + n), hashed(R(hb, 2 * PC, 2 * PC + 2 * n), R(hb, 2 * PC, 2 * PC + n), "I3", 2 * a, "I4", a))
                 continue
             c0, W = 16 - t, 16 + t
             tag[:] = "gather", ch + 1
-            mm([(R(Q, (8 * k + 4 * h) * W, (8 * k + 4 * h + 4) * W), [(half("pen", h), R3("PR", 4 * k, 4 * k + 4, c0, 32))])
+            mm([(R(Q, (8 * k + 4 * h) * W, (8 * k + 4 * h + 4) * W), [(half("pen", h) if t else full("pen"), R3("PR", 4 * k, 4 * k + 4, c0, 32))])
                 for h in range(2) for k in range(2)], last=False, one=True)
             ops[-1]["wr"] = [R(Q, 0, 512)]
             for h in range(2):
@@ -450,15 +468,21 @@ def build(M):
                     act(dd, dd, AF.Abs)
                     tt(gg, dd, free, ALU.is_gt)
                     return
-                mm(([(dd, [(full("MI"), free)])] if free else []) + [(o, [(full("nI"), zz)]) for o, _, zz in parts], last=False, one=True)
+                mm(([(dd, [(full("MI"), free)])] if free else []) + [(o, [(full("nI"), zz)]) for o, _, zz in parts], last=False, one=True,
+                   parts=OPT["SP"][4 if free else 5])
                 ops[-1]["wr"] = [R(bk, 0, 512)]
                 more = [(full("MN"), free)] if free else []
                 if scalar:
                     more += [(full(m), R("one", 0, dd[2])) for m in ("C1", "C2")]
-                mm([(o, [(full("sI"), x)]) for o, x, _ in parts] + [(dd, [m]) for m in more], first=False, one=True)
+                mm([(o, [(full("sI"), x)]) for o, x, _ in parts] + [(dd, [m]) for m in more], first=False, one=True,
+                   parts=OPT["SP"][4] if free else 1)
                 ops[-1]["wr"] = [R(bk, 0, 512)]
                 if scalar:
                     act(gg, dd, AF.Abs, bias=-3.0 * 2 ** 22 - 1, scale=2.0 ** -8)
+                elif OPT["CS"] >> ch & 1 and not free:
+                    g0, _, a, b, _ = gg[4]
+                    for k in range(2):
+                        ts(R3("G", g0 + 4 * k, g0 + 4 * k + 4, a, b), R(bk, 256 * k, 256 * k + 256), CR, ALU.add, CR, ALU.not_equal)
                 else:
                     ts(gg, dd, CR, ALU.add, CR, ALU.not_equal)
 
@@ -469,7 +493,7 @@ def build(M):
                 if bl[0] >= 16:
                     n, g0, a = len(bl) * PC, gb + bl[0] * PC, mb + (bl[0] - 16) * PC
                     differ(R("G", g0, g0 + n), [(R(bk, j * PC, j * PC + PC), slot("Xh", s), z) for j, s in enumerate(bl)],
-                           R("TH", a, a + n), OPT["CA"][ch] >> 4 & 3)
+                           R("TH" if t >= OPT["CT"][ch] else "NM", a, a + n), 2 if t >= OPT["CT"][ch] else 0)
                     count(bl)
                 else:
                     h, k = bl
@@ -482,8 +506,8 @@ def build(M):
                             count(range(8 * h + a, 8 * h + a + OPT["NK"]))
             tag[0] = "miss"
             mm([(mr(0, 0), [(full("qI"), full("one")), (full("hI"), z), (full("gI"), slot("Xh", 15 + t if t else 0))]
-                 + ([(full("RI"), full("one")), (full("RN"), full("one"))] if OPT["YA"] >> ch & 1 else []))])
-            if OPT["YA"] >> ch & 1:
+                 + ([(full("RI"), full("one")), (full("RN"), full("one"))] if OPT["YA"][t] >> ch & 1 else []))])
+            if OPT["YA"][t] >> ch & 1:
                 lin(slot("Xh", MISS), mr(0, 0), 1.0)
             else:
                 ts(slot("Xh", MISS), mr(0, 0), 1.5 * 2.0 ** 23, ALU.add, 1.5 * 2.0 ** 23, ALU.subtract)
@@ -508,7 +532,7 @@ def build(M):
             tag[0] = "header"
             win = R("Xh", xb, xb + XS)
             new = R("yzb", 256 * t + pb, 256 * t + pb + PC)
-            if OPT["HA"] >> ch & 1:
+            if OPT["HA"][t] >> ch & 1:
                 gat(pt("ds"), win, ix)
                 mm([(mr(5, 3 * PC), [(full("gI"), z), (full("hI"), pt("ds"))])])
                 act(new, mr(5, 3 * PC), AF.Abs, scale=2.0)
@@ -524,7 +548,12 @@ def build(M):
                 a, b = WIN[q]
                 cb = 512 * q + wb
                 lo = 2.0 ** (34 - 5 * (b + 1)) if b < 15 else 0.0
-                ts(both("Cq", cb), both("H"), 2.0 ** (34 - 5 * (a - 1)), ALU.min, lo, ALU.max)
+                hi = 2.0 ** (34 - 5 * (a - 1))
+                if OPT["QA"][ch] >> q & 1 and t == RO - 1:
+                    act(both("Ct", 256 * (q % 2)), both("H"), AF.Relu, bias=hi, scale=-1.0)
+                    act(both("Cq", cb), both("Ct", 256 * (q % 2)), AF.Relu, bias=hi - lo, scale=-1.0)
+                else:
+                    ts(both("Cq", cb), both("H"), hi, ALU.min, lo, ALU.max)
                 terms += [(half("Lq", h, 256 * k), half("Cq", h, cb)) for k in ([q] if q < 4 else [4, 5]) for h in range(2)]
             xx = R(Q, 2 * PC, 3 * PC)
             terms.insert(OPT["MSP"], (full("uI"), pt("ms")))
@@ -533,7 +562,11 @@ def build(M):
                 mm([(xx, terms[a:b])], first=not a, last=b == len(terms))
                 if not a:
                     ops[-1]["rd"].append(both("b"))
-            ts(pt("e1"), xx, magic, ALU.add, magic, ALU.subtract)
+            if OPT["EA"] >> ch & 1:
+                act(pt("y1"), xx, AF.Identity, bias=magic)
+                act(pt("e1"), pt("y1"), AF.Identity, bias=nomagic)
+            else:
+                ts(pt("e1"), xx, magic, ALU.add, magic, ALU.subtract)
             U = slot("Mw", 16 + t) if t < RO - 1 else R("ymb", pb, pb + PC)
             tt(U, xx, pt("e1"), ALU.is_gt)
             tag[0] = "rank"
@@ -542,11 +575,14 @@ def build(M):
                 lin(pt("rk"), mr(2, 0), 1.0)
             else:
                 sp = mr(2, 2 * PC, 2 * PC)
-                mm([(sp, [(full("L"), both("b")), (ID, both("rank"))])])
-                lin(both("rank"), sp, 1.0)
-                lin(R("TH", mb + t * PC, mb + t * PC + PC), U, *((-236.0, 300.0) if OPT["CA"][ch] & 32 else (-1.0, 1.0)))
+                mm([(sp, [(full("L"), both("b"))] + ([(ID, both("rank"))] if t else []))])
+                lin(both("rank"), sp, 1.0, 0.0 if t else first)
+                if OPT["CT"][ch] < RO:
+                    lin(R("TH", mb + t * PC, mb + t * PC + PC), U, -236.0, 300.0)
+                if t + 1 < OPT["CT"][ch]:
+                    lin(R("NM", mb + t * PC, mb + t * PC + PC), U, -1.0, 1.0)
                 tag[0] = "name"
-                zs, uz, n = mr(3, 0), R3("UZ", 8 * ch, 8 * ch + 8, 0, 16), 8 * NB
+                zs, uz, n = mr(3, OPT["ZS"]), R3("UZ", 8 * ch, 8 * ch + 8, 0, 16), 8 * NB
                 if OPT["UZA"] >> ch & 1:
                     mm([(zs, [(ID, z), (full("K8"), U)])])
                     act(uz, zs, AF.Relu, bias=-256.0)
@@ -569,20 +605,20 @@ def build(M):
                 ts(w, u, 1184.0, ALU.mult, -FOLD, ALU.add)
                 tt(v, u, v, ALU.mult)
                 tt(x, v, w, ALU.add)
-                ts(R("J3", jb, jb + CC), x, 5, ALU.arith_shift_right, 8128, ALU.bitwise_and)
-                ts(R("J3", jb + CC, jb + 2 * CC), x, 5, ALU.arith_shift_right, 63, ALU.bitwise_and)
-                cp(R("hl", jb, jb + 2 * CC), R("J3", jb, jb + 2 * CC))
-                terms = [(ID, full("Cd"))] + [
-                    (R("Dm", 128 * r, 128 * r + 128) if r < 15 else ID, R("hl", jb + CC * k, jb + CC * k + CC),
-                     R(Q, 2 * PC + r, 3 * PC, 16)) for k in range(2) for r in range(16)]
-                if OPT["PRE"] & 4:
-                    mm([(xx, terms[:1])], last=False)
-                    mm([(xx, terms[1:])], first=False)
-                else:
-                    mm([(xx, terms)])
-                act(pt("aD"), xx, AF.Abs)
-                scan(pt("sD"), full("Kn"), pt("aD"), 0.0, ALU.add, ALU.min)
-                cp(R("xo", jb, jb + 2 * CC, 2), R("sD", pb + 15, pb + PC, 16))
+                for h in range(2):
+                    for k, bits in enumerate((8128, 63)):
+                        ts(RH("J3", jb + CC * h, jb + CC * h + CC, k), RH(x[0], x[1], x[2], h), 5, ALU.arith_shift_right, bits, ALU.bitwise_and)
+                hl, dd, db = R("hl", jb, jb + 2 * CC), R(Q, 2 * PC, 2 * PC + 144), 144 * ch
+                cp(hl, R("J3", jb, jb + 2 * CC))
+                mm([(dd, [(ID, R("Cd", 0, 144))])], last=False)
+                mm([(dd, [(R("Dm", 128 * r, 128 * r + 128), hl, R(Q, 2 * PC + r, 2 * PC + 144, 9)) for r in range(8)])], first=False)
+                act(R("aD", db, db + 144), dd, AF.Abs)
+                scan(R("sD", db, db + 144), R("Kn", 0, 144), R("aD", db, db + 144), 0.0, ALU.add, ALU.min)
+                own = R(Q, 0, CC)
+                mm([(own, [(R("Wd", 64 - 64 * h, 192 - 64 * h), R("hl", jb + CC * h, jb + CC * h + CC)) for h in range(2)])], last=False)
+                ops[-1]["wr"] = [R(Q, 0, 512)]
+                mm([(own, [(R("Wd", 64 - 64 * h, 192 - 64 * h), R("sD", db + 72 * h + 8, db + 72 * h + 72, 9)) for h in range(2)])], first=False)
+                ts(R("xo", jb, jb + 2 * CC, 2), own, 16.0 - 32768.0, ALU.add, rc, ALU.max)
         tag[:] = "first", 3
         old, low, pe = R("PA", 96 * t + 16, 96 * t + 96), R("PA", 96 * t, 96 * t + 80), R("P" + OPT["BK"][3], 384, 464)
         gat(R("AJ", 0, 80), wide("sc"), R("lr", 0, 5))
@@ -594,6 +630,14 @@ def build(M):
             r = R("yzb", 256 * t, 256 * t + 256)
             dma(("yz", 256 * t, 256 * t + 256), r, [r], [], 65536)
             break
+        if t == 2:
+            tag[0] = "last"
+            select(wide("PN"), wide("one"), [[-128, 2], [32, 8], [1, 16]], 16, -1)
+            mm([(R("P0", 256, 384), [(full("L"), ID)])])
+            lin(full("LT"), R("P0", 256, 384), 1.0)
+            mm([(R("P0", 256, 512), [(full("LT"), wide("PN"))])])
+            lin(wide("PL"), R("P0", 256, 512), 1.0)
+            tag[0] = "rank"
         pa = R("P" + OPT["BK"][2], 511, 512)
         mm([(pa, [(full("Af"), c1("mcnt", ch)) for ch in range(NC)])], f=4)
         cp(c1("ai", 0), pa)
@@ -952,7 +996,7 @@ def plan(iters=None, seed=1):
     user = {b: -1 for bs in banks for b in bs}
     prio = [rest[0][k] + o.get("boost", 0.0) + OPT["START"].get(o["grp"], 0.0) for k, o in enumerate(base)]
     lean = [OPT["BIAS"]] * N
-    for stage in range(RO - 1):
+    for stage in range(RO):
         act = [k for k in range(N) if not fixed[k] and base[k]["step"] <= stage + 1]
         loc = {k: i for i, k in enumerate(act)}
         n = len(act)
@@ -1006,9 +1050,14 @@ def plan(iters=None, seed=1):
         for i, k in enumerate(act):
             kin.setdefault(base[k]["key"], []).append(i)
             gin.setdefault(base[k]["grp"] + (base[k]["step"],), []).append(i)
+            ch, name = base[k]["grp"]
+            if name in ("miss", "header", "mz", "hash", "dyn"):
+                for c in ((ch, 4) if OPT["LOOP"] else ()):
+                    gin.setdefault((c, "loop", base[k]["step"] + (name in ("miss", "header"))), []).append(i)
         grps, keys = sorted(gin), sorted(k for k in kin if k[0] or not stage)
+        grps += [x for x in grps if x[1] == "loop"] * OPT["LOOP"]
         kof = [kin[base[k]["key"]] for k in act]
-        span = iters // (RO - 1)
+        span = iters // (RO + 1) * (1 if stage else 2)
         cp, cb, cur, own, pairs, ceo, best = [prio[k] for k in act], [lean[k] for k in act], None, 0.0, [], None, None
         for it in range(span + 1):
             p, b, d, moved = list(cp), cb, 0.0, []
@@ -1055,7 +1104,7 @@ def plan(iters=None, seed=1):
             if best is None or val < best[0]:
                 best = (val, st, eo, p, b)
         value, st, eo, p, b = best
-        cut = max(st[loc[k]] for k in act if base[k]["call"][0] == "sca" and base[k]["step"] == stage) if stage < RO - 2 else 1e18
+        cut = max(st[loc[k]] for k in act if base[k]["call"][0] == "sca" and base[k]["step"] == stage) if stage < RO - 1 else 1e18
         learnt = {}
         for i, k in enumerate(act):
             prio[k], lean[k] = p[i], b[i]
@@ -1114,6 +1163,8 @@ def rank_program(g, core, T, topo):
     def ap(r):
         if not isinstance(r, tuple):
             return r
+        if len(r) == 6:
+            return T[r[0]][r[5]:r[5] + 64, r[1]:r[2]]
         if len(r) == 5:
             g0, g1, a, b, step = r[4]
             return T[r[0]][:, g0:g1, a:b] if step == 1 else T[r[0]][:, g0:g1, a:b:step]
@@ -1122,29 +1173,26 @@ def rank_program(g, core, T, topo):
         return T[r[0]][:, r[1]:r[2]] if len(r) == 3 or r[3] == 1 else T[r[0]][:, r[1]:r[2]:r[3]]
 
     pos = {k: i for i, k in enumerate(order)}
-    need = set()
-    for o in ops:
-        last = {}
-        o["w"] = []
-        for j in o["deps"]:
-            if inline(ops[j], o):
-                continue
-            if ops[j]["call"][0] in ("dma", "send"):
+    need, know, clock = set(), {e: {} for e in Q}, {}
+    for k in order:
+        o = ops[k]
+        seen, o["w"] = know[o["eng"]], []
+        for j in sorted(o["deps"], key=lambda j: -pos[j]):
+            s = j if ops[j]["call"][0] in ("dma", "send") else ops[j]["eng"]
+            if not inline(ops[j], o) and seen.get(s, -1) < pos[j]:
                 o["w"].append(j)
-            elif pos[j] > pos[last.get(ops[j]["eng"], j)] or ops[j]["eng"] not in last:
-                last[ops[j]["eng"]] = j
-        o["w"] += list(last.values())
-        need.update(last.values())
+                for x, v in clock[j].items():
+                    seen[x] = max(seen.get(x, -1), v)
+        need.update(o["w"])
+        clock[k] = {} if o["call"][0] == "send" else dict(seen)
+        clock[k][k if o["call"][0] in ("dma", "send") else o["eng"]] = pos[k]
     cnt = {e: 0 for e in "vapg"}
-    token, seen, sends = {}, {}, 0
+    token, sends = {}, 0
     for k in order:
         o = ops[k]
         q, c = Q[o["eng"]], o["call"]
-        for j in sorted(o["w"]):
-            s, v = token[j]
-            if seen.get((o["eng"], s), 0) < v:
-                q.wait_ge(T.sem[s], v)
-                seen[(o["eng"], s)] = v
+        for j in o["w"]:
+            q.wait_ge(T.sem[token[j][0]], token[j][1])
         f = c[0]
         if f == "dma":
             q.dma_start(ap(c[1]), ap(c[2])).then_inc(T.sem["d%d" % c[3]], 16)

@@ -11,23 +11,24 @@ H54 = 2.0 ** 54
 FOLD = 41.0 * 2 ** 18
 
 BF, F32, I32, U16 = "bfloat16", "float32", "int32", "uint16"
-MAT = "sI nI hI gI qI uI dI K8 C1 C2 C3 MI MN RI RN".split()
+MAT = "sI nI hI gI qI uI dI K8 C3 MI MN".split()
 _S = dict(
-    X=(8208, BF), Xh=(NC * XS, BF), Mw=(NC * XS, BF),
+    X=(8224, BF), Xh=(NC * XS, BF), Mw=(NC * XS, BF),
     zin=(6 * 256, BF), yzb=(6 * 256, BF), ymb=(4096, BF), m0s=(16, BF), wts=(16, BF),
-    MZ=(NC * 5 * PC, BF), TH=(NC * 5 * PC, BF), NM=(NC * 5 * PC, BF), I1=(512, I32), I2=(256, I32), off=(256, U16), F1=(512, F32),
+    MZ=(NC * 5 * PC, BF), NM=(NC * 5 * PC, BF), I2=(256, I32), off=(256, U16), F1=(512, F32),
     I3=(160, I32), I4=(80, I32), ofd=(80, U16), H=(512, BF), b=(512, BF), Cq=(5 * 512, BF), rank=(512, BF), pen=(512, BF),
-    mcnt=(8, F32), sc=(256, F32), idx=(16, U16), ds=(256, BF), ms=(256, BF), e1=(256, F32), y1=(256, F32), Ct=(512, F32),
-    J1=(48, F32), J2=(16, I32), J3=(32, I32), hl=(32, BF), aD=(288, F32), sD=(288, BF), Wd=(192, BF), xo=(32, U16), ai=(8, I32),
+    mcnt=(8, F32), sc=(256, F32), idx=(16, U16), ds=(256, BF), ms=(256, BF), e1=(256, F32), Ct=(512, F32),
+    J1=(48, F32), J2=(16, I32), J3=(32, I32), hl=(32, BF), aD=(432, F32), sD=(48, BF), Wd=(192, BF), Oh=(64, BF),
+    Rt=(1024, BF), xo=(16, U16), ai=(8, I32),
     su=(32 * NB, F32), Ku=(16 * NB, F32), rk=(256, BF), Es=(20 * PC, BF), to=(80, U16),
     PA=(7 * 96, F32), AJ=(80, F32), lr=(8, U16), BI=(128, F32), NI=(128, F32),
-    pi=(8, I32), col=(40, F32), penb=(8, F32), Gn=(128, F32), Gw=(256, F32), G32=(128, F32), Rn=(128, F32), R32=(32, F32),
+    pi=(8, I32), col=(40, F32), penb=(8, F32), Gn=(128, F32), Rn=(128, F32), R32=(32, F32),
     ge=(32, F32), eq=(32, F32), Nn=(288, F32), N8=(128, F32), Id=(136, BF), O=(128, BF), E=(144, BF), A=(144, BF), B=(144, BF),
-    ub=(16, BF), PL=(256, BF), LT=(128, BF), mf=(16, F32), wf=(8, F32), pw=(16, F32), pc=(32, F32), dl=(128, F32), RB=(16, BF),
-    IB=(256, BF), PN=(256, BF), L=(128, BF), L2=(128, BF),
+    ub=(16, BF), PL=(256, BF), LT=(128, BF), wf=(8, F32), pw=(16, F32), pc=(32, F32), dl=(128, F32), RB=(16, BF),
+    IB=(256, BF), PN=(256, BF), L=(128, BF),
     one=(512, BF), AN=(512, BF), BN=(512, BF), mat=(128 * len(MAT), BF),
     KD=(KO[RO], BF), rm=(2 * 168, BF), t1=(128, BF), t2=(128, BF), Dm=(8 * 128, BF), Ci=(PC, BF), Kx=(PC, BF),
-    Kn=(144, BF), Cd=(144, BF), Af=(128, F32), Oa=(128, BF), Ob=(128, BF), MT=(128, BF),
+    Kn=(216, BF), Cd=(216, BF), Af=(128, F32), Oa=(128, BF), Ob=(128, BF), MT=(128, BF),
 )
 SCRATCH = {k: ("sbuf", [128, n], d) for k, (n, d) in _S.items()}
 W3 = dict(Hs0=32, Hs1=32, PR=32, OM=16, AH=16, BH=16, Of=16, Lq=16, G=PC, UZ=NB, Cm=NB, RS=128)
@@ -41,17 +42,17 @@ NDMA = 16
 SEMAPHORES = (["cv", "ca", "cp", "cg", "sent"] + ["d%d" % k for k in range(NDMA)]
               + ["r%d_%d" % (t, c) for t in range(1, RO) for c in range(NC)])
 
-_M = dict(CY=0.87, PCY=0.46, LAT=180.0, RLAT=3000.0, OV=50.0, AO=30.0, GF=1.56, SF=3.8, BW=400.0, R0=2000.0, MINC=0.0, PS=0.0,
+_M = dict(CY=0.87, PCY=0.46, LAT=220.0, RLAT=2800.0, OV=40.0, AO=30.0, GF=1.56, SF=3.8, BW=400.0, R0=2000.0, MINC=0.0, PS=0.0,
           DLAT=1100.0)
 MODELS = [_M]
 OPT = dict(JUDGE=[dict(_M, MINC=64.0, OV=25.0, RLAT=4000.0, LAT=230.0, BW=240.0, DLAT=2200.0, W=0.95),
-                  dict(_M, PS=60.0, AO=80.0, CY=0.95, PCY=0.52, GF=1.8, LAT=130.0, W=0.87),
-                  dict(_M, MINC=64.0, OV=45.0, CY=0.83, PCY=0.5, LAT=110.0, RLAT=2400.0, BW=400.0, DLAT=1000.0, W=1.0)],
-           HB=("P4", "P3"), HA=(0, 0, 0, 0, 0, 0), BK=("401024", "355435", "1", "1"), KG=((6, 8), (8, 12), (12, 16), (1, 4), (4, 6), (0, 1)),
-           MZB=((("P0", 0, 3), ("P1", 0, 2)), (("P5", 0, 4), ("P5", 0, 1))), PM=3, PRE=7, ND=3, DB=("P5", "P5"), DY=0, MZA=3, UZA=0, YA=(0, 0, 0, 0, 0, 0), CT=(6, 6), FM=3, DF=(4, 4),
-           CA=(0, 0), NK=8, WO=(4, 0, 1, 2, 3),
-           START={(1, "header"): 3000.0, (1, "dyn"): 1000.0}, MSP=12, CUT=(4, 8, 10, 12), GM=2, GD=128, QA=(0, 0), EA=0, ZS=384, SP=(6, 4, 4, 2, 2, 2), CS=0, P0=1,
-           BIAS=300.0, TEMP=40.0, PK=0.4, PR=0.4, FB=10, LOOP=3, FAR=600.0, ITER=50000)
+                  dict(_M, PS=30.0, AO=50.0, OV=60.0, CY=1.2, PCY=0.66, GF=1.8, SF=5.0, LAT=140.0, W=1.0),
+                  dict(_M, MINC=64.0, OV=45.0, CY=0.83, PCY=0.5, LAT=110.0, RLAT=2400.0, BW=400.0, DLAT=1000.0, W=1.5)],
+           HB=("P4", "P3"), DA=1, YA=3, HA=0, UA=2, EA=0, QA=(0, 0), BK=("401024", "355435", "1", "1"), KG=((6, 8), (8, 12), (12, 16), (1, 4), (4, 6), (0, 1)),
+           MZB=((("P0", 3), ("P1", 2)), (("P5", 4), ("P5", 1))), DB=("P5", "P5"), DY=0, PM=0,
+           ORD="uuuuUllllL", DN=4, WO=(4, 0, 1, 2, 3), CUT=(4, 8, 10, 12), GD=128, SP=(3, 4, 4, 2),
+           START={(1, "header"): 3000.0, (1, "dyn"): 1000.0},
+           BIAS=300.0, TEMP=40.0, PK=0.4, PR=0.4, FB=10, LOOP=3, FAR=600.0, RUNS=2, ITER=50000)
 
 
 def R(n, a, b, s=1):
@@ -87,7 +88,7 @@ def build(M):
 
     def add(eng, call, rd, wr, cost, lat=LAT, **kw):
         w = wr[0] if wr else ("", 0)
-        a = w[1] % 256 if w[0] in ("zin", "yzb") else 0 if w[0] in ("TH", "NM", "penb", "MZ", "P0", "P1", "P2") else w[1]
+        a = w[1] % 256 if w[0] in ("zin", "yzb") else 0 if w[0] in ("NM", "penb", "MZ", "P0", "P1", "P2") else w[1]
         if w[0] in ("Mw", "Xh") and w[1] % XS < B1:
             a = -1
         if w[0] == "PA":
@@ -189,11 +190,10 @@ def build(M):
     dma(R("wts", 0, 2), ("wt", 0, 2), [], [R("wts", 0, 2)], 512, boost=30000.0)
     dma(R("zin", 0, 256), ("z0", 0, 256), [], [R("zin", 0, 256)], 65536, boost=20000.0)
     for k in range(2):
-        r = R("X", 16 + 4096 * k, 16 + 4096 * (k + 1))
+        r = R("X", 32 + 4096 * k, 32 + 4096 * (k + 1))
         dma(r, ("xr", 4096 * k, 4096 * (k + 1)), [], [r], 1 << 20)
 
     ID = R("Id", 1, 129)
-    unused = ([] if (OPT["CA"][0] | OPT["CA"][1]) & 31 else ["C1", "C2"]) + ([] if OPT["PM"] else ["C3"]) + ([] if any(OPT["YA"]) else ["RI", "RN"])
     ms(R("one", 0, 512), 1.0)
     iota(c1("pi", 0), [[0, 1]], 0, 1)
     iota(full("Gn"), [[16, 8], [0, 16]], 0, 0)
@@ -240,10 +240,8 @@ def build(M):
     ts(full("RS"), R("P3", 0, 128), -H54, ALU.mult, H54, ALU.mult)
     lin(R("RS", 128, 256), R("P3", 0, 128), wc)
     for n, v in (("sI", SC), ("nI", -SC), ("hI", 0.5), ("gI", -0.5), ("qI", 0.25), ("uI", unit), ("K8", 256.0),
-                 ("C1", CR), ("MI", M12), ("MN", -M12), ("RI", 1.5 * 2 ** 23), ("RN", -1.5 * 2 ** 23),
-                 ("dI", -16384.0)):
-        if n not in unused:
-            lin(full(n), ID, v)
+                 ("MI", M12), ("MN", -M12), ("dI", -1.0)):
+        lin(full(n), ID, v)
     ops[-1]["boost"] = 20000.0
     magic = column(unit, 1.5 * 2.0 ** 28, ALU.mult)
     nomagic = column(unit, -1.5 * 2.0 ** 28, ALU.mult) if OPT["EA"] else None
@@ -251,10 +249,8 @@ def build(M):
     ts(R("ge", 0, 32), R("R32", 0, 32), row, ALU.is_le)
     ts(R("eq", 0, 32), R("R32", 0, 32), row, ALU.is_equal)
     live, r0 = c1("ge", 11), c1("eq", 0)
-    for n, a, b in (("C2", CR, 256.0), ("C3", 2048.0, -0.5)):
-        if n not in unused:
-            lin(full(n), full("one"), column(column(r0, a / b, ALU.mult, c1("eq", 1), ALU.add), b / 4, ALU.mult))
     if OPT["PM"]:
+        lin(full("C3"), full("one"), column(column(r0, -4096.0, ALU.mult, c1("eq", 1), ALU.add), -0.125, ALU.mult))
         for n in "AB":
             lin(R(n + "N", 0, 512), R(n + "H", 0, 512), -1.0)
     select(wide("Of"), wide("one"), [[128, 2], [-32, 8], [0, 16]], 0, 1, ALU.is_ge)
@@ -285,7 +281,7 @@ def build(M):
     for ch in range(NC):
         fill(R3("Hs%d" % ch, 0, 8, 0, 16), 0.0)
         fill(R3("Hs%d" % ch, 0, 8, 0, 1), 2.0 ** 78)
-    for n, w, k, v in (("Kx", 128, 16, -2.0 ** 22), ("Kn", 144, 9, 2.0 ** 29)):
+    for n, w, k, v in (("Kx", 128, 16, -2.0 ** 22), ("Kn", 216, 9, 1.0)):
         fill(R(n, 0, w), 0.0)
         fill(R(n, 0, w, k), v)
     fill(R("Ku", 0, 16 * NB), 0.0)
@@ -303,19 +299,22 @@ def build(M):
     ts(R("lr", 0, 6), R("one", 0, 6), column(rc, 16.0, ALU.mult, 15.0, ALU.add), ALU.mult)
     lin(full("BI"), ID, 8192.0)
     lin(full("NI"), ID, -8192.0)
-    iota(R("Nn", 144, 288), [[0, 16], [2, 9]], 0, 0)
+    iota(R("Nn", 144, 288), [[0, 16], [2, 9]], -2, 0)
+    ts(R("Cd", 0, 144), R("Nn", 144, 288), column(column(gc, 64.0, ALU.is_ge, -1.0, ALU.mult), rc, ALU.add), ALU.is_ge, 16384.0, ALU.mult)
+    fill(R("Cd", 144, 216), 0.0)
     for h in range(2):
-        ts(RH("Cd", 0, 144, h), RH("Nn", 144, 288, h), float(h), ALU.add, RH("col", 1, 2, h), ALU.is_ge)
         fill(R("Wd", 128 * h, 128 * h + 64), 0.0)
         lin(RH("Wd", 64, 128, h), RH("Id", 1 + 64 * h, 65 + 64 * h, h), 1.0)
-    lin(R("Cd", 0, 144), R("Cd", 0, 144), 2.0 ** 28)
-    fill(R("Cd", 8, 144, 9), 16384.0)
+        lin(RH("Oh", 0, 64, h), RH("O", 64 * h, 64 * h + 64, h), 1.0)
+    for r in range(16):
+        lin(R("Rt", 64 * r, 64 * r + 64), R("Oh", 0, 64), c1("dl", r))
+    spare = rc, column(rc, 16.0, ALU.add)
     for v in (64, -64):
-        select(full("dI"), full("dI"), [[1, 128]], v, -1, ALU.not_equal, -16384.0)
+        select(full("dI"), full("dI"), [[1, 128]], v, -1, ALU.not_equal, -1.0)
     for r in range(8):
         d = R("Dm", 128 * r, 128 * r + 128)
         for h in range(2):
-            select(d, d if h else full("dI"), [[-1, 2], [1, 64]], 64 * h - 1 - 2 * r, -1, ALU.not_equal, 16384.0)
+            select(d, d if h else full("dI"), [[-1, 2], [1, 64]], 64 * h - 1 - 2 * r, -1, ALU.not_equal, 1.0)
     a = XS * (NC - 1)
     for h in range(2):
         n, o = 8, a + (B1, B2)[h]
@@ -326,12 +325,7 @@ def build(M):
             else:
                 select(R("Mw", o + n, o + 2 * n), R("Mw", o, o + n), [[0, n]], 0, 0)
             n *= 2
-        if OPT["GM"] == 2:
-            dma(R("Mw", o - a, o - a + n), R("Mw", o, o + n), [R("Mw", o, o + n)], [R("Mw", o - a - 8, o - a + n + 8)], 256 * n)
-        elif OPT["GM"]:
-            select(R("Mw", o - a, o - a + n), R("Mw", o, o + n), [[0, n]], 0, 0)
-        else:
-            lin(R("Mw", o - a, o - a + n), R("Mw", o, o + n), 1.0)
+        dma(R("Mw", o - a, o - a + n), R("Mw", o, o + n), [R("Mw", o, o + n)], [R("Mw", o - a - 8, o - a + n + 8)], 256 * n)
     for ch in range(NC):
         fill(R("Mw", XS * ch + B3, XS * ch + B3 + 8 * PC - 7, 8), 0.0)
 
@@ -366,13 +360,19 @@ def build(M):
     rot = [0]
 
     def dbank():
-        rot[0] = (rot[0] + 1) % OPT["ND"]
+        rot[0] = (rot[0] + 1) % 3
         return "P%d" % rot[0]
 
-    Xg = R("X", 16, 8208)
+    Xg = R("X", 32, 8224)
     for t in range(RO):
         now[0] = t
-        for part, ch in ((0, 1), (0, 0), (1, 1), (1, 0)):
+        nb = [10, 10]
+        blocks = []
+        for x in OPT["ORD"]:
+            ch = int(x in "uU")
+            blocks += [(14, ch), (15, ch)] if x in "UL" else [(nb[ch], ch)]
+            nb[ch] += x in "ul"
+        for part, ch in [(0, 1), (0, 0), (1, 1), (1, 0)] + blocks + [(2, 1), (2, 0)]:
             z = R("zin", 256 * t + PC * ch, 256 * t + PC * ch + PC)
             xb, gb, mb, wb, pb = XS * ch, 21 * PC * ch, 5 * PC * ch, 256 * ch, PC * ch
             Q, Hs, hb = "Q%d" % ch, "Hs%d" % ch, OPT["HB"][ch]
@@ -395,27 +395,22 @@ def build(M):
 
             if not part:
                 tag[:] = "mz", ch + 1
-                zb = t * PC * ch
-                if OPT["MZA"] >> ch & 1:
-                    a = 0
-                    for bk, o, n in OPT["MZB"][ch]:
-                        ks = list(range(a, min(a + n, t)))
-                        if ks:
-                            mm([(R(bk, (o + k - a) * PC, (o + 1 + k - a) * PC), [(ID, z), (full("K8"), slot("Mw", 16 + k))]) for k in ks],
-                               parts=min(OPT["SP"][3], len(ks)))
-                            act(R("MZ", zb + a * PC, zb + (ks[-1] + 1) * PC), R(bk, o * PC, (o + len(ks)) * PC), AF.Relu, bias=-256.0)
-                        a += n
-                elif t:
-                    mm([(R(hb, 3 * PC, 4 * PC), [(ID, z)])])
-                    for k in range(t):
-                        tt(R("MZ", zb + k * PC, zb + k * PC + PC), slot("Mw", 16 + k), R(hb, 3 * PC, 4 * PC), ALU.mult)
+                zb, a = t * PC * ch, 0
+                for bk, n in OPT["MZB"][ch]:
+                    ks = list(range(a, min(a + n, t)))
+                    if ks:
+                        mm([(R(bk, (k - a) * PC, (1 + k - a) * PC), [(ID, z), (full("K8"), slot("Mw", 16 + k))]) for k in ks],
+                           parts=min(OPT["SP"][3], len(ks)))
+                        act(R("MZ", zb + a * PC, zb + (ks[-1] + 1) * PC), R(bk, 0, len(ks) * PC), AF.Relu, bias=-256.0)
+                    a += n
                 tag[0] = "hash"
+
                 def sums(sign):
                     return [(R(hb, k * PC + 64 * h, k * PC + 64 * h + 64),
                              [(R("AB"[k] + sign, 128 * (2 * h + b), 128 * (2 * h + b + 1)), R(z[0], z[1] + b, z[2], 2)) for b in range(2)])
                             for k in range(2) for h in range(2)]
 
-                if OPT["PM"] >> ch & 1 and t >= OPT["P0"]:
+                if OPT["PM"] >> ch & 1 and t:
                     uv = R(hb, 0, 2 * PC)
                     mm([(uv, [(full("C3"), wide("one"))])], last=False)
                     ops[-1]["wr"] = [R(hb, 0, 512)]
@@ -430,7 +425,7 @@ def build(M):
                     place_list(pt("off"), pt("I2"))
                 else:
                     mm(sums("H"))
-                    place_list(pt("off"), hashed(R(hb, 0, 2 * PC), R(hb, 0, PC), "F1" if OPT["FM"] >> ch & 1 else "I1", wb, "I2", pb))
+                    place_list(pt("off"), hashed(R(hb, 0, 2 * PC), R(hb, 0, PC), "F1", wb, "I2", pb))
                 if t and (OPT["DY"] or not ch):
                     tag[0], n, hb = "dyn", (1 if OPT["DY"] else 2) * t * CC, OPT["DB"][ch]
                     a = n * ch
@@ -441,15 +436,17 @@ def build(M):
                 continue
             c0, W = 16 - t, 16 + t
             tag[:] = "gather", ch + 1
-            mm([(R(Q, (8 * k + 4 * h) * W, (8 * k + 4 * h + 4) * W), [(half("pen", h) if t else full("pen"), R3("PR", 4 * k, 4 * k + 4, c0, 32))])
-                for h in range(2) for k in range(2)], last=False, one=True)
-            ops[-1]["wr"] = [R(Q, 0, 512)]
-            for h in range(2):
-                for k in range(2):
-                    a = xb + (B1, B2)[h] + 512 * k
-                    gat(R("Xh", a, a + 512), Xg, R("off", pb + 64 * h + 32 * k, pb + 64 * h + 32 * (k + 1)))
-            for k in range(t):
-                gat(slot("Xh", 16 + k), Xg, R("ofd", CC * (t * ch + k), CC * (t * ch + k + 1)))
+            if part == 1:
+                mm([(R(Q, (8 * k + 4 * h) * W, (8 * k + 4 * h + 4) * W), [(half("pen", h) if t else full("pen"), R3("PR", 4 * k, 4 * k + 4, c0, 32))])
+                    for h in range(2) for k in range(2)], last=False, one=True)
+                ops[-1]["wr"] = [R(Q, 0, 512)]
+                for h in range(2):
+                    for k in range(2):
+                        a = xb + (B1, B2)[h] + 512 * k
+                        gat(R("Xh", a, a + 512), Xg, R("off", pb + 64 * h + 32 * k, pb + 64 * h + 32 * (k + 1)))
+                for k in range(t):
+                    gat(slot("Xh", 16 + k), Xg, R("ofd", CC * (t * ch + k), CC * (t * ch + k + 1)))
+                continue
             tag[0] = "compare"
 
             def count(ss):
@@ -458,9 +455,9 @@ def build(M):
                     for s in ss], first=False, last=False, one=True)
                 ops[-1]["gid"] = (t, ch)
 
-            def differ(gg, parts, free, scalar):
+            def differ(gg, parts, free):
                 dd = R(bk, 0, width(gg))
-                if scalar == 2:
+                if free and OPT["DA"] >> ch & 1:
                     mm([(o, [(full("nI"), zz)]) for o, _, zz in parts], last=False, one=True)
                     ops[-1]["wr"] = [R(bk, 0, 512)]
                     mm([(o, [(full("sI"), x)]) for o, x, _ in parts], first=False, one=True)
@@ -468,47 +465,34 @@ def build(M):
                     act(dd, dd, AF.Abs)
                     tt(gg, dd, free, ALU.is_gt)
                     return
-                mm(([(dd, [(full("MI"), free)])] if free else []) + [(o, [(full("nI"), zz)]) for o, _, zz in parts], last=False, one=True,
-                   parts=OPT["SP"][4 if free else 5])
+                mm(([(dd, [(full("MI"), free)])] if free else []) + [(o, [(full("nI"), zz)]) for o, _, zz in parts], last=False, one=True, parts=2)
+                mm([(o, [(full("sI"), x)]) for o, x, _ in parts] + ([(dd, [(full("MN"), free)])] if free else []), first=False, one=True,
+                   parts=2 if free else 1)
                 ops[-1]["wr"] = [R(bk, 0, 512)]
-                more = [(full("MN"), free)] if free else []
-                if scalar:
-                    more += [(full(m), R("one", 0, dd[2])) for m in ("C1", "C2")]
-                mm([(o, [(full("sI"), x)]) for o, x, _ in parts] + [(dd, [m]) for m in more], first=False, one=True,
-                   parts=OPT["SP"][4] if free else 1)
-                ops[-1]["wr"] = [R(bk, 0, 512)]
-                if scalar:
-                    act(gg, dd, AF.Abs, bias=-3.0 * 2 ** 22 - 1, scale=2.0 ** -8)
-                elif OPT["CS"] >> ch & 1 and not free:
-                    g0, _, a, b, _ = gg[4]
-                    for k in range(2):
-                        ts(R3("G", g0 + 4 * k, g0 + 4 * k + 4, a, b), R(bk, 256 * k, 256 * k + 256), CR, ALU.add, CR, ALU.not_equal)
-                else:
-                    ts(gg, dd, CR, ALU.add, CR, ALU.not_equal)
+                ts(gg, dd, CR, ALU.add, CR, ALU.not_equal)
 
-            blocks = [(h, k) for h in range(2) for k in range(2)]
-            dblk = [list(range(16 + a, 16 + min(a + 4, t))) for a in range(0, t, 4)]
-            for bl in blocks[:OPT["DF"][ch]] + dblk + blocks[OPT["DF"][ch]:]:
-                bk = dbank()
-                if bl[0] >= 16:
-                    n, g0, a = len(bl) * PC, gb + bl[0] * PC, mb + (bl[0] - 16) * PC
-                    differ(R("G", g0, g0 + n), [(R(bk, j * PC, j * PC + PC), slot("Xh", s), z) for j, s in enumerate(bl)],
-                           R("TH" if t >= OPT["CT"][ch] else "NM", a, a + n), 2 if t >= OPT["CT"][ch] else 0)
+            if part >= 14:
+                n = OPT["DN"] if t > 4 else 4
+                bl = range(16, 16 + min(t, n)) if part == 14 else range(16 + n, 16 + t)
+                if bl:
+                    bk, n, g0, a = dbank(), len(bl) * PC, gb + bl[0] * PC, mb + (bl[0] - 16) * PC
+                    differ(R("G", g0, g0 + n), [(R(bk, j * PC, j * PC + PC), slot("Xh", s), z) for j, s in enumerate(bl)], R("NM", a, a + n))
                     count(bl)
-                else:
-                    h, k = bl
-                    a = xb + (B1, B2)[h] + 512 * k
-                    differ(R3("G", 21 * ch + 8 * h, 21 * ch + 8 * h + 8, 64 * k, 64 * k + 64),
-                           [(R(bk, 64 * s, 64 * s + 64), R("Xh", a + s, a + 512, 8), R("zin", z[1] + 64 * k, z[1] + 64 * k + 64))
-                            for s in range(8)], None, OPT["CA"][ch] >> (2 * h + k) & 1)
-                    if k:
-                        for a in range(0, 8, OPT["NK"]):
-                            count(range(8 * h + a, 8 * h + a + OPT["NK"]))
+                continue
+            if part >= 10:
+                h, k = divmod(part - 10, 2)
+                bk, a = dbank(), xb + (B1, B2)[h] + 512 * k
+                differ(R3("G", 21 * ch + 8 * h, 21 * ch + 8 * h + 8, 64 * k, 64 * k + 64),
+                       [(R(bk, 64 * s, 64 * s + 64), R("Xh", a + s, a + 512, 8), R("zin", z[1] + 64 * k, z[1] + 64 * k + 64))
+                        for s in range(8)], None)
+                if k:
+                    count(range(8 * h, 8 * h + 8))
+                continue
             tag[0] = "miss"
-            mm([(mr(0, 0), [(full("qI"), full("one")), (full("hI"), z), (full("gI"), slot("Xh", 15 + t if t else 0))]
-                 + ([(full("RI"), full("one")), (full("RN"), full("one"))] if OPT["YA"][t] >> ch & 1 else []))])
-            if OPT["YA"][t] >> ch & 1:
-                lin(slot("Xh", MISS), mr(0, 0), 1.0)
+            mm([(mr(0, 0), [(full("qI"), full("one")), (full("hI"), z), (full("gI"), slot("Xh", 15 + t if t else 0))])])
+            if OPT["YA"] >> ch & 1:
+                act(mr(0, 0), mr(0, 0), AF.Identity, bias=1.5 * 2.0 ** 23)
+                act(slot("Xh", MISS), mr(0, 0), AF.Identity, bias=-1.5 * 2.0 ** 23)
             else:
                 ts(slot("Xh", MISS), mr(0, 0), 1.5 * 2.0 ** 23, ALU.add, 1.5 * 2.0 ** 23, ALU.subtract)
             tag[0] = "match"
@@ -518,13 +502,10 @@ def build(M):
             mm([(R(Q, PC * h, PC * h + PC), [(R(Hs, PC * h, PC * h + PC), ID)]) for h in range(2)])
             act(both("b"), R(Q, 0, 256), AF.Relu, bias=1.0, scale=-2.0 ** -106, acc=c1("mcnt", ch))
             act(both("H"), R(Q, 0, 256), AF.Sqrt)
-            if OPT["PRE"] & 2:
-                mm([(mr(1, PC), [(ID, full("Ci"))])], last=False)
-                ops[-1]["wr"] = [mr(1, 0, 512)]
-                mm([(mr(1, PC), [(half("IB", h, 0), half("b", h)) for h in range(2)])], first=False)
-                ops[-1]["wr"] = [mr(1, 0, 512)]
-            else:
-                mm([(mr(1, PC), [(ID, full("Ci"))] + [(half("IB", h, 0), half("b", h)) for h in range(2)])])
+            mm([(mr(1, PC), [(ID, full("Ci"))])], last=False)
+            ops[-1]["wr"] = [mr(1, 0, 512)]
+            mm([(mr(1, PC), [(half("IB", h, 0), half("b", h)) for h in range(2)])], first=False)
+            ops[-1]["wr"] = [mr(1, 0, 512)]
             scan(pt("sc"), R("Kx", 0, PC), mr(1, PC), 0.0, ALU.add, ALU.max)
             ix = R("idx", CC * ch, CC * ch + CC)
             ts(ix, R("sc", pb + 15, pb + PC, 16), g128, ALU.add)
@@ -532,7 +513,7 @@ def build(M):
             tag[0] = "header"
             win = R("Xh", xb, xb + XS)
             new = R("yzb", 256 * t + pb, 256 * t + pb + PC)
-            if OPT["HA"][t] >> ch & 1:
+            if OPT["HA"] >> ch & 1:
                 gat(pt("ds"), win, ix)
                 mm([(mr(5, 3 * PC), [(full("gI"), z), (full("hI"), pt("ds"))])])
                 act(new, mr(5, 3 * PC), AF.Abs, scale=2.0)
@@ -549,22 +530,22 @@ def build(M):
                 cb = 512 * q + wb
                 lo = 2.0 ** (34 - 5 * (b + 1)) if b < 15 else 0.0
                 hi = 2.0 ** (34 - 5 * (a - 1))
-                if OPT["QA"][ch] >> q & 1 and t == RO - 1:
-                    act(both("Ct", 256 * (q % 2)), both("H"), AF.Relu, bias=hi, scale=-1.0)
-                    act(both("Cq", cb), both("Ct", 256 * (q % 2)), AF.Relu, bias=hi - lo, scale=-1.0)
+                if OPT["QA"][ch] >> q & 1:
+                    act(both("Ct"), both("H"), AF.Relu, bias=hi, scale=-1.0)
+                    act(both("Cq", cb), both("Ct"), AF.Relu, bias=hi - lo, scale=-1.0)
                 else:
                     ts(both("Cq", cb), both("H"), hi, ALU.min, lo, ALU.max)
                 terms += [(half("Lq", h, 256 * k), half("Cq", h, cb)) for k in ([q] if q < 4 else [4, 5]) for h in range(2)]
             xx = R(Q, 2 * PC, 3 * PC)
-            terms.insert(OPT["MSP"], (full("uI"), pt("ms")))
+            terms.append((full("uI"), pt("ms")))
             cuts = [0] + list(OPT["CUT"]) + [len(terms)]
             for a, b in zip(cuts, cuts[1:]):
                 mm([(xx, terms[a:b])], first=not a, last=b == len(terms))
                 if not a:
                     ops[-1]["rd"].append(both("b"))
             if OPT["EA"] >> ch & 1:
-                act(pt("y1"), xx, AF.Identity, bias=magic)
-                act(pt("e1"), pt("y1"), AF.Identity, bias=nomagic)
+                act(pt("e1"), xx, AF.Identity, bias=magic)
+                act(pt("e1"), pt("e1"), AF.Identity, bias=nomagic)
             else:
                 ts(pt("e1"), xx, magic, ALU.add, magic, ALU.subtract)
             U = slot("Mw", 16 + t) if t < RO - 1 else R("ymb", pb, pb + PC)
@@ -577,48 +558,47 @@ def build(M):
                 sp = mr(2, 2 * PC, 2 * PC)
                 mm([(sp, [(full("L"), both("b"))] + ([(ID, both("rank"))] if t else []))])
                 lin(both("rank"), sp, 1.0, 0.0 if t else first)
-                if OPT["CT"][ch] < RO:
-                    lin(R("TH", mb + t * PC, mb + t * PC + PC), U, -236.0, 300.0)
-                if t + 1 < OPT["CT"][ch]:
-                    lin(R("NM", mb + t * PC, mb + t * PC + PC), U, -1.0, 1.0)
+                lin(R("NM", mb + t * PC, mb + t * PC + PC), U, *((-236.0, 300.0) if OPT["DA"] >> ch & 1 else (-1.0, 1.0)))
                 tag[0] = "name"
-                zs, uz, n = mr(3, OPT["ZS"]), R3("UZ", 8 * ch, 8 * ch + 8, 0, 16), 8 * NB
-                if OPT["UZA"] >> ch & 1:
+                zs, n = mr(3, 3 * PC), 8 * NB
+                if OPT["UA"] >> ch & 1:
                     mm([(zs, [(ID, z), (full("K8"), U)])])
-                    act(uz, zs, AF.Relu, bias=-256.0)
+                    act(R3("UZ", 8 * ch, 8 * ch + 8, 0, 16), zs, AF.Relu, bias=-256.0)
                 else:
                     mm([(zs, [(ID, z)])])
-                    tt(uz, U, zs, ALU.mult)
+                    tt(R3("UZ", 8 * ch, 8 * ch + 8, 0, 16), U, zs, ALU.mult)
                 jb, uz = 2 * CC * ch, R("UZ", n * ch, n * ch + n)
-                if OPT["PRE"] & 1:
-                    mm([(mr(4, k * n, n), [(ID, R("Cm", 0, n))]) for k in range(2)], last=False, one=True)
-                    ops[-1]["wr"] = [mr(4, 0, 512)]
-                    mm([(mr(4, k * n, n), [(full(m), uz)]) for k, m in enumerate(("Oa", "Ob"))], first=False, one=True)
-                    ops[-1]["wr"] = [mr(4, 0, 512)]
-                else:
-                    mm([(mr(4, k * n, n), [(ID, R("Cm", 0, n)), (full(m), uz)]) for k, m in enumerate(("Oa", "Ob"))])
+                mm([(mr(4, k * n, n), [(ID, R("Cm", 0, n))]) for k in range(2)], last=False, one=True)
+                ops[-1]["wr"] = [mr(4, 0, 512)]
+                mm([(mr(4, k * n, n), [(full(m), uz)]) for k, m in enumerate(("Oa", "Ob"))], first=False, one=True)
+                ops[-1]["wr"] = [mr(4, 0, 512)]
                 sb, j1 = 2 * n * ch, 3 * CC * ch
                 scan(R("su", sb, sb + 2 * n), R("Ku", 0, 2 * n), mr(4, 0, 2 * n), 0.0, ALU.add, ALU.max)
                 tt(R("J1", j1, j1 + 2 * CC), R("su", sb + 15, sb + 2 * n, NB), R("su", sb + 18, sb + 2 * n, NB), ALU.subtract)
                 u, v, w = [R("J1", j1 + k * CC, j1 + k * CC + CC) for k in range(3)]
                 x = R("J2", CC * ch, CC * ch + CC)
-                ts(w, u, 1184.0, ALU.mult, -FOLD, ALU.add)
+                lin(w, u, 1184.0, -FOLD)
                 tt(v, u, v, ALU.mult)
                 tt(x, v, w, ALU.add)
                 for h in range(2):
                     for k, bits in enumerate((8128, 63)):
                         ts(RH("J3", jb + CC * h, jb + CC * h + CC, k), RH(x[0], x[1], x[2], h), 5, ALU.arith_shift_right, bits, ALU.bitwise_and)
-                hl, dd, db = R("hl", jb, jb + 2 * CC), R(Q, 2 * PC, 2 * PC + 144), 144 * ch
+                hl, dd, db = R("hl", jb, jb + 2 * CC), R(Q, 2 * PC, 2 * PC + 216), 216 * ch
                 cp(hl, R("J3", jb, jb + 2 * CC))
-                mm([(dd, [(ID, R("Cd", 0, 144))])], last=False)
-                mm([(dd, [(R("Dm", 128 * r, 128 * r + 128), hl, R(Q, 2 * PC + r, 2 * PC + 144, 9)) for r in range(8)])], first=False)
-                act(R("aD", db, db + 144), dd, AF.Abs)
-                scan(R("sD", db, db + 144), R("Kn", 0, 144), R("aD", db, db + 144), 0.0, ALU.add, ALU.min)
-                own = R(Q, 0, CC)
-                mm([(own, [(R("Wd", 64 - 64 * h, 192 - 64 * h), R("hl", jb + CC * h, jb + CC * h + CC)) for h in range(2)])], last=False)
+                mm([(dd, [(ID, R("Cd", 0, 216))])], last=False)
+                mm([(dd, [(R("Dm", 128 * r, 128 * r + 128), hl, R(Q, 2 * PC + 1 + r, 2 * PC + 144, 9)) for r in range(8)]
+                     + [(m, R("hl", jb + k, jb + 2 * CC, 2), R(Q, 2 * PC + 145 + r, 2 * PC + 216, 9))
+                        for r in range(8) for k, m in enumerate((R("Rt", 128 * r, 128 * r + 128), full("dI")))])], first=False, parts=OPT["SP"][0])
+                scan(R("aD", db, db + 216), dd, R("Kn", 0, 216), 0.0, ALU.mult, ALU.add)
+                db = 24 * ch
+                ts(R("sD", db, db + 24), R("aD", 9 * db + 8, 9 * db + 216, 9), 0.0, ALU.not_equal, 16384.0, ALU.mult)
+                own, wd = R(Q, 0, CC), [R("Wd", 64 - 64 * h, 192 - 64 * h) for h in range(2)]
+                mm([(own, [(wd[h], R("hl", jb + CC * h, jb + CC * h + CC)) for h in range(2)])], last=False)
                 ops[-1]["wr"] = [R(Q, 0, 512)]
-                mm([(own, [(R("Wd", 64 - 64 * h, 192 - 64 * h), R("sD", db + 72 * h + 8, db + 72 * h + 72, 9)) for h in range(2)])], first=False)
-                ts(R("xo", jb, jb + 2 * CC, 2), own, 16.0 - 32768.0, ALU.add, rc, ALU.max)
+                mm([(own, [(wd[h], R("sD", db + 8 * h, db + 8 * h + 8)) for h in range(2)]
+                     + [(wd[h], R("sD", db + 16 + 4 * h, db + 20 + 4 * h), R(Q, 1, CC, 2)) for h in range(2)])], first=False)
+                for k in range(2):
+                    ts(R("xo", CC * ch + k, CC * ch + CC, 2), R(Q, k, CC, 2), 32.0 - 32768.0 * (k + 1), ALU.add, spare[k], ALU.max)
         tag[:] = "first", 3
         old, low, pe = R("PA", 96 * t + 16, 96 * t + 96), R("PA", 96 * t, 96 * t + 80), R("P" + OPT["BK"][3], 384, 464)
         gat(R("AJ", 0, 80), wide("sc"), R("lr", 0, 5))
@@ -645,10 +625,10 @@ def build(M):
         ts(c1("penb", (t + 1) % 2), c1("ai", 0), r0, ALU.mult, base, ALU.add)
         for ch in range(NC - 1, -1, -1):
             penalty(ch, t + 1)
-        for c in range(15, -1, -1):
-            tag[:] = "write", 1 + c // CC
-            zz = R("zin", 256 * t + 16 * c, 256 * t + 16 * c + 16)
-            add("v", ("sca", R("X", 0, 8208), c1("xo", 2 * c), zz), [zz, c1("xo", 2 * c)], [R("X", 0, 8208)], 50 + 16 * SF * CY)
+        for c in range(7, -1, -1):
+            tag[:] = "write", 1 + c // 4
+            zz, xo = R("zin", 256 * t + 32 * c, 256 * t + 32 * c + 32), R("xo", 2 * c, 2 * c + 2)
+            add("v", ("sca", R("X", 0, 8224), xo, zz), [zz, xo], [R("X", 0, 8224)], 50 + 32 * SF * CY)
         if t == RO - 2:
             r = R("yzb", 0, 256 * t + 256)
             dma(("yz", 0, 256 * t + 256), r, [r, Xg], [], 65536 * (t + 1))
@@ -677,7 +657,7 @@ def depend(ops):
     hist = {}
     for k, o in enumerate(ops):
         deps = set()
-        use = [(r[0], sum(1 << c for c in columns(r)), w) for rs, w in ((o["rd"], False), (o["wr"], True)) for r in rs]
+        use = [(r[0], sum((1 + r[5] // 64 if len(r) == 6 else 3) << 2 * c for c in columns(r)), w) for rs, w in ((o["rd"], False), (o["wr"], True)) for r in rs]
         for name, m, w in use:
             deps.update(j for j, mm, ww in hist.get(name, []) if (w or ww) and m & mm)
         for name, m, w in use:
@@ -701,192 +681,8 @@ def inline(p, o):
     return p["eng"] == o["eng"] == "p"
 
 
-def place(P, prio, bias):
-    succ, eng, cost, lat, banks = P
-    n = len(eng)
-    p = prio
-    at, by, held, st, eo = [0.0] * n, [-1] * n, [-1] * n, [0.0] * n, list(eng)
-    qs = {e: ([], [], []) for e in "vapgs"}
-    bk = {b: ([], []) for bs in banks for b in bs}
-    end, last = 0.0, 0
-    for k in sorted(range(n), key=lambda k: -p[k]):
-        best, la = None, lat[k]
-        for e in (eo[k] or "av"):
-            c, t, h = cost[k][e], at[k], -1
-            ss, ee, who = qs[e]
-            m = i = len(ss)
-            while i and ee[i - 1] > t:
-                i -= 1
-            moved = True
-            while moved:
-                while i < m and ss[i] < t + c:
-                    if ee[i] > t:
-                        t, h = ee[i], who[i]
-                    i += 1
-                moved = False
-                for b in banks[k]:
-                    s0, iv = bk[b]
-                    j = len(s0)
-                    while j and s0[j - 1] > t - 1800.0:
-                        j -= 1
-                    while j < len(s0) and s0[j] < t + c + la:
-                        if iv[j][1] != e and t < iv[j][0]:
-                            t, moved, h = iv[j][0], True, iv[j][2]
-                        j += 1
-                while moved and i < m and ee[i] <= t:
-                    i += 1
-            v = t + c + (bias[k] if e == "v" else 0.0)
-            if best is None or v < best[0]:
-                best = (v, t, c, e, i, h)
-        _, t, c, e, i, held[k] = best
-        for x, y in zip(qs[e], (t, t + c, k)):
-            x.insert(i, y)
-        for b in banks[k]:
-            s0, iv = bk[b]
-            j = len(s0)
-            while j and s0[j - 1] > t:
-                j -= 1
-            s0.insert(j, t)
-            iv.insert(j, (t + c + la, e, k))
-        st[k], eo[k] = t, e
-        x = t + c
-        if x + la > end:
-            end, last = x + la, k
-        for j, pp in succ[k]:
-            y = x if pp else x + la
-            if y > at[j]:
-                at[j], by[j] = y, k
-    pairs = []
-    while last >= 0:
-        if held[last] >= 0:
-            pairs.append((last, held[last]))
-        last = held[last] if held[last] >= 0 else by[last]
-    return st, eo, end, pairs
-
-
 def prices(ops):
     return [({e: c for e, (_, c) in o["alt"].items()} if "alt" in o else {o["eng"]: o["cost"]}, o["lat"]) for o in ops]
-
-
-def plan(iters=None, seed=1):
-    base = build(MODELS[0])
-    depend(base)
-    n, iters = len(base), OPT["ITER"] if iters is None else iters
-    above, pre, succ = [0] * n, [], [[] for _ in base]
-    for k, o in enumerate(base):
-        for j in o["deps"]:
-            above[k] |= above[j]
-        pre.append([(j, inline(base[j], o)) for j in sorted(o["deps"]) if not above[k] >> j & 1])
-        for j, pp in pre[k]:
-            succ[j].append((k, pp))
-        for j in o["deps"]:
-            above[k] |= 1 << j
-    P = (succ, [None if "alt" in o else o["eng"] for o in base], [c for c, _ in prices(base)],
-         [o["lat"] for o in base], [sorted(o["banks"]) for o in base])
-    others = [prices(build(m)) for m in OPT["JUDGE"]]
-
-    def judged(st, eo, val):
-        if not others:
-            return val
-        order, last, wait = sorted(range(n), key=lambda k: st[k]), {}, [None] * n
-        for k in order:
-            w = pre[k]
-            for b in P[4][k]:
-                if b in last and eo[last[b]] != eo[k]:
-                    w = w + [(last[b], False)]
-                last[b] = k
-            wait[k] = w
-        for cs, m in zip(others, OPT["JUDGE"]):
-            free, end, done = dict.fromkeys("vapgs", 0.0), [0.0] * n, [0.0] * n
-            for k in order:
-                e = eo[k]
-                t = free[e]
-                for j, pp in wait[k]:
-                    x = end[j] if pp else done[j]
-                    if x > t:
-                        t = x
-                c, la = cs[k]
-                end[k] = free[e] = t = t + c[e]
-                done[k] = t + la
-            val += max(done) * m["W"]
-        return val / (1 + len(others))
-
-    state = [seed]
-
-    def rnd():
-        state[0] = (state[0] * 6364136223846793005 + 1442695040888963407) % 2 ** 64
-        return ((state[0] >> 33) + 1) / 2.0 ** 31
-
-    def one(xs):
-        return xs[min(int(rnd() * len(xs)), len(xs) - 1)]
-
-    kin, gin = {}, {}
-    for k, o in enumerate(base):
-        kin.setdefault(o["key"], []).append(k)
-        gin.setdefault(o["grp"], []).append(k)
-    grps, keys = sorted(gin), sorted(k for k in kin if k[0])
-    starts = [[o["pr"] + o.get("boost", 0.0) + s.get(o["grp"], 0.0) for o in base] for s in OPT["START"]]
-    best, short = None, iters // (2 * len(starts)) if len(starts) > 1 else iters + 1
-    for step in range(iters + 1):
-        run, it = divmod(step, short)
-        if run >= len(starts):
-            it, span = step - short * len(starts) + 1, iters - short * len(starts) + 1
-            if it == 1:
-                cur, _, ceo, cp, cb, own, pairs = best
-        elif not it:
-            cp, cb, cur, own, pairs, ceo, span = starts[run], [OPT["BIAS"]] * n, None, 0.0, [], None, short
-        p, b, d = list(cp), cb, 0.0 if it else 1.0
-        if it and (rnd() < 0.3 or not pairs):
-            d = (rnd() * 2 - 1) * 1500
-            for k in gin[one(grps)] if rnd() < 0.3 else kin[one(keys)]:
-                p[k] += d
-        elif it:
-            k, h = one(pairs)
-            wide, y = rnd() < OPT["PK"], rnd()
-            alts = [j for j in (k, h) if "alt" in base[j]]
-            if alts and y < 0.4:
-                j, b = one(alts), list(cb)
-                for i in kin[base[j]["key"]] if wide else [j]:
-                    b[i] = 5000.0 if ceo[j] == "v" else -5000.0
-            else:
-                d = max(p[h] - p[k], 0.0) + 1.0 + 200 * rnd()
-                j, d = (k, d) if y < 0.7 else (h, -d)
-                for i in kin[base[j]["key"]] if wide else [j]:
-                    p[i] += d
-        if d > 0:
-            for k in range(n - 1, -1, -1):
-                for j, _ in succ[k]:
-                    if p[j] > p[k]:
-                        p[k] = p[j]
-        elif d < 0:
-            for k in range(n):
-                x = p[k]
-                for j, _ in succ[k]:
-                    if p[j] > x:
-                        p[j] = x
-        st, eo, val, pp = place(P, p, b)
-        if cur is not None and val > own + 1500.0:
-            continue
-        mine, val = val, judged(st, eo, val)
-        if cur is None or val <= cur - OPT["TEMP"] * max(0.02, 1 - it / span) * math.log(rnd()):
-            cp, cb, cur, own, pairs, ceo = p, b, val, mine, pp, eo
-        if best is None or val < best[0]:
-            best = (val, st, eo, p, b, mine, pp)
-    order = sorted(range(n), key=lambda k: (best[1][k], k))
-    last = {base[k]["gid"]: k for k in order if "gid" in base[k]}
-    for k in order:
-        o = base[k]
-        if "gid" in o:
-            c = o["call"][1]
-            o["call"] = ("mm", c[:-1] + [c[-1][:4] + (last[o["gid"]] == k,)])
-        o["eng"] = best[2][k]
-        if "alt" in o:
-            o["call"], o["cost"] = o["alt"][o["eng"]]
-        for b in o["banks"]:
-            if b in last and base[last[b]]["eng"] != o["eng"]:
-                o["deps"].add(last[b])
-            last[b] = k
-    return base, order, best[0]
 
 
 def place(P, p, bias, back=False):
@@ -1057,9 +853,10 @@ def plan(iters=None, seed=1):
         grps, keys = sorted(gin), sorted(k for k in kin if k[0] or not stage)
         grps += [x for x in grps if x[1] == "loop"] * OPT["LOOP"]
         kof = [kin[base[k]["key"]] for k in act]
-        span = iters // (RO + 1) * (1 if stage else 2)
-        cp, cb, cur, own, pairs, ceo, best = [prio[k] for k in act], [lean[k] for k in act], None, 0.0, [], None, None
-        for it in range(span + 1):
+        span, best = iters // (RO + 1) * (1 if stage else 2) // OPT["RUNS"], None
+        for it in list(range(span)) * OPT["RUNS"]:
+            if not it:
+                cp, cb, cur, own, pairs, ceo = [prio[k] for k in act], [lean[k] for k in act], None, 0.0, [], None
             p, b, d, moved = list(cp), cb, 0.0, []
             if not it:
                 d, moved = 1e-3, list(range(n))

import math
from concourse.mybir import AluOpType as ALU, AxisListType, ActivationFunctionType as AF

NC, PC, CC, RO = 2, 128, 8, 6
B1, B2, B3, XS, MISS = 1028, 2059, 3090, 4112, 21
WIN = [(0, 2), (3, 5), (6, 8), (9, 11), (12, 15)]
SC, CR = 113.0 / 128, 1.5 * 2.0 ** 30
NB, M12 = 19, 1.5 * 2.0 ** 35
KO = [sum(8 * (16 + i) for i in range(t)) for t in range(RO + 1)]
H54 = 2.0 ** 54
FOLD = 41.0 * 2 ** 18

BF, F32, I32, U16 = "bfloat16", "float32", "int32", "uint16"
MAT = "sI nI hI gI qI uI dI K8 C3 MI MN".split()
_S = dict(
    X=(8224, BF), Xh=(NC * XS, BF), Mw=(NC * XS, BF),
    zin=(6 * 256, BF), yzb=(6 * 256, BF), ymb=(4096, BF), m0s=(16, BF), wts=(16, BF),
    MZ=(NC * 5 * PC, BF), NM=(NC * 5 * PC, BF), I2=(256, I32), off=(256, U16), F1=(512, F32),
    I3=(160, I32), I4=(80, I32), ofd=(80, U16), H=(512, BF), b=(512, BF), Cq=(5 * 512, BF), rank=(512, BF), pen=(512, BF),
    mcnt=(8, F32), sc=(256, F32), idx=(16, U16), ds=(256, BF), ms=(256, BF), e1=(256, F32), Ct=(512, F32),
    J1=(48, F32), J2=(16, I32), J3=(32, I32), hl=(32, BF), aD=(432, F32), sD=(48, BF), Wd=(192, BF), Oh=(64, BF),
    Rt=(1024, BF), xo=(16, U16), ai=(8, I32),
    su=(32 * NB, F32), Ku=(16 * NB, F32), rk=(256, BF), Es=(20 * PC, BF), to=(80, U16),
    PA=(7 * 96, F32), AJ=(80, F32), lr=(8, U16), BI=(128, F32), NI=(128, F32),
    pi=(8, I32), col=(40, F32), penb=(8, F32), Gn=(128, F32), Rn=(128, F32), R32=(32, F32),
    ge=(32, F32), eq=(32, F32), Nn=(288, F32), N8=(128, F32), Id=(136, BF), O=(128, BF), E=(144, BF), A=(144, BF), B=(144, BF),
    ub=(16, BF), PL=(256, BF), LT=(128, BF), wf=(8, F32), pw=(16, F32), pc=(32, F32), dl=(128, F32), RB=(16, BF),
    IB=(256, BF), PN=(256, BF), L=(128, BF),
    one=(512, BF), AN=(512, BF), BN=(512, BF), mat=(128 * len(MAT), BF),
    KD=(KO[RO], BF), rm=(2 * 168, BF), t1=(128, BF), t2=(128, BF), Dm=(8 * 128, BF), Ci=(PC, BF), Kx=(PC, BF),
    Kn=(216, BF), Cd=(216, BF), Af=(128, F32), Oa=(128, BF), Ob=(128, BF), MT=(128, BF),
)
SCRATCH = {k: ("sbuf", [128, n], d) for k, (n, d) in _S.items()}
W3 = dict(Hs0=32, Hs1=32, PR=32, OM=16, AH=16, BH=16, Of=16, Lq=16, G=PC, UZ=NB, Cm=NB, RS=128)
for _k, _n in (("Hs0", 8), ("Hs1", 8), ("PR", 8), ("OM", 8), ("AH", 32), ("BH", 32), ("Of", 16), ("Lq", 96),
               ("G", NC * 21), ("UZ", 16), ("Cm", 8), ("RS", 2)):
    SCRATCH[_k] = ("sbuf", [128, _n, W3[_k]], BF)
    _S[_k] = (W3[_k] * _n, BF)
for _b in ("P0", "P1", "P2", "P3", "P4", "P5", "Q0", "Q1"):
    SCRATCH[_b] = ("psum", [128, 512], F32)
NDMA = 16
SEMAPHORES = (["cv", "ca", "cp", "cg", "sent"] + ["d%d" % k for k in range(NDMA)]
              + ["r%d_%d" % (t, c) for t in range(1, RO) for c in range(NC)])

_M = dict(CY=0.87, PCY=0.46, LAT=220.0, RLAT=2800.0, OV=40.0, AO=30.0, GF=1.56, SF=3.8, BW=400.0, R0=2000.0, MINC=0.0, PS=0.0,
          DLAT=1100.0)
MODELS = [_M]
OPT = dict(JUDGE=[dict(_M, MINC=64.0, OV=25.0, RLAT=4000.0, LAT=230.0, BW=240.0, DLAT=2200.0, W=0.95),
                  dict(_M, PS=30.0, AO=50.0, OV=60.0, CY=1.2, PCY=0.66, GF=1.8, SF=5.0, LAT=140.0, W=1.0),
                  dict(_M, MINC=64.0, OV=45.0, CY=0.83, PCY=0.5, LAT=110.0, RLAT=2400.0, BW=400.0, DLAT=1000.0, W=1.5)],
           HB=("P4", "P3"), DA=1, YA=3, HA=0, UA=2, EA=0, QA=(0, 0), BK=("401024", "355435", "1", "1"), KG=((6, 8), (8, 12), (12, 16), (1, 4), (4, 6), (0, 1)),
           MZB=((("P0", 3), ("P1", 2)), (("P5", 4), ("P5", 1))), DB=("P5", "P5"), DY=0, PM=0,
           ORD="uuuuUllllL", DN=4, WO=(4, 0, 1, 2, 3), CUT=(4, 8, 10, 12), GD=128, SP=(3, 4, 4, 2),
           START={(1, "header"): 3000.0, (1, "dyn"): 1000.0},
           BIAS=300.0, TEMP=40.0, PK=0.4, PR=0.4, FB=10, LOOP=3, FAR=600.0, RUNS=2, ITER=50000)


def R(n, a, b, s=1):
    return (n, a, b, s)


def R3(n, g0, g1, a, b, s=1):
    return (n, W3[n] * g0 + a, W3[n] * (g1 - 1) + b, 1, (g0, g1, a, b, s))


def RH(n, a, b, h):
    return (n, a, b, 1, None, 64 * h)


def columns(r):
    if len(r) == 5:
        return [W3[r[0]] * g + c for g in range(r[4][0], r[4][1]) for c in range(*r[4][2:])]
    return range(*r[1:4])


def width(r):
    return len(columns(r))


def two(*rs):
    return all(r[0] in _S and _S[r[0]][1] in (BF, U16) for r in rs)


def build(M):
    CY, PCY, LAT, RLAT, OV, AO, GF, SF, BW = [M[k] for k in ("CY", "PCY", "LAT", "RLAT", "OV", "AO", "GF", "SF", "BW")]
    ops = []
    tag, now = ["set", 0], [0]

    def add(eng, call, rd, wr, cost, lat=LAT, **kw):
        w = wr[0] if wr else ("", 0)
        a = w[1] % 256 if w[0] in ("zin", "yzb") else 0 if w[0] in ("NM", "penb", "MZ", "P0", "P1", "P2") else w[1]
        if w[0] in ("Mw", "Xh") and w[1] % XS < B1:
            a = -1
        if w[0] == "PA":
            a = w[1] % 96
        if w[0][:1] == "Q" and tag[0] == "compare":
            a = min(call[1][0][1][1] % (21 * PC), 16 * PC)
        key = (tag[1], tag[0], call[0], "P0" if w[0] in ("P1", "P2") else w[0], a)
        if eng in "va" and any(r[0] not in _S for r in list(rd) + wr if isinstance(r, tuple)):
            cost += M["PS"]
        ops.append(dict(eng=eng, call=call, rd=[r for r in rd if isinstance(r, tuple)], wr=wr, cost=cost, lat=lat,
                        grp=(tag[1], tag[0]), key=key, step=now[0], **kw))

    def vc(n):
        return OV + max(n, M["MINC"]) * CY

    def ts(o, i, s1, op0, s2=None, op1=None):
        add("v", ("ts", o, i, s1, s2, op0, op1), [i, s1, s2], [o], vc(width(o) * (0.5 if two(o, i) else 1)))

    def tt(o, a, b, op):
        ps = a[0] not in _S or b[0] not in _S
        add("v", ("tt", o, a, b, op), [a, b], [o], vc(width(o) * (1 if ps else 2)))

    def cp(o, i):
        add("v", ("cp", o, i), [i], [o], vc(width(o) * (0.5 if two(o, i) else 1)))

    def ms(o, v):
        add("v", ("ms", o, v), [], [o], vc(width(o) * 0.5))

    def scan(o, d0, d1, init, op0, op1):
        add("v", ("scan", o, d0, d1, init, op0, op1), [d0, d1], [o], vc(width(o)))

    def red(o, i):
        add("v", ("red", o, i), [i], [o], vc(width(i)))

    def act(o, i, f, bias=0.0, scale=1.0, acc=None):
        add("a", ("act", o, i, f, bias, scale, acc), [i, bias, scale], [o] + ([acc] if acc else []), vc(width(o)) + AO)

    def either(fa, fv):
        fa()
        fv()
        v, a = ops.pop(), ops.pop()
        ops.append(dict(a, rd=a["rd"] + v["rd"], alt={"a": (a["call"], a["cost"]), "v": (v["call"], v["cost"])}))

    def gat(o, win, offs, plus=None):
        either(*[lambda e=e: add(e, ("gat", e, o, win, offs, plus), [win, offs, plus], [o], 60 + GF * CY * width(o)) for e in "av"])

    def lin(o, i, scale, bias=0.0):
        either(lambda: act(o, i, AF.Identity, bias=bias, scale=scale), lambda: ts(o, i, scale, ALU.mult, bias, ALU.add))

    def fill(o, v):
        either(lambda: act(o, R("one", 0, width(o)), AF.Identity, bias=v, scale=0.0), lambda: ms(o, v))

    def iota(o, pat, base, cm):
        add("g", ("iota", o, pat, base, cm), [], [o], 130 + 2 * CY * width(o))

    def select(o, i, pat, base, cm, op=ALU.is_equal, fill=0.0):
        add("g", ("sel", o, i, pat, base, cm, op, fill), [i], [o], 170 + 2 * CY * width(o))

    def mm(groups, first=True, last=True, f=1, one=False, parts=None):
        calls = []
        for n, (o, terms) in enumerate(groups):
            for k, tm in enumerate(terms):
                oo = tm[2] if len(tm) > 2 else o
                calls.append((oo, tm[0], tm[1], first and k == 0 and not (one and n),
                              last and k == len(terms) - 1 and not (one and n < len(groups) - 1)))
        n, wr = 1 if parts is None else parts, [o for o, _ in groups]
        for k in range(n):
            some = calls[k * len(calls) // n:(k + 1) * len(calls) // n]
            add("p", ("mm", some), [x for c in some for x in c[1:3]], wr if n == 1 else [R(wr[0][0], 0, 512)],
                (30.0 if n == 1 else 10.0) + sum(max(64, width(c[2])) * PCY * f for c in some))
            ops[-1]["key"] += (k,)

    nd = [0]

    def dma(o, i, rd, wr, nbytes, **kw):
        add("s", ("dma", o, i, nd[0]), rd, wr, max(60.0, nbytes / BW), lat=M["DLAT"], **kw)
        nd[0] += 1

    def full(n):
        return R("mat", 128 * MAT.index(n), 128 * MAT.index(n) + 128) if n in MAT else R(n, 0, 128)

    def wide(n):
        return R(n, 0, 256)

    def c1(n, k):
        return R(n, k, k + 1)

    def view(n, r):
        return R(n, 15 - r, 143 - r)

    ncol = [4]

    def column(src, s1, op0, s2=None, op1=None):
        ncol[0] += 1
        ts(c1("col", ncol[0]), src, s1, op0, s2, op1)
        return c1("col", ncol[0])

    dma(R("m0s", 0, 16), ("m0", 0, 16), [], [R("m0s", 0, 16)], 4096, boost=30000.0)
    dma(R("wts", 0, 2), ("wt", 0, 2), [], [R("wts", 0, 2)], 512, boost=30000.0)
    dma(R("zin", 0, 256), ("z0", 0, 256), [], [R("zin", 0, 256)], 65536, boost=20000.0)
    for k in range(2):
        r = R("X", 32 + 4096 * k, 32 + 4096 * (k + 1))
        dma(r, ("xr", 4096 * k, 4096 * (k + 1)), [], [r], 1 << 20)

    ID = R("Id", 1, 129)
    ms(R("one", 0, 512), 1.0)
    iota(c1("pi", 0), [[0, 1]], 0, 1)
    iota(full("Gn"), [[16, 8], [0, 16]], 0, 0)
    select(R("Id", 0, 129), R("one", 0, 129), [[1, 129]], -1, -1)
    iota(R("R32", 0, 32), [[1, 32]], 0, 0)
    iota(R("Nn", 0, 144), [[1, 144]], -15, 0)
    iota(full("Rn"), [[0, 8], [1, 16]], 0, 0)
    iota(full("N8"), [[PC, 8], [0, 16]], 0, 8)
    for k, v in enumerate((15, 112, 31)):
        ts(c1("pi", 1 + k), c1("pi", 0), v, ALU.bitwise_and)
    cp(R("col", 0, 4), R("pi", 0, 4))
    rc, gc, row = [c1("col", k) for k in range(1, 4)]
    ts(full("O"), full("Gn"), gc, ALU.is_equal)
    ts(R("E", 0, 144), R("Nn", 0, 144), gc, ALU.is_equal)
    cp(R("wf", 0, 2), R("wts", 0, 2))
    mm([(R("P4", 16 * g, 16 * g + 16), [(ID, R("m0s", 0, 16))]) for g in range(8)])
    tt(full("OM"), R("P4", 0, 128), full("O"), ALU.mult)
    for k, n in enumerate("AB"):
        ms(R(n + "H", 0, 512), 0.0)
        lin(R(n, 0, 144), R("E", 0, 144), c1("wf", k))
        lin(full("O" + n.lower()), full("O"), c1("wf", k))
        for h in range(2):
            for b in range(2):
                a = 8 * (2 * h + b)
                lin(R3(n + "H", a, a + 8, 8 * b, 8 * b + 8), R3("OM", 0, 8, 8 * h, 8 * h + 8), c1("wf", k))
    ts(full("dl"), full("Rn"), rc, ALU.is_equal)
    ms(R("pc", 0, 16), 2.0 ** -10)
    ms(R("pc", 16, 32), 0.0)
    scan(R("pw", 0, 16), R("pc", 0, 16), R("pc", 16, 32), 2.0 ** 78, ALU.mult, ALU.add)
    act(R("ub", 0, 16), R("pw", 0, 16), AF.Sqrt)
    ops[-1]["cost"] += 1300.0
    ops[-1]["boost"] = 20000.0
    tt(R("pc", 0, 16), R("ub", 0, 16), R("dl", 0, 16), ALU.mult)
    ncol[0] += 1
    unit = c1("col", ncol[0])
    red(unit, R("pc", 0, 16))
    wc = column(unit, unit, ALU.mult)
    ts(R("RB", 0, 8), R("O", 0, 128, 16), -H54, ALU.mult, H54, ALU.mult)
    ts(R("RB", 8, 16), R("O", 0, 128, 16), wc, ALU.mult)
    mm([(R("P0", 0, 128), [(full("OM"), ID)])])
    lin(full("MT"), R("P0", 0, 128), 1.0)
    select(full("t1"), full("one"), [[-1, 16], [-16, 8]], 0, 1)
    mm([(R("P3", 0, 128), [(full("MT"), full("t1"))])])
    ts(full("RS"), R("P3", 0, 128), -H54, ALU.mult, H54, ALU.mult)
    lin(R("RS", 128, 256), R("P3", 0, 128), wc)
    for n, v in (("sI", SC), ("nI", -SC), ("hI", 0.5), ("gI", -0.5), ("qI", 0.25), ("uI", unit), ("K8", 256.0),
                 ("MI", M12), ("MN", -M12), ("dI", -1.0)):
        lin(full(n), ID, v)
    ops[-1]["boost"] = 20000.0
    magic = column(unit, 1.5 * 2.0 ** 28, ALU.mult)
    nomagic = column(unit, -1.5 * 2.0 ** 28, ALU.mult) if OPT["EA"] else None
    less = column(rc, 14.5, ALU.is_lt, -0.75, ALU.mult)
    ts(R("ge", 0, 32), R("R32", 0, 32), row, ALU.is_le)
    ts(R("eq", 0, 32), R("R32", 0, 32), row, ALU.is_equal)
    live, r0 = c1("ge", 11), c1("eq", 0)
    if OPT["PM"]:
        lin(full("C3"), full("one"), column(column(r0, -4096.0, ALU.mult, c1("eq", 1), ALU.add), -0.125, ALU.mult))
        for n in "AB":
            lin(R(n + "N", 0, 512), R(n + "H", 0, 512), -1.0)
    select(wide("Of"), wide("one"), [[128, 2], [-32, 8], [0, 16]], 0, 1, ALU.is_ge)
    select(wide("Of"), wide("Of"), [[-128, 2], [32, 8], [0, 16]], 31, -1, ALU.is_ge)
    for k in range(6):
        fill(R("Lq", 256 * k, 256 * k + 256), 0.0)
    lowr = column(column(r0, -8.0, ALU.mult, live, ALU.add), c1("ge", 22), ALU.subtract)
    for k, c in enumerate([live] * 4 + [lowr, c1("ge", 22)]):
        a, b = WIN[min(k, 4)]
        lin(R3("Lq", 16 * k, 16 * k + 16, a, b + 1), R3("Of", 0, 16, a, b + 1), c)
    ncol[0] += 1
    step = c1("col", ncol[0])
    red(step, R("eq", 15, 32, 8))
    step = column(step, 1023.0, ALU.mult, live, ALU.add)
    g128 = column(gc, -8.0, ALU.mult)
    lin(wide("IB"), wide("Of"), step)
    base = column(r0, 16.5, ALU.mult, -15.0, ALU.add)
    lin(full("pen"), full("one"), column(r0, 1.5, ALU.mult))
    first = column(row, -16.0, ALU.add, live, ALU.mult)
    select(full("L"), ID, [[1, 128]], -1, -1, ALU.not_equal, 64.0)
    select(full("L"), full("L"), [[1, 128]], 0, -1, ALU.not_equal, -63.0)
    select(full("L"), full("L"), [[0, 4], [1, 32]], -11, 0, ALU.is_ge)
    select(full("t2"), full("one"), [[-32, 4], [0, 32]], 0, 1)
    select(full("t2"), full("t2"), [[1, 128]], 0, -1, ALU.not_equal, -64.0)
    ts(full("PR"), full("t2"), H54, ALU.mult, H54, ALU.mult)
    lin(R("PR", 128, 256), ID, 2.0 ** 78)
    lin(full("Af"), full("one"), c1("eq", 31))
    for ch in range(NC):
        fill(R3("Hs%d" % ch, 0, 8, 0, 16), 0.0)
        fill(R3("Hs%d" % ch, 0, 8, 0, 1), 2.0 ** 78)
    for n, w, k, v in (("Kx", 128, 16, -2.0 ** 22), ("Kn", 216, 9, 1.0)):
        fill(R(n, 0, w), 0.0)
        fill(R(n, 0, w, k), v)
    fill(R("Ku", 0, 16 * NB), 0.0)
    for k, v in ((0, -2.0 ** 22), (16, -2047.5), (17, M12), (18, -M12)):
        fill(R("Ku", k, 16 * NB, NB), v)
    for t in range(RO):
        select(R("KD", KO[t], KO[t + 1]), R("one", 0, 8 * (16 + t)), [[0, 8], [1, 16 + t]], 0, 0, ALU.not_equal)
    fill(R3("UZ", 0, 16, 16, NB), 0.0)
    fill(R3("Cm", 0, 8, 16, NB), -2.0 ** 21)
    lin(R3("Cm", 0, 8, 0, 16), full("dl"), 2.0 ** 21, -2.0 ** 21)
    tt(full("Ci"), full("N8"), R3("Cm", 0, 8, 0, 16), ALU.add)
    iota(R("PA", 0, 96), [[1, 6], [0, 2], [PC, 8]], B1, 8)
    for t in range(1, RO):
        iota(R("PA", 96 * t, 96 * t + 16), [[0, 2], [PC, 8]], 5 - t, 8)
    ts(R("lr", 0, 6), R("one", 0, 6), column(rc, 16.0, ALU.mult, 15.0, ALU.add), ALU.mult)
    lin(full("BI"), ID, 8192.0)
    lin(full("NI"), ID, -8192.0)
    iota(R("Nn", 144, 288), [[0, 16], [2, 9]], -2, 0)
    ts(R("Cd", 0, 144), R("Nn", 144, 288), column(column(gc, 64.0, ALU.is_ge, -1.0, ALU.mult), rc, ALU.add), ALU.is_ge, 16384.0, ALU.mult)
    fill(R("Cd", 144, 216), 0.0)
    for h in range(2):
        fill(R("Wd", 128 * h, 128 * h + 64), 0.0)
        lin(RH("Wd", 64, 128, h), RH("Id", 1 + 64 * h, 65 + 64 * h, h), 1.0)
        lin(RH("Oh", 0, 64, h), RH("O", 64 * h, 64 * h + 64, h), 1.0)
    for r in range(16):
        lin(R("Rt", 64 * r, 64 * r + 64), R("Oh", 0, 64), c1("dl", r))
    spare = rc, column(rc, 16.0, ALU.add)
    for v in (64, -64):
        select(full("dI"), full("dI"), [[1, 128]], v, -1, ALU.not_equal, -1.0)
    for r in range(8):
        d = R("Dm", 128 * r, 128 * r + 128)
        for h in range(2):
            select(d, d if h else full("dI"), [[-1, 2], [1, 64]], 64 * h - 1 - 2 * r, -1, ALU.not_equal, 1.0)
    a = XS * (NC - 1)
    for h in range(2):
        n, o = 8, a + (B1, B2)[h]
        cp(R("Mw", o, o + 8), R("m0s", 8 * h, 8 * h + 8))
        while n < 8 * PC:
            if n < OPT["GD"]:
                lin(R("Mw", o + n, o + 2 * n), R("Mw", o, o + n), 1.0)
            else:
                select(R("Mw", o + n, o + 2 * n), R("Mw", o, o + n), [[0, n]], 0, 0)
            n *= 2
        dma(R("Mw", o - a, o - a + n), R("Mw", o, o + n), [R("Mw", o, o + n)], [R("Mw", o - a - 8, o - a + n + 8)], 256 * n)
    for ch in range(NC):
        fill(R("Mw", XS * ch + B3, XS * ch + B3 + 8 * PC - 7, 8), 0.0)

    def penalty(ch, t):
        o, i, c = R("pen", 256 * ch, 256 * ch + 256), R("rank", 256 * ch, 256 * ch + 256), c1("penb", t % 2)
        either(lambda: act(o, i, AF.Relu, bias=c), lambda: ts(o, i, c, ALU.add, 0.0, ALU.max))

    def hashed(src, up, i1, a1, i2, a2):
        n = width(up)
        uv, u, v, x = R(i1, a1, a1 + 2 * n), R(i1, a1, a1 + n), R(i1, a1 + n, a1 + 2 * n), R(i2, a2, a2 + n)
        if _S[i1][1] == F32:
            act(uv, src, AF.Identity, bias=2.0 ** 23 - 0.5, scale=2.0 ** -12 + 2.0 ** -34)
            act(uv, uv, AF.Relu, bias=-2.0 ** 35, scale=4096.0)
            vp = R(src[0], src[1] + n, src[2])
            tt(u, up, u, ALU.subtract)
            tt(vp, vp, v, ALU.subtract)
            lin(v, u, 1184.0, -FOLD)
            tt(vp, vp, u, ALU.mult)
            tt(x, vp, v, ALU.add)
        else:
            cp(uv, src)
            ts(uv, uv, 4095, ALU.bitwise_and)
            ts(up, u, 1184.0, ALU.mult, -FOLD, ALU.add)
            tt(x, u, v, ALU.mult)
            tt(x, x, up, ALU.add)
        return x

    def place_list(o, x):
        ts(x, x, 5, ALU.arith_shift_right, 8191, ALU.bitwise_and)
        cp(o, x)

    rot = [0]

    def dbank():
        rot[0] = (rot[0] + 1) % 3
        return "P%d" % rot[0]

    Xg = R("X", 32, 8224)
    for t in range(RO):
        now[0] = t
        nb = [10, 10]
        blocks = []
        for x in OPT["ORD"]:
            ch = int(x in "uU")
            blocks += [(14, ch), (15, ch)] if x in "UL" else [(nb[ch], ch)]
            nb[ch] += x in "ul"
        for part, ch in [(0, 1), (0, 0), (1, 1), (1, 0)] + blocks + [(2, 1), (2, 0)]:
            z = R("zin", 256 * t + PC * ch, 256 * t + PC * ch + PC)
            xb, gb, mb, wb, pb = XS * ch, 21 * PC * ch, 5 * PC * ch, 256 * ch, PC * ch
            Q, Hs, hb = "Q%d" % ch, "Hs%d" % ch, OPT["HB"][ch]

            def slot(n, s):
                a = xb + ((B1, B2)[s // 8] + s % 8 if s < 16 else B3 if s == MISS else 20 - s)
                return R(n, a, a + 8 * PC - 7, 8)

            def half(n, k, base=wb):
                return R(n, base + k * PC, base + k * PC + PC)

            def both(n, base=wb):
                return R(n, base, base + 2 * PC)

            def pt(n):
                return R(n, pb, pb + PC)

            def mr(kind, a, n=PC):
                return R("P" + OPT["BK"][ch][kind], a, a + n)

            if not part:
                tag[:] = "mz", ch + 1
                zb, a = t * PC * ch, 0
                for bk, n in OPT["MZB"][ch]:
                    ks = list(range(a, min(a + n, t)))
                    if ks:
                        mm([(R(bk, (k - a) * PC, (1 + k - a) * PC), [(ID, z), (full("K8"), slot("Mw", 16 + k))]) for k in ks],
                           parts=min(OPT["SP"][3], len(ks)))
                        act(R("MZ", zb + a * PC, zb + (ks[-1] + 1) * PC), R(bk, 0, len(ks) * PC), AF.Relu, bias=-256.0)
                    a += n
                tag[0] = "hash"

                def sums(sign):
                    return [(R(hb, k * PC + 64 * h, k * PC + 64 * h + 64),
                             [(R("AB"[k] + sign, 128 * (2 * h + b), 128 * (2 * h + b + 1)), R(z[0], z[1] + b, z[2], 2)) for b in range(2)])
                            for k in range(2) for h in range(2)]

                if OPT["PM"] >> ch & 1 and t:
                    uv = R(hb, 0, 2 * PC)
                    mm([(uv, [(full("C3"), wide("one"))])], last=False)
                    ops[-1]["wr"] = [R(hb, 0, 512)]
                    mm(sums("N") + [(uv, [(full("MN"), wide("one")), (full("MI"), wide("one"))])] + sums("H"), first=False, one=True,
                       parts=OPT["SP"][1])
                    ops[-1]["wr"] = [R(hb, 0, 512)]
                    u, w, vp = half("F1", 0), half("F1", 1), R(hb, PC, 2 * PC)
                    lin(u, R(hb, 0, PC), 1.0)
                    lin(w, u, 1184.0, -FOLD)
                    tt(vp, vp, u, ALU.mult)
                    tt(pt("I2"), vp, w, ALU.add)
                    place_list(pt("off"), pt("I2"))
                else:
                    mm(sums("H"))
                    place_list(pt("off"), hashed(R(hb, 0, 2 * PC), R(hb, 0, PC), "F1", wb, "I2", pb))
                if t and (OPT["DY"] or not ch):
                    tag[0], n, hb = "dyn", (1 if OPT["DY"] else 2) * t * CC, OPT["DB"][ch]
                    a = n * ch
                    for k, m in enumerate("AB"):
                        mm([(R(hb, 2 * PC + k * n, 2 * PC + k * n + n), [(view(m, r), R("MZ", 16 * a + r, 16 * (a + n), 16)) for r in range(16)])],
                           parts=OPT["SP"][2])
                    place_list(R("ofd", a, a + n), hashed(R(hb, 2 * PC, 2 * PC + 2 * n), R(hb, 2 * PC, 2 * PC + n), "I3", 2 * a, "I4", a))
                continue
            c0, W = 16 - t, 16 + t
            tag[:] = "gather", ch + 1
            if part == 1:
                mm([(R(Q, (8 * k + 4 * h) * W, (8 * k + 4 * h + 4) * W), [(half("pen", h) if t else full("pen"), R3("PR", 4 * k, 4 * k + 4, c0, 32))])
                    for h in range(2) for k in range(2)], last=False, one=True)
                ops[-1]["wr"] = [R(Q, 0, 512)]
                for h in range(2):
                    for k in range(2):
                        a = xb + (B1, B2)[h] + 512 * k
                        gat(R("Xh", a, a + 512), Xg, R("off", pb + 64 * h + 32 * k, pb + 64 * h + 32 * (k + 1)))
                for k in range(t):
                    gat(slot("Xh", 16 + k), Xg, R("ofd", CC * (t * ch + k), CC * (t * ch + k + 1)))
                continue
            tag[0] = "compare"

            def count(ss):
                mm([(R(Q, t + s if s < 16 else t + 15 - s, 16 * W, W),
                     [(R("G", gb + s * PC, gb + s * PC + PC), R3("RS", 0, 2, 8 * s, 8 * s + 8) if s < 16 else R("RB", 0, 16))])
                    for s in ss], first=False, last=False, one=True)
                ops[-1]["gid"] = (t, ch)

            def differ(gg, parts, free):
                dd = R(bk, 0, width(gg))
                if free and OPT["DA"] >> ch & 1:
                    mm([(o, [(full("nI"), zz)]) for o, _, zz in parts], last=False, one=True)
                    ops[-1]["wr"] = [R(bk, 0, 512)]
                    mm([(o, [(full("sI"), x)]) for o, x, _ in parts], first=False, one=True)
                    ops[-1]["wr"] = [R(bk, 0, 512)]
                    act(dd, dd, AF.Abs)
                    tt(gg, dd, free, ALU.is_gt)
                    return
                mm(([(dd, [(full("MI"), free)])] if free else []) + [(o, [(full("nI"), zz)]) for o, _, zz in parts], last=False, one=True, parts=2)
                mm([(o, [(full("sI"), x)]) for o, x, _ in parts] + ([(dd, [(full("MN"), free)])] if free else []), first=False, one=True,
                   parts=2 if free else 1)
                ops[-1]["wr"] = [R(bk, 0, 512)]
                ts(gg, dd, CR, ALU.add, CR, ALU.not_equal)

            if part >= 14:
                n = OPT["DN"] if t > 4 else 4
                bl = range(16, 16 + min(t, n)) if part == 14 else range(16 + n, 16 + t)
                if bl:
                    bk, n, g0, a = dbank(), len(bl) * PC, gb + bl[0] * PC, mb + (bl[0] - 16) * PC
                    differ(R("G", g0, g0 + n), [(R(bk, j * PC, j * PC + PC), slot("Xh", s), z) for j, s in enumerate(bl)], R("NM", a, a + n))
                    count(bl)
                continue
            if part >= 10:
                h, k = divmod(part - 10, 2)
                bk, a = dbank(), xb + (B1, B2)[h] + 512 * k
                differ(R3("G", 21 * ch + 8 * h, 21 * ch + 8 * h + 8, 64 * k, 64 * k + 64),
                       [(R(bk, 64 * s, 64 * s + 64), R("Xh", a + s, a + 512, 8), R("zin", z[1] + 64 * k, z[1] + 64 * k + 64))
                        for s in range(8)], None)
                if k:
                    count(range(8 * h, 8 * h + 8))
                continue
            tag[0] = "miss"
            mm([(mr(0, 0), [(full("qI"), full("one")), (full("hI"), z), (full("gI"), slot("Xh", 15 + t if t else 0))])])
            if OPT["YA"] >> ch & 1:
                act(mr(0, 0), mr(0, 0), AF.Identity, bias=1.5 * 2.0 ** 23)
                act(slot("Xh", MISS), mr(0, 0), AF.Identity, bias=-1.5 * 2.0 ** 23)
            else:
                ts(slot("Xh", MISS), mr(0, 0), 1.5 * 2.0 ** 23, ALU.add, 1.5 * 2.0 ** 23, ALU.subtract)
            tag[0] = "match"
            rm = R("rm", 168 * ch, 168 * ch + 8 * W)
            scan(rm, R("KD", KO[t], KO[t + 1]), R(Q, 0, 8 * W), 0.0, ALU.mult, ALU.max)
            tt(R3(Hs, 0, 8, c0, 32), R(Q, 8 * W, 16 * W), rm, ALU.max)
            mm([(R(Q, PC * h, PC * h + PC), [(R(Hs, PC * h, PC * h + PC), ID)]) for h in range(2)])
            act(both("b"), R(Q, 0, 256), AF.Relu, bias=1.0, scale=-2.0 ** -106, acc=c1("mcnt", ch))
            act(both("H"), R(Q, 0, 256), AF.Sqrt)
            mm([(mr(1, PC), [(ID, full("Ci"))])], last=False)
            ops[-1]["wr"] = [mr(1, 0, 512)]
            mm([(mr(1, PC), [(half("IB", h, 0), half("b", h)) for h in range(2)])], first=False)
            ops[-1]["wr"] = [mr(1, 0, 512)]
            scan(pt("sc"), R("Kx", 0, PC), mr(1, PC), 0.0, ALU.add, ALU.max)
            ix = R("idx", CC * ch, CC * ch + CC)
            ts(ix, R("sc", pb + 15, pb + PC, 16), g128, ALU.add)
            gat(pt("ms"), R("Mw", xb, xb + XS), ix, less)
            tag[0] = "header"
            win = R("Xh", xb, xb + XS)
            new = R("yzb", 256 * t + pb, 256 * t + pb + PC)
            if OPT["HA"] >> ch & 1:
                gat(pt("ds"), win, ix)
                mm([(mr(5, 3 * PC), [(full("gI"), z), (full("hI"), pt("ds"))])])
                act(new, mr(5, 3 * PC), AF.Abs, scale=2.0)
            else:
                add("v", ("gtt", pt("ds"), win, ix, z, ALU.subtract), [win, ix, z], [pt("ds")], 60 + GF * CY * PC)
                act(new, pt("ds"), AF.Abs)
            if t < RO - 1:
                zn = R("zin", 256 * (t + 1) + pb, 256 * (t + 1) + pb + PC)
                add("g", ("send", zn, new, "r%d_%d" % (t + 1, ch)), [new], [zn], 300.0, lat=RLAT + (0 if t else M["R0"]))
            tag[0] = "mask"
            terms = []
            for q in OPT["WO"]:
                a, b = WIN[q]
                cb = 512 * q + wb
                lo = 2.0 ** (34 - 5 * (b + 1)) if b < 15 else 0.0
                hi = 2.0 ** (34 - 5 * (a - 1))
                if OPT["QA"][ch] >> q & 1:
                    act(both("Ct"), both("H"), AF.Relu, bias=hi, scale=-1.0)
                    act(both("Cq", cb), both("Ct"), AF.Relu, bias=hi - lo, scale=-1.0)
                else:
                    ts(both("Cq", cb), both("H"), hi, ALU.min, lo, ALU.max)
                terms += [(half("Lq", h, 256 * k), half("Cq", h, cb)) for k in ([q] if q < 4 else [4, 5]) for h in range(2)]
            xx = R(Q, 2 * PC, 3 * PC)
            terms.append((full("uI"), pt("ms")))
            cuts = [0] + list(OPT["CUT"]) + [len(terms)]
            for a, b in zip(cuts, cuts[1:]):
                mm([(xx, terms[a:b])], first=not a, last=b == len(terms))
                if not a:
                    ops[-1]["rd"].append(both("b"))
            if OPT["EA"] >> ch & 1:
                act(pt("e1"), xx, AF.Identity, bias=magic)
                act(pt("e1"), pt("e1"), AF.Identity, bias=nomagic)
            else:
                ts(pt("e1"), xx, magic, ALU.add, magic, ALU.subtract)
            U = slot("Mw", 16 + t) if t < RO - 1 else R("ymb", pb, pb + PC)
            tt(U, xx, pt("e1"), ALU.is_gt)
            tag[0] = "rank"
            if t == RO - 1:
                mm([(mr(2, 0), [(half("PN", h, 0), half("rank", h)) for h in range(2)] + [(half("PL", h, 0), half("b", h)) for h in range(2)])])
                lin(pt("rk"), mr(2, 0), 1.0)
            else:
                sp = mr(2, 2 * PC, 2 * PC)
                mm([(sp, [(full("L"), both("b"))] + ([(ID, both("rank"))] if t else []))])
                lin(both("rank"), sp, 1.0, 0.0 if t else first)
                lin(R("NM", mb + t * PC, mb + t * PC + PC), U, *((-236.0, 300.0) if OPT["DA"] >> ch & 1 else (-1.0, 1.0)))
                tag[0] = "name"
                zs, n = mr(3, 3 * PC), 8 * NB
                if OPT["UA"] >> ch & 1:
                    mm([(zs, [(ID, z), (full("K8"), U)])])
                    act(R3("UZ", 8 * ch, 8 * ch + 8, 0, 16), zs, AF.Relu, bias=-256.0)
                else:
                    mm([(zs, [(ID, z)])])
                    tt(R3("UZ", 8 * ch, 8 * ch + 8, 0, 16), U, zs, ALU.mult)
                jb, uz = 2 * CC * ch, R("UZ", n * ch, n * ch + n)
                mm([(mr(4, k * n, n), [(ID, R("Cm", 0, n))]) for k in range(2)], last=False, one=True)
                ops[-1]["wr"] = [mr(4, 0, 512)]
                mm([(mr(4, k * n, n), [(full(m), uz)]) for k, m in enumerate(("Oa", "Ob"))], first=False, one=True)
                ops[-1]["wr"] = [mr(4, 0, 512)]
                sb, j1 = 2 * n * ch, 3 * CC * ch
                scan(R("su", sb, sb + 2 * n), R("Ku", 0, 2 * n), mr(4, 0, 2 * n), 0.0, ALU.add, ALU.max)
                tt(R("J1", j1, j1 + 2 * CC), R("su", sb + 15, sb + 2 * n, NB), R("su", sb + 18, sb + 2 * n, NB), ALU.subtract)
                u, v, w = [R("J1", j1 + k * CC, j1 + k * CC + CC) for k in range(3)]
                x = R("J2", CC * ch, CC * ch + CC)
                lin(w, u, 1184.0, -FOLD)
                tt(v, u, v, ALU.mult)
                tt(x, v, w, ALU.add)
                for h in range(2):
                    for k, bits in enumerate((8128, 63)):
                        ts(RH("J3", jb + CC * h, jb + CC * h + CC, k), RH(x[0], x[1], x[2], h), 5, ALU.arith_shift_right, bits, ALU.bitwise_and)
                hl, dd, db = R("hl", jb, jb + 2 * CC), R(Q, 2 * PC, 2 * PC + 216), 216 * ch
                cp(hl, R("J3", jb, jb + 2 * CC))
                mm([(dd, [(ID, R("Cd", 0, 216))])], last=False)
                mm([(dd, [(R("Dm", 128 * r, 128 * r + 128), hl, R(Q, 2 * PC + 1 + r, 2 * PC + 144, 9)) for r in range(8)]
                     + [(m, R("hl", jb + k, jb + 2 * CC, 2), R(Q, 2 * PC + 145 + r, 2 * PC + 216, 9))
                        for r in range(8) for k, m in enumerate((R("Rt", 128 * r, 128 * r + 128), full("dI")))])], first=False, parts=OPT["SP"][0])
                scan(R("aD", db, db + 216), dd, R("Kn", 0, 216), 0.0, ALU.mult, ALU.add)
                db = 24 * ch
                ts(R("sD", db, db + 24), R("aD", 9 * db + 8, 9 * db + 216, 9), 0.0, ALU.not_equal, 16384.0, ALU.mult)
                own, wd = R(Q, 0, CC), [R("Wd", 64 - 64 * h, 192 - 64 * h) for h in range(2)]
                mm([(own, [(wd[h], R("hl", jb + CC * h, jb + CC * h + CC)) for h in range(2)])], last=False)
                ops[-1]["wr"] = [R(Q, 0, 512)]
                mm([(own, [(wd[h], R("sD", db + 8 * h, db + 8 * h + 8)) for h in range(2)]
                     + [(wd[h], R("sD", db + 16 + 4 * h, db + 20 + 4 * h), R(Q, 1, CC, 2)) for h in range(2)])], first=False)
                for k in range(2):
                    ts(R("xo", CC * ch + k, CC * ch + CC, 2), R(Q, k, CC, 2), 32.0 - 32768.0 * (k + 1), ALU.add, spare[k], ALU.max)
        tag[:] = "first", 3
        old, low, pe = R("PA", 96 * t + 16, 96 * t + 96), R("PA", 96 * t, 96 * t + 80), R("P" + OPT["BK"][3], 384, 464)
        gat(R("AJ", 0, 80), wide("sc"), R("lr", 0, 5))
        mm([(pe, [(full("BI"), old), (full("NI"), R("AJ", 0, 80))])], f=4)
        tt(pe, pe, low, ALU.max)
        tt(R("PA", 96 * t + 112, 96 * t + 192), pe, old, ALU.min)
        tag[:] = "rank", 3
        if t == RO - 1:
            r = R("yzb", 256 * t, 256 * t + 256)
            dma(("yz", 256 * t, 256 * t + 256), r, [r], [], 65536)
            break
        if t == 2:
            tag[0] = "last"
            select(wide("PN"), wide("one"), [[-128, 2], [32, 8], [1, 16]], 16, -1)
            mm([(R("P0", 256, 384), [(full("L"), ID)])])
            lin(full("LT"), R("P0", 256, 384), 1.0)
            mm([(R("P0", 256, 512), [(full("LT"), wide("PN"))])])
            lin(wide("PL"), R("P0", 256, 512), 1.0)
            tag[0] = "rank"
        pa = R("P" + OPT["BK"][2], 511, 512)
        mm([(pa, [(full("Af"), c1("mcnt", ch)) for ch in range(NC)])], f=4)
        cp(c1("ai", 0), pa)
        ts(c1("ai", 0), c1("ai", 0), 1, ALU.bitwise_and)
        ts(c1("penb", (t + 1) % 2), c1("ai", 0), r0, ALU.mult, base, ALU.add)
        for ch in range(NC - 1, -1, -1):
            penalty(ch, t + 1)
        for c in range(7, -1, -1):
            tag[:] = "write", 1 + c // 4
            zz, xo = R("zin", 256 * t + 32 * c, 256 * t + 32 * c + 32), R("xo", 2 * c, 2 * c + 2)
            add("v", ("sca", R("X", 0, 8224), xo, zz), [zz, xo], [R("X", 0, 8224)], 50 + 32 * SF * CY)
        if t == RO - 2:
            r = R("yzb", 0, 256 * t + 256)
            dma(("yz", 0, 256 * t + 256), r, [r, Xg], [], 65536 * (t + 1))

    tag[:] = "end", 10
    ts(R("to", 0, 80), R("PA", 96 * RO + 16, 96 * RO + 96), g128, ALU.add)
    for k in range(1, 6):
        for ch in range(NC):
            a = 16 * (k - 1) + CC * ch
            gat(R("ymb", 256 * k + PC * ch, 256 * k + PC * ch + PC), R("Mw", XS * ch, XS * ch + XS), R("to", a, a + CC))
    tag[1] = 12
    for k in range(6, 16, 2):
        for j in range(k, k + 2):
            ts(R("Es", 256 * (j - 6), 256 * (j - 5)), wide("rk"), float(j), ALU.is_equal)
        pp = R(("P3", "P4", "P5")[k // 2 % 3], 0, 512)
        mm([(pp, [(full("MT"), R("Es", 256 * (k - 6), 256 * (k - 4)))])])
        lin(R("ymb", 256 * k, 256 * k + 512), pp, 1.0)
    for a, b in OPT["KG"]:
        r = R("ymb", 256 * a, 256 * b)
        dma(("ym", 256 * a, 256 * b), r, [r], [], 65536 * (b - a))
    return ops


def depend(ops):
    n = len(ops)
    hist = {}
    for k, o in enumerate(ops):
        deps = set()
        use = [(r[0], sum((1 + r[5] // 64 if len(r) == 6 else 3) << 2 * c for c in columns(r)), w) for rs, w in ((o["rd"], False), (o["wr"], True)) for r in rs]
        for name, m, w in use:
            deps.update(j for j, mm, ww in hist.get(name, []) if (w or ww) and m & mm)
        for name, m, w in use:
            h = hist.setdefault(name, [])
            if w:
                h[:] = [x for x in h if x[1] & ~m]
            h.append((k, m, w))
        o["deps"] = deps
        o["banks"] = set(r[0] for r in o["rd"] + o["wr"] if r[0] not in _S)
    succ = [[] for _ in ops]
    for k, o in enumerate(ops):
        for j in o["deps"]:
            succ[j].append(k)
    pr = [0.0] * n
    for k in range(n - 1, -1, -1):
        pr[k] = ops[k]["cost"] + ops[k]["lat"] + max([pr[j] for j in succ[k]] + [0.0])
        ops[k]["pr"], ops[k]["succ"] = pr[k], succ[k]


def inline(p, o):
    return p["eng"] == o["eng"] == "p"


def prices(ops):
    return [({e: c for e, (_, c) in o["alt"].items()} if "alt" in o else {o["eng"]: o["cost"]}, o["lat"]) for o in ops]


def place(P, p, bias, back=False):
    succ, cost, lat, banks, at0, tail, free0, bank0 = P
    n = len(cost)
    at, by, held, st, eo = list(at0), [-1] * n, [-1] * n, [0.0] * n, [""] * n
    qs = {e: ([-1e9], [free0[e]], [-1]) for e in "vapgs"}
    bk = {b: ([-1e9], [x], [e], [-1]) for b, (x, e) in bank0.items()}
    end, last = 0.0, 0
    for _, k in sorted(zip(p, range(n)), reverse=True):
        best, bs = 1e18, banks[k]
        l0, l1 = (lat[k], 0.0) if back else (0.0, lat[k])
        for e, c in cost[k]:
            t, h = at[k], -1
            ss, ee, who = qs[e]
            m = i = len(ss)
            while i and ee[i - 1] > t:
                i -= 1
            moved = True
            while moved:
                while i < m and ss[i] < t + c:
                    if ee[i] > t:
                        t, h = ee[i], who[i]
                    i += 1
                moved = False
                for b in bs:
                    s0, e0, en, w0 = bk[b]
                    j, x, y = len(s0) - 1, t + c + l1, t - 2500.0
                    while s0[j] >= x:
                        j -= 1
                    while j >= 0:
                        if e0[j] > t - l0 + 1e-6 and en[j] != e:
                            t, moved, h = e0[j] + l0, True, w0[j]
                            break
                        if s0[j] < y:
                            break
                        j -= 1
                while moved and i < m and ee[i] <= t:
                    i += 1
            v = t + c + bias[k] if e == "v" else t + c
            if v < best:
                best, bt, bc, be, bi, bh = v, t, c, e, i, h
        held[k], st[k], eo[k] = bh, bt, be
        x = bt + bc
        ss, ee, who = qs[be]
        ss.insert(bi, bt)
        ee.insert(bi, x)
        who.insert(bi, k)
        y = x + l1
        for b in bs:
            s0, e0, en, w0 = bk[b]
            j = len(s0)
            while s0[j - 1] > bt - l0:
                j -= 1
            s0.insert(j, bt - l0)
            e0.insert(j, y)
            en.insert(j, be)
            w0.insert(j, k)
        if y + tail[k] > end:
            end, last = y + tail[k], k
        for j, d in succ[k]:
            if x + d > at[j]:
                at[j], by[j] = x + d, k
    pairs = []
    while last >= 0:
        if held[last] >= 0:
            pairs.append((last, held[last]))
        last = held[last] if held[last] >= 0 else by[last]
    return st, eo, end, pairs


def plan(iters=None, seed=1):
    base = build(MODELS[0])
    depend(base)
    N, iters = len(base), OPT["ITER"] if iters is None else iters
    above, pre, succ = [0] * N, [], [[] for _ in base]
    for k, o in enumerate(base):
        for j in o["deps"]:
            above[k] |= above[j]
        pre.append([(j, inline(base[j], o)) for j in sorted(o["deps"]) if not above[k] >> j & 1])
        for j, pp in pre[k]:
            succ[j].append((k, pp))
        for j in o["deps"]:
            above[k] |= 1 << j
    models = [prices(base)] + [prices(build(m)) for m in OPT["JUDGE"]]
    weight = [1.0] + [m["W"] for m in OPT["JUDGE"]]
    rest = []
    for cs in models:
        r = [0.0] * N
        for k in range(N - 1, -1, -1):
            c, la = min(cs[k][0].values()), cs[k][1]
            r[k] = c + max([la] + [r[j] + (0.0 if pp else la) for j, pp in succ[k]])
        rest.append(r)
    state = [seed]

    def rnd():
        state[0] = (state[0] * 6364136223846793005 + 1442695040888963407) % 2 ** 64
        return ((state[0] >> 33) + 1) / 2.0 ** 31

    def one(xs):
        return xs[min(int(rnd() * len(xs)), len(xs) - 1)]

    banks = [sorted(o["banks"]) for o in base]
    order, engine, fixed = [], [None] * N, [False] * N
    free = [dict.fromkeys("vapgs", 0.0) for _ in models]
    ends, dones = [[0.0] * N for _ in models], [[0.0] * N for _ in models]
    user = {b: -1 for bs in banks for b in bs}
    prio = [rest[0][k] + o.get("boost", 0.0) + OPT["START"].get(o["grp"], 0.0) for k, o in enumerate(base)]
    lean = [OPT["BIAS"]] * N
    for stage in range(RO):
        act = [k for k in range(N) if not fixed[k] and base[k]["step"] <= stage + 1]
        loc = {k: i for i, k in enumerate(act)}
        n = len(act)
        lc = [[cs[k] for k in act] for cs in models]
        lat = [la for _, la in lc[0]]
        ls = [[(loc[j], 0.0 if pp else lat[i]) for j, pp in succ[k] if j in loc] for i, k in enumerate(act)]
        lp = [[(loc[j], pp) for j, pp in pre[k] if j in loc] for k in act]
        at0 = [[max([0.0] + [en[j] if pp else do[j] for j, pp in pre[k] if fixed[j]]) for k in act] for en, do in zip(ends, dones)]
        tail = [[max([0.0] + [r[j] - (cs[k][1] if pp else 0.0) for j, pp in succ[k] if j not in loc]) for k in act]
                for r, cs in zip(rest, models)]
        lb = [banks[k] for k in act]
        P = (ls, [list(c.items()) for c, _ in lc[0]], lat, lb, at0[0], tail[0], free[0],
             {b: (dones[0][j], engine[j]) if j >= 0 else (0.0, "") for b, j in user.items()})
        rp = [[(j, 0.0 if pp else lat[j]) for j, pp in lp[k]] for k in range(n)]
        late = [lat[k] + tail[0][k] for k in range(n)], [0.0] * n, dict.fromkeys("vapgs", 0.0), dict.fromkeys(user, (-1e8, ""))

        def judged(st, eo, val):
            seq, last, wait, out = [k for _, k in sorted(zip(st, range(n)))], {}, [None] * n, [None] * n
            for k in seq if len(models) > 1 else []:
                w = lp[k]
                for b in lb[k]:
                    if b not in last:
                        if user[b] >= 0 and engine[user[b]] != eo[k]:
                            out[k] = (out[k] or []) + [user[b]]
                    elif eo[last[b]] != eo[k]:
                        w = w + [(last[b], False)]
                    last[b] = k
                wait[k] = w
            for m in range(1, len(models)):
                fr, end, done, cs, a0, tl, top = dict(free[m]), [0.0] * n, [0.0] * n, lc[m], at0[m], tail[m], 0.0
                for k in seq:
                    e = eo[k]
                    t = fr[e]
                    if a0[k] > t:
                        t = a0[k]
                    for j, pp in wait[k]:
                        x = end[j] if pp else done[j]
                        if x > t:
                            t = x
                    if out[k]:
                        t = max([t] + [dones[m][j] for j in out[k]])
                    c, la = cs[k]
                    end[k] = fr[e] = t = t + c[e]
                    done[k] = t = t + la
                    if t + tl[k] > top:
                        top = t + tl[k]
                val += top * weight[m]
            return val / len(models)

        kin, gin = {}, {}
        for i, k in enumerate(act):
            kin.setdefault(base[k]["key"], []).append(i)
            gin.setdefault(base[k]["grp"] + (base[k]["step"],), []).append(i)
            ch, name = base[k]["grp"]
            if name in ("miss", "header", "mz", "hash", "dyn"):
                for c in ((ch, 4) if OPT["LOOP"] else ()):
                    gin.setdefault((c, "loop", base[k]["step"] + (name in ("miss", "header"))), []).append(i)
        grps, keys = sorted(gin), sorted(k for k in kin if k[0] or not stage)
        grps += [x for x in grps if x[1] == "loop"] * OPT["LOOP"]
        kof = [kin[base[k]["key"]] for k in act]
        span, best = iters // (RO + 1) * (1 if stage else 2) // OPT["RUNS"], None
        for it in list(range(span)) * OPT["RUNS"]:
            if not it:
                cp, cb, cur, own, pairs, ceo = [prio[k] for k in act], [lean[k] for k in act], None, 0.0, [], None
            p, b, d, moved = list(cp), cb, 0.0, []
            if not it:
                d, moved = 1e-3, list(range(n))
            elif rnd() < OPT["PR"] or not pairs:
                d, x = (rnd() * 2 - 1) * 1500, rnd()
                moved = gin[one(grps)] if x < 0.3 else kin[one(keys)] if x < 0.7 else [one(kin[one(keys)])]
            else:
                k, h = one(pairs)
                wide, y = rnd() < OPT["PK"], rnd()
                alts = [j for j in (k, h) if len(P[1][j]) > 1]
                if alts and y < 0.4:
                    j, b = one(alts), list(cb)
                    for i in kof[j] if wide else [j]:
                        b[i] = 5000.0 if ceo[j] == "v" else -5000.0
                else:
                    d = max(p[h] - p[k], 0.0) + 1.0 + 200 * rnd()
                    j, d = (k, d) if y < 0.7 else (h, -d)
                    moved = kof[j] if wide else [j]
            for i in moved:
                p[i] += d
            todo = list(moved)
            while todo:
                k = todo.pop()
                x = p[k]
                for j, _ in (lp if d > 0 else ls)[k]:
                    if (p[j] <= x) if d > 0 else (p[j] >= x):
                        p[j] = x + (1e-3 if d > 0 else -1e-3)
                        todo.append(j)
            st, eo, val, pp = place(P, p, b)
            if it % OPT["FB"] == 0:
                fix = [[x for x in P[1][k] if x[0] == eo[k]] for k in range(n)]
                rs = place((rp, fix, lat, lb) + late, [st[k] + fix[k][0][1] + 1e-6 * k for k in range(n)], b, True)[0]
                q = [rs[k] + fix[k][0][1] - 1e-6 * k for k in range(n)]
                again = place(P, q, b)
                if again[2] <= val + 100.0:
                    (st, eo, val, pp), p = again, q
            if cur is not None and val > own + OPT["FAR"]:
                continue
            mine, val = val, judged(st, eo, val)
            if cur is None or val <= cur - OPT["TEMP"] * max(0.02, 1 - it / span) * math.log(rnd()):
                cp, cb, cur, own, pairs, ceo = p, b, val, mine, pp, eo
            if best is None or val < best[0]:
                best = (val, st, eo, p, b)
        value, st, eo, p, b = best
        cut = max(st[loc[k]] for k in act if base[k]["call"][0] == "sca" and base[k]["step"] == stage) if stage < RO - 1 else 1e18
        learnt = {}
        for i, k in enumerate(act):
            prio[k], lean[k] = p[i], b[i]
            if base[k]["step"] == stage + 1:
                learnt[base[k]["key"]] = (p[i] - rest[0][k], b[i])
        for k, o in enumerate(base):
            if o["step"] == stage + 2 and o["key"] in learnt:
                prio[k], lean[k] = rest[0][k] + learnt[o["key"]][0], learnt[o["key"]][1]
        for i in sorted(range(n), key=lambda i: (st[i], i)):
            if st[i] > cut:
                break
            k, e = act[i], eo[i]
            fixed[k], engine[k] = True, e
            order.append(k)
            for m, cs in enumerate(models):
                t = max([free[m][e]] + [ends[m][j] if pp else dones[m][j] for j, pp in pre[k]]
                        + [dones[m][user[x]] for x in banks[k] if user[x] >= 0 and engine[user[x]] != e])
                ends[m][k] = free[m][e] = t + cs[k][0][e]
                dones[m][k] = ends[m][k] + cs[k][1]
            for x in banks[k]:
                user[x] = k
    last = {base[k]["gid"]: k for k in order if "gid" in base[k]}
    for k in order:
        o = base[k]
        if "gid" in o:
            c = o["call"][1]
            o["call"] = ("mm", c[:-1] + [c[-1][:4] + (last[o["gid"]] == k,)])
        o["eng"] = engine[k]
        if "alt" in o:
            o["call"], o["cost"] = o["alt"][o["eng"]]
        for b in o["banks"]:
            if b in last and base[last[b]]["eng"] != o["eng"]:
                o["deps"].add(last[b])
            last[b] = k
    return base, order, [round(max(d)) for d in dones]


_PLAN = []


def rank_program(g, core, T, topo):
    rank = T.rank_of(core)
    if rank is None:
        return
    if not _PLAN:
        _PLAN.extend(plan()[:2])
    ops, order = _PLAN
    nxt = T.cores[(rank + 1) % len(T.cores)]
    prv = T.cores[(rank - 1) % len(T.cores)]
    rid, pid, _ = topo.addr(nxt)
    nout = nin = 8
    mask = sum(1 << e for e in topo.engines(core, nxt)[:nout])
    assert len(topo.engines(prv, core)) >= nin and topo.may_write(core, nxt)
    Q = dict(v=g.vector, a=g.scalar, p=g.tensor, g=g, s=g.sync)

    def ap(r):
        if not isinstance(r, tuple):
            return r
        if len(r) == 6:
            return T[r[0]][r[5]:r[5] + 64, r[1]:r[2]]
        if len(r) == 5:
            g0, g1, a, b, step = r[4]
            return T[r[0]][:, g0:g1, a:b] if step == 1 else T[r[0]][:, g0:g1, a:b:step]
        if r[0] in W3:
            return T[r[0]][:, r[1] // W3[r[0]]:r[2] // W3[r[0]], :]
        return T[r[0]][:, r[1]:r[2]] if len(r) == 3 or r[3] == 1 else T[r[0]][:, r[1]:r[2]:r[3]]

    pos = {k: i for i, k in enumerate(order)}
    need, know, clock = set(), {e: {} for e in Q}, {}
    for k in order:
        o = ops[k]
        seen, o["w"] = know[o["eng"]], []
        for j in sorted(o["deps"], key=lambda j: -pos[j]):
            s = j if ops[j]["call"][0] in ("dma", "send") else ops[j]["eng"]
            if not inline(ops[j], o) and seen.get(s, -1) < pos[j]:
                o["w"].append(j)
                for x, v in clock[j].items():
                    seen[x] = max(seen.get(x, -1), v)
        need.update(o["w"])
        clock[k] = {} if o["call"][0] == "send" else dict(seen)
        clock[k][k if o["call"][0] in ("dma", "send") else o["eng"]] = pos[k]
    cnt = {e: 0 for e in "vapg"}
    token, sends = {}, 0
    for k in order:
        o = ops[k]
        q, c = Q[o["eng"]], o["call"]
        for j in o["w"]:
            q.wait_ge(T.sem[token[j][0]], token[j][1])
        f = c[0]
        if f == "dma":
            q.dma_start(ap(c[1]), ap(c[2])).then_inc(T.sem["d%d" % c[3]], 16)
            token[k] = ("d%d" % c[3], 16)
            continue
        if f == "send":
            g.remote_dma(ap(c[1]), ap(c[2]), T.sem[c[3]], T.sem.sent, pid, rid, mask)
            token[k] = (c[3], nin)
            sends += nout
            continue
        if f == "ts":
            ins = (q.tensor_scalar(ap(c[1]), ap(c[2]), ap(c[3]), None, c[5]) if c[6] is None
                   else q.tensor_scalar(ap(c[1]), ap(c[2]), ap(c[3]), ap(c[4]), c[5], c[6]))
        elif f == "tt":
            ins = q.tensor_tensor(ap(c[1]), ap(c[2]), ap(c[3]), c[4])
        elif f == "gtt":
            ins = q.tensor_tensor(ap(c[1]), ap(c[2]).indirect(ap(c[3])), ap(c[4]), c[5])
        elif f == "cp":
            ins = q.tensor_copy(ap(c[1]), ap(c[2]))
        elif f == "ms":
            ins = q.memset(ap(c[1]), c[2])
        elif f == "scan":
            ins = q.tensor_tensor_scan(ap(c[1]), ap(c[2]), ap(c[3]), c[4], c[5], c[6])
        elif f == "red":
            ins = q.tensor_reduce(ap(c[1]), ap(c[2]), AxisListType.X, ALU.add)
        elif f == "act":
            ins = q.activation(ap(c[1]), ap(c[2]), c[3], bias=ap(c[4]), scale=ap(c[5]), accum_out=ap(c[6]))
        elif f == "gat":
            src = ap(c[3]).indirect(ap(c[4]))
            if c[5]:
                ins = (q.tensor_scalar(ap(c[2]), src, ap(c[5]), None, ALU.add) if c[1] == "v"
                       else q.activation(ap(c[2]), src, AF.Identity, bias=ap(c[5])))
            else:
                ins = q.tensor_copy(ap(c[2]), src) if c[1] == "v" else q.activation(ap(c[2]), src, AF.Copy)
        elif f == "sca":
            ins = q.tensor_copy(ap(c[1]).indirect(ap(c[2])), ap(c[3]))
        elif f == "sel":
            ins = q.affine_select(ap(c[1]), ap(c[2]), c[3], c[6], c[7], c[4], c[5])
        elif f == "iota":
            ins = (q.iota(ap(c[1]), c[2], c[3], c[4]) if _S[c[1][0]][1] == I32
                   else q.iota(ap(c[1]), c[2], c[3], c[4], allow_small_or_imprecise_dtypes=True))
        else:
            for m in c[1]:
                ins = q.matmul(ap(m[0]), ap(m[1]), ap(m[2]), m[3], m[4])
        if k in need:
            cnt[o["eng"]] += 1
            ins.then_inc(T.sem["c" + o["eng"]], 1)
            token[k] = ("c" + o["eng"], cnt[o["eng"]])
    for k, (s, v) in token.items():
        if ops[k]["call"][0] == "dma":
            g.sync.wait_ge(T.sem[s], v)
    g.wait_ge(T.sem.sent, sends)
